import numpy as np, ml_dtypes
CORES = [48,51,52,55]
N = 4
BF = ml_dtypes.bfloat16
def gentries(a):
    return np.ascontiguousarray(a.reshape(8, 16, -1).transpose(0, 2, 1)).reshape(8, -1)
def gtable(e):
    e = np.asarray(e); return np.ascontiguousarray(e.reshape(8, -1, 16).transpose(0, 2, 1)).reshape(128, -1).astype(np.int32)
PN, NT, ND, L, V, ST, H = 4096, 1024, 1024, 256, 4, 3, 1
def parts(rng):
    prog = rng.integers(0, 16, (N, 8, 16, PN)); eff = rng.integers(0, 16, (N, 8, 16, ND)); x = rng.integers(0, 16, (N, 8, 16, L)); goal = rng.integers(0, 16, (N, 8, 16, L))
    wt = rng.integers(0, 256, (N, 8, 16)); team = rng.integers(0, PN, (N, 8, 16, NT)); start = rng.integers(0, NT, (N, 8, L))
    hub = rng.integers(0, NT, (8, 12)); gi = np.arange(8)[None, :, None]; u = rng.random((N, 8, PN))
    act = np.where(u < 0.4, rng.integers(0, NT, u.shape), np.where(u < 0.65, hub[gi, rng.integers(0, 12, u.shape)], NT + rng.integers(0, ND, u.shape)))
    start = np.where(rng.random(start.shape) < 0.3, hub[gi, rng.integers(0, 12, start.shape)], start)
    return [prog, act, team, eff, x, goal, wt, start]
def pack(p):
    prog, act, team, eff, x, goal, wt, start = p
    def b(a): return np.ascontiguousarray(a.reshape(N, 128, -1)).astype(np.float32).astype(BF)
    def i(a): return np.ascontiguousarray(a.reshape(N, 128, -1)).astype(np.int32)
    return {"prog": b(prog), "act": np.ascontiguousarray(act).astype(np.int32), "team": i(team), "eff": b(eff), "x0": b(x), "goal": b(goal), "wt": i(wt), "start": np.stack([gtable(a) for a in start])}
def setup_inputs(rng):
    p = parts(rng); prog, act, team, eff, x, goal, wt, start = p
    for q in range(N):
        for g in range(8):
            t = rng.permutation(NT)[:2]; j = rng.permutation(L)[:6]
            team[q, g][:, t] = 0; act[q, g, 0] = t[0]; start[q, g, j[:3]] = t[0]; start[q, g, j[3:]] = t[1]
    return pack(p)
def setup_inputs_corners(rng):
    p = parts(rng); prog, act, team, eff, x, goal, wt, start = p
    for q in range(N):
        for g in range(8):
            m = (g + q) % 8
            if m == 0: act[q, g] = rng.integers(0, NT, PN)
            elif m == 1: act[q, g] = NT + rng.integers(0, ND, PN); goal[q, g] = x[q, g]
            elif m == 2: act[q, g] = rng.choice(np.array([0, NT - 1]), PN); start[q, g] = rng.choice(np.array([0, NT - 1, 1, NT - 2]), L)
            elif m == 3:
                t = int(rng.choice(np.array([0, NT - 1, NT // 2]))); act[q, g] = t; start[q, g, ::2] = t
            elif m == 4:
                start[q, g] = NT - 1; team[q, g, :, NT - 1] = 0
                act[q, g] = np.where(rng.random(PN) < 0.5, rng.integers(1, 9, PN), NT + rng.integers(0, ND, PN)); act[q, g, 0] = 0
            elif m == 5:
                act[q, g] = NT + rng.integers(0, ND, PN); eff[q, g] = 7; goal[q, g] = np.abs(x[q, g] - 7); team[q, g] = rng.choice(np.array([0, 1, PN - 2, PN - 1]), (16, NT))
            elif m == 6: prog[q, g] = prog[q, g, :, :1].copy(); wt[q, g] = 255 * rng.integers(0, 2, 16)
            else: eff[q, g, :, ::2] = 0; wt[q, g] = 0; x[q, g, :, ::4] = 0; x[q, g, :, 1::4] = 15
    return pack(p)
def two(rng, hi, n):
    return hi * np.where(rng.random((N, 8, 1, n)) < 0.5, rng.integers(0, 2, (N, 8, 1, n)), rng.integers(0, 2, (N, 8, 16, n)))
def setup_inputs_ends(rng):
    prog = two(rng, 15, PN); eff = two(rng, 15, ND); x = two(rng, 15, L); goal = two(rng, 15, L); wt = 255 * rng.integers(0, 2, (N, 8, 16))
    team = np.where(rng.random((N, 8, 16, NT)) < 0.8, two(rng, PN - 1, NT), rng.integers(0, PN, (N, 8, 16, NT)))
    s = (N, 8, PN); far = np.where(rng.random(s) < 0.5, rng.choice(np.array([1, NT - 1, NT, NT + ND - 2]), s), rng.integers(0, NT + ND, s))
    act = np.where(rng.random(s) < 0.75, (NT + ND - 1) * rng.integers(0, 2, s), far)
    s = (N, 8, L); start = np.where(rng.random(s) < 0.8, (NT - 1) * rng.integers(0, 2, s), rng.integers(0, NT, s))
    a6 = act[:, 6]; a6[a6 == NT - 1] = NT
    start[:, 6] = np.where(rng.random((N, L)) < 0.75, 0, rng.integers(1, NT - 1, (N, L))); start[:, 6, L - 1] = NT - 1
    wt[:, 6] = 0; wt[:, 6, 1::2] = 255; wt[:, 6, 0] = 17; x[:, 6, ::2, L - 1] = 15; x[:, 6, 1::2, L - 1] = 0; goal[:, 6, :, L - 1] = x[:, 6, :, L - 1]
    team[:, 6, :, NT - 1] = PN - 1; act[:, 6, ((((PN - 1) * 511) >> 5) + PN - 1) & (PN - 1)] = NT + ND - 1; eff[:, 6, :, ND - 1] = 15
    c = np.arange(PN); c = int(np.flatnonzero((((c >> 5) + c) & (PN - 1)) == PN - 1)[0])
    wt[:, 7] = 255; prog[:, 7, :, 0] = 15; prog[:, 7, :, PN - 1] = 15; team[:, 7, :, NT - 1] = 0; team[:, 7, 0, NT - 1] = c
    act[:, 7, PN - 1] = NT + ND - 1; act[:, 7, 0] = NT; eff[:, 7, :, ND - 1] = 15; eff[:, 7, :, 0] = 0
    x[:, 7, :, L - 1] = 0; goal[:, 7, :, L - 1] = 15; x[:, 7, :, L - 2] = 0; goal[:, 7, :, L - 2] = 0; x[:, 7, :, 0] = 15; goal[:, 7, :, 0] = 0
    start[:, 7, L - 2:] = NT - 1; start[:, 7, 0] = NT - 1
    x[:, 5, :, L - 1] = 0; goal[:, 5] = x[:, 5]; goal[:, 5, :, L - 1] = 15; start[:, 5, L - 1] = NT // 2
    team[:, 5, :, NT // 2] = c; team[:, 5, :, 0] = 0; team[:, 5, :, NT - 1] = PN - 1
    act[:, 5, PN - 1] = 0; act[:, 5, 0] = NT - 1; act[:, 5, (((PN - 1) >> 5) + PN - 1) & (PN - 1)] = NT + ND - 1; eff[:, 5, :, ND - 1] = 15
    return pack([prog, act, team, eff, x, goal, wt, start])
def setup_inputs_full(rng):
    p = parts(rng); prog, act, team, eff, x, goal, wt, start = p
    keys = np.array([3, 7, 11, 15]); c = np.arange(PN)
    same = np.stack([np.flatnonzero(((13 * c + 97 * int(e) + 1) & (PN - 1)) == c)[:4] for e in keys])
    for q in range(N):
        for g in range(8):
            m = (0, 1, 2, 3, 4, 1, 3, 0)[g]; S = rng.permutation(NT); o = rng.permutation(PN - PN // 16); n = o + (o >> 5)
            if m == 0:
                act[q, g] = NT + rng.integers(0, ND, PN); start[q, g] = S[:L]; eff[q, g] = 0; eff[q, g, :8] = 2
                x[q, g, :8] = rng.integers(2 * V, 16, (8, L)); near = np.argsort(rng.random((8, L)), axis=0) < rng.permutation(np.arange(L) % 5)[None, :]
                goal[q, g, :8] = x[q, g, :8] - 2 * V + 2 * near; goal[q, g, :8, int(rng.integers(0, L))] = 15
            elif m == 1:
                wt[q, g] = 0; start[q, g] = S[:L]; x[q, g] = rng.integers(8, 16, (16, L)); goal[q, g] = 0; eff[q, g] = rng.integers(0, 8, (16, ND)); eff[q, g, 0] = np.maximum(eff[q, g, 0], 1)
                act[q, g, n[:4 * L]] = S[L + rng.integers(0, L, 4 * L)]; act[q, g, n[4 * L:8 * L]] = S[2 * L + rng.integers(0, L, 4 * L)]; act[q, g, n[8 * L:12 * L]] = NT + rng.integers(0, ND, 4 * L)
                team[q, g][:, S[:L]] = o[:4 * L].reshape(4, L)[rng.integers(0, 4, (16, L)), np.arange(L)[None, :]]
                team[q, g][:, S[L:2 * L]] = o[4 * L + rng.integers(0, 4 * L, (16, L))]; team[q, g][:, S[2 * L:3 * L]] = o[8 * L + rng.integers(0, 4 * L, (16, L))]
            elif m == 2:
                act[q, g] = NT + rng.integers(0, ND, PN); start[q, g] = S[:L]; goal[q, g] = x[q, g]; eff[q, g] = np.maximum(eff[q, g], 1)
            elif m == 3:
                h = L // 4; j = rng.permutation(L); a, b = j[:h], j[h:2 * h]; ab = j[:2 * h]
                start[q, g] = S[rng.integers(2 * h, NT, L)]; start[q, g, ab] = S[:2 * h]; x[q, g][:, ab] = 0; goal[q, g][:, ab] = 15
                d = rng.permutation(ND)[:2]; eff[q, g, :, d[0]] = 15; eff[q, g, :, d[1]] = 0; eff[q, g, int(rng.integers(0, 16)), d[1]] = 1
                prog[q, g, :, n[0]] = 15; prog[q, g, :, n[1]] = 15; prog[q, g, int(rng.integers(0, 16)), n[1]] = 14; prog[q, g][:, n[2:2 + h]] = 0
                act[q, g, n[0]] = NT + d[0]; act[q, g, n[1]] = NT + d[1]; act[q, g, n[2:2 + h]] = S[h:2 * h]
                team[q, g][:, S[:2 * h]] = o[0]; team[q, g][rng.integers(1, 16, h), S[:h]] = o[1]
                team[q, g][rng.integers(0, 16, h) * rng.permutation(np.arange(h) % 2), S[h:2 * h]] = o[2:2 + h]
            else:
                h = L // 2; j = np.sort(rng.permutation(L).reshape(h, 2), axis=1); w = rng.integers(0, 4, h)
                wt[q, g] = 0; wt[q, g, 0] = 1; act[q, g] = NT + rng.integers(0, ND, PN); eff[q, g] = np.maximum(eff[q, g], 1); eff[q, g, 0] = 0
                x[q, g, 0, j[:, 0]] = keys[w]; x[q, g, 0, j[:, 1]] = 2 * rng.integers(0, 8, h); goal[q, g] = x[q, g]
                start[q, g, j[:, 0]] = S[:h]; start[q, g, j[:, 1]] = S[:h]; team[q, g][:, S[:h]] = same[w[None, :], rng.integers(0, same.shape[1], (16, h))]
    return pack(p)
def setup_inputs_spread(rng):
    def v(n): return rng.integers(0, 16, (N, 8, 16, n)) >> rng.integers(0, 4, (N, 8, 1, n))
    def w(n, shape):
        k = rng.choice(np.array([0.5, 1.0, 2.0, 3.0]), (N, 8) + (1,) * (len(shape) - 2)); return np.minimum((n * rng.random(shape) ** k).astype(np.int64), n - 1)
    return pack([v(PN), w(NT + ND, (N, 8, PN)), w(PN, (N, 8, 16, NT)), v(ND), v(L), v(L), w(256, (N, 8, 16)), w(NT, (N, 8, L))])
def setup_inputs_ties(rng):
    p = parts(rng); prog, act, team, eff, x, goal, wt, start = p
    pat = rng.integers(0, 3, (N, 8, 16, 32)); prog = np.take_along_axis(pat, rng.integers(0, 32, (N, 8, 1, PN)), 3)
    eff = rng.integers(0, 3, eff.shape); x = rng.integers(0, 3, x.shape); goal = rng.integers(0, 3, goal.shape)
    team[:, :, 8:, ::2] = team[:, :, :8, ::2]
    return pack([prog, act, team, eff, x, goal, wt, start])
def check_inputs(d):
    bad = []
    for k, lo, hi in (("prog", 0, 15), ("act", 0, NT + ND - 1), ("team", 0, PN - 1), ("eff", 0, 15), ("x0", 0, 15), ("goal", 0, 15), ("wt", 0, 255), ("start", 0, NT - 1)):
        a = np.asarray(d[k]).astype(np.float64)
        if not (np.min(a) >= lo and np.max(a) <= hi): bad.append("range of " + k)
        elif np.any(a != np.floor(a)): bad.append("whole numbers in " + k)
    return bad
def nums(a, n):
    return a.astype(np.float32).astype(np.int32).reshape(N, 8, 16, n)
def reference(prog, act, team, eff, x0, goal, wt, start):
    P = nums(prog, PN); D = nums(eff, ND); x = nums(x0, L); z = nums(goal, L); w = nums(wt, 1)
    T = team.astype(np.int64).reshape(N, 8, 16, NT); a = act.astype(np.int64)
    s = np.stack([gentries(t) for t in start]).astype(np.int64); A = np.zeros((N, 8), np.int64)
    for v in range(V):
        nx = np.zeros_like(x); ns = np.zeros_like(s)
        for r in range(N):
            q = (r + H * v) % N; X = x[r]; Y = X; cur = s[r]; trail = [cur]
            e = np.add.reduce(w[q] * X, axis=1).astype(np.int64) & 255
            go = np.ones((8, L), bool); won = np.zeros((8, L), bool); lastk = np.zeros((8, L), np.int64); lastt = np.zeros((8, L), np.int64); first = lastk
            for i in range(ST):
                c = np.take_along_axis(T[q], cur[:, None, :], 2)
                n = (((c * (2 * e[:, None, :] + 1)) >> 5) + c) & (PN - 1)
                d = np.take_along_axis(P[q], n.reshape(8, 1, 16 * L), 2).reshape(8, 16, 16, L) - X[:, :, None, :]
                score = np.add.reduce(np.abs(d), axis=1)
                ak = np.take_along_axis(a[q], n.reshape(8, 16 * L), 1).reshape(8, 16, L)
                bar = np.zeros((8, 16, L), bool)
                for t in trail: bar = bar | (ak == t[:, None, :])
                k = np.argmin(np.where(bar, 1000000, score), axis=1)
                ok = go & ~np.all(bar, axis=1)
                an = np.take_along_axis(ak, k[:, None, :], 1)[:, 0]
                if i == 0: first = np.take_along_axis(n, k[:, None, :], 1)[:, 0]
                lastk = np.where(ok, k, lastk); lastt = np.where(ok, cur, lastt); won = won | ok
                fin = ok & (an >= NT); j = np.where(fin, an - NT, 0)
                Y = np.where(fin[:, None, :], np.abs(X - np.take_along_axis(D[q], j[:, None, :], 2)), Y)
                go = ok & ~fin; cur = np.where(go, an, cur); trail.append(cur)
            old = np.add.reduce(np.abs(X - z[r]), axis=1); new = np.add.reduce(np.abs(Y - z[r]), axis=1)
            good = new < old - (A[q] & 7)[:, None]
            up = good & (cur != s[r]); fail = won & ~good
            for g in range(8):
                j = np.flatnonzero(up[g]); u, ix = np.unique(first[g, j], return_index=True); a[q, g, u] = cur[g, j[ix]]
                j = np.flatnonzero(fail[g]); u, ix = np.unique(lastt[g, j], return_index=True); j = j[ix]; k = lastk[g, j]
                T[q, g, k, u] = (13 * T[q, g, k, u] + 97 * e[g, j] + 1) & (PN - 1)
            A[q] = A[q] + np.add.reduce(good.astype(np.int64), axis=1)
            nx[r] = Y; ns[r] = cur
        x, s = nx, ns
    return {"yteam": T.reshape(N, 128, NT).astype(np.float32), "yact": a.astype(np.float32), "yx": x.reshape(N, 128, L).astype(np.float32).astype(BF)}

@@ -1,0 +1,690 @@
+import numpy as np
+from concourse.bass import DstId, RemoteDMATransfer
+from concourse.mybir import AluOpType as ALU, AxisListType, ActivationFunctionType as ACT
+
+NV = 4
+ZC, DC, TC, DT, WS, WN = 4096, 4112, 4240, 5264, 5392, 6288
+VCH, SCH = 4, 2
+XV = 4
+PENV = (1, 1, 1)
+MNV = 4
+ROUNDS = 6
+LEAD, SEED, NOISE = 5.0, 1, 0.3
+F, B, I, U = "float32", "bfloat16", "int32", "uint16"
+
+
+def sb(n, d):
+    return ("sbuf", [128, n], d)
+
+
+SCRATCH = {
+    "Y": sb(1280, F), "cA": sb(2048, F), "goals": sb(1024, B), "land": sb(6 * 144, F), "snd": sb(6 * 144, F),
+    "landb": sb(256, B), "xb": sb(256, B), "xn": sb(256, B), "wtI": sb(8, I), "stI": sb(16, I), "actI": sb(512, I),
+    "ci": sb(16, I), "cf": sb(24, F), "io2": sb(128, F), "io3": sb(128, F), "io4": sb(128, F), "idn": sb(128, F),
+    "blk": sb(128, F), "blk256": sb(128, F), "blk2": sb(128, F), "blk8": sb(8, F), "msk": sb(128, F), "rst": sb(128, F),
+    "PA": sb(128, F), "PB": sb(128, F), "nI256": sb(128, F), "nI23": sb(128, B), "pI23": sb(128, B),
+    "Wm": sb(8, B), "Wp": sb(32, B), "Ws": sb(128, B), "Wx": sb(128, B), "We": sb(256, B),
+    "WN": sb(144, B), "WD": sb(144, B), "ones": sb(128, B), "Cm": sb(128, B), "Jm": sb(128, B), "m8": sb(8, B),
+    "OH": sb(32, F), "KP": sb(32, F), "l15": sb(8, U), "l1": sb(8, U),
+    "cj": sb(8, F), "cdum": sb(8, F), "ctop": sb(8, F), "cb": sb(8, F), "cnb": sb(8, F),
+    "cK": sb(256, F), "mK": sb(256, I), "nK": sb(256, I), "n16": sb(256, U), "TK": sb(768, B), "pen": sb(768, B),
+    "pab": sb(768, B), "Z": sb(256, F), "E": sb(256, F), "eI": sb(256, I), "eM": sb(256, I), "NK": sb(256, B),
+    "ad": sb(256, B), "EQ": sb(1152, F), "kp": sb(256, F), "aK": sb(256, F), "bK": sb(256, F), "NW": sb(512, F),
+    "BI1": sb(16, I), "BI2": sb(16, I), "a1": sb(16, I), "a2": sb(16, I), "A0": sb(16, F), "off": sb(48, U),
+    "A0p": sb(16, F), "p2": sb(16, B), "p3": sb(16, B), "kk1": sb(16, I), "q1": sb(16, F), "q2": sb(16, F),
+    "q3": sb(16, F), "q4": sb(16, F), "i2": sb(16, I),
+    "Bw2": sb(16, I), "lt0": sb(16, F), "lt2": sb(16, I), "Bw": sb(16, I), "aw": sb(16, I), "le": sb(16, U),
+    "lt": sb(16, I), "P0": sb(48, I), "P1": sb(48, F), "Df": sb(48, F), "Dg": sb(48, F),
+    "Sel": sb(48, F), "ls": sb(48, U), "l2": sb(16, U), "thr": sb(16, F), "good": sb(16, F), "nb": sb(16, F),
+    "mn": sb(16, F), "acc": sb(16, F), "lfv": sb(16, F), "lf": sb(32, U),
+    "cnt": sb(8, F), "Aa": sb(8, I), "A7": sb(8, I), "A7f": sb(8, F),
+}
+for s_ in "01":
+    for nm, n_, d_ in (("prg", 4096, B), ("W", WN, F), ("ef", 2048, B), ("teamI", 1024, I), ("Gm", 2048, B),
+                       ("Gp", 2048, B), ("xr", 2048, B)):
+        SCRATCH[nm + s_] = sb(n_, d_)
+    for nm in ("pK", "pT", "pU", "pE"):
+        SCRATCH[nm + s_] = ("psum", [128, 512], F)
+PSUM = ("pK0", "pK1", "pT0", "pT1", "pU0", "pU1", "pE0", "pE1")
+
+NDMA = 70
+SEMAPHORES = ["cV", "cS", "cP", "cG", "sent", "gin"] + ["d%d" % i for i in range(NDMA)] + ["r%d" % i for i in range(8)]
+
+CY = 1.04e-3
+GA, SC = 1.56, 3.8
+WAKE = 0.12
+BW = 200000.0
+
+
+def build_ops(g, T, topo, core, rank):
+    ops = []
+    N = len(T.cores)
+    V, S, P = g.vector, g.scalar, g.tensor
+
+    def add(eng, dur, fn, r, w, kind="c", lat=0.0, extra=None):
+        ops.append({"e": eng, "d": dur, "f": fn, "r": list(r), "w": list(w), "k": kind, "lat": lat, "x": extra})
+
+    def cyc(n):
+        return max(64, n) * CY + 0.02
+
+    def wd(ap):
+        return int(ap.shape[1])
+
+    def ts(out, in0, s1, s2, o0, o1, r, w, c=1.0):
+        if o1 is None:
+            add("V", cyc(wd(out) * c), lambda: V.tensor_scalar(out, in0, s1, None, o0), r, w)
+        else:
+            add("V", cyc(wd(out) * c), lambda: V.tensor_scalar(out, in0, s1, s2, o0, o1), r, w)
+
+    def tt(out, a, b, op, r, w, c=2.0):
+        add("V", cyc(wd(out) * c), lambda: V.tensor_tensor(out, a, b, op), r, w)
+
+    def cp(out, a, r, w, c=1.0):
+        add("V", cyc(wd(out) * c), lambda: V.tensor_copy(out, a), r, w)
+
+    def gtt(out, win, off, b, op, r, w):
+        add("V", 0.06 + wd(out) * GA * CY, lambda: V.tensor_tensor(out, win.indirect(off), b, op), r, w)
+
+    def ms(ap, val, w, c=1.0):
+        add("V", cyc(wd(ap) * c), lambda: V.memset(ap, val), [], w)
+
+    def act(out, a, fn, r, w, bias=0.0, scale=1.0, acc=None):
+        if acc is None:
+            add("S", cyc(wd(out)) + 0.04, lambda: S.activation(out, a, fn, bias=bias, scale=scale), r, w)
+        else:
+            add("S", cyc(wd(out)) + 0.06, lambda: S.activation(out, a, fn, bias=bias, scale=scale, accum_out=acc), r, w)
+
+    def sga(out, win, off, r, w, scale=1.0):
+        add("S", 0.08 + wd(out) * GA * CY, lambda: S.activation(out, win.indirect(off), ACT.Copy, scale=scale), r, w)
+
+    def mm(out, l, rh, st, sp, r, w, f32=False):
+        add("P", max(64, wd(out)) * (4 if f32 else 1) * CY, lambda: P.matmul(out, l, rh, st, sp), r, w)
+
+    def dma(q, out, a, nbytes, r, w):
+        qq = {"Y": g.sync, "S": g.scalar, "G": g}[q]
+        add(q, 0.1, lambda: qq.dma_start(out, a), r, w, kind="dma", lat=nbytes)
+
+    def iota(out, pat, base, cm, w, flt=True):
+        if flt:
+            add("G", 0.15 + 2 * wd(out) * CY, lambda: g.iota(out, pat, base, cm, allow_small_or_imprecise_dtypes=True), [], w)
+        else:
+            add("G", 0.15 + 2 * wd(out) * CY, lambda: g.iota(out, pat, base, cm), [], w)
+
+    def split_mask(dst, part, parts):
+        en = topo.engines(core, dst)
+        n = len(en) // parts
+        m = 0
+        for e in en[part * n:(part + 1) * n]:
+            m |= 1 << e
+        return m, n
+
+    AND, SHR = ALU.bitwise_and, ALU.logical_shift_right
+    MUL, ADD, SUB, MAX, MIN, EQ, LT = ALU.mult, ALU.add, ALU.subtract, ALU.max, ALU.min, ALU.is_equal, ALU.is_lt
+    CPY, IDN, ABS, RELU = ACT.Copy, ACT.Identity, ACT.Abs, ACT.Relu
+    Y, cA, ci, cf = T.Y, T.cA, T.ci, T.cf
+
+    def loads(s):
+        H = str(s)
+        R = slice(64 * s, 64 * s + 64)
+        q = "S" if s == 0 else "Y"
+        after = [] if s == 0 else ["cA20"]
+        HV = [(h, slice(64 * h, 64 * h + 64), H + "ab"[h]) for h in range(2)]
+        for h, D, t in HV:
+            dma(q, T.actI[D, 256 * s:256 * s + 256], T.act[4 * s:4 * s + 4, :], 65536, [], ["actI" + t])
+        for h, D, t in HV:
+            dma(q, T.xb[D, 128 * s:128 * s + 128], T.x0[R, 128 * h:128 * h + 128], 16384, [], ["xb" + t])
+            dma(q, T.wtI[D, 4 * s:4 * s + 1], T.wt[R, :], 4096, [], ["wtI" + t])
+            dma(q, T.stI[D, 8 * s:8 * s + 8], T.start[R, 8 * h:8 * h + 8], 4096, [], ["stI" + t])
+        for c in range(4):
+            for h, D, t in HV:
+                dma("Y", T["prg" + H][D, 1024 * c:1024 * c + 1024], T.prog[R, 1024 * c:1024 * c + 1024], 131072, after,
+                    ["prg%d%s" % (c, t)])
+                ops[-1]["soft"] = c + h > 0
+        for h, D, t in HV:
+            dma("Y", T["teamI" + H][D, :], T.team[R, :], 262144, after, ["teamI" + t])
+            ops[-1]["soft"] = True
+
+    for s in range(2):
+        for h in range(2):
+            dma("G", T.goals[64 * h:64 * h + 64, 128 * s:128 * s + 128], T.goal[64 * s:64 * s + 64, 128 * h:128 * h + 128],
+                16384, [], ["goal0%d%s" % (s, "ab"[h])])
+
+    def send_goals():
+        tr = []
+        for v in range(1, NV):
+            dst = T.cores[(rank + v) % N]
+            rid, pid, se = topo.addr(dst)
+            m, n = split_mask(dst, v, 4)
+            tr.append(RemoteDMATransfer(dst_ids=[DstId(rid=rid, pnc=pid)], dma_engine_mask=m, remote_sem=T.sem.gin,
+                                        src=T.goals[:, 0:256], dst=T.goals[:, 256 * v:256 * v + 256]))
+        return g.remote_dma_fused(tr, local_sem=T.sem.sent)
+    ngo = sum(split_mask(T.cores[(rank + v) % N], v, 4)[1] for v in range(1, NV))
+    add("G", 1.5, send_goals, ["goal00a", "goal00b", "goal01a", "goal01b"], ["goalx"], kind="rem", lat=2.5, extra=("gin", ngo))
+
+    iota(ci[:, 0:1], [[0, 1]], 0, 1, ["ci0"], False)
+    iota(T.E[:, 0:128], [[1, 8], [0, 16]], 0, 0, ["E0"])
+    iota(T.io2[:], [[0, 8], [1, 16]], 0, 0, ["io2"])
+    iota(T.io3[:], [[1, 128]], 0, 0, ["io3"])
+    iota(T.io4[:], [[0, 2], [1, 64]], 0, 0, ["io4"])
+    iota(T.eM[:], [[1, 256]], 0, 256, ["eM0", "eM1"], False)
+    ts(ci[:, 4:5], ci[:, 0:1], 15, None, AND, None, ["ci0"], ["ci4"])
+    ts(ci[:, 8:9], ci[:, 0:1], 4, None, SHR, None, ["ci0"], ["ci8"])
+    cp(cf[:, 0:9:4], ci[:, 0:9:4], ["ci0", "ci4", "ci8"], ["cf"])
+    pc, rc, gc_ = cf[:, 0:1], cf[:, 4:5], cf[:, 8:9]
+    ts(T.blk[:], T.E[:, 0:128], gc_, None, EQ, None, ["E0", "cf"], ["blk"])
+    ts(T.msk[:], T.io2[:], rc, None, EQ, None, ["io2", "cf"], ["msk"])
+    ts(T.idn[:], T.io3[:], pc, None, EQ, None, ["io3", "cf"], ["idn"])
+    ts(T.rst[:], T.io2[:], 0.5, None, ALU.is_gt, None, ["io2"], ["rst"])
+    ts(T.PA[:], T.io4[:], pc, None, EQ, None, ["io4", "cf"], ["PA"])
+    ts(T.PB[:], T.io4[:], 64.0, pc, ADD, EQ, ["io4", "cf"], ["PB"])
+    tt(T.blk2[:, 0:64], T.blk[:, 0:64], T.blk[:, 64:128], ADD, ["blk"], ["blk2a"])
+    act(T.blk2[:, 64:128], T.blk2[:, 0:64], CPY, ["blk2a"], ["blk2b"])
+    act(T.Wx[:], T.blk[:], CPY, ["blk"], ["Wx"], scale=32768.0)
+    act(T.blk256[:], T.blk[:], CPY, ["blk"], ["blk256"], scale=256.0)
+    act(T.blk8[:], T.blk[:, 0:128:16], CPY, ["blk"], ["blk8"])
+    act(T.Wm[:], T.blk[:, 0:128:16], CPY, ["blk"], ["Wm"], scale=-65536.0)
+    act(T.nI256[:], T.idn[:], CPY, ["idn"], ["nI256"], scale=-256.0)
+    act(T.nI23[:], T.idn[:], CPY, ["idn"], ["nI23"], scale=-8388608.0)
+    act(T.pI23[:], T.idn[:], CPY, ["idn"], ["pI23"], scale=8388608.0)
+    m = T.msk
+    tt(cf[:, 1:2], m[:, 0:1], m[:, 1:2], ADD, ["msk"], ["r01"])
+    tt(cf[:, 2:3], m[:, 3:4], m[:, 4:5], ADD, ["msk"], ["r34"])
+    ts(cf[:, 3:4], m[:, 2:3], 32768.0, cf[:, 1:2], MUL, SUB, ["msk", "r01"], ["rp"])
+    act(T.Wp[:, 0:8], T.blk8[:], CPY, ["blk8", "rp"], ["Wp0"], scale=cf[:, 3:4])
+    for j in range(1, 4):
+        act(T.Wp[:, 8 * j:8 * j + 8], T.blk8[:], CPY, ["blk8", "r01"], ["Wp%d" % j], scale=cf[:, 1:2])
+    WP = ["Wp0", "Wp1", "Wp2", "Wp3"]
+    ts(T.Ws[:], T.blk[:], cf[:, 2:3], -1.0, MUL, MUL, ["blk", "r34"], ["Ws"])
+    ms(T.WN[:], 0.0, ["WN"], 0.5)
+    ms(T.WD[:], 0.0, ["WD"], 0.5)
+    act(T.WN[:, 15:143:16], T.blk8[:], CPY, ["blk8", "r34"], ["WN"], scale=cf[:, 2:3])
+    act(T.WD[:, 15:143:16], T.blk8[:], CPY, ["blk8"], ["WD"])
+    ms(T.ones[:], 1.0, ["ones"], 0.5)
+    ms(T.m8[:], -0.0625, ["m8"], 0.5)
+    idn = T.idn
+    ts(cf[:, 5:6], idn[:, 0:1], 241.0 * 32768.0, None, MUL, None, ["idn"], ["k0"])
+    ts(cf[:, 6:7], idn[:, 2:3], 7.0, cf[:, 5:6], MUL, ADD, ["idn", "k0"], ["k1"])
+    ts(cf[:, 7:8], idn[:, 1:2], -2048.0, None, MUL, None, ["idn"], ["k2"])
+    ts(T.Z[:, 0:128], T.io2[:], -16.0, cf[:, 7:8], ADD, MUL, ["io2", "k2"], ["Z0"])
+    ts(T.Cm[:], T.Z[:, 0:128], cf[:, 6:7], None, ADD, None, ["Z0", "k1"], ["Cm"])
+    act(T.Jm[:], T.io3[:], CPY, ["io3", "idn"], ["Jm"], scale=idn[:, 0:1])
+    ts(T.Z[:, 128:144], T.io3[:, 0:16], -1.0, 15.0, MUL, ADD, ["io3"], ["Z1"])
+    ts(T.OH[:, 0:16], T.Z[:, 128:144], rc, None, EQ, None, ["Z1", "cf"], ["OHa"])
+    ts(T.OH[:, 16:32], T.io3[:, 0:16], 0.0, cf[:, 1:2], MUL, ADD, ["io3", "r01"], ["OHb"])
+    act(T.KP[:], T.OH[:], IDN, ["OHa", "OHb"], ["KP"], bias=1.0, scale=-1.0)
+    ts(T.l15[:], T.io3[:, 0:8], 16.0, 15.0, MUL, ADD, ["io3"], ["l15"])
+    cp(T.l1[:], T.io3[:, 0:8], ["io3"], ["l1"])
+    ts(T.cj[:], T.io3[:, 0:8], 16.0, rc, MUL, ADD, ["io3", "cf"], ["cj"])
+    act(T.cdum[:], T.cj[:], IDN, ["cj"], ["cdum"], bias=float(DC))
+    act(T.ctop[:], T.cj[:], IDN, ["cj"], ["ctop"], bias=float(DT))
+    act(T.cb[:], T.cj[:], IDN, ["cj"], ["cb"], bias=15.0, scale=16.0)
+    act(T.cnb[:], T.cj[:], IDN, ["cj"], ["cnb"], bias=-0.25, scale=1.0 / 256.0)
+    ms(T.Aa[:], 0, ["Aa0", "Aa1"])
+    ms(T.A7f[:], 0.0, ["A7f0", "A7f1"])
+    ts(T.eI[:], T.eM[:], 4095, None, AND, None, ["eM0", "eM1"], ["eI0", "eI1"])
+    cp(cA[:, 1536:1792], T.eI[:], ["eI0", "eI1"], ["cN"])
+    act(T.pen[:, 0:256], cA[:, 1536:1792], CPY, ["cN"], ["pen0"])
+    tt(cA[:, 1792:2048], cA[:, 1536:1792], T.pen[:, 0:256], SUB, ["cN", "pen0"], ["cN8"])
+    act(cA[:, 1792:2048], cA[:, 1792:2048], IDN, ["cN8"], ["cN8"], bias=8.0)
+
+    def k_to_l(out, Wb, src, c0, first, lastf, r, w):
+        for rr in range(16):
+            mm(out, Wb[:, 15 - rr:143 - rr], src[:, c0 + rr:c0 + 128:16], first and rr == 0, lastf and rr == 15, r, w)
+
+    nxt = T.cores[(rank + 1) % N]
+    nrid, npid, nse = topo.addr(nxt)
+    nmask, neng = split_mask(nxt, 0, 1)
+    nsend = [0]
+
+    def send(out, src, r, w):
+        sem = "r%d" % nsend[0]
+        nsend[0] += 1
+        add("G", 1.0, lambda: g.remote_dma(out, src, T.sem[sem], T.sem.sent, npid, nrid, nmask), r, w,
+            kind="rem", lat=2.0, extra=(sem, neng))
+
+    def stream(s):
+        H = str(s)
+        loads(s)
+
+        def k(*names):
+            return [n + H for n in names]
+
+        def ab(*names):
+            return [n + H + x for n in names for x in "ab"]
+        W, prg, ef, Gm, Gp, xr = T["W" + H], T["prg" + H], T["ef" + H], T["Gm" + H], T["Gp" + H], T["xr" + H]
+        pK, pT, pU, pE = T["pK" + H], T["pT" + H], T["pU" + H], T["pE" + H]
+        K = slice(128 * s, 128 * s + 128)
+        L = slice(8 * s, 8 * s + 8)
+        c4 = slice(4 * s, 4 * s + 1)
+        PAY = k("W0", "W1", "W2", "W4")
+        FILL = k("Wfa", "Wfb", "Wfc", "Wfd")
+        WALL = PAY + k("Wt", "Wz", "Wx")
+        PRG = ab("prg0", "prg1", "prg2", "prg3")
+        XB = ab("xb")
+        xb = T.xb[:, K]
+
+        if s == 0:
+            iota(W[:, 0:1024], [[1, 1024]], 0, 0, k("Wfa"))
+            act(W[:, 1024:2048], W[:, 0:1024], IDN, k("Wfa"), k("Wfb"), bias=1024.0)
+            act(W[:, 2048:3072], W[:, 0:1024], IDN, k("Wfa"), k("Wfc"), bias=2048.0)
+            iota(W[:, 3072:4096], [[1, 1024]], 3072, 0, k("Wfd"))
+        else:
+            for j, t in enumerate(FILL):
+                iota(W[:, 1024 * j:1024 * j + 1024], [[1, 1024]], 1024 * j, 0, [t])
+        ms(W[:, ZC:TC], 0.0, k("Wz"))
+        if s == 0:
+            ms(W[:, DT:WN], 0.0, k("Wx"))
+        else:
+            iota(W[:, DT:WN], [[0, WN - DT]], 0, 0, k("Wx"))
+        ms(ef[:, 0:1024], 0.0, k("ef0"), 0.5)
+        cp(W[:, TC:DT], T["teamI" + H][:], ab("teamI"), k("Wt"))
+        c0 = 768 * s
+        cp(cA[:, c0:c0 + 256], T.actI[:, 256 * s:256 * s + 256], ab("actI"), k("cA0"))
+        hb = T.pab[:, 384 * s:384 * s + 256]
+        act(hb, cA[:, c0:c0 + 256], CPY, k("cA0"), k("pab"))
+        tt(cA[:, c0 + 256:c0 + 512], cA[:, c0:c0 + 256], hb, SUB, k("cA0", "pab"), k("cA1"))
+        act(cA[:, c0 + 256:c0 + 512], cA[:, c0 + 256:c0 + 512], IDN, k("cA1"), k("cA1"), bias=8.0)
+        for q in range(16):
+            mm(pU[:, 0:256], T.WD[:, 15 - q:143 - q], prg[:, 256 * q:256 * q + 256], q == 0, q == 15,
+               ["WD"] + ab("prg%d" % (q // 4)), k("pU"))
+        act(cA[:, c0 + 512:c0 + 768], pU[:, 0:256], CPY, k("pU"), k("cA2"))
+        for row, a, tok in ((4, 1792, "cN8"), (0, c0, "cA0" + H), (1, c0 + 256, "cA1" + H), (2, c0 + 512, "cA2" + H)):
+            dma("Y", W[row:128:16, 0:4096], cA[:, a:a + 256], 131072, [tok] + FILL, k("W%d" % row))
+        for h in range(2):
+            dma("Y", ef[64 * h:64 * h + 64, 1024:2048], T.eff[64 * s:64 * s + 64, :], 131072, k("cA2"), ["ef1" + H + "ab"[h]])
+        if s == 0:
+            iota(Y[:, 128:1152], [[0, 1024]], 0, 0, ["Yf"])
+            dma("Y", Y[0:128:16, 128:1152], W[3:128:16, 0:1024], 32768, ["Yf", "Wfa0", "W40"], ["Y0"])
+            dma("Y", Y[1:128:16, 128:1152], W[4:128:16, 0:1024], 32768, ["Yf", "W40"], ["Y1"])
+        cp(cf[:, 12 + s:13 + s], T.wtI[:, c4], ab("wtI"), k("wf"))
+        act(T.We[:, K], T.blk[:], CPY, ["blk"] + k("wf"), k("We"), scale=cf[:, 12 + s:13 + s])
+        ts(T.P0[:, 24 * s + 8:24 * s + 16], T.cj[:], 1024.0 * s, None, ADD, None, ["cj"], k("P0b"))
+        ms(T.P1[:, 24 * s + 16:24 * s + 24], 16.0, k("P1c"))
+
+        def distance(x, xt, goal, gt):
+            mm(pE[:, 0:128], T.pI23[:], x, True, False, ["pI23"] + xt, k("pE"))
+            mm(pE[:, 0:128], T.nI23[:], goal, False, True, ["nI23"] + gt, k("pE"))
+            act(T.ad[:, K], pE[:, 0:128], ABS, k("pE"), k("ad"), scale=1.0 / 8388608.0)
+            k_to_l(pU[:, 24:32], T.WD, T.ad, 128 * s, True, True, ["WD"] + k("ad"), k("pU"))
+        ts(T.A0[:, L], T.stI[:, L], -1.0, 1023.0, MUL, ADD, ab("stI"), k("A0"))
+
+        for v in range(NV):
+            last = v == NV - 1
+            if v > 0:
+                b0 = 144 * (2 * (v - 1) + s)
+                tok = ["land%d_%d" % (v - 1, s)]
+                act(xb, T.land[:, b0:b0 + 128], CPY, tok, XB)
+                A0, a0t = T.land[:, b0 + 128:b0 + 136], tok
+                ts(T.off[:, L], A0, -1.0, 1023.0, MUL, ADD, tok, k("offa"))
+                ts(T.thr[:, L], T.land[:, b0 + 136:b0 + 144], T.A7f[:, c4], None, SUB, None, tok + k("A7f"), k("thr"))
+            else:
+                A0, a0t = T.A0[:, L], k("A0")
+                cp(T.off[:, L], T.stI[:, L], ab("stI"), k("offa"))
+            mm(pE[:, 128:256], T.We[:, K], xb, True, True, k("We") + XB, k("pE"))
+            cp(T.eI[:, K], pE[:, 128:256], k("pE"), k("eI"))
+            ts(T.eM[:, K], T.eI[:, K], 255, None, AND, None, k("eI"), k("eM"))
+            uu, ut = T.cK[:, K], k("uK")
+            ts(uu, T.eM[:, K], 2.0, 33.0, MUL, ADD, k("eM"), ut)
+            XR = k(*["xr%d_" % j for j in range(16)])
+            for j in range(16):
+                if j < XV:
+                    cp(xr[:, j:2048:16], xb, XB, [XR[j]], 0.5)
+                else:
+                    act(xr[:, j:2048:16], xb, CPY, XB, [XR[j]])
+            act(Y[:, 1152 * s:1152 * s + 128], uu, IDN, ut, k("Ye"), bias=-1599.5, scale=48.5)
+            act(T.A0p[:, L], A0, IDN, a0t, k("A0p"), bias=1024.0)
+
+            for st in range(3):
+                nt = st + 1
+                of = T.off[:, 16 * st + 8 * s:16 * st + 8 * s + 8]
+                oft = k("off" + "abc"[st])
+                TKc = 384 * s
+                sga(T.TK[:, TKc + 128 * st:TKc + 128 * st + 128], W[:, 0:2048], of, oft + PAY, k("TK%d" % st))
+                gtt(T.mK[:, K], W[:, TC:WN], of, T.cK[:, K], MUL, oft + k("Wt", "Wx", "uK"), k("mK"))
+                ts(T.nK[:, K], T.mK[:, K], 5, 4095, SHR, AND, k("mK"), k("nK"))
+                cp(T.n16[:, K], T.nK[:, K], k("nK"), k("n16"))
+                GM = k(*["Gm%d_" % c for c in range(VCH)])
+                GP = k(*["Gp%d_" % c for c in range(SCH)])
+                w = 128 // VCH
+                for c in range(VCH):
+                    gtt(Gm[:, 16 * w * c:16 * w * (c + 1)], prg[:], T.n16[:, 128 * s + w * c:128 * s + w * (c + 1)],
+                        xr[:, 16 * w * c:16 * w * (c + 1)], MAX, k("n16") + PRG + XR, [GM[c]])
+                    ops[-1]["soft"] = c > 0
+                w = 128 // SCH
+                for c in range(SCH):
+                    sga(Gp[:, 16 * w * c:16 * w * (c + 1)], W[:, 0:4096], T.n16[:, 128 * s + w * c:128 * s + w * (c + 1)],
+                        k("n16") + PAY, [GP[c]])
+                    ops[-1]["soft"] = c > 0
+                for t in range(nt):
+                    mm(pU[:, 128 + 128 * t:256 + 128 * t], T.TK[:, TKc + 128 * t:TKc + 128 * t + 128], T.Ws[:],
+                       t == 0, False, k("TK%d" % t) + ["Ws"], k("pU"))
+                for j in range(16):
+                    mm(pU[:, 128 + j:128 * (nt + 1):16], Gp[:, j:2048:16], T.Wp[:, 8:8 * (nt + 1)], False, j == 15, GP + WP, k("pU"))
+                pen = T.pen[:, TKc:TKc + 128 * nt]
+                if PENV[st]:
+                    ts(pen, pU[:, 128:128 + 128 * nt], 0.0, None, EQ, None, k("pU"), k("pen"))
+                else:
+                    pab = T.pab[:, TKc:TKc + 128 * nt]
+                    act(pab, pU[:, 128:128 + 128 * nt], ABS, k("pU"), k("pab"))
+                    act(pen, pab, RELU, k("pab"), k("pen"), bias=1.0, scale=-1.0)
+                mm(pK[:, 0:128], T.ones[:], T.Cm[:], True, False, ["ones", "Cm"], k("pK"))
+                for j in range(16):
+                    mm(pK[:, j:128:16], Gp[:, j:2048:16], T.Wp[:, 0:8], False, False, GP + WP, k("pK"))
+                for t in range(nt):
+                    mm(pK[:, 0:128], T.nI23[:], T.pen[:, TKc + 128 * t:TKc + 128 * t + 128], False, False,
+                       ["nI23"] + k("pen"), k("pK"))
+                for j in range(16):
+                    mm(pK[:, j:128:16], Gm[:, j:2048:16], T.Wm[:], False, False, GM + ["Wm"], k("pK"))
+                mm(pK[:, 0:128], xb, T.Wx[:], False, True, XB + ["Wx"], k("pK"))
+                add("V", cyc(128), lambda: V.tensor_tensor_scan(T.Z[:, K], T.rst[:], pK[:, 0:128], 0.0, MUL, MAX),
+                    ["rst"] + k("pK"), k("Z"))
+                gtt(T.E[:, K], T.Z[:, K], T.l15[:], T.msk[:], MUL, k("Z") + ["l15", "msk"], k("E"))
+                ps = pT[:, 0:8]
+                if st > 0:
+                    mm(ps, T.nI23[:], (T.p2, T.p3)[st - 1][:, L], True, False, ["nI23"] + k("p%d" % nt), k("pT"))
+                mm(ps, T.E[:, K], T.blk8[:], st == 0, True, k("E") + ["blk8"], k("pT"), True)
+                if st < 2:
+                    bi, a = (T.BI1, T.BI2)[st][:, L], (T.a1, T.a2)[st][:, L]
+                    bt, at = k("BI%d" % nt), k("a%d" % nt)
+                    ts(bi, ps, 0.0, None, MAX, None, k("pT"), bt)
+                    ts(a, bi, 2047, None, AND, None, bt, at)
+                    ts(T.off[:, 16 * nt + 8 * s:16 * nt + 8 * s + 8], a, -1.0, 2047.0, MUL, ADD, at, k("off" + "abc"[nt]))
+                    ts((T.p2, T.p3)[st][:, L], a, 1024.0, None, LT, None, at, k("p%d" % (nt + 1)))
+                if st == 0:
+                    act(T.q2[:, L], ps, IDN, k("pT"), k("q2"), bias=4096.0, scale=-1.0)
+                    ts(T.kk1[:, L], bi, 11, 15, SHR, AND, bt, k("kk1"))
+                    tt(T.q1[:, L], T.cb[:], T.kk1[:, L], SUB, ["cb"] + k("kk1"), k("q1"))
+                    cp(T.le[:, L], T.q1[:, L], k("q1"), k("le"))
+                    sga(T.NK[:, K], Gp[:], T.le[:, L], GP + k("le"), k("NK"))
+                    mm(pE[:, 0:8], T.ones[:], T.m8[:], True, False, ["ones", "m8"], k("pE"))
+                    mm(pE[:, 0:8], T.pI23[:], T.p2[:, L], False, False, ["pI23"] + k("p2"), k("pE"))
+                    k_to_l(pE[:, 0:8], T.WN, T.NK, 128 * s, False, True, ["WN"] + k("NK"), k("pE"))
+                    tt(T.P1[:, 24 * s:24 * s + 8], pE[:, 0:8], T.cdum[:], MIN, k("pE") + ["cdum"], k("P1a"))
+                    tt(T.i2[:, L], bi, T.A0p[:, L], MAX, bt + k("A0p"), k("i2"))
+                    ts(T.Bw[:, L], T.i2[:, L], 32767, None, AND, None, k("i2"), k("Bw"))
+                    tt(T.lt0[:, L], T.q2[:, L], A0, MAX, k("q2") + a0t, k("lt0"))
+                    if v == 0:
+                        distance(xb, XB, T.goals[:, K], ab("goal0"))
+                        act(T.thr[:, L], pU[:, 24:32], CPY, k("pU"), k("thr"))
+                if st == 1:
+                    tt(T.kk1[:, L], bi, T.Bw[:, L], MAX, bt + k("Bw"), k("kk1"))
+                    ts(T.Bw2[:, L], T.kk1[:, L], 32767, None, AND, None, k("kk1"), k("Bw2"))
+                    tt(T.q1[:, L], bi, T.a1[:, L], MIN, bt + k("a1"), k("q1"))
+                    tt(T.i2[:, L], T.q1[:, L], T.lt0[:, L], MAX, k("q1", "lt0"), k("i2"))
+                    ts(T.lt2[:, L], T.i2[:, L], 5119, None, AND, None, k("i2"), k("lt2"))
+
+            ps = pT[:, 0:8]
+            tt(T.Bw[:, L], ps, T.Bw2[:, L], MAX, k("pT", "Bw2"), k("Bw"))
+            tt(T.q1[:, L], ps, T.a2[:, L], MIN, k("pT", "a2"), k("q1"))
+            ts(T.aw[:, L], T.Bw[:, L], 2047, None, AND, None, k("Bw"), k("aw"))
+            ts(T.le[:, L], T.aw[:, L], -1.0, 2047.0, MUL, ADD, k("aw"), k("le"))
+            gtt(T.NK[:, K], ef[:], T.le[:, L], xb, SUB, k("le", "ef0") + XB + ab("ef1"), k("NK"))
+            act(T.xn[:, K], T.NK[:, K], ABS, k("NK"), k("xn"))
+            b0 = 144 * (2 * v + s)
+            if last:
+                send(T.landb[:, K], T.xn[:, K], k("xn"), k("landb"))
+                for h in range(2):
+                    dma("Y", T.yx[64 * s:64 * s + 64, 128 * h:128 * h + 128], T.landb[64 * h:64 * h + 64, K], 16384, k("landb"), [])
+            else:
+                act(T.snd[:, b0:b0 + 128], T.NK[:, K], ABS, k("NK"), k("sx%d" % v))
+            distance(T.xn[:, K], k("xn"), T.goals[:, 256 * v + 128 * s:256 * v + 128 * s + 128],
+                     ab("goal0") if v == 0 else ["goalx"])
+            tt(T.good[:, L], pU[:, 24:32], T.thr[:, L], LT, k("pU", "thr"), k("good"))
+            tt(T.i2[:, L], T.q1[:, L], T.lt2[:, L], MAX, k("q1", "lt2"), k("i2"))
+            ts(T.lt[:, L], T.i2[:, L], 5119, None, AND, None, k("i2"), k("lt"))
+            ts(T.q2[:, L], T.aw[:, L], 1024.0, 8192.0, LT, MUL, k("aw"), k("q2"))
+            tt(T.q3[:, L], T.q2[:, L], T.lt[:, L], MIN, k("q2", "lt"), k("q3"))
+            ts(T.q4[:, L], T.aw[:, L], -1024.0, None, ADD, None, k("aw"), k("q4"))
+            cur, ct = (T.lfv[:, L], k("lfv")) if last else (T.snd[:, b0 + 128:b0 + 136], k("sa%d" % v))
+            tt(cur, T.q3[:, L], T.q4[:, L], MAX, k("q3", "q4"), ct)
+            act(T.P1[:, 24 * s + 8:24 * s + 16], cur, IDN, ct, k("P1b"), bias=1023.0 + 128 * (1 - s), scale=-1.0)
+            if not last:
+                act(T.snd[:, b0 + 136:b0 + 144], pU[:, 24:32], CPY, k("pU"), k("sd%d" % v))
+                send(T.land[:, b0:b0 + 144], T.snd[:, b0:b0 + 144], k("sx%d" % v, "sa%d" % v, "sd%d" % v),
+                     ["land%d_%d" % (v, s)])
+
+            X = slice(24 * s, 24 * s + 24)
+            ts(T.P0[:, 24 * s + 16:24 * s + 24], T.Bw[:, L], 11, 15, SHR, AND, k("Bw"), k("P0c"))
+            ts(T.q1[:, L], T.lt[:, L], -1.0, float(TC + 1023), MUL, ADD, k("lt"), k("q1"))
+            tt(T.P0[:, 24 * s:24 * s + 8], T.q1[:, L], T.cdum[:], MAX, k("q1") + ["cdum"], k("P0a"))
+            tt(T.Df[:, X], T.P1[:, X], T.P0[:, X], SUB, k("P0a", "P0b", "P0c", "P1a", "P1b", "P1c"), k("Df"))
+            for j in range(3):
+                c = slice(24 * s + 8 * j, 24 * s + 8 * j + 8)
+                tt(T.Dg[:, c], T.Df[:, c], T.good[:, L], MUL, k("Df", "good"), k("Dg%d" % j))
+            tt(T.Sel[:, X], T.Dg[:, X], T.P0[:, X], ADD, k("Dg0", "Dg1", "Dg2", "P0a", "P0b", "P0c"), k("Sel"))
+            idv = T.Sel[:, 24 * s:24 * s + 8]
+            cp(T.ls[:, X], T.Sel[:, X], k("Sel"), k("ls"))
+            ts(T.l2[:, L], idv, float(ZC), None, MAX, None, k("Sel"), k("l2"))
+            gtt(T.E[:, K], idv, T.l1[:], T.msk[:], MUL, k("Sel") + ["l1", "msk"], k("E"))
+            mm(pT[:, 16:24], T.nI256[:], T.cnb[:], True, False, ["nI256", "cnb"], k("pT"), True)
+            mm(pT[:, 16:24], T.nI256[:], idv, False, True, ["nI256"] + k("Sel"), k("pT"), True)
+            act(T.nb[:, L], pT[:, 16:24], CPY, k("pT"), k("nb"))
+            mm(pE[:, 0:128], T.ones[:], T.Jm[:], True, False, ["ones", "Jm"], k("pE"))
+            mm(pE[:, 0:128], T.blk256[:], T.E[:, K], False, True, ["blk256"] + k("E"), k("pE"), True)
+            o = 576 * s
+            AC = []
+            for c in range(7, -1, -1):
+                wdt = 16 * c + 16
+                e = T.EQ[:, o:o + wdt]
+                et = k("EQ%d_" % c)
+                act(e, pE[:, 0:wdt], ABS, k("pE", "nb"), et, bias=T.nb[:, 8 * s + c:8 * s + c + 1])
+                if c >= 8 - MNV:
+                    mo = T.mn[:, 8 * s + c:8 * s + c + 1]
+                    add("V", cyc(wdt), lambda mo=mo, e=e: V.tensor_reduce(mo, e, AxisListType.X, MIN), et, k("mn%d_" % c))
+                else:
+                    act(e, e, RELU, et, et + k("acc%d_" % c), bias=63.5 * 16384.0, scale=-16384.0,
+                        acc=T.acc[:, 8 * s + c:8 * s + c + 1])
+                    AC += k("acc%d_" % c)
+                o += wdt
+            if MNV:
+                c = slice(8 * s + 8 - MNV, 8 * s + 8)
+                act(T.acc[:, c], T.mn[:, c], RELU, k(*["mn%d_" % j for j in range(8 - MNV, 8)]), k("accv"),
+                    bias=63.5 * 16384.0, scale=-16384.0)
+                AC += k("accv")
+            tt(T.q2[:, L], T.acc[:, L], T.ctop[:], MIN, AC + ["ctop"], k("q2"))
+            tt(T.lfv[:, L], T.q2[:, L], idv, MAX, k("q2", "Sel"), k("lfv"))
+            mm(pT[:, 32:40], T.PB[:], T.lfv[:, L], True, True, ["PB"] + k("lfv"), k("pT"), True)
+            mm(pT[:, 40:48], T.PA[:], T.lfv[:, L], True, True, ["PA"] + k("lfv"), k("pT"), True)
+            cp(T.lf[:, 16 * s:16 * s + 16], pT[:, 32:48], k("pT"), k("lf"))
+            lk = T.ls[:, 24 * s + 16:24 * s + 24]
+            sga(T.Z[:, K], W[:, 0:WS], T.l2[:, L], k("l2") + WALL, k("Z"), scale=13.0)
+            sga(T.kp[:, K], T.KP[:], lk, k("ls") + ["KP"], k("kp"))
+            gtt(T.mK[:, K], Y[:, 128 * s:128 * s + 1152], T.ls[:, 24 * s + 8:24 * s + 16], T.Z[:, K], ADD,
+                k("ls", "Z", "Ye") + ["Yf", "Y0", "Y1"], k("mK"))
+            ts(T.nK[:, K], T.mK[:, K], 4095, None, AND, None, k("mK"), k("nK"))
+            gtt(T.aK[:, K], W[:, 0:WS], T.ls[:, 24 * s:24 * s + 8], T.kp[:, K], MUL, k("ls", "kp") + WALL, k("aK"))
+            gtt(T.bK[:, K], T.OH[:], lk, T.nK[:, K], MUL, k("ls", "nK") + ["OHa", "OHb"], k("bK"))
+            for h, Pm, pt in ((0, T.PB, "PB"), (1, T.PA, "PA")):
+                mm(pK[:, 128 * h:128 * h + 128], Pm[:], T.aK[:, K], True, False, [pt] + k("aK"), k("pK"), True)
+                mm(pK[:, 128 * h:128 * h + 128], Pm[:], T.bK[:, K], False, True, [pt] + k("bK"), k("pK"), True)
+            act(T.NW[:, 256 * s:256 * s + 256], pK[:, 0:256], CPY, k("pK"), k("NW"))
+            for h in range(2):
+                add("V", 0.06 + 128 * SC * CY,
+                    lambda h=h: V.tensor_copy(W[:, 0:WS].indirect(T.lf[:, 16 * s + 8 * h:16 * s + 8 * h + 8]),
+                                              T.NW[:, 256 * s + 128 * h:256 * s + 128 * h + 128]),
+                    k("lf", "NW"), WALL)
+            if not last:
+                act(T.q4[:, L], T.good[:, L], CPY, k("good"), k("q4", "cnt"), acc=T.cnt[:, c4])
+                mm(pU[:, 48:49], T.blk2[:], T.cnt[:, c4], True, True, ["blk2a", "blk2b"] + k("cnt"), k("pU"), True)
+                tt(T.Aa[:, c4], pU[:, 48:49], T.Aa[:, c4], ADD, k("pU", "Aa"), k("Aa"))
+                ts(T.A7[:, c4], T.Aa[:, c4], 7, None, AND, None, k("Aa"), k("A7"))
+                cp(T.A7f[:, c4], T.A7[:, c4], k("A7"), k("A7f"))
+
+        dma("Y", T.yteam[64 * s:64 * s + 64, :], W[0:64, TC:DT], 262144, WALL, [])
+        dma("Y", T.yact[4 * s:4 * s + 4, :], W[64:128:16, 0:4096], 65536, WALL, [])
+
+    a = len(ops)
+    stream(0)
+    b = len(ops)
+    stream(1)
+    return ops, (a, b)
+
+
+def depend(ops):
+    lastw, readers = {}, {}
+    deps = []
+    for i, o in enumerate(ops):
+        d = set()
+        for t in o["r"]:
+            if t in lastw:
+                d.add(lastw[t])
+            if t in PSUM:
+                for j in readers.get(t, []):
+                    if ops[j]["e"] != o["e"]:
+                        d.add(j)
+        for t in o["w"]:
+            if t in lastw:
+                d.add(lastw[t])
+            d.update(readers.get(t, []))
+        d.discard(i)
+        deps.append(sorted(d))
+        for t in o["r"]:
+            readers.setdefault(t, []).append(i)
+        for t in o["w"]:
+            lastw[t] = i
+            readers[t] = []
+    return deps
+
+
+def place(ops, pred, succ, pr):
+    n = len(ops)
+    left = [len(d) for d in pred]
+    rdy = [0.0] * n
+    free, cand = {}, {}
+    for i in range(n):
+        free[ops[i]["e"]] = 0.0
+        cand.setdefault(ops[i]["e"], [])
+        if left[i] == 0:
+            cand[ops[i]["e"]].append(i)
+    order, bus, t0, t1 = [], 0.0, [0.0] * n, [0.0] * n
+    while len(order) < n:
+        best = None
+        for e in cand:
+            if cand[e]:
+                t = max(free[e], min(rdy[i] for i in cand[e]))
+                if best is None or t < best[0]:
+                    best = (t, e)
+        t, e = best
+        i = max((j for j in cand[e] if rdy[j] <= t + 1e-9), key=lambda j: (pr[j], -j))
+        cand[e].remove(i)
+        o = ops[i]
+        free[e] = t + o["d"]
+        if o["k"] == "dma":
+            bus = max(bus, t + 1.5) + o["lat"] / BW
+            fin = bus + 0.5
+        else:
+            fin = t + o["d"] + o["lat"]
+        t0[i], t1[i] = t, fin
+        order.append(i)
+        for j in succ[i]:
+            if abs(i - j) == 1 and ops[max(i, j)].get("soft"):
+                rdy[j] = max(rdy[j], free[e])
+            else:
+                rdy[j] = max(rdy[j], fin + (0.0 if e == "P" and ops[j]["e"] == "P" else WAKE))
+            left[j] -= 1
+            if left[j] == 0:
+                cand[ops[j]["e"]].append(j)
+    return order, t0, t1
+
+
+def schedule(ops, hard, cut, lead, seed=0, noise=0.0):
+    n = len(ops)
+    deps = [hard[i] + ([i - 1] if ops[i].get("soft") else []) for i in range(n)]
+    succ = [[] for i in range(n)]
+    for i in range(n):
+        for j in deps[i]:
+            succ[j].append(i)
+    pr = [0.0] * n
+    rs = np.random.default_rng(seed)
+    for i in range(n - 1, -1, -1):
+        o = ops[i]
+        lat = 2.0 + o["lat"] / BW if o["k"] == "dma" else o["d"] + o["lat"]
+        pr[i] = max([pr[j] + (o["d"] if j == i + 1 and ops[j].get("soft") else
+                              lat if o["e"] == "P" and ops[j]["e"] == "P" else lat + WAKE) for j in succ[i]]
+                    or [lat + (lead if cut[0] <= i < cut[1] else 0.0)])
+    best = None
+    for rnd in range(ROUNDS):
+        order, t0, t1 = place(ops, deps, succ, pr)
+        if best is None or max(t1) < best[0]:
+            best = (max(t1), order, t0, t1)
+        pr = place(ops, succ, deps, [t + noise * float(x) for t, x in zip(t1, rs.random(n))])[2]
+    for i in range(n):
+        ops[i]["t0"], ops[i]["t1"] = best[2][i], best[3][i]
+    return best[1], best[0]
+
+
+def emit(g, T, ops, deps, order):
+    Q = {"V": g.vector, "S": g.scalar, "P": g.tensor, "Y": g.sync, "G": g}
+    pos, cnt = {}, {}
+    for i in order:
+        if ops[i]["k"] == "c":
+            e = ops[i]["e"]
+            cnt[e] = cnt.get(e, 0) + 1
+            pos[i] = cnt[e]
+    know = {e: {} for e in Q}
+    clock, waits, need = {}, {}, set()
+    for i in order:
+        o = ops[i]
+        k = know[o["e"]]
+        ws = []
+        for j in sorted(deps[i], key=lambda j: -ops[j]["t1"]):
+            p = ops[j]
+            if p["k"] == "c":
+                if p["e"] == "P" and o["e"] == "P":
+                    continue
+                key, val = p["e"], pos[j]
+            else:
+                key, val = j, 1
+            if k.get(key, 0) >= val:
+                continue
+            ws.append(j)
+            need.add(j)
+            k[key] = val
+            if p["k"] != "rem":
+                for a, b in clock[j].items():
+                    if k.get(a, 0) < b:
+                        k[a] = b
+        waits[i] = ws
+        clock[i] = dict(k)
+    semv, run, nd, fin, sent = {}, {}, 0, [], 0
+    for i in order:
+        o = ops[i]
+        q = Q[o["e"]]
+        top = {}
+        for j in waits[i]:
+            s, val = semv[j]
+            top[s] = max(top.get(s, 0), val)
+        for s in top:
+            q.wait_ge(T.sem[s], top[s])
+        ins = o["f"]()
+        if o["k"] == "c":
+            if i in need:
+                s = "c" + o["e"]
+                run[s] = run.get(s, 0) + 1
+                ins.then_inc(T.sem[s], 1)
+                semv[i] = (s, run[s])
+        elif o["k"] == "dma":
+            s = "d%d" % nd
+            nd += 1
+            ins.then_inc(T.sem[s], 16)
+            semv[i] = (s, 16)
+            fin.append(semv[i])
+        else:
+            semv[i] = o["x"]
+            fin.append(semv[i])
+            sent += o["x"][1]
+    for s in run:
+        g.wait_ge(T.sem[s], run[s])
+    for s, val in fin:
+        g.wait_ge(T.sem[s], val)
+    g.wait_ge(T.sem.sent, sent)
+
+
+def rank_program(g, core, T, topo):
+    rank = T.rank_of(core)
+    if rank is None:
+        return
+    ops, cut = build_ops(g, T, topo, core, rank)
+    deps = depend(ops)
+    order, end = schedule(ops, deps, cut, LEAD, SEED, NOISE)
+    emit(g, T, ops, deps, order)

@@ -4,12 +4,15 @@ from concourse.mybir import AluOpType as ALU, AxisListType, ActivationFunctionTy
 
 NV = 4
 ZC, DC, TC, DT, WS, WN = 4096, 4112, 4240, 5264, 5392, 6288
-VCH, SCH = 4, 2
-XV = 4
+VCH, SCH = (32, 32, 32, 32), 2
+PV = (4, 4)
+XV = 2
+XV0 = (12, 4)
 PENV = (1, 1, 1)
-MNV = 4
-ROUNDS = 6
-LEAD, SEED, NOISE = 5.0, 1, 0.3
+MNV = 6
+ROUNDS, CLIMB = 6, 0
+FUSE = 1
+LEAD, SEED, NOISE = 4.0, 1, 0.3
 F, B, I, U = "float32", "bfloat16", "int32", "uint16"
 
 
@@ -18,13 +21,13 @@ def sb(n, d):
 
 
 SCRATCH = {
-    "Y": sb(1280, F), "cA": sb(2048, F), "goals": sb(1024, B), "land": sb(6 * 144, F), "snd": sb(6 * 144, F),
-    "landb": sb(256, B), "xb": sb(256, B), "xn": sb(256, B), "wtI": sb(8, I), "stI": sb(16, I), "actI": sb(512, I),
-    "ci": sb(16, I), "cf": sb(24, F), "io2": sb(128, F), "io3": sb(128, F), "io4": sb(128, F), "idn": sb(128, F),
+    "Y": sb(1280, F), "cA": sb(2048, F), "goals": sb(1024, B), "land": sb(96, F), "snd": sb(96, F),
+    "landb": sb(1024, B), "xb": sb(256, B), "xn": sb(1024, B), "wtI": sb(8, I), "stI": sb(16, I), "actI": sb(512, I),
+    "ci": sb(16, I), "cf": sb(24, F), "io2": sb(128, F), "io3": sb(128, F), "idn": sb(128, F),
     "blk": sb(128, F), "blk256": sb(128, F), "blk2": sb(128, F), "blk8": sb(8, F), "msk": sb(128, F), "rst": sb(128, F),
     "PA": sb(128, F), "PB": sb(128, F), "nI256": sb(128, F), "nI23": sb(128, B), "pI23": sb(128, B),
     "Wm": sb(8, B), "Wp": sb(32, B), "Ws": sb(128, B), "Wx": sb(128, B), "We": sb(256, B),
-    "WN": sb(144, B), "WD": sb(144, B), "ones": sb(128, B), "Cm": sb(128, B), "Jm": sb(128, B), "m8": sb(8, B),
+    "WN": sb(144, B), "WD": sb(144, B), "WE": sb(144, B), "ones": sb(128, B), "Cm": sb(128, B), "Jm": sb(128, B), "m8": sb(8, B),
     "OH": sb(32, F), "KP": sb(32, F), "l15": sb(8, U), "l1": sb(8, U),
     "cj": sb(8, F), "cdum": sb(8, F), "ctop": sb(8, F), "cb": sb(8, F), "cnb": sb(8, F),
     "cK": sb(256, F), "mK": sb(256, I), "nK": sb(256, I), "n16": sb(256, U), "TK": sb(768, B), "pen": sb(768, B),
@@ -48,11 +51,13 @@ for s_ in "01":
 PSUM = ("pK0", "pK1", "pT0", "pT1", "pU0", "pU1", "pE0", "pE1")
 
 NDMA = 70
-SEMAPHORES = ["cV", "cS", "cP", "cG", "sent", "gin"] + ["d%d" % i for i in range(NDMA)] + ["r%d" % i for i in range(8)]
+SEMAPHORES = ["cV", "cS", "cP", "cG", "sent", "gin"] + ["d%d" % i for i in range(NDMA)] + ["r%d" % i for i in range(14)]
 
 CY = 1.04e-3
+PEC = 1.04e-3
+LOOK, BETA = 0.2, 15.0
 GA, SC = 1.56, 3.8
-WAKE = 0.12
+WAKE = 0.17
 BW = 200000.0
 
 
@@ -98,7 +103,7 @@ def build_ops(g, T, topo, core, rank):
         add("S", 0.08 + wd(out) * GA * CY, lambda: S.activation(out, win.indirect(off), ACT.Copy, scale=scale), r, w)
 
     def mm(out, l, rh, st, sp, r, w, f32=False):
-        add("P", max(64, wd(out)) * (4 if f32 else 1) * CY, lambda: P.matmul(out, l, rh, st, sp), r, w)
+        add("P", max(64, wd(out)) * (4 if f32 else 1) * PEC, lambda: P.matmul(out, l, rh, st, sp), r, w)
 
     def dma(q, out, a, nbytes, r, w):
         qq = {"Y": g.sync, "S": g.scalar, "G": g}[q]
@@ -106,7 +111,8 @@ def build_ops(g, T, topo, core, rank):
 
     def iota(out, pat, base, cm, w, flt=True):
         if flt:
-            add("G", 0.15 + 2 * wd(out) * CY, lambda: g.iota(out, pat, base, cm, allow_small_or_imprecise_dtypes=True), [], w)
+            add("G", 0.15 + 2 * wd(out) * CY, lambda: g.iota(out, pat, base, cm, allow_small_or_imprecise_dtypes=True),
+                ["io2", "io3"] if wd(out) > 128 else [], w)
         else:
             add("G", 0.15 + 2 * wd(out) * CY, lambda: g.iota(out, pat, base, cm), [], w)
 
@@ -135,14 +141,19 @@ def build_ops(g, T, topo, core, rank):
             dma(q, T.xb[D, 128 * s:128 * s + 128], T.x0[R, 128 * h:128 * h + 128], 16384, [], ["xb" + t])
             dma(q, T.wtI[D, 4 * s:4 * s + 1], T.wt[R, :], 4096, [], ["wtI" + t])
             dma(q, T.stI[D, 8 * s:8 * s + 8], T.start[R, 8 * h:8 * h + 8], 4096, [], ["stI" + t])
+        prg = T["prg" + H]
         for c in range(4):
-            for h, D, t in HV:
-                dma("Y", T["prg" + H][D, 1024 * c:1024 * c + 1024], T.prog[R, 1024 * c:1024 * c + 1024], 131072, after,
-                    ["prg%d%s" % (c, t)])
-                ops[-1]["soft"] = c + h > 0
-        for h, D, t in HV:
-            dma("Y", T["teamI" + H][D, :], T.team[R, :], 262144, after, ["teamI" + t])
-            ops[-1]["soft"] = True
+            C = slice(1024 * c, 1024 * c + 1024)
+            dma("Y", prg[0:64, C], T.prog[R, C], 131072, after, ["prg%d%sa" % (c, H)])
+            ops[-1]["soft"] = c > 0
+        dma("Y", T["teamI" + H][0:64, :], T.team[R, :], 262144, after, ["teamI" + H])
+        ops[-1]["soft"] = True
+        for c in range(4):
+            C = slice(1024 * c, 1024 * c + 1024)
+            if c < PV[s]:
+                cp(prg[64:128, C], prg[0:64, C], ["prg%d%sa" % (c, H)], ["prg%d%sb" % (c, H)], 0.5)
+            else:
+                act(prg[64:128, C], prg[0:64, C], CPY, ["prg%d%sa" % (c, H)], ["prg%d%sb" % (c, H)])
 
     for s in range(2):
         for h in range(2):
@@ -154,18 +165,19 @@ def build_ops(g, T, topo, core, rank):
         for v in range(1, NV):
             dst = T.cores[(rank + v) % N]
             rid, pid, se = topo.addr(dst)
-            m, n = split_mask(dst, v, 4)
+            m, n = split_mask(dst, *GM3[v])
             tr.append(RemoteDMATransfer(dst_ids=[DstId(rid=rid, pnc=pid)], dma_engine_mask=m, remote_sem=T.sem.gin,
                                         src=T.goals[:, 0:256], dst=T.goals[:, 256 * v:256 * v + 256]))
         return g.remote_dma_fused(tr, local_sem=T.sem.sent)
-    ngo = sum(split_mask(T.cores[(rank + v) % N], v, 4)[1] for v in range(1, NV))
+    GM3 = (None, (0, 2), (2, 4), (3, 4))
+    ngo = sum(split_mask(T.cores[(rank + v) % N], *GM3[v])[1] for v in range(1, NV))
     add("G", 1.5, send_goals, ["goal00a", "goal00b", "goal01a", "goal01b"], ["goalx"], kind="rem", lat=2.5, extra=("gin", ngo))
 
     iota(ci[:, 0:1], [[0, 1]], 0, 1, ["ci0"], False)
     iota(T.E[:, 0:128], [[1, 8], [0, 16]], 0, 0, ["E0"])
     iota(T.io2[:], [[0, 8], [1, 16]], 0, 0, ["io2"])
     iota(T.io3[:], [[1, 128]], 0, 0, ["io3"])
-    iota(T.io4[:], [[0, 2], [1, 64]], 0, 0, ["io4"])
+    iota(T.aK[:, 0:128], [[0, 2], [1, 64]], 0, 0, ["aK0"])
     iota(T.eM[:], [[1, 256]], 0, 256, ["eM0", "eM1"], False)
     ts(ci[:, 4:5], ci[:, 0:1], 15, None, AND, None, ["ci0"], ["ci4"])
     ts(ci[:, 8:9], ci[:, 0:1], 4, None, SHR, None, ["ci0"], ["ci8"])
@@ -175,8 +187,8 @@ def build_ops(g, T, topo, core, rank):
     ts(T.msk[:], T.io2[:], rc, None, EQ, None, ["io2", "cf"], ["msk"])
     ts(T.idn[:], T.io3[:], pc, None, EQ, None, ["io3", "cf"], ["idn"])
     ts(T.rst[:], T.io2[:], 0.5, None, ALU.is_gt, None, ["io2"], ["rst"])
-    ts(T.PA[:], T.io4[:], pc, None, EQ, None, ["io4", "cf"], ["PA"])
-    ts(T.PB[:], T.io4[:], 64.0, pc, ADD, EQ, ["io4", "cf"], ["PB"])
+    ts(T.PA[:], T.aK[:, 0:128], pc, None, EQ, None, ["aK0", "cf"], ["PA"])
+    ts(T.PB[:], T.aK[:, 0:128], 64.0, pc, ADD, EQ, ["aK0", "cf"], ["PB"])
     tt(T.blk2[:, 0:64], T.blk[:, 0:64], T.blk[:, 64:128], ADD, ["blk"], ["blk2a"])
     act(T.blk2[:, 64:128], T.blk2[:, 0:64], CPY, ["blk2a"], ["blk2b"])
     act(T.Wx[:], T.blk[:], CPY, ["blk"], ["Wx"], scale=32768.0)
@@ -199,6 +211,9 @@ def build_ops(g, T, topo, core, rank):
     ms(T.WD[:], 0.0, ["WD"], 0.5)
     act(T.WN[:, 15:143:16], T.blk8[:], CPY, ["blk8", "r34"], ["WN"], scale=cf[:, 2:3])
     act(T.WD[:, 15:143:16], T.blk8[:], CPY, ["blk8"], ["WD"])
+    ms(T.WE[:], 0.0, ["WE"], 0.5)
+    cp(T.WE[:, 15:79:16], T.blk2[:, 0:64:16], ["blk2a"], ["WE"])
+    cp(T.WE[:, 79:143:16], T.blk2[:, 0:64:16], ["blk2a"], ["WE"])
     ms(T.ones[:], 1.0, ["ones"], 0.5)
     ms(T.m8[:], -0.0625, ["m8"], 0.5)
     idn = T.idn
@@ -258,7 +273,7 @@ def build_ops(g, T, topo, core, rank):
         c4 = slice(4 * s, 4 * s + 1)
         PAY = k("W0", "W1", "W2", "W4")
         FILL = k("Wfa", "Wfb", "Wfc", "Wfd")
-        WALL = PAY + k("Wt", "Wz", "Wx")
+        WALL = PAY + k("Wt", "Wu", "Wz", "Wx")
         PRG = ab("prg0", "prg1", "prg2", "prg3")
         XB = ab("xb")
         xb = T.xb[:, K]
@@ -276,8 +291,9 @@ def build_ops(g, T, topo, core, rank):
             ms(W[:, DT:WN], 0.0, k("Wx"))
         else:
             iota(W[:, DT:WN], [[0, WN - DT]], 0, 0, k("Wx"))
-        ms(ef[:, 0:1024], 0.0, k("ef0"), 0.5)
-        cp(W[:, TC:DT], T["teamI" + H][:], ab("teamI"), k("Wt"))
+        iota(ef[:, 0:1024], [[0, 1024]], 0, 0, k("ef0"))
+        cp(W[0:64, TC:DT], T["teamI" + H][0:64, :], k("teamI"), k("Wt"))
+        act(W[64:128, TC:DT], W[0:64, TC:DT], CPY, k("Wt"), k("Wu"))
         c0 = 768 * s
         cp(cA[:, c0:c0 + 256], T.actI[:, 256 * s:256 * s + 256], ab("actI"), k("cA0"))
         hb = T.pab[:, 384 * s:384 * s + 256]
@@ -285,8 +301,8 @@ def build_ops(g, T, topo, core, rank):
         tt(cA[:, c0 + 256:c0 + 512], cA[:, c0:c0 + 256], hb, SUB, k("cA0", "pab"), k("cA1"))
         act(cA[:, c0 + 256:c0 + 512], cA[:, c0 + 256:c0 + 512], IDN, k("cA1"), k("cA1"), bias=8.0)
         for q in range(16):
-            mm(pU[:, 0:256], T.WD[:, 15 - q:143 - q], prg[:, 256 * q:256 * q + 256], q == 0, q == 15,
-               ["WD"] + ab("prg%d" % (q // 4)), k("pU"))
+            mm(pU[:, 0:256], T.WE[0:64, 15 - q:143 - q], prg[0:64, 256 * q:256 * q + 256], q == 0, q == 15,
+               ["WE", "prg%d%sa" % (q // 4, H)], k("pU"))
         act(cA[:, c0 + 512:c0 + 768], pU[:, 0:256], CPY, k("pU"), k("cA2"))
         for row, a, tok in ((4, 1792, "cN8"), (0, c0, "cA0" + H), (1, c0 + 256, "cA1" + H), (2, c0 + 512, "cA2" + H)):
             dma("Y", W[row:128:16, 0:4096], cA[:, a:a + 256], 131072, [tok] + FILL, k("W%d" % row))
@@ -311,12 +327,13 @@ def build_ops(g, T, topo, core, rank):
         for v in range(NV):
             last = v == NV - 1
             if v > 0:
-                b0 = 144 * (2 * (v - 1) + s)
+                b0 = 16 * (2 * (v - 1) + s)
                 tok = ["land%d_%d" % (v - 1, s)]
-                act(xb, T.land[:, b0:b0 + 128], CPY, tok, XB)
-                A0, a0t = T.land[:, b0 + 128:b0 + 136], tok
+                x0 = 256 * (v - 1) + 128 * s
+                xb, XB = T.landb[:, x0:x0 + 128], k("landb%d" % (v - 1))
+                A0, a0t = T.land[:, b0:b0 + 8], tok
                 ts(T.off[:, L], A0, -1.0, 1023.0, MUL, ADD, tok, k("offa"))
-                ts(T.thr[:, L], T.land[:, b0 + 136:b0 + 144], T.A7f[:, c4], None, SUB, None, tok + k("A7f"), k("thr"))
+                ts(T.thr[:, L], T.land[:, b0 + 8:b0 + 16], T.A7f[:, c4], None, SUB, None, tok + k("A7f"), k("thr"))
             else:
                 A0, a0t = T.A0[:, L], k("A0")
                 cp(T.off[:, L], T.stI[:, L], ab("stI"), k("offa"))
@@ -327,7 +344,7 @@ def build_ops(g, T, topo, core, rank):
             ts(uu, T.eM[:, K], 2.0, 33.0, MUL, ADD, k("eM"), ut)
             XR = k(*["xr%d_" % j for j in range(16)])
             for j in range(16):
-                if j < XV:
+                if j < (XV if v else XV0[s]):
                     cp(xr[:, j:2048:16], xb, XB, [XR[j]], 0.5)
                 else:
                     act(xr[:, j:2048:16], xb, CPY, XB, [XR[j]])
@@ -340,26 +357,29 @@ def build_ops(g, T, topo, core, rank):
                 oft = k("off" + "abc"[st])
                 TKc = 384 * s
                 sga(T.TK[:, TKc + 128 * st:TKc + 128 * st + 128], W[:, 0:2048], of, oft + PAY, k("TK%d" % st))
-                gtt(T.mK[:, K], W[:, TC:WN], of, T.cK[:, K], MUL, oft + k("Wt", "Wx", "uK"), k("mK"))
+                gtt(T.mK[:, K], W[:, TC:WN], of, T.cK[:, K], MUL, oft + k("Wt", "Wu", "Wx", "uK"), k("mK"))
                 ts(T.nK[:, K], T.mK[:, K], 5, 4095, SHR, AND, k("mK"), k("nK"))
                 cp(T.n16[:, K], T.nK[:, K], k("nK"), k("n16"))
-                GM = k(*["Gm%d_" % c for c in range(VCH)])
+                GM = k(*["Gm%d_" % c for c in range(len(VCH))])
                 GP = k(*["Gp%d_" % c for c in range(SCH)])
-                w = 128 // VCH
-                for c in range(VCH):
-                    gtt(Gm[:, 16 * w * c:16 * w * (c + 1)], prg[:], T.n16[:, 128 * s + w * c:128 * s + w * (c + 1)],
-                        xr[:, 16 * w * c:16 * w * (c + 1)], MAX, k("n16") + PRG + XR, [GM[c]])
+                a0 = 0
+                for c, w in enumerate(VCH):
+                    gtt(Gm[:, 16 * a0:16 * (a0 + w)], prg[:], T.n16[:, 128 * s + a0:128 * s + a0 + w],
+                        xr[:, 16 * a0:16 * (a0 + w)], MAX, k("n16") + PRG + XR, [GM[c]])
                     ops[-1]["soft"] = c > 0
+                    a0 += w
                 w = 128 // SCH
                 for c in range(SCH):
                     sga(Gp[:, 16 * w * c:16 * w * (c + 1)], W[:, 0:4096], T.n16[:, 128 * s + w * c:128 * s + w * (c + 1)],
                         k("n16") + PAY, [GP[c]])
                     ops[-1]["soft"] = c > 0
+                mm(pU[:, 0:128], T.ones[:], T.Cm[:], True, False, ["ones", "Cm"], k("pU"))
                 for t in range(nt):
                     mm(pU[:, 128 + 128 * t:256 + 128 * t], T.TK[:, TKc + 128 * t:TKc + 128 * t + 128], T.Ws[:],
-                       t == 0, False, k("TK%d" % t) + ["Ws"], k("pU"))
+                       False, False, k("TK%d" % t) + ["Ws"], k("pU"))
                 for j in range(16):
-                    mm(pU[:, 128 + j:128 * (nt + 1):16], Gp[:, j:2048:16], T.Wp[:, 8:8 * (nt + 1)], False, j == 15, GP + WP, k("pU"))
+                    mm(pU[:, j:128 * (nt + 1):16], Gp[:, j:2048:16], T.Wp[:, 0:8 * (nt + 1)], False, j == 15, GP + WP, k("pU"))
+                act(T.kp[:, K], pU[:, 0:128], CPY, k("pU"), k("kp"))
                 pen = T.pen[:, TKc:TKc + 128 * nt]
                 if PENV[st]:
                     ts(pen, pU[:, 128:128 + 128 * nt], 0.0, None, EQ, None, k("pU"), k("pen"))
@@ -367,15 +387,13 @@ def build_ops(g, T, topo, core, rank):
                     pab = T.pab[:, TKc:TKc + 128 * nt]
                     act(pab, pU[:, 128:128 + 128 * nt], ABS, k("pU"), k("pab"))
                     act(pen, pab, RELU, k("pab"), k("pen"), bias=1.0, scale=-1.0)
-                mm(pK[:, 0:128], T.ones[:], T.Cm[:], True, False, ["ones", "Cm"], k("pK"))
-                for j in range(16):
-                    mm(pK[:, j:128:16], Gp[:, j:2048:16], T.Wp[:, 0:8], False, False, GP + WP, k("pK"))
-                for t in range(nt):
-                    mm(pK[:, 0:128], T.nI23[:], T.pen[:, TKc + 128 * t:TKc + 128 * t + 128], False, False,
-                       ["nI23"] + k("pen"), k("pK"))
+                mm(pK[:, 0:128], xb, T.Wx[:], True, False, XB + ["Wx"], k("pK"))
                 for j in range(16):
                     mm(pK[:, j:128:16], Gm[:, j:2048:16], T.Wm[:], False, False, GM + ["Wm"], k("pK"))
-                mm(pK[:, 0:128], xb, T.Wx[:], False, True, XB + ["Wx"], k("pK"))
+                mm(pK[:, 0:128], T.idn[:], T.kp[:, K], False, False, ["idn"] + k("kp"), k("pK"), True)
+                for t in range(nt):
+                    mm(pK[:, 0:128], T.nI23[:], T.pen[:, TKc + 128 * t:TKc + 128 * t + 128], False, t == st,
+                       ["nI23"] + k("pen"), k("pK"))
                 add("V", cyc(128), lambda: V.tensor_tensor_scan(T.Z[:, K], T.rst[:], pK[:, 0:128], 0.0, MUL, MAX),
                     ["rst"] + k("pK"), k("Z"))
                 gtt(T.E[:, K], T.Z[:, K], T.l15[:], T.msk[:], MUL, k("Z") + ["l15", "msk"], k("E"))
@@ -419,15 +437,15 @@ def build_ops(g, T, topo, core, rank):
             ts(T.aw[:, L], T.Bw[:, L], 2047, None, AND, None, k("Bw"), k("aw"))
             ts(T.le[:, L], T.aw[:, L], -1.0, 2047.0, MUL, ADD, k("aw"), k("le"))
             gtt(T.NK[:, K], ef[:], T.le[:, L], xb, SUB, k("le", "ef0") + XB + ab("ef1"), k("NK"))
-            act(T.xn[:, K], T.NK[:, K], ABS, k("NK"), k("xn"))
-            b0 = 144 * (2 * v + s)
+            X0 = slice(256 * v + 128 * s, 256 * v + 128 * s + 128)
+            act(T.xn[:, X0], T.NK[:, K], ABS, k("NK"), k("xn%d" % v))
+            b0 = 16 * (2 * v + s)
+            send(T.landb[:, X0], T.xn[:, X0], k("xn%d" % v), k("landb%d" % v))
             if last:
-                send(T.landb[:, K], T.xn[:, K], k("xn"), k("landb"))
                 for h in range(2):
-                    dma("Y", T.yx[64 * s:64 * s + 64, 128 * h:128 * h + 128], T.landb[64 * h:64 * h + 64, K], 16384, k("landb"), [])
-            else:
-                act(T.snd[:, b0:b0 + 128], T.NK[:, K], ABS, k("NK"), k("sx%d" % v))
-            distance(T.xn[:, K], k("xn"), T.goals[:, 256 * v + 128 * s:256 * v + 128 * s + 128],
+                    dma("Y", T.yx[64 * s:64 * s + 64, 128 * h:128 * h + 128], T.landb[64 * h:64 * h + 64, X0], 16384,
+                        k("landb%d" % v), [])
+            distance(T.xn[:, X0], k("xn%d" % v), T.goals[:, 256 * v + 128 * s:256 * v + 128 * s + 128],
                      ab("goal0") if v == 0 else ["goalx"])
             tt(T.good[:, L], pU[:, 24:32], T.thr[:, L], LT, k("pU", "thr"), k("good"))
             tt(T.i2[:, L], T.q1[:, L], T.lt2[:, L], MAX, k("q1", "lt2"), k("i2"))
@@ -435,12 +453,12 @@ def build_ops(g, T, topo, core, rank):
             ts(T.q2[:, L], T.aw[:, L], 1024.0, 8192.0, LT, MUL, k("aw"), k("q2"))
             tt(T.q3[:, L], T.q2[:, L], T.lt[:, L], MIN, k("q2", "lt"), k("q3"))
             ts(T.q4[:, L], T.aw[:, L], -1024.0, None, ADD, None, k("aw"), k("q4"))
-            cur, ct = (T.lfv[:, L], k("lfv")) if last else (T.snd[:, b0 + 128:b0 + 136], k("sa%d" % v))
+            cur, ct = (T.lfv[:, L], k("lfv")) if last else (T.snd[:, b0:b0 + 8], k("sa%d" % v))
             tt(cur, T.q3[:, L], T.q4[:, L], MAX, k("q3", "q4"), ct)
             act(T.P1[:, 24 * s + 8:24 * s + 16], cur, IDN, ct, k("P1b"), bias=1023.0 + 128 * (1 - s), scale=-1.0)
             if not last:
-                act(T.snd[:, b0 + 136:b0 + 144], pU[:, 24:32], CPY, k("pU"), k("sd%d" % v))
-                send(T.land[:, b0:b0 + 144], T.snd[:, b0:b0 + 144], k("sx%d" % v, "sa%d" % v, "sd%d" % v),
+                act(T.snd[:, b0 + 8:b0 + 16], pU[:, 24:32], CPY, k("pU"), k("sd%d" % v))
+                send(T.land[:, b0:b0 + 16], T.snd[:, b0:b0 + 16], k("sa%d" % v, "sd%d" % v),
                      ["land%d_%d" % (v, s)])
 
             X = slice(24 * s, 24 * s + 24)
@@ -510,7 +528,8 @@ def build_ops(g, T, topo, core, rank):
                 ts(T.A7[:, c4], T.Aa[:, c4], 7, None, AND, None, k("Aa"), k("A7"))
                 cp(T.A7f[:, c4], T.A7[:, c4], k("A7"), k("A7f"))
 
-        dma("Y", T.yteam[64 * s:64 * s + 64, :], W[0:64, TC:DT], 262144, WALL, [])
+        dma("Y", T.yteam[64 * s:64 * s + 64, 0:512], W[0:64, TC:TC + 512], 131072, WALL, [])
+        dma("S", T.yteam[64 * s:64 * s + 64, 512:1024], W[64:128, TC + 512:DT], 131072, WALL, [])
         dma("Y", T.yact[4 * s:4 * s + 4, :], W[64:128:16, 0:4096], 65536, WALL, [])
 
     a = len(ops)
@@ -565,7 +584,8 @@ def place(ops, pred, succ, pr):
                 if best is None or t < best[0]:
                     best = (t, e)
         t, e = best
-        i = max((j for j in cand[e] if rdy[j] <= t + 1e-9), key=lambda j: (pr[j], -j))
+        i = max((j for j in cand[e] if rdy[j] <= t + LOOK), key=lambda j: (pr[j] - BETA * max(0.0, rdy[j] - t), -j))
+        t = max(t, rdy[i])
         cand[e].remove(i)
         o = ops[i]
         free[e] = t + o["d"]
@@ -606,8 +626,19 @@ def schedule(ops, hard, cut, lead, seed=0, noise=0.0):
     for rnd in range(ROUNDS):
         order, t0, t1 = place(ops, deps, succ, pr)
         if best is None or max(t1) < best[0]:
-            best = (max(t1), order, t0, t1)
+            best = (max(t1), order, t0, t1, pr)
         pr = place(ops, succ, deps, [t + noise * float(x) for t, x in zip(t1, rs.random(n))])[2]
+    pr = np.array(best[4])
+    for rnd in range(CLIMB):
+        p = pr.copy()
+        for rep in range(3):
+            a = int(rs.integers(cut[0], n))
+            b = a + int(rs.choice([1, 3, 10, 40, 100]))
+            p[a:b] += float(rs.normal()) * float(rs.choice([0.3, 1.0, 3.0]))
+        order, t0, t1 = place(ops, deps, succ, p.tolist())
+        if max(t1) <= best[0]:
+            best = (max(t1), order, t0, t1)
+            pr = p
     for i in range(n):
         ops[i]["t0"], ops[i]["t1"] = best[2][i], best[3][i]
     return best[1], best[0]
@@ -680,11 +711,18 @@ def emit(g, T, ops, deps, order):
     g.wait_ge(T.sem.sent, sent)
 
 
+ORDER = []
+
+
 def rank_program(g, core, T, topo):
     rank = T.rank_of(core)
     if rank is None:
         return
     ops, cut = build_ops(g, T, topo, core, rank)
     deps = depend(ops)
-    order, end = schedule(ops, deps, cut, LEAD, SEED, NOISE)
-    emit(g, T, ops, deps, order)
+    if not ORDER:
+        order, end = schedule(ops, deps, cut, LEAD, SEED, NOISE)
+        ORDER.append((order, [o["t1"] for o in ops]))
+    for o, t in zip(ops, ORDER[0][1]):
+        o["t1"] = t
+    emit(g, T, ops, deps, ORDER[0][0])

@@ -6,13 +6,14 @@ NV = 4
 ZC, DC, TC, DT, WS, WN = 4096, 4112, 4240, 5264, 5392, 6288
 VCH, SCH = (32, 32, 32, 32), 2
 PV = (4, 4)
-XV = 2
-XV0 = (12, 4)
-PENV = (1, 1, 1)
-MNV = 6
-ROUNDS, CLIMB = 6, 0
-FUSE = 1
-LEAD, SEED, NOISE = 4.0, 1, 0.3
+XV = 0
+XV0 = (8, 0)
+PENV = (0, 0, 0)
+MNV = 0
+ROUNDS, CLIMB = 20, 0
+EXTRA = 0
+XG = 12
+LEAD, SEED, NOISE = 4.0, 3, 0.3
 F, B, I, U = "float32", "bfloat16", "int32", "uint16"
 
 
@@ -27,7 +28,7 @@ SCRATCH = {
     "blk": sb(128, F), "blk256": sb(128, F), "blk2": sb(128, F), "blk8": sb(8, F), "msk": sb(128, F), "rst": sb(128, F),
     "PA": sb(128, F), "PB": sb(128, F), "nI256": sb(128, F), "nI23": sb(128, B), "pI23": sb(128, B),
     "Wm": sb(8, B), "Wp": sb(32, B), "Ws": sb(128, B), "Wx": sb(128, B), "We": sb(256, B),
-    "WN": sb(144, B), "WD": sb(144, B), "WE": sb(144, B), "ones": sb(128, B), "Cm": sb(128, B), "Jm": sb(128, B), "m8": sb(8, B),
+    "WN": sb(144, B), "WD": sb(144, B), "WE": sb(144, B), "ones": sb(128, B), "Cm": sb(128, B), "Jm": sb(128, B), "m8": sb(144, B),
     "OH": sb(32, F), "KP": sb(32, F), "l15": sb(8, U), "l1": sb(8, U),
     "cj": sb(8, F), "cdum": sb(8, F), "ctop": sb(8, F), "cb": sb(8, F), "cnb": sb(8, F),
     "cK": sb(256, F), "mK": sb(256, I), "nK": sb(256, I), "n16": sb(256, U), "TK": sb(768, B), "pen": sb(768, B),
@@ -46,6 +47,7 @@ for s_ in "01":
     for nm, n_, d_ in (("prg", 4096, B), ("W", WN, F), ("ef", 2048, B), ("teamI", 1024, I), ("Gm", 2048, B),
                        ("Gp", 2048, B), ("xr", 2048, B)):
         SCRATCH[nm + s_] = sb(n_, d_)
+    SCRATCH["Gm" + s_] = ("sbuf", [128, 4, 512], B)
     for nm in ("pK", "pT", "pU", "pE"):
         SCRATCH[nm + s_] = ("psum", [128, 512], F)
 PSUM = ("pK0", "pK1", "pT0", "pT1", "pU0", "pU1", "pE0", "pE1")
@@ -53,11 +55,11 @@ PSUM = ("pK0", "pK1", "pT0", "pT1", "pU0", "pU1", "pE0", "pE1")
 NDMA = 70
 SEMAPHORES = ["cV", "cS", "cP", "cG", "sent", "gin"] + ["d%d" % i for i in range(NDMA)] + ["r%d" % i for i in range(14)]
 
-CY = 1.04e-3
-PEC = 1.04e-3
+CY = 0.83e-3
+PEC = 0.415e-3
 LOOK, BETA = 0.2, 15.0
 GA, SC = 1.56, 3.8
-WAKE = 0.17
+WAKE = 0.1
 BW = 200000.0
 
 
@@ -73,7 +75,7 @@ def build_ops(g, T, topo, core, rank):
         return max(64, n) * CY + 0.02
 
     def wd(ap):
-        return int(ap.shape[1])
+        return int(np.prod(ap.shape[1:]))
 
     def ts(out, in0, s1, s2, o0, o1, r, w, c=1.0):
         if o1 is None:
@@ -215,7 +217,8 @@ def build_ops(g, T, topo, core, rank):
     cp(T.WE[:, 15:79:16], T.blk2[:, 0:64:16], ["blk2a"], ["WE"])
     cp(T.WE[:, 79:143:16], T.blk2[:, 0:64:16], ["blk2a"], ["WE"])
     ms(T.ones[:], 1.0, ["ones"], 0.5)
-    ms(T.m8[:], -0.0625, ["m8"], 0.5)
+    ms(T.m8[:, 0:8], -0.0625, ["m8"], 0.5)
+    ms(T.m8[:, 16:144], 0.0, ["idn8"], 0.5)
     idn = T.idn
     ts(cf[:, 5:6], idn[:, 0:1], 241.0 * 32768.0, None, MUL, None, ["idn"], ["k0"])
     ts(cf[:, 6:7], idn[:, 2:3], 7.0, cf[:, 5:6], MUL, ADD, ["idn", "k0"], ["k1"])
@@ -346,6 +349,9 @@ def build_ops(g, T, topo, core, rank):
             for j in range(16):
                 if j < (XV if v else XV0[s]):
                     cp(xr[:, j:2048:16], xb, XB, [XR[j]], 0.5)
+                elif v and j >= 16 - XG:
+                    add("G", 0.17 + 256 * CY, lambda j=j, xb=xb: g.affine_select(
+                        xr[:, j:2048:16], xb, [[0, 128]], ALU.is_ge, 0.0, 0, 0), XB, [XR[j]])
                 else:
                     act(xr[:, j:2048:16], xb, CPY, XB, [XR[j]])
             act(Y[:, 1152 * s:1152 * s + 128], uu, IDN, ut, k("Ye"), bias=-1599.5, scale=48.5)
@@ -364,7 +370,7 @@ def build_ops(g, T, topo, core, rank):
                 GP = k(*["Gp%d_" % c for c in range(SCH)])
                 a0 = 0
                 for c, w in enumerate(VCH):
-                    gtt(Gm[:, 16 * a0:16 * (a0 + w)], prg[:], T.n16[:, 128 * s + a0:128 * s + a0 + w],
+                    gtt(Gm[:, c, :], prg[:], T.n16[:, 128 * s + a0:128 * s + a0 + w],
                         xr[:, 16 * a0:16 * (a0 + w)], MAX, k("n16") + PRG + XR, [GM[c]])
                     ops[-1]["soft"] = c > 0
                     a0 += w
@@ -388,8 +394,11 @@ def build_ops(g, T, topo, core, rank):
                     act(pab, pU[:, 128:128 + 128 * nt], ABS, k("pU"), k("pab"))
                     act(pen, pab, RELU, k("pab"), k("pen"), bias=1.0, scale=-1.0)
                 mm(pK[:, 0:128], xb, T.Wx[:], True, False, XB + ["Wx"], k("pK"))
+                for rep in range(EXTRA):
+                    mm(pK[:, 0:128], T.pI23[:], T.m8[:, 16:144], False, False, ["pI23", "idn8"], k("pK"))
+                    mm(pK[:, 0:128], T.nI23[:], T.m8[:, 16:144], False, False, ["nI23", "idn8"], k("pK"))
                 for j in range(16):
-                    mm(pK[:, j:128:16], Gm[:, j:2048:16], T.Wm[:], False, False, GM + ["Wm"], k("pK"))
+                    mm(pK[:, j:128:16], Gm[:, :, j:512:16], T.Wm[:], False, False, GM + ["Wm"], k("pK"))
                 mm(pK[:, 0:128], T.idn[:], T.kp[:, K], False, False, ["idn"] + k("kp"), k("pK"), True)
                 for t in range(nt):
                     mm(pK[:, 0:128], T.nI23[:], T.pen[:, TKc + 128 * t:TKc + 128 * t + 128], False, t == st,
@@ -414,7 +423,7 @@ def build_ops(g, T, topo, core, rank):
                     tt(T.q1[:, L], T.cb[:], T.kk1[:, L], SUB, ["cb"] + k("kk1"), k("q1"))
                     cp(T.le[:, L], T.q1[:, L], k("q1"), k("le"))
                     sga(T.NK[:, K], Gp[:], T.le[:, L], GP + k("le"), k("NK"))
-                    mm(pE[:, 0:8], T.ones[:], T.m8[:], True, False, ["ones", "m8"], k("pE"))
+                    mm(pE[:, 0:8], T.ones[:], T.m8[:, 0:8], True, False, ["ones", "m8"], k("pE"))
                     mm(pE[:, 0:8], T.pI23[:], T.p2[:, L], False, False, ["pI23"] + k("p2"), k("pE"))
                     k_to_l(pE[:, 0:8], T.WN, T.NK, 128 * s, False, True, ["WN"] + k("NK"), k("pE"))
                     tt(T.P1[:, 24 * s:24 * s + 8], pE[:, 0:8], T.cdum[:], MIN, k("pE") + ["cdum"], k("P1a"))

@@ -3,17 +3,23 @@ from concourse.bass import DstId, RemoteDMATransfer
 from concourse.mybir import AluOpType as ALU, AxisListType, ActivationFunctionType as ACT
 
 NV = 4
-ZC, DC, TC, DT, WS, WN = 4096, 4112, 4240, 5264, 5392, 6288
-VCH, SCH = (32, 32, 32, 32), 2
-PV = (4, 4)
-XV = 0
-XV0 = (8, 0)
-PENV = (0, 0, 0)
-MNV = 0
-ROUNDS, CLIMB = 20, 0
-EXTRA = 0
-XG = 12
-LEAD, SEED, NOISE = 4.0, 3, 0.3
+TC, PC, DC, DT, WS = 128, 1152, 5248, 5376, 5504
+SW = 2
+VCH, SCH = ((4, 4, 4, 4), (2, 2, 2, 2, 2, 2, 2)), (8, 8)
+PV = ("VVVVS", "VVVVS")
+XE = (("V", "VVVV", "VVSS"), ("S", "SSSS", "VSSS"), ("S", "VVSS", "GGSV"))
+PENV = (1, 1, 1)
+EV = (1, 0)
+NKV = 1
+MNV = 8
+RV = 0
+ONV = ()
+N16 = 0
+NY = 4
+SHARE = ((1, 1, 1), (1, 1, 1))
+G3 = 0
+ROUNDS, CLIMB = 20, 1300
+LEAD, SEED, NOISE = 4.0, 3, 0.6
 F, B, I, U = "float32", "bfloat16", "int32", "uint16"
 
 
@@ -22,48 +28,60 @@ def sb(n, d):
 
 
 SCRATCH = {
-    "Y": sb(1280, F), "cA": sb(2048, F), "goals": sb(1024, B), "land": sb(96, F), "snd": sb(96, F),
-    "landb": sb(1024, B), "xb": sb(256, B), "xn": sb(1024, B), "wtI": sb(8, I), "stI": sb(16, I), "actI": sb(512, I),
+    "Y": sb(1280, F), "cA": sb(2048, F), "goals": sb(1024, B), "land": sb(192, F), "snd": sb(192, F),
+    "landb": sb(1024, B), "xb": sb(256, B), "xp": sb(1280, B), "xn": sb(1024, B), "wtI": sb(8, I), "stI": sb(16, I), "actI": sb(512, I),
     "ci": sb(16, I), "cf": sb(24, F), "io2": sb(128, F), "io3": sb(128, F), "idn": sb(128, F),
-    "blk": sb(128, F), "blk256": sb(128, F), "blk2": sb(128, F), "blk8": sb(8, F), "msk": sb(128, F), "rst": sb(128, F),
-    "PA": sb(128, F), "PB": sb(128, F), "nI256": sb(128, F), "nI23": sb(128, B), "pI23": sb(128, B),
-    "Wm": sb(8, B), "Wp": sb(32, B), "Ws": sb(128, B), "Wx": sb(128, B), "We": sb(256, B),
-    "WN": sb(144, B), "WD": sb(144, B), "WE": sb(144, B), "ones": sb(128, B), "Cm": sb(128, B), "Jm": sb(128, B), "m8": sb(144, B),
-    "OH": sb(32, F), "KP": sb(32, F), "l15": sb(8, U), "l1": sb(8, U),
-    "cj": sb(8, F), "cdum": sb(8, F), "ctop": sb(8, F), "cb": sb(8, F), "cnb": sb(8, F),
-    "cK": sb(256, F), "mK": sb(256, I), "nK": sb(256, I), "n16": sb(256, U), "TK": sb(768, B), "pen": sb(768, B),
+    "blk": sb(128, F), "blkE": sb(128, F), "blk2": sb(128, F), "blk8": sb(8, F), "msk": sb(128, F),
+    "PA": sb(128, F), "PB": sb(128, F), "nI23": sb(128, B), "pI23": sb(128, B), "nI512": sb(128, F),
+    "lp": sb(8, U), "nI24": sb(128, B), "SelY": sb(128, F), "CI": sb(384, B), "Gs": sb(1024, B), "rst": sb(128, F),
+    "Wm": sb(144, B), "Wp": sb(40, B), "We": sb(256, B), "c1": sb(128, B), "c2": sb(128, B),
+    "WN": sb(144, B), "WD": sb(144, B), "WE": sb(144, B), "ones": sb(128, B), "Jm": sb(128, B), "m8": sb(8, B),
+    "OH": sb(32, F), "KP": sb(32, F), "l1": sb(8, U), "cs": sb(40, F),
+    "EQ": sb(1152, F),
+    "cK": sb(256, F), "mK": sb(256, I), "nK": sb(256, I), "n16": sb(256, U), "TT": sb(768, F), "pen": sb(768, B),
     "pab": sb(768, B), "Z": sb(256, F), "E": sb(256, F), "eI": sb(256, I), "eM": sb(256, I), "NK": sb(256, B),
-    "ad": sb(256, B), "EQ": sb(1152, F), "kp": sb(256, F), "aK": sb(256, F), "bK": sb(256, F), "NW": sb(512, F),
-    "BI1": sb(16, I), "BI2": sb(16, I), "a1": sb(16, I), "a2": sb(16, I), "A0": sb(16, F), "off": sb(48, U),
-    "A0p": sb(16, F), "p2": sb(16, B), "p3": sb(16, B), "kk1": sb(16, I), "q1": sb(16, F), "q2": sb(16, F),
-    "q3": sb(16, F), "q4": sb(16, F), "i2": sb(16, I),
+    "kp": sb(256, F), "aK": sb(256, F), "bK": sb(256, F), "NW": sb(512, F), "nb": sb(16, F), "hE": sb(256, F),
+    "ad": ("sbuf", [128, 6, 128], B),
+    "ZW": sb(256, F), "AF": sb(32, F), "go": sb(40, B), "BI": sb(48, I),
+    "a1": sb(16, I), "a2": sb(16, I), "A0": sb(16, F), "off": sb(48, U),
+    "A0p": sb(16, F), "kk1": sb(16, I), "q1": sb(16, F), "q2": sb(16, F),
+    "acc": sb(16, F), "q3": sb(16, F), "q4": sb(16, F), "i2": sb(16, I),
     "Bw2": sb(16, I), "lt0": sb(16, F), "lt2": sb(16, I), "Bw": sb(16, I), "aw": sb(16, I), "le": sb(16, U),
     "lt": sb(16, I), "P0": sb(48, I), "P1": sb(48, F), "Df": sb(48, F), "Dg": sb(48, F),
-    "Sel": sb(48, F), "ls": sb(48, U), "l2": sb(16, U), "thr": sb(16, F), "good": sb(16, F), "nb": sb(16, F),
-    "mn": sb(16, F), "acc": sb(16, F), "lfv": sb(16, F), "lf": sb(32, U),
-    "cnt": sb(8, F), "Aa": sb(8, I), "A7": sb(8, I), "A7f": sb(8, F),
+    "Sel": sb(48, F), "ls": sb(48, U), "Pq": sb(256, B), "thr": sb(48, F), "good": sb(48, F),
+    "mn": sb(16, F), "lfv": sb(16, F), "lf": sb(32, U),
+    "cnt": sb(8, F), "An": sb(16, F),
 }
 for s_ in "01":
-    for nm, n_, d_ in (("prg", 4096, B), ("W", WN, F), ("ef", 2048, B), ("teamI", 1024, I), ("Gm", 2048, B),
-                       ("Gp", 2048, B), ("xr", 2048, B)):
+    for nm, n_, d_ in (("prg", 4096, B), ("W", WS, F), ("ef", 1040, B), ("teamI", 1024, I), ("xr", 2048, B),
+                       ("Gm", 2048, B), ("Gp", 2048, B)):
         SCRATCH[nm + s_] = sb(n_, d_)
-    SCRATCH["Gm" + s_] = ("sbuf", [128, 4, 512], B)
-    for nm in ("pK", "pT", "pU", "pE"):
-        SCRATCH[nm + s_] = ("psum", [128, 512], F)
+    SCRATCH["pK" + s_] = ("psum", [128, 512], F)
+    SCRATCH["pT" + s_] = ("psum", [128, 512], F)
+    SCRATCH["pU" + s_] = ("psum", [128, 4, 128], F)
+    SCRATCH["pE" + s_] = ("psum", [128, 4, 128], F)
 PSUM = ("pK0", "pK1", "pT0", "pT1", "pU0", "pU1", "pE0", "pE1")
 
 NDMA = 70
 SEMAPHORES = ["cV", "cS", "cP", "cG", "sent", "gin"] + ["d%d" % i for i in range(NDMA)] + ["r%d" % i for i in range(14)]
 
-CY = 0.83e-3
-PEC = 0.415e-3
-LOOK, BETA = 0.2, 15.0
-GA, SC = 1.56, 3.8
-WAKE = 0.1
+COSTS = ((0.83e-3, 0.44e-3, 1.56, 3.8, 0.115, 0.8, 2.0, 64, 0.0, -0.015, -0.015, 1.1),
+         (0.85e-3, 0.5e-3, 1.1, 1.8, 0.08, 1.4, 2.8, 64, 0.0, -0.015, -0.015, 1.25),
+         (1.0e-3, 0.52e-3, 1.3, 5.0, 0.17, 1.5, 3.0, 64, 0.0, -0.015, -0.015, 1.1))
+LOOK, BETA = 0.15, 15.0
+WAKE = COSTS[0][4]
+GAMMA = 1.0
+NX = 0.0
+OWN = 1.8
+LOADS = ("prg00a", "prg10a", "teamI0", "prg20a", "prg30a", "W40", "W00", "W10", "W20", "prg01a", "prg11a", "prg21a",
+         "prg31a", "teamI1", "W41", "W01", "W11", "W21", "ef10a", "ef10b", "ef11a", "ef11b")
+F32 = (4, 0.0)
+BUNDLE = 512
 BW = 200000.0
 
 
-def build_ops(g, T, topo, core, rank):
+def build_ops(g, T, topo, core, rank, cost):
+    CY, PEC, GA, SC = cost[:4]
     ops = []
     N = len(T.cores)
     V, S, P = g.vector, g.scalar, g.tensor
@@ -72,7 +90,7 @@ def build_ops(g, T, topo, core, rank):
         ops.append({"e": eng, "d": dur, "f": fn, "r": list(r), "w": list(w), "k": kind, "lat": lat, "x": extra})
 
     def cyc(n):
-        return max(64, n) * CY + 0.02
+        return max(64, n) * CY
 
     def wd(ap):
         return int(np.prod(ap.shape[1:]))
@@ -90,22 +108,31 @@ def build_ops(g, T, topo, core, rank):
         add("V", cyc(wd(out) * c), lambda: V.tensor_copy(out, a), r, w)
 
     def gtt(out, win, off, b, op, r, w):
-        add("V", 0.06 + wd(out) * GA * CY, lambda: V.tensor_tensor(out, win.indirect(off), b, op), r, w)
+        add("V", 0.05 + wd(out) * GA * CY, lambda: V.tensor_tensor(out, win.indirect(off), b, op), r, w)
 
     def ms(ap, val, w, c=1.0):
         add("V", cyc(wd(ap) * c), lambda: V.memset(ap, val), [], w)
 
     def act(out, a, fn, r, w, bias=0.0, scale=1.0, acc=None):
-        if acc is None:
-            add("S", cyc(wd(out)) + 0.04, lambda: S.activation(out, a, fn, bias=bias, scale=scale), r, w)
+        if "".join(c for c in w[0] if c.isalpha()) in ONV:
+            if acc is not None:
+                add("V", cyc(wd(out)), lambda: V.tensor_reduce(acc, a, AxisListType.X, ALU.add), r, w)
+            elif fn == ACT.Relu:
+                ts(out, a, scale, 0.0, ALU.mult, ALU.max, r, w)
+            else:
+                ts(out, a, scale, bias, ALU.mult, ALU.add, r, w)
+        elif acc is None:
+            add("S", cyc(wd(out)) + 0.04 + cost[9], lambda: S.activation(out, a, fn, bias=bias, scale=scale), r, w)
         else:
-            add("S", cyc(wd(out)) + 0.06, lambda: S.activation(out, a, fn, bias=bias, scale=scale, accum_out=acc), r, w)
+            add("S", cyc(wd(out)) + 0.06 + cost[9], lambda: S.activation(out, a, fn, bias=bias, scale=scale, accum_out=acc), r, w)
 
     def sga(out, win, off, r, w, scale=1.0):
-        add("S", 0.08 + wd(out) * GA * CY, lambda: S.activation(out, win.indirect(off), ACT.Copy, scale=scale), r, w)
+        add("S", 0.08 + cost[10] + wd(out) * GA * CY, lambda: S.activation(out, win.indirect(off), ACT.Copy, scale=scale), r, w)
 
     def mm(out, l, rh, st, sp, r, w, f32=False):
-        add("P", max(64, wd(out)) * (4 if f32 else 1) * PEC, lambda: P.matmul(out, l, rh, st, sp), r, w)
+        n = max(min(64, wd(l)), wd(rh)) * (4 if f32 else 1)
+        add("P", max(min(cost[7], wd(l)), wd(rh)) * (F32[0] if f32 else 1) * PEC + F32[1],
+            lambda: P.matmul(out, l, rh, st, sp), r, w, lat=cost[8], extra=n)
 
     def dma(q, out, a, nbytes, r, w):
         qq = {"Y": g.sync, "S": g.scalar, "G": g}[q]
@@ -117,6 +144,15 @@ def build_ops(g, T, topo, core, rank):
                 ["io2", "io3"] if wd(out) > 128 else [], w)
         else:
             add("G", 0.15 + 2 * wd(out) * CY, lambda: g.iota(out, pat, base, cm), [], w)
+
+    def move(e, out, src, r, w, c=1.0):
+        if e == "V":
+            cp(out, src, r, w, c)
+        elif e == "S":
+            act(out, src, ACT.Copy, r, w)
+        else:
+            add("G", (0.17 + 2 * wd(out) * CY) * cost[11], lambda: g.affine_select(
+                out, src, [[0, wd(out)]], ALU.is_ge, 0.0, 0, 0), r, w)
 
     def split_mask(dst, part, parts):
         en = topo.engines(core, dst)
@@ -135,7 +171,7 @@ def build_ops(g, T, topo, core, rank):
         H = str(s)
         R = slice(64 * s, 64 * s + 64)
         q = "S" if s == 0 else "Y"
-        after = [] if s == 0 else ["cA20"]
+        after = []
         HV = [(h, slice(64 * h, 64 * h + 64), H + "ab"[h]) for h in range(2)]
         for h, D, t in HV:
             dma(q, T.actI[D, 256 * s:256 * s + 256], T.act[4 * s:4 * s + 4, :], 65536, [], ["actI" + t])
@@ -147,15 +183,10 @@ def build_ops(g, T, topo, core, rank):
         for c in range(4):
             C = slice(1024 * c, 1024 * c + 1024)
             dma("Y", prg[0:64, C], T.prog[R, C], 131072, after, ["prg%d%sa" % (c, H)])
-            ops[-1]["soft"] = c > 0
         dma("Y", T["teamI" + H][0:64, :], T.team[R, :], 262144, after, ["teamI" + H])
-        ops[-1]["soft"] = True
         for c in range(4):
             C = slice(1024 * c, 1024 * c + 1024)
-            if c < PV[s]:
-                cp(prg[64:128, C], prg[0:64, C], ["prg%d%sa" % (c, H)], ["prg%d%sb" % (c, H)], 0.5)
-            else:
-                act(prg[64:128, C], prg[0:64, C], CPY, ["prg%d%sa" % (c, H)], ["prg%d%sb" % (c, H)])
+            move(PV[s][c], prg[64:128, C], prg[0:64, C], ["prg%d%sa" % (c, H)], ["prg%d%sb" % (c, H)], 0.5)
 
     for s in range(2):
         for h in range(2):
@@ -179,7 +210,6 @@ def build_ops(g, T, topo, core, rank):
     iota(T.E[:, 0:128], [[1, 8], [0, 16]], 0, 0, ["E0"])
     iota(T.io2[:], [[0, 8], [1, 16]], 0, 0, ["io2"])
     iota(T.io3[:], [[1, 128]], 0, 0, ["io3"])
-    iota(T.aK[:, 0:128], [[0, 2], [1, 64]], 0, 0, ["aK0"])
     iota(T.eM[:], [[1, 256]], 0, 256, ["eM0", "eM1"], False)
     ts(ci[:, 4:5], ci[:, 0:1], 15, None, AND, None, ["ci0"], ["ci4"])
     ts(ci[:, 8:9], ci[:, 0:1], 4, None, SHR, None, ["ci0"], ["ci8"])
@@ -188,16 +218,30 @@ def build_ops(g, T, topo, core, rank):
     ts(T.blk[:], T.E[:, 0:128], gc_, None, EQ, None, ["E0", "cf"], ["blk"])
     ts(T.msk[:], T.io2[:], rc, None, EQ, None, ["io2", "cf"], ["msk"])
     ts(T.idn[:], T.io3[:], pc, None, EQ, None, ["io3", "cf"], ["idn"])
-    ts(T.rst[:], T.io2[:], 0.5, None, ALU.is_gt, None, ["io2"], ["rst"])
-    ts(T.PA[:], T.aK[:, 0:128], pc, None, EQ, None, ["aK0", "cf"], ["PA"])
-    ts(T.PB[:], T.aK[:, 0:128], 64.0, pc, ADD, EQ, ["aK0", "cf"], ["PB"])
+    def pick(out, pat, base, val, w):
+        iota(out, [[0, wd(out)]], val, 0, w)
+        add("G", 0.17 + 2 * wd(out) * CY, lambda: g.affine_select(out, out, pat, EQ, 0.0, base, 1), w, w)
+    pick(T.SelY[0:8, :], [[-1, 8], [0, 16]], 0, 1, ["SelY"])
+    pick(T.PA[:], [[0, 2], [-1, 64]], 0, 1, ["PA"])
+    pick(T.PB[:], [[0, 2], [-1, 64]], -64, 1, ["PB"])
+    act(T.nI24[:], T.idn[:], CPY, ["idn"], ["nI24"], scale=-16777216.0)
     tt(T.blk2[:, 0:64], T.blk[:, 0:64], T.blk[:, 64:128], ADD, ["blk"], ["blk2a"])
     act(T.blk2[:, 64:128], T.blk2[:, 0:64], CPY, ["blk2a"], ["blk2b"])
-    act(T.Wx[:], T.blk[:], CPY, ["blk"], ["Wx"], scale=32768.0)
-    act(T.blk256[:], T.blk[:], CPY, ["blk"], ["blk256"], scale=256.0)
+    act(T.blkE[:], T.blk[:], CPY, ["blk"], ["blkE"], scale=256.0)
+    act(T.Jm[:], T.io3[:], CPY, ["io3", "idn"], ["Jm"], scale=T.idn[:, 0:1])
     act(T.blk8[:], T.blk[:, 0:128:16], CPY, ["blk"], ["blk8"])
-    act(T.Wm[:], T.blk[:, 0:128:16], CPY, ["blk"], ["Wm"], scale=-65536.0)
-    act(T.nI256[:], T.idn[:], CPY, ["idn"], ["nI256"], scale=-256.0)
+    ms(T.Wm[:], 0.0, ["Wm"], 0.5)
+    act(T.Wm[:, 15:143:16], T.blk[:, 0:128:16], CPY, ["blk"], ["Wm"], scale=-65536.0)
+    act(T.CI[:, 0:128], T.idn[:], CPY, ["idn"], ["CI"], scale=482.0 * 32768.0)
+    ts(cf[:, 7:8], rc, 15.5 - SW, -240.0 * 32768.0, ALU.is_gt, MUL, ["cf"], ["k7"])
+    act(T.CI[:, 128:256], T.idn[:], CPY, ["idn", "k7"], ["CJ"], scale=cf[:, 7:8])
+    act(T.nI512[:], T.idn[:], CPY, ["idn"], ["nI512"], scale=-512.0)
+    ts(T.rst[:], T.io2[:], 0.5, None, ALU.is_gt, None, ["io2"], ["rst"])
+    act(T.Wp[:, 32:40], T.blk8[:], CPY, ["blk8"], ["Wm8"], scale=-65536.0)
+    ms(T.c1[:], -255.0 / 128.0, ["c1"], 0.5)
+    ms(T.c2[:], 1.5 * 2.0 ** 25, ["c2"], 0.5)
+    ts(cf[:, 5:6], rc, -2048.0, 32768.0, MUL, ADD, ["cf"], ["kb"])
+    act(T.CI[:, 256:384], T.idn[:], CPY, ["idn", "kb"], ["CK"], scale=cf[:, 5:6])
     act(T.nI23[:], T.idn[:], CPY, ["idn"], ["nI23"], scale=-8388608.0)
     act(T.pI23[:], T.idn[:], CPY, ["idn"], ["pI23"], scale=8388608.0)
     m = T.msk
@@ -208,7 +252,6 @@ def build_ops(g, T, topo, core, rank):
     for j in range(1, 4):
         act(T.Wp[:, 8 * j:8 * j + 8], T.blk8[:], CPY, ["blk8", "r01"], ["Wp%d" % j], scale=cf[:, 1:2])
     WP = ["Wp0", "Wp1", "Wp2", "Wp3"]
-    ts(T.Ws[:], T.blk[:], cf[:, 2:3], -1.0, MUL, MUL, ["blk", "r34"], ["Ws"])
     ms(T.WN[:], 0.0, ["WN"], 0.5)
     ms(T.WD[:], 0.0, ["WD"], 0.5)
     act(T.WN[:, 15:143:16], T.blk8[:], CPY, ["blk8", "r34"], ["WN"], scale=cf[:, 2:3])
@@ -217,37 +260,37 @@ def build_ops(g, T, topo, core, rank):
     cp(T.WE[:, 15:79:16], T.blk2[:, 0:64:16], ["blk2a"], ["WE"])
     cp(T.WE[:, 79:143:16], T.blk2[:, 0:64:16], ["blk2a"], ["WE"])
     ms(T.ones[:], 1.0, ["ones"], 0.5)
-    ms(T.m8[:, 0:8], -0.0625, ["m8"], 0.5)
-    ms(T.m8[:, 16:144], 0.0, ["idn8"], 0.5)
-    idn = T.idn
-    ts(cf[:, 5:6], idn[:, 0:1], 241.0 * 32768.0, None, MUL, None, ["idn"], ["k0"])
-    ts(cf[:, 6:7], idn[:, 2:3], 7.0, cf[:, 5:6], MUL, ADD, ["idn", "k0"], ["k1"])
-    ts(cf[:, 7:8], idn[:, 1:2], -2048.0, None, MUL, None, ["idn"], ["k2"])
-    ts(T.Z[:, 0:128], T.io2[:], -16.0, cf[:, 7:8], ADD, MUL, ["io2", "k2"], ["Z0"])
-    ts(T.Cm[:], T.Z[:, 0:128], cf[:, 6:7], None, ADD, None, ["Z0", "k1"], ["Cm"])
-    act(T.Jm[:], T.io3[:], CPY, ["io3", "idn"], ["Jm"], scale=idn[:, 0:1])
+    ms(T.m8[:, 0:8], (PC - 8) / 128.0, ["m8"], 0.5)
     ts(T.Z[:, 128:144], T.io3[:, 0:16], -1.0, 15.0, MUL, ADD, ["io3"], ["Z1"])
     ts(T.OH[:, 0:16], T.Z[:, 128:144], rc, None, EQ, None, ["Z1", "cf"], ["OHa"])
     ts(T.OH[:, 16:32], T.io3[:, 0:16], 0.0, cf[:, 1:2], MUL, ADD, ["io3", "r01"], ["OHb"])
-    act(T.KP[:], T.OH[:], IDN, ["OHa", "OHb"], ["KP"], bias=1.0, scale=-1.0)
-    ts(T.l15[:], T.io3[:, 0:8], 16.0, 15.0, MUL, ADD, ["io3"], ["l15"])
+    act(T.KP[:, 0:16], T.OH[:, 0:16], IDN, ["OHa"], ["KPa"], bias=1.0, scale=12.0)
+    act(T.KP[:, 16:32], T.OH[:, 16:32], IDN, ["OHb"], ["KPb"], bias=1.0, scale=-1.0)
+    act(T.Pq[:, 0:128], T.PB[:], CPY, ["PB"], ["Pq0"], scale=-4096.0)
+    act(T.Pq[:, 128:256], T.PA[:], CPY, ["PA"], ["Pq1"], scale=-4096.0)
     cp(T.l1[:], T.io3[:, 0:8], ["io3"], ["l1"])
-    ts(T.cj[:], T.io3[:, 0:8], 16.0, rc, MUL, ADD, ["io3", "cf"], ["cj"])
-    act(T.cdum[:], T.cj[:], IDN, ["cj"], ["cdum"], bias=float(DC))
-    act(T.ctop[:], T.cj[:], IDN, ["cj"], ["ctop"], bias=float(DT))
-    act(T.cb[:], T.cj[:], IDN, ["cj"], ["cb"], bias=15.0, scale=16.0)
-    act(T.cnb[:], T.cj[:], IDN, ["cj"], ["cnb"], bias=-0.25, scale=1.0 / 256.0)
-    ms(T.Aa[:], 0, ["Aa0", "Aa1"])
-    ms(T.A7f[:], 0.0, ["A7f0", "A7f1"])
+    cj, cdum, ctop, cnb, cb = [T.cs[:, 8 * j:8 * j + 8] for j in range(5)]
+    ts(cj, T.io3[:, 0:8], 16.0, rc, MUL, ADD, ["io3", "cf"], ["cj"])
+    act(cdum, cj, IDN, ["cj"], ["cdum"], bias=float(DC))
+    act(ctop, cj, IDN, ["cj"], ["ctop"], bias=float(DT))
+    act(cnb, cj, IDN, ["cj"], ["cnb"], bias=-0.25, scale=1.0 / 256.0)
+    ts(cf[:, 6:7], rc, 128.0, 15.0, MUL, ADD, ["cf"], ["k6"])
+    act(cb, T.io3[:, 0:8], IDN, ["io3", "k6"], ["cb"], bias=cf[:, 6:7], scale=16.0)
+    ts(ci[:, 12:13], ci[:, 0:1], 7, None, AND, None, ["ci0"], ["ci12"])
+    ts(ci[:, 13:14], ci[:, 0:1], 3, 1, SHR, AND, ["ci0"], ["ci13"])
+    cp(cf[:, 16:17], ci[:, 13:14], ["ci13"], ["k16"])
+    ts(cf[:, 17:18], ci[:, 12:13], 16.0, cf[:, 16:17], MUL, ADD, ["ci12", "k16"], ["k17"])
+    ts(T.lp[:], T.io3[:, 0:8], 2.0, cf[:, 17:18], MUL, ADD, ["io3", "k17"], ["lp"])
+    ms(T.An[:], -1032.0, ["An0", "An1", "A70", "A71"])
     ts(T.eI[:], T.eM[:], 4095, None, AND, None, ["eM0", "eM1"], ["eI0", "eI1"])
     cp(cA[:, 1536:1792], T.eI[:], ["eI0", "eI1"], ["cN"])
     act(T.pen[:, 0:256], cA[:, 1536:1792], CPY, ["cN"], ["pen0"])
     tt(cA[:, 1792:2048], cA[:, 1536:1792], T.pen[:, 0:256], SUB, ["cN", "pen0"], ["cN8"])
     act(cA[:, 1792:2048], cA[:, 1792:2048], IDN, ["cN8"], ["cN8"], bias=8.0)
 
-    def k_to_l(out, Wb, src, c0, first, lastf, r, w):
+    def k_to_l(out, Wb, src, first, lastf, r, w):
         for rr in range(16):
-            mm(out, Wb[:, 15 - rr:143 - rr], src[:, c0 + rr:c0 + 128:16], first and rr == 0, lastf and rr == 15, r, w)
+            mm(out, Wb[:, 15 - rr:143 - rr], src(rr), first and rr == 0, lastf and rr == 15, r, w)
 
     nxt = T.cores[(rank + 1) % N]
     nrid, npid, nse = topo.addr(nxt)
@@ -257,8 +300,8 @@ def build_ops(g, T, topo, core, rank):
     def send(out, src, r, w):
         sem = "r%d" % nsend[0]
         nsend[0] += 1
-        add("G", 1.0, lambda: g.remote_dma(out, src, T.sem[sem], T.sem.sent, npid, nrid, nmask), r, w,
-            kind="rem", lat=2.0, extra=(sem, neng))
+        add("G", cost[5], lambda: g.remote_dma(out, src, T.sem[sem], T.sem.sent, npid, nrid, nmask), r, w,
+            kind="rem", lat=cost[6], extra=(sem, neng))
 
     def stream(s):
         H = str(s)
@@ -279,24 +322,22 @@ def build_ops(g, T, topo, core, rank):
         WALL = PAY + k("Wt", "Wu", "Wz", "Wx")
         PRG = ab("prg0", "prg1", "prg2", "prg3")
         XB = ab("xb")
+        NK = k("NK")
         xb = T.xb[:, K]
 
         if s == 0:
-            iota(W[:, 0:1024], [[1, 1024]], 0, 0, k("Wfa"))
-            act(W[:, 1024:2048], W[:, 0:1024], IDN, k("Wfa"), k("Wfb"), bias=1024.0)
-            act(W[:, 2048:3072], W[:, 0:1024], IDN, k("Wfa"), k("Wfc"), bias=2048.0)
-            iota(W[:, 3072:4096], [[1, 1024]], 3072, 0, k("Wfd"))
+            iota(W[:, PC:PC + 1024], [[1, 1024]], 0, 0, k("Wfa"))
+            act(W[:, PC + 1024:PC + 2048], W[:, PC:PC + 1024], IDN, k("Wfa"), k("Wfb"), bias=1024.0)
+            act(W[:, PC + 2048:PC + 3072], W[:, PC:PC + 1024], IDN, k("Wfa"), k("Wfc"), bias=2048.0)
+            iota(W[:, PC + 3072:DC], [[1, 1024]], 3072, 0, k("Wfd"))
         else:
             for j, t in enumerate(FILL):
-                iota(W[:, 1024 * j:1024 * j + 1024], [[1, 1024]], 1024 * j, 0, [t])
-        ms(W[:, ZC:TC], 0.0, k("Wz"))
-        if s == 0:
-            ms(W[:, DT:WN], 0.0, k("Wx"))
-        else:
-            iota(W[:, DT:WN], [[0, WN - DT]], 0, 0, k("Wx"))
-        iota(ef[:, 0:1024], [[0, 1024]], 0, 0, k("ef0"))
-        cp(W[0:64, TC:DT], T["teamI" + H][0:64, :], k("teamI"), k("Wt"))
-        act(W[64:128, TC:DT], W[0:64, TC:DT], CPY, k("Wt"), k("Wu"))
+                iota(W[:, PC + 1024 * j:PC + 1024 * j + 1024], [[1, 1024]], 1024 * j, 0, [t])
+        iota(W[:, 0:TC], [[0, TC]], 0, 0, k("Wz"))
+        iota(W[:, DC:WS], [[0, WS - DC]], 0, 0, k("Wx"))
+        iota(ef[:, 0:16], [[0, 16]], 0, 0, k("ef0"))
+        cp(W[0:64, TC:PC], T["teamI" + H][0:64, :], k("teamI"), k("Wt"))
+        move(PV[s][4], W[64:128, TC:PC], W[0:64, TC:PC], k("Wt"), k("Wu"))
         c0 = 768 * s
         cp(cA[:, c0:c0 + 256], T.actI[:, 256 * s:256 * s + 256], ab("actI"), k("cA0"))
         hb = T.pab[:, 384 * s:384 * s + 256]
@@ -304,56 +345,81 @@ def build_ops(g, T, topo, core, rank):
         tt(cA[:, c0 + 256:c0 + 512], cA[:, c0:c0 + 256], hb, SUB, k("cA0", "pab"), k("cA1"))
         act(cA[:, c0 + 256:c0 + 512], cA[:, c0 + 256:c0 + 512], IDN, k("cA1"), k("cA1"), bias=8.0)
         for q in range(16):
-            mm(pU[:, 0:256], T.WE[0:64, 15 - q:143 - q], prg[0:64, 256 * q:256 * q + 256], q == 0, q == 15,
+            mm(pU[:, 0:2, :], T.WE[0:64, 15 - q:143 - q], prg[0:64, 256 * q:256 * q + 256], q == 0, q == 15,
                ["WE", "prg%d%sa" % (q // 4, H)], k("pU"))
-        act(cA[:, c0 + 512:c0 + 768], pU[:, 0:256], CPY, k("pU"), k("cA2"))
+        act(cA[:, c0 + 512:c0 + 768], pU[:, 0:2, :], CPY, k("pU"), k("cA2"))
         for row, a, tok in ((4, 1792, "cN8"), (0, c0, "cA0" + H), (1, c0 + 256, "cA1" + H), (2, c0 + 512, "cA2" + H)):
-            dma("Y", W[row:128:16, 0:4096], cA[:, a:a + 256], 131072, [tok] + FILL, k("W%d" % row))
+            dma("Y", W[row:128:16, PC:DC], cA[:, a:a + 256], 131072, [tok] + FILL, k("W%d" % row))
         for h in range(2):
-            dma("Y", ef[64 * h:64 * h + 64, 1024:2048], T.eff[64 * s:64 * s + 64, :], 131072, k("cA2"), ["ef1" + H + "ab"[h]])
+            dma("Y", ef[64 * h:64 * h + 64, 16:1040], T.eff[64 * s:64 * s + 64, :], 131072, [], ["ef1" + H + "ab"[h]])
         if s == 0:
             iota(Y[:, 128:1152], [[0, 1024]], 0, 0, ["Yf"])
-            dma("Y", Y[0:128:16, 128:1152], W[3:128:16, 0:1024], 32768, ["Yf", "Wfa0", "W40"], ["Y0"])
-            dma("Y", Y[1:128:16, 128:1152], W[4:128:16, 0:1024], 32768, ["Yf", "W40"], ["Y1"])
-        cp(cf[:, 12 + s:13 + s], T.wtI[:, c4], ab("wtI"), k("wf"))
+            dma("Y", Y[0:128:16, 128:1152], W[3:128:16, PC:PC + 1024], 32768, ["Yf", "Wfa0", "W40"], ["Y0"])
+            dma("Y", Y[1:128:16, 128:1152], W[4:128:16, PC:PC + 1024], 32768, ["Yf", "W40"], ["Y1"])
+        ts(cf[:, 12 + s:13 + s], T.wtI[:, c4], 2.0, None, MUL, None, ab("wtI"), k("wf"))
         act(T.We[:, K], T.blk[:], CPY, ["blk"] + k("wf"), k("We"), scale=cf[:, 12 + s:13 + s])
-        ts(T.P0[:, 24 * s + 8:24 * s + 16], T.cj[:], 1024.0 * s, None, ADD, None, ["cj"], k("P0b"))
+        nd = 3 if G3 else 1
+        D = slice(24, 24 + 8 * nd)
+        TH = slice(24 * s, 24 * s + 8 * nd)
+        ts(T.P0[:, 24 * s + 8:24 * s + 16], cj, 1024.0 * s, None, ADD, None, ["cj"], k("P0b"))
         ms(T.P1[:, 24 * s + 16:24 * s + 24], 16.0, k("P1c"))
 
         def distance(x, xt, goal, gt):
-            mm(pE[:, 0:128], T.pI23[:], x, True, False, ["pI23"] + xt, k("pE"))
-            mm(pE[:, 0:128], T.nI23[:], goal, False, True, ["nI23"] + gt, k("pE"))
-            act(T.ad[:, K], pE[:, 0:128], ABS, k("pE"), k("ad"), scale=1.0 / 8388608.0)
-            k_to_l(pU[:, 24:32], T.WD, T.ad, 128 * s, True, True, ["WD"] + k("ad"), k("pU"))
+            for j in range(nd):
+                mm(pE[:, j, :], T.nI23[:], goal, j == 0, False, ["nI23"] + gt, k("pE"))
+            for j in range(nd):
+                mm(pE[:, j, :], T.pI23[:], x, False, j == nd - 1, ["pI23"] + xt, k("pE"))
+            act(T.ad[:, 3 * s:3 * s + nd, :], pE[:, 0:nd, :], ABS, k("pE"), k("ad"), scale=1.0 / 8388608.0)
+            k_to_l(pU[:, 0, D], T.WD, lambda rr: T.ad[:, 3 * s:3 * s + nd, rr:128:16], True, True, ["WD"] + k("ad"), k("pU"))
+
+        def turn(src, n, j, r, bias):
+            mm(pT[0:n, 128:256], src, T.idn[:], True, True, ["idn"] + r, k("pT"), True)
+            act(T.TT[0:n, 384 * s + 128 * j:384 * s + 128 * j + 128], pT[0:n, 128:256], IDN, k("pT"), k("TT%d" % j),
+                bias=bias)
         ts(T.A0[:, L], T.stI[:, L], -1.0, 1023.0, MUL, ADD, ab("stI"), k("A0"))
 
         for v in range(NV):
             last = v == NV - 1
             if v > 0:
-                b0 = 16 * (2 * (v - 1) + s)
-                tok = ["land%d_%d" % (v - 1, s)]
+                b0 = 32 * (2 * (v - 1) + s)
                 x0 = 256 * (v - 1) + 128 * s
                 xb, XB = T.landb[:, x0:x0 + 128], k("landb%d" % (v - 1))
-                A0, a0t = T.land[:, b0:b0 + 8], tok
-                ts(T.off[:, L], A0, -1.0, 1023.0, MUL, ADD, tok, k("offa"))
-                ts(T.thr[:, L], T.land[:, b0 + 8:b0 + 16], T.A7f[:, c4], None, SUB, None, tok + k("A7f"), k("thr"))
+                A0, a0t = T.land[:, b0:b0 + 8], k("land%d" % (v - 1))
+                ts(T.off[:, L], A0, -1.0, 1023.0, MUL, ADD, a0t, k("offa"))
+                bar = (T.land[:, b0 + 8:b0 + 8 + 8 * nd], k("land%d" % (v - 1), "A7"))
             else:
                 A0, a0t = T.A0[:, L], k("A0")
                 cp(T.off[:, L], T.stI[:, L], ab("stI"), k("offa"))
-            mm(pE[:, 128:256], T.We[:, K], xb, True, True, k("We") + XB, k("pE"))
-            cp(T.eI[:, K], pE[:, 128:256], k("pE"), k("eI"))
-            ts(T.eM[:, K], T.eI[:, K], 255, None, AND, None, k("eI"), k("eM"))
+            turn(A0, 8, 0, a0t, -1031.0)
             uu, ut = T.cK[:, K], k("uK")
-            ts(uu, T.eM[:, K], 2.0, 33.0, MUL, ADD, k("eM"), ut)
-            XR = k(*["xr%d_" % j for j in range(16)])
-            for j in range(16):
-                if j < (XV if v else XV0[s]):
-                    cp(xr[:, j:2048:16], xb, XB, [XR[j]], 0.5)
-                elif v and j >= 16 - XG:
-                    add("G", 0.17 + 256 * CY, lambda j=j, xb=xb: g.affine_select(
-                        xr[:, j:2048:16], xb, [[0, 128]], ALU.is_ge, 0.0, 0, 0), XB, [XR[j]])
+            if EV[min(v, 1)]:
+                mm(pE[:, 1, :], T.We[:, K], xb, True, True, k("We") + XB, k("pE"))
+                cp(T.eI[:, K], pE[:, 1, :], k("pE"), k("eI"))
+                ts(T.eM[:, K], T.eI[:, K], 511, None, AND, None, k("eI"), k("eM"))
+                ts(uu, T.eM[:, K], 33.0, None, ADD, None, k("eM"), ut)
+            else:
+                mm(pE[:, 1, :], T.c1[:], T.ones[:], True, False, ["c1", "ones"], k("pE"))
+                mm(pE[:, 1, :], T.We[:, K], xb, False, True, k("We") + XB, k("pE"))
+                act(T.hE[:, K], pE[:, 1, :], IDN, k("pE"), k("hE"), bias=1.5 * 2.0 ** 23, scale=1.0 / 512.0)
+                mm(pE[:, 2, :], T.nI512[:], T.hE[:, K], True, False, ["nI512"] + k("hE"), k("pE"), True)
+                mm(pE[:, 2, :], T.c2[:], T.ones[:], False, False, ["c2", "ones"], k("pE"))
+                mm(pE[:, 2, :], T.We[:, K], xb, False, True, k("We") + XB, k("pE"))
+                act(uu, pE[:, 2, :], IDN, k("pE"), ut, bias=33.0)
+            first, who, parts = XE[s] if v == 0 else XE[2]
+            out, ot = T.xp[:, K], k("xp")
+            if first == "V":
+                add("V", 0.06 + 128 * GA * CY, lambda xb=xb, out=out: V.tensor_copy(out, xb.indirect(T.lp[:])),
+                    XB + ["lp"], ot)
+            else:
+                sga(out, xb, T.lp[:], XB + ["lp"], ot)
+            XJ = k(*["xj%d_" % j for j in range(4)])
+            x4, X4 = T.xp[:, 256 + 512 * s:768 + 512 * s], k(*["xq%d_" % j for j in range(4)])
+            for j, e in enumerate(who + parts):
+                if j < 4:
+                    out, src, rd, wr = T.xp[:, 256 + 512 * s + j:768 + 512 * s:4], T.xp[:, K], k("xp"), [X4[j]]
                 else:
-                    act(xr[:, j:2048:16], xb, CPY, XB, [XR[j]])
+                    out, src, rd, wr = xr[:, j - 4:2048:4], x4, X4, [XJ[j - 4]]
+                move(e, out, src, rd, wr, 0.5)
             act(Y[:, 1152 * s:1152 * s + 128], uu, IDN, ut, k("Ye"), bias=-1599.5, scale=48.5)
             act(T.A0p[:, L], A0, IDN, a0t, k("A0p"), bias=1024.0)
 
@@ -362,77 +428,117 @@ def build_ops(g, T, topo, core, rank):
                 of = T.off[:, 16 * st + 8 * s:16 * st + 8 * s + 8]
                 oft = k("off" + "abc"[st])
                 TKc = 384 * s
-                sga(T.TK[:, TKc + 128 * st:TKc + 128 * st + 128], W[:, 0:2048], of, oft + PAY, k("TK%d" % st))
-                gtt(T.mK[:, K], W[:, TC:WN], of, T.cK[:, K], MUL, oft + k("Wt", "Wu", "Wx", "uK"), k("mK"))
-                ts(T.nK[:, K], T.mK[:, K], 5, 4095, SHR, AND, k("mK"), k("nK"))
-                cp(T.n16[:, K], T.nK[:, K], k("nK"), k("n16"))
-                GM = k(*["Gm%d_" % c for c in range(len(VCH))])
-                GP = k(*["Gp%d_" % c for c in range(SCH)])
-                a0 = 0
-                for c, w in enumerate(VCH):
-                    gtt(Gm[:, c, :], prg[:], T.n16[:, 128 * s + a0:128 * s + a0 + w],
-                        xr[:, 16 * a0:16 * (a0 + w)], MAX, k("n16") + PRG + XR, [GM[c]])
-                    ops[-1]["soft"] = c > 0
-                    a0 += w
-                w = 128 // SCH
-                for c in range(SCH):
-                    sga(Gp[:, 16 * w * c:16 * w * (c + 1)], W[:, 0:4096], T.n16[:, 128 * s + w * c:128 * s + w * (c + 1)],
-                        k("n16") + PAY, [GP[c]])
-                    ops[-1]["soft"] = c > 0
-                mm(pU[:, 0:128], T.ones[:], T.Cm[:], True, False, ["ones", "Cm"], k("pU"))
+                gtt(T.mK[:, K], W[:, TC:TC + (2048 if st else 1024)], of, T.cK[:, K], MUL,
+                    oft + k("Wt", "Wu", "uK") + (PAY if st else []), k("mK"))
+                if N16:
+                    add("V", 0.06 + 128 * GA * CY, lambda: V.tensor_scalar(
+                        T.n16[:, K], T.mK[:, K].indirect(T.lp[:]), 5, 4095, SHR, AND), k("mK") + ["lp"], k("n16"))
+                else:
+                    ts(T.nK[:, K], T.mK[:, K], 5, 4095, SHR, AND, k("mK"), k("nK"))
+                    add("V", NX + 0.06 + 128 * GA * CY, lambda: V.tensor_copy(T.n16[:, K], T.nK[:, K].indirect(T.lp[:])),
+                        k("nK") + ["lp"], k("n16"))
+                share = SHARE[s][st]
+                GM, GP = k(*["Gm%d_" % r for r in range(16)]), k(*["Gp%d_" % r for r in range(16)])
+                a = 0
+                for w in VCH[share]:
+                    gtt(Gm[:, 128 * a:128 * (a + w)], prg[:], T.n16[:, 128 * s + 8 * a:128 * s + 8 * (a + w)],
+                        xr[:, 128 * a:128 * (a + w)], MAX, k("n16") + PRG + XJ, GM[a:a + w])
+                    ops[-1]["soft"] = a > 0
+                    a += w
+                if share:
+                    gs = T.Gs[:, 512 * s:512 * s + 128 * SW]
+                    sga(gs, prg[:], T.n16[:, 128 * s + 8 * a:128 * s + 128], k("n16") + PRG, k("Gs"))
+                    mm(pE[:, 0:SW, :], T.nI23[:], xr[:, 128 * a:2048], True, False, ["nI23"] + XJ, k("pE"))
+                    mm(pE[:, 0:SW, :], T.pI23[:], gs, False, True, ["pI23"] + k("Gs"), k("pE"))
+                    act(Gm[:, 128 * a:2048], pE[:, 0:SW, :], RELU, k("pE"), GM[a:16], scale=1.0 / 8388608.0)
+                a = 0
+                for w in SCH:
+                    sga(Gp[:, 128 * a:128 * (a + w)], W[:, PC:DC], T.n16[:, 128 * s + 8 * a:128 * s + 8 * (a + w)],
+                        k("n16") + PAY, GP[a:a + w])
+                    ops[-1]["soft"] = a > 0
+                    a += w
+                mm(pU[:, 0, :], T.CI[:, 256:384], T.ones[:], True, False, ["CK", "ones"], k("pU"))
                 for t in range(nt):
-                    mm(pU[:, 128 + 128 * t:256 + 128 * t], T.TK[:, TKc + 128 * t:TKc + 128 * t + 128], T.Ws[:],
-                       False, False, k("TK%d" % t) + ["Ws"], k("pU"))
-                for j in range(16):
-                    mm(pU[:, j:128 * (nt + 1):16], Gp[:, j:2048:16], T.Wp[:, 0:8 * (nt + 1)], False, j == 15, GP + WP, k("pU"))
-                act(T.kp[:, K], pU[:, 0:128], CPY, k("pU"), k("kp"))
+                    mm(pU[:, 1 + t, :], T.SelY[0:8, :], T.TT[0:8, TKc + 128 * t:TKc + 128 * t + 128], False, False,
+                       ["SelY"] + k("TT%d" % t), k("pU"), True)
+                jobs, a = [], 0
+                for w in SCH:
+                    jobs.append((a + w, 1, a, w))
+                    a += w
+                a = 0
+                for w in VCH[share][:NY]:
+                    jobs.append((a + w, 0, a, w))
+                    a += w
+                ny = a
+                jobs.sort()
+                for job in jobs:
+                    a, w = job[2:]
+                    for r in range(a, a + w):
+                        end = job is jobs[-1] and r == a + w - 1
+                        if job[1]:
+                            mm(pU[:, 0:nt + 1, r:128:16], Gp[:, 128 * r:128 * r + 128], T.Wp[:, 0:8 * (nt + 1)], False, end,
+                               GP[a:a + w] + WP, k("pU"))
+                        else:
+                            mm(pU[:, 0, r:128:16], Gm[:, 128 * r:128 * r + 128], T.Wp[:, 32:40], False, end,
+                               GM[a:a + w] + ["Wm8"], k("pU"))
+                act(T.kp[:, K], pU[:, 0, :], IDN, k("pU"), k("kp"), bias=7.0)
                 pen = T.pen[:, TKc:TKc + 128 * nt]
                 if PENV[st]:
-                    ts(pen, pU[:, 128:128 + 128 * nt], 0.0, None, EQ, None, k("pU"), k("pen"))
+                    ts(pen, pU[:, 1:nt + 1, :], 0.0, None, EQ, None, k("pU"), k("pen"))
                 else:
                     pab = T.pab[:, TKc:TKc + 128 * nt]
-                    act(pab, pU[:, 128:128 + 128 * nt], ABS, k("pU"), k("pab"))
+                    act(pab, pU[:, 1:nt + 1, :], ABS, k("pU"), k("pab"))
                     act(pen, pab, RELU, k("pab"), k("pen"), bias=1.0, scale=-1.0)
-                mm(pK[:, 0:128], xb, T.Wx[:], True, False, XB + ["Wx"], k("pK"))
-                for rep in range(EXTRA):
-                    mm(pK[:, 0:128], T.pI23[:], T.m8[:, 16:144], False, False, ["pI23", "idn8"], k("pK"))
-                    mm(pK[:, 0:128], T.nI23[:], T.m8[:, 16:144], False, False, ["nI23", "idn8"], k("pK"))
-                for j in range(16):
-                    mm(pK[:, j:128:16], Gm[:, :, j:512:16], T.Wm[:], False, False, GM + ["Wm"], k("pK"))
-                mm(pK[:, 0:128], T.idn[:], T.kp[:, K], False, False, ["idn"] + k("kp"), k("pK"), True)
+                KX = pK[:, 0:128]
+                mm(KX, T.CI[:, 0:128], T.ones[:], True, False, ["CI", "ones"], k("pK"))
+                if share:
+                    mm(KX, T.CI[:, 128:256], T.ones[:], False, False, ["CJ", "ones"], k("pK"))
+                a = ny
+                for w in VCH[share][NY:] + ((SW,) if share else ()):
+                    for r in range(a, a + w):
+                        mm(KX, T.Wm[:, 15 - r:143 - r], Gm[:, 128 * r:128 * r + 128], False, False,
+                           GM[a:a + w] + ["Wm"], k("pK"))
+                    a += w
+                mm(KX, T.kp[:, K], T.idn[:], False, False, ["idn"] + k("kp"), k("pK"), True)
                 for t in range(nt):
-                    mm(pK[:, 0:128], T.nI23[:], T.pen[:, TKc + 128 * t:TKc + 128 * t + 128], False, t == st,
-                       ["nI23"] + k("pen"), k("pK"))
-                add("V", cyc(128), lambda: V.tensor_tensor_scan(T.Z[:, K], T.rst[:], pK[:, 0:128], 0.0, MUL, MAX),
-                    ["rst"] + k("pK"), k("Z"))
-                gtt(T.E[:, K], T.Z[:, K], T.l15[:], T.msk[:], MUL, k("Z") + ["l15", "msk"], k("E"))
-                ps = pT[:, 0:8]
-                if st > 0:
-                    mm(ps, T.nI23[:], (T.p2, T.p3)[st - 1][:, L], True, False, ["nI23"] + k("p%d" % nt), k("pT"))
-                mm(ps, T.E[:, K], T.blk8[:], st == 0, True, k("E") + ["blk8"], k("pT"), True)
+                    mm(KX, T.pen[:, TKc + 128 * t:TKc + 128 * t + 128], T.nI24[:], False, t == st,
+                       ["nI24"] + k("pen"), k("pK"))
+                ps, pst = T.ZW[:, 128 * s + 15:128 * s + 128:16], k("ZW")
+                add("V", cyc(128), lambda: V.tensor_tensor_scan(T.ZW[:, K], T.rst[:], pK[:, 0:128], 0.0, MUL, MAX),
+                    k("pK") + ["rst"], pst)
+                bi, bt = T.BI[:, 24 * s + 8 * st:24 * s + 8 * st + 8], k("BI%d" % nt)
+                if st == 0:
+                    cp(bi, ps, pst, bt)
+                else:
+                    tt(bi, ps, T.go[:, 16 * s + 8 * st - 8:16 * s + 8 * st], MUL, pst + k("go%d" % st), bt)
                 if st < 2:
-                    bi, a = (T.BI1, T.BI2)[st][:, L], (T.a1, T.a2)[st][:, L]
-                    bt, at = k("BI%d" % nt), k("a%d" % nt)
-                    ts(bi, ps, 0.0, None, MAX, None, k("pT"), bt)
+                    a, at = (T.a1, T.a2)[st][:, L], k("a%d" % nt)
+                    f0 = 16 * s + 8 * st
                     ts(a, bi, 2047, None, AND, None, bt, at)
                     ts(T.off[:, 16 * nt + 8 * s:16 * nt + 8 * s + 8], a, -1.0, 2047.0, MUL, ADD, at, k("off" + "abc"[nt]))
-                    ts((T.p2, T.p3)[st][:, L], a, 1024.0, None, LT, None, at, k("p%d" % (nt + 1)))
+                    ts(T.AF[:, f0:f0 + 8], a, -2055.0, None, ADD, None, at, k("af%d" % nt))
+                    ts(T.go[:, f0:f0 + 8], a, 1024.0, None, ALU.is_ge, None, at, k("go%d" % nt))
+                    turn(T.AF[:, f0:f0 + 8], 8, nt, k("af%d" % nt), 0.0)
                 if st == 0:
-                    act(T.q2[:, L], ps, IDN, k("pT"), k("q2"), bias=4096.0, scale=-1.0)
+                    act(T.q2[:, L], ps, IDN, pst, k("none", "q2"), bias=4096.0, scale=-1.0)
                     ts(T.kk1[:, L], bi, 11, 15, SHR, AND, bt, k("kk1"))
-                    tt(T.q1[:, L], T.cb[:], T.kk1[:, L], SUB, ["cb"] + k("kk1"), k("q1"))
+                    tt(T.q1[:, L], cb, T.kk1[:, L], SUB, ["cb"] + k("kk1"), k("q1"))
                     cp(T.le[:, L], T.q1[:, L], k("q1"), k("le"))
-                    sga(T.NK[:, K], Gp[:], T.le[:, L], GP + k("le"), k("NK"))
-                    mm(pE[:, 0:8], T.ones[:], T.m8[:, 0:8], True, False, ["ones", "m8"], k("pE"))
-                    mm(pE[:, 0:8], T.pI23[:], T.p2[:, L], False, False, ["pI23"] + k("p2"), k("pE"))
-                    k_to_l(pE[:, 0:8], T.WN, T.NK, 128 * s, False, True, ["WN"] + k("NK"), k("pE"))
-                    tt(T.P1[:, 24 * s:24 * s + 8], pE[:, 0:8], T.cdum[:], MIN, k("pE") + ["cdum"], k("P1a"))
+                    sga(T.NK[:, K], Gp[:], T.le[:, L], GP + k("le"), NK)
+                    mm(pT[:, 0:8], T.ones[:], T.m8[:, 0:8], True, False, ["ones", "m8"], k("pT"))
+                    mm(pT[:, 0:8], T.pI23[:], T.ones[:, 0:8], False, False, ["pI23", "ones"], k("pT"))
+                    mm(pT[:, 0:8], T.nI23[:], T.go[:, f0:f0 + 8], False, False, ["nI23"] + k("go1"), k("pT"))
+                    k_to_l(pT[:, 0:8], T.WN, lambda rr: T.NK[:, 128 * s + rr:128 * s + 128:16], False, True,
+                           ["WN"] + NK, k("pT"))
+                    tt(T.P1[:, 24 * s:24 * s + 8], pT[:, 0:8], cdum, MIN, k("pT") + ["cdum"], k("P1a"))
                     tt(T.i2[:, L], bi, T.A0p[:, L], MAX, bt + k("A0p"), k("i2"))
                     ts(T.Bw[:, L], T.i2[:, L], 32767, None, AND, None, k("i2"), k("Bw"))
                     tt(T.lt0[:, L], T.q2[:, L], A0, MAX, k("q2") + a0t, k("lt0"))
                     if v == 0:
                         distance(xb, XB, T.goals[:, K], ab("goal0"))
-                        act(T.thr[:, L], pU[:, 24:32], CPY, k("pU"), k("thr"))
+                        act(T.thr[:, TH], pU[:, 0, D], CPY, k("pU"), k("thr"))
+                    else:
+                        act(T.thr[:, TH], bar[0], IDN, bar[1], k("thr"), bias=T.An[:, 8 * s + 4:8 * s + 5])
                 if st == 1:
                     tt(T.kk1[:, L], bi, T.Bw[:, L], MAX, bt + k("Bw"), k("kk1"))
                     ts(T.Bw2[:, L], T.kk1[:, L], 32767, None, AND, None, k("kk1"), k("Bw2"))
@@ -440,15 +546,20 @@ def build_ops(g, T, topo, core, rank):
                     tt(T.i2[:, L], T.q1[:, L], T.lt0[:, L], MAX, k("q1", "lt0"), k("i2"))
                     ts(T.lt2[:, L], T.i2[:, L], 5119, None, AND, None, k("i2"), k("lt2"))
 
-            ps = pT[:, 0:8]
-            tt(T.Bw[:, L], ps, T.Bw2[:, L], MAX, k("pT", "Bw2"), k("Bw"))
-            tt(T.q1[:, L], ps, T.a2[:, L], MIN, k("pT", "a2"), k("q1"))
+            tt(T.Bw[:, L], bi, T.Bw2[:, L], MAX, k("BI3", "Bw2"), k("Bw"))
+            tt(T.q1[:, L], bi, T.a2[:, L], MIN, k("BI3", "a2"), k("q1"))
             ts(T.aw[:, L], T.Bw[:, L], 2047, None, AND, None, k("Bw"), k("aw"))
-            ts(T.le[:, L], T.aw[:, L], -1.0, 2047.0, MUL, ADD, k("aw"), k("le"))
-            gtt(T.NK[:, K], ef[:], T.le[:, L], xb, SUB, k("le", "ef0") + XB + ab("ef1"), k("NK"))
+            ts(T.le[:, L], T.aw[:, L], -1.0, 1039.0, MUL, ADD, k("aw"), k("le"))
             X0 = slice(256 * v + 128 * s, 256 * v + 128 * s + 128)
-            act(T.xn[:, X0], T.NK[:, K], ABS, k("NK"), k("xn%d" % v))
-            b0 = 16 * (2 * v + s)
+            if NKV:
+                gtt(T.NK[:, K], ef[:], T.le[:, L], xb, SUB, k("le", "ef0") + XB + ab("ef1"), NK)
+                act(T.xn[:, X0], T.NK[:, K], ABS, NK, k("xn%d" % v))
+            else:
+                sga(T.NK[:, K], ef[:], T.le[:, L], k("le", "ef0") + ab("ef1"), NK)
+                mm(pE[:, 3, :], T.pI23[:], xb, True, False, ["pI23"] + XB, k("pE"))
+                mm(pE[:, 3, :], T.nI23[:], T.NK[:, K], False, True, ["nI23"] + NK, k("pE"))
+                act(T.xn[:, X0], pE[:, 3, :], ABS, k("pE"), k("xn%d" % v), scale=1.0 / 8388608.0)
+            b0 = 32 * (2 * v + s)
             send(T.landb[:, X0], T.xn[:, X0], k("xn%d" % v), k("landb%d" % v))
             if last:
                 for h in range(2):
@@ -456,7 +567,7 @@ def build_ops(g, T, topo, core, rank):
                         k("landb%d" % v), [])
             distance(T.xn[:, X0], k("xn%d" % v), T.goals[:, 256 * v + 128 * s:256 * v + 128 * s + 128],
                      ab("goal0") if v == 0 else ["goalx"])
-            tt(T.good[:, L], pU[:, 24:32], T.thr[:, L], LT, k("pU", "thr"), k("good"))
+            tt(T.good[:, TH], pU[:, 0, D], T.thr[:, TH], LT, k("pU", "thr"), k("good"))
             tt(T.i2[:, L], T.q1[:, L], T.lt2[:, L], MAX, k("q1", "lt2"), k("i2"))
             ts(T.lt[:, L], T.i2[:, L], 5119, None, AND, None, k("i2"), k("lt"))
             ts(T.q2[:, L], T.aw[:, L], 1024.0, 8192.0, LT, MUL, k("aw"), k("q2"))
@@ -466,38 +577,35 @@ def build_ops(g, T, topo, core, rank):
             tt(cur, T.q3[:, L], T.q4[:, L], MAX, k("q3", "q4"), ct)
             act(T.P1[:, 24 * s + 8:24 * s + 16], cur, IDN, ct, k("P1b"), bias=1023.0 + 128 * (1 - s), scale=-1.0)
             if not last:
-                act(T.snd[:, b0 + 8:b0 + 16], pU[:, 24:32], CPY, k("pU"), k("sd%d" % v))
-                send(T.land[:, b0:b0 + 16], T.snd[:, b0:b0 + 16], k("sa%d" % v, "sd%d" % v),
-                     ["land%d_%d" % (v, s)])
+                act(T.snd[:, b0 + 8:b0 + 8 + 8 * nd], pU[:, 0, D], CPY, k("pU"), k("sd%d" % v))
+                send(T.land[:, b0:b0 + 8 + 8 * nd], T.snd[:, b0:b0 + 8 + 8 * nd], k("sa%d" % v, "sd%d" % v), k("land%d" % v))
 
             X = slice(24 * s, 24 * s + 24)
             ts(T.P0[:, 24 * s + 16:24 * s + 24], T.Bw[:, L], 11, 15, SHR, AND, k("Bw"), k("P0c"))
             ts(T.q1[:, L], T.lt[:, L], -1.0, float(TC + 1023), MUL, ADD, k("lt"), k("q1"))
-            tt(T.P0[:, 24 * s:24 * s + 8], T.q1[:, L], T.cdum[:], MAX, k("q1") + ["cdum"], k("P0a"))
+            tt(T.P0[:, 24 * s:24 * s + 8], T.q1[:, L], cj, MAX, k("q1") + ["cj"], k("P0a"))
             tt(T.Df[:, X], T.P1[:, X], T.P0[:, X], SUB, k("P0a", "P0b", "P0c", "P1a", "P1b", "P1c"), k("Df"))
-            for j in range(3):
-                c = slice(24 * s + 8 * j, 24 * s + 8 * j + 8)
-                tt(T.Dg[:, c], T.Df[:, c], T.good[:, L], MUL, k("Df", "good"), k("Dg%d" % j))
+            for j in range(3 // nd):
+                c = slice(24 * s + 8 * j, 24 * s + 8 * j + 8 * nd)
+                tt(T.Dg[:, c], T.Df[:, c], T.good[:, TH], MUL, k("Df", "good"),
+                   k("Dg0", "Dg1", "Dg2") if G3 else k("Dg%d" % j))
             tt(T.Sel[:, X], T.Dg[:, X], T.P0[:, X], ADD, k("Dg0", "Dg1", "Dg2", "P0a", "P0b", "P0c"), k("Sel"))
             idv = T.Sel[:, 24 * s:24 * s + 8]
             cp(T.ls[:, X], T.Sel[:, X], k("Sel"), k("ls"))
-            ts(T.l2[:, L], idv, float(ZC), None, MAX, None, k("Sel"), k("l2"))
             gtt(T.E[:, K], idv, T.l1[:], T.msk[:], MUL, k("Sel") + ["l1", "msk"], k("E"))
-            mm(pT[:, 16:24], T.nI256[:], T.cnb[:], True, False, ["nI256", "cnb"], k("pT"), True)
-            mm(pT[:, 16:24], T.nI256[:], idv, False, True, ["nI256"] + k("Sel"), k("pT"), True)
-            act(T.nb[:, L], pT[:, 16:24], CPY, k("pT"), k("nb"))
-            mm(pE[:, 0:128], T.ones[:], T.Jm[:], True, False, ["ones", "Jm"], k("pE"))
-            mm(pE[:, 0:128], T.blk256[:], T.E[:, K], False, True, ["blk256"] + k("E"), k("pE"), True)
-            o = 576 * s
-            AC = []
+            mm(pT[:, 16:24], T.nI512[:], cnb, True, False, ["nI512", "cnb"], k("pT"), True)
+            mm(pT[:, 16:24], T.nI512[:], idv, False, True, ["nI512"] + k("Sel"), k("pT"), True)
+            act(T.nb[:, L], pT[:, 16:24], CPY, k("pT"), k("nb"), scale=0.5)
+            mm(pE[:, 0, :], T.ones[:], T.Jm[:], True, False, ["ones", "Jm"], k("pE"))
+            mm(pE[:, 0, :], T.blkE[:], T.E[:, K], False, True, ["blkE"] + k("E"), k("pE"), True)
+            o, AC = 576 * s, []
             for c in range(7, -1, -1):
                 wdt = 16 * c + 16
-                e = T.EQ[:, o:o + wdt]
-                et = k("EQ%d_" % c)
-                act(e, pE[:, 0:wdt], ABS, k("pE", "nb"), et, bias=T.nb[:, 8 * s + c:8 * s + c + 1])
+                e, et = T.EQ[:, o:o + wdt], k("EQ%d_" % c)
+                act(e, pE[:, 0, 0:wdt], ABS, k("pE", "nb"), et, bias=T.nb[:, 8 * s + c:8 * s + c + 1])
                 if c >= 8 - MNV:
-                    mo = T.mn[:, 8 * s + c:8 * s + c + 1]
-                    add("V", cyc(wdt), lambda mo=mo, e=e: V.tensor_reduce(mo, e, AxisListType.X, MIN), et, k("mn%d_" % c))
+                    add("V", cyc(wdt), lambda mo=T.mn[:, 8 * s + c:8 * s + c + 1], e=e:
+                        V.tensor_reduce(mo, e, AxisListType.X, MIN), et, k("mn%d_" % c))
                 else:
                     act(e, e, RELU, et, et + k("acc%d_" % c), bias=63.5 * 16384.0, scale=-16384.0,
                         acc=T.acc[:, 8 * s + c:8 * s + c + 1])
@@ -505,47 +613,84 @@ def build_ops(g, T, topo, core, rank):
                 o += wdt
             if MNV:
                 c = slice(8 * s + 8 - MNV, 8 * s + 8)
-                act(T.acc[:, c], T.mn[:, c], RELU, k(*["mn%d_" % j for j in range(8 - MNV, 8)]), k("accv"),
-                    bias=63.5 * 16384.0, scale=-16384.0)
+                MN = k(*["mn%d_" % j for j in range(8 - MNV, 8)])
+                if RV:
+                    ts(T.acc[:, c], T.mn[:, c], 63.5, 8192.0, LT, MUL, MN, k("accv"))
+                else:
+                    act(T.acc[:, c], T.mn[:, c], RELU, MN, k("accv"), bias=63.5 * 16384.0, scale=-16384.0)
                 AC += k("accv")
-            tt(T.q2[:, L], T.acc[:, L], T.ctop[:], MIN, AC + ["ctop"], k("q2"))
+            tt(T.q2[:, L], T.acc[:, L], ctop, MIN, AC + ["ctop"], k("q2"))
             tt(T.lfv[:, L], T.q2[:, L], idv, MAX, k("q2", "Sel"), k("lfv"))
             mm(pT[:, 32:40], T.PB[:], T.lfv[:, L], True, True, ["PB"] + k("lfv"), k("pT"), True)
             mm(pT[:, 40:48], T.PA[:], T.lfv[:, L], True, True, ["PA"] + k("lfv"), k("pT"), True)
             cp(T.lf[:, 16 * s:16 * s + 16], pT[:, 32:48], k("pT"), k("lf"))
             lk = T.ls[:, 24 * s + 16:24 * s + 24]
-            sga(T.Z[:, K], W[:, 0:WS], T.l2[:, L], k("l2") + WALL, k("Z"), scale=13.0)
-            sga(T.kp[:, K], T.KP[:], lk, k("ls") + ["KP"], k("kp"))
-            gtt(T.mK[:, K], Y[:, 128 * s:128 * s + 1152], T.ls[:, 24 * s + 8:24 * s + 16], T.Z[:, K], ADD,
-                k("ls", "Z", "Ye") + ["Yf", "Y0", "Y1"], k("mK"))
-            ts(T.nK[:, K], T.mK[:, K], 4095, None, AND, None, k("mK"), k("nK"))
+            sga(T.Z[:, K], Y[:, 128 * s:128 * s + 1152], T.ls[:, 24 * s + 8:24 * s + 16],
+                k("ls", "Ye") + ["Yf", "Y0", "Y1"], k("Z"))
+            sga(T.kp[:, K], T.KP[:], lk, k("ls") + ["KPa", "KPb"], k("kp"))
             gtt(T.aK[:, K], W[:, 0:WS], T.ls[:, 24 * s:24 * s + 8], T.kp[:, K], MUL, k("ls", "kp") + WALL, k("aK"))
-            gtt(T.bK[:, K], T.OH[:], lk, T.nK[:, K], MUL, k("ls", "nK") + ["OHa", "OHb"], k("bK"))
-            for h, Pm, pt in ((0, T.PB, "PB"), (1, T.PA, "PA")):
-                mm(pK[:, 128 * h:128 * h + 128], Pm[:], T.aK[:, K], True, False, [pt] + k("aK"), k("pK"), True)
-                mm(pK[:, 128 * h:128 * h + 128], Pm[:], T.bK[:, K], False, True, [pt] + k("bK"), k("pK"), True)
-            act(T.NW[:, 256 * s:256 * s + 256], pK[:, 0:256], CPY, k("pK"), k("NW"))
+            gtt(T.bK[:, K], T.OH[:], lk, T.Z[:, K], MUL, k("ls", "Z") + ["OHa", "OHb"], k("bK"))
+            mm(pU[:, 1, :], T.idn[:], T.aK[:, K], True, False, ["idn"] + k("aK"), k("pU"), True)
+            mm(pU[:, 1, :], T.idn[:], T.bK[:, K], False, True, ["idn"] + k("bK"), k("pU"), True)
+            act(T.NK[:, K], pU[:, 1, :], IDN, k("pU"), NK, bias=128.5 + 2.0 ** -13, scale=1.0 / 4096.0)
+            for x, xt in ((T.aK, "aK"), (T.bK, "bK")):
+                for h, Pm, pt in ((0, T.PB, "PB"), (1, T.PA, "PA")):
+                    mm(pK[:, 128 * h:128 * h + 128], Pm[:], x[:, K], (xt, h) == ("aK", 0), False, [pt] + k(xt), k("pK"), True)
+            for h in range(2):
+                mm(pK[:, 128 * h:128 * h + 128], T.Pq[:, 128 * h:128 * h + 128], T.NK[:, K], False, h == 1,
+                   ["Pq0", "Pq1"] + NK, k("pK"))
+            act(T.NW[:, 256 * s:256 * s + 256], pK[:, 0:256], IDN, k("pK"), k("NW"), bias=129.0 * 4096.0)
             for h in range(2):
                 add("V", 0.06 + 128 * SC * CY,
                     lambda h=h: V.tensor_copy(W[:, 0:WS].indirect(T.lf[:, 16 * s + 8 * h:16 * s + 8 * h + 8]),
                                               T.NW[:, 256 * s + 128 * h:256 * s + 128 * h + 128]),
                     k("lf", "NW"), WALL)
             if not last:
-                act(T.q4[:, L], T.good[:, L], CPY, k("good"), k("q4", "cnt"), acc=T.cnt[:, c4])
-                mm(pU[:, 48:49], T.blk2[:], T.cnt[:, c4], True, True, ["blk2a", "blk2b"] + k("cnt"), k("pU"), True)
-                tt(T.Aa[:, c4], pU[:, 48:49], T.Aa[:, c4], ADD, k("pU", "Aa"), k("Aa"))
-                ts(T.A7[:, c4], T.Aa[:, c4], 7, None, AND, None, k("Aa"), k("A7"))
-                cp(T.A7f[:, c4], T.A7[:, c4], k("A7"), k("A7f"))
+                an = T.An[:, 8 * s + v + 1:8 * s + v + 2]
+                act(T.q4[:, L], T.good[:, 24 * s:24 * s + 8], CPY, k("good"), k("cnt", "q4"), acc=T.cnt[:, c4])
+                mm(pT[:, 48:49], T.blk2[:], T.cnt[:, c4], True, True, ["blk2a", "blk2b"] + k("cnt"), k("pT"), True)
+                act(an, pT[:, 48:49], IDN, k("pT", "An"), k("An"), bias=T.An[:, 8 * s + v:8 * s + v + 1], scale=-1.0)
+                aq = T.go[:, 32 + 4 * s:33 + 4 * s]
+                act(aq, an, IDN, k("An"), k("Aq"), bias=-0.4375, scale=-0.125)
+                act(T.An[:, 8 * s + 4:8 * s + 5], aq, IDN, k("Aq", "An"), k("A7"), bias=an, scale=8.0)
 
         dma("Y", T.yteam[64 * s:64 * s + 64, 0:512], W[0:64, TC:TC + 512], 131072, WALL, [])
-        dma("S", T.yteam[64 * s:64 * s + 64, 512:1024], W[64:128, TC + 512:DT], 131072, WALL, [])
-        dma("Y", T.yact[4 * s:4 * s + 4, :], W[64:128:16, 0:4096], 65536, WALL, [])
+        dma("S", T.yteam[64 * s:64 * s + 64, 512:1024], W[64:128, TC + 512:PC], 131072, WALL, [])
+        dma("Y", T.yact[4 * s:4 * s + 4, :], W[64:128:16, PC:DC], 65536, WALL, [])
 
     a = len(ops)
     stream(0)
     b = len(ops)
     stream(1)
-    return ops, (a, b)
+    return bundle(ops, a, b)
+
+
+def bundle(ops, a, b):
+    times = {}
+    for o in ops:
+        for t in o["w"]:
+            times[t] = times.get(t, 0) + 1
+    fixed = set(t for o in ops[:a] for t in o["w"])
+    for o in ops[a:]:
+        fixed.difference_update(o["w"])
+    out, cut, room = [], [0, 0], 0.0
+    for i, o in enumerate(ops):
+        cut = [len(out) if i == a else cut[0], len(out) if i == b else cut[1]]
+        p = out[-1] if out else None
+        if (o["e"] == "P" and p["e"] == "P" and p["w"] == o["w"] and set(o["r"]) - fixed <= set(p["r"])
+                and (room + o["x"] <= BUNDLE)):
+            p["fs"].append(o["f"])
+            p["d"] += o["d"]
+            p["r"] = sorted(set(p["r"] + o["r"]))
+            room += o["x"]
+        else:
+            if o["e"] == "P":
+                fs = [o["f"]]
+                o["fs"] = fs
+                o["f"] = lambda fs=fs: [f() for f in fs][-1]
+                room = o["x"]
+            out.append(o)
+    return out, cut
 
 
 def depend(ops):
@@ -593,7 +738,8 @@ def place(ops, pred, succ, pr):
                 if best is None or t < best[0]:
                     best = (t, e)
         t, e = best
-        i = max((j for j in cand[e] if rdy[j] <= t + LOOK), key=lambda j: (pr[j] - BETA * max(0.0, rdy[j] - t), -j))
+        i = max((j for j in cand[e] if rdy[j] <= t + LOOK),
+                key=lambda j: (pr[j] - GAMMA * ops[j]["d"] - BETA * max(0.0, rdy[j] - t), -j))
         t = max(t, rdy[i])
         cand[e].remove(i)
         o = ops[i]
@@ -606,19 +752,46 @@ def place(ops, pred, succ, pr):
         t0[i], t1[i] = t, fin
         order.append(i)
         for j in succ[i]:
-            if abs(i - j) == 1 and ops[max(i, j)].get("soft"):
+            if ops[j]["behind"] == i or o["behind"] == j:
                 rdy[j] = max(rdy[j], free[e])
             else:
-                rdy[j] = max(rdy[j], fin + (0.0 if e == "P" and ops[j]["e"] == "P" else WAKE))
+                rdy[j] = max(rdy[j], free[e] if e == "P" and ops[j]["e"] == "P" else fin + (OWN if e == ops[j]["e"] else 1.0) * WAKE)
             left[j] -= 1
             if left[j] == 0:
                 cand[ops[j]["e"]].append(j)
     return order, t0, t1
 
 
-def schedule(ops, hard, cut, lead, seed=0, noise=0.0):
+def replay(ops, deps, order, wake):
+    free, fin, bus = {}, [0.0] * len(ops), 0.0
+    for i in order:
+        o = ops[i]
+        e = o["e"]
+        t = free.get(e, 0.0)
+        for j in deps[i]:
+            x = fin[j] + wake if e != ops[j]["e"] else 0.0 if e == "P" else fin[j] + OWN * wake
+            if x > t:
+                t = x
+        free[e] = t + o["d"]
+        if o["k"] == "dma":
+            bus = max(bus, t + 1.5) + o["lat"] / BW
+            fin[i] = bus + 0.5
+        else:
+            fin[i] = t + o["d"] + o["lat"]
+    return max(fin)
+
+
+def schedule(ops, hard, cut, others, lead, seed=0, noise=0.0):
     n = len(ops)
-    deps = [hard[i] + ([i - 1] if ops[i].get("soft") else []) for i in range(n)]
+
+    def worth(order, t1):
+        return float(np.log(max(t1)) + sum(np.log(replay(o, hard, order, w)) for o, w in others))
+    for i in range(n):
+        ops[i]["behind"] = i - 1 if ops[i].get("soft") else -1
+    where = {o["w"][0]: i for i, o in enumerate(ops) if o["k"] == "dma" and o["w"]}
+    for a, b in zip(LOADS, LOADS[1:]):
+        ops[where[b]]["behind"] = where[a]
+    deps = [hard[i] + ([ops[i]["behind"]] if ops[i]["behind"] >= 0 else []) for i in range(n)]
     succ = [[] for i in range(n)]
     for i in range(n):
         for j in deps[i]:
@@ -628,29 +801,40 @@ def schedule(ops, hard, cut, lead, seed=0, noise=0.0):
     for i in range(n - 1, -1, -1):
         o = ops[i]
         lat = 2.0 + o["lat"] / BW if o["k"] == "dma" else o["d"] + o["lat"]
-        pr[i] = max([pr[j] + (o["d"] if j == i + 1 and ops[j].get("soft") else
-                              lat if o["e"] == "P" and ops[j]["e"] == "P" else lat + WAKE) for j in succ[i]]
+        pr[i] = max([pr[j] + (o["d"] if ops[j]["behind"] == i else
+                              o["d"] if o["e"] == "P" and ops[j]["e"] == "P" else
+                              lat + (OWN if o["e"] == ops[j]["e"] else 1.0) * WAKE) for j in succ[i]]
                     or [lat + (lead if cut[0] <= i < cut[1] else 0.0)])
     best = None
     for rnd in range(ROUNDS):
         order, t0, t1 = place(ops, deps, succ, pr)
-        if best is None or max(t1) < best[0]:
-            best = (max(t1), order, t0, t1, pr)
+        if best is None or worth(order, t1) < best[0]:
+            best = (worth(order, t1), order, t0, t1, pr)
         pr = place(ops, succ, deps, [t + noise * float(x) for t, x in zip(t1, rs.random(n))])[2]
+    kinds, seen, kind = {}, {}, []
+    for i, o in enumerate(ops):
+        w = (o["w"] or ["out"])[0]
+        if w.startswith("offa") or i in cut:
+            seen = {}
+        key = o["e"] + "".join(c for c in w if c.isalpha())
+        seen[key] = seen.get(key, 0) + 1
+        kind.append(kinds.setdefault((key, seen[key], i >= cut[0]), len(kinds)))
+    kind = np.array(kind)
     pr = np.array(best[4])
     for rnd in range(CLIMB):
-        p = pr.copy()
-        for rep in range(3):
-            a = int(rs.integers(cut[0], n))
-            b = a + int(rs.choice([1, 3, 10, 40, 100]))
-            p[a:b] += float(rs.normal()) * float(rs.choice([0.3, 1.0, 3.0]))
+        d = np.zeros(len(kinds))
+        for rep in range(int(rs.integers(1, 4))):
+            d[rs.integers(len(kinds))] += rs.normal() * rs.choice([0.3, 1.0, 2.0])
+        p = pr + d[kind]
         order, t0, t1 = place(ops, deps, succ, p.tolist())
-        if max(t1) <= best[0]:
-            best = (max(t1), order, t0, t1)
-            pr = p
+        if max(t1) <= max(best[3]) + 1.0:
+            x = worth(order, t1)
+            if x <= best[0]:
+                best = (x, order, t0, t1)
+                pr = p
     for i in range(n):
         ops[i]["t0"], ops[i]["t1"] = best[2][i], best[3][i]
-    return best[1], best[0]
+    return best[1], max(best[3])
 
 
 def emit(g, T, ops, deps, order):
@@ -727,10 +911,11 @@ def rank_program(g, core, T, topo):
     rank = T.rank_of(core)
     if rank is None:
         return
-    ops, cut = build_ops(g, T, topo, core, rank)
+    ops, cut = build_ops(g, T, topo, core, rank, COSTS[0])
     deps = depend(ops)
     if not ORDER:
-        order, end = schedule(ops, deps, cut, LEAD, SEED, NOISE)
+        others = [(build_ops(g, T, topo, core, rank, c)[0], c[4]) for c in COSTS[1:]]
+        order, end = schedule(ops, deps, cut, others, LEAD, SEED, NOISE)
         ORDER.append((order, [o["t1"] for o in ops]))
     for o, t in zip(ops, ORDER[0][1]):
         o["t1"] = t

@@ -3,22 +3,21 @@ from concourse.bass import DstId, RemoteDMATransfer
 from concourse.mybir import AluOpType as ALU, AxisListType, ActivationFunctionType as ACT
 
 NV = 4
-TC, PC, DC, DT, WS = 128, 1152, 5248, 5376, 5504
-SW = 2
-VCH, SCH = ((4, 4, 4, 4), (2, 2, 2, 2, 2, 2, 2)), (8, 8)
-PV = ("VVVVS", "VVVVS")
+TC, PC, DC, DT, PL, DC2, DT2, WS = 128, 1152, 5248, 5376, 5504, 9600, 9728, 9856
+HALF = (((2, 2), "V", 4), ((2, 2), "V", 4))
+SUB_ = ("pE", "pT")
+READ = ("kap", "kap")
+PV = ("VSVSVSVSS", "VSVSVSVSS")
 XE = (("V", "VVVV", "VVSS"), ("S", "SSSS", "VSSS"), ("S", "VVSS", "GGSV"))
-PENV = (1, 1, 1)
+HI0 = "S"
 EV = (1, 0)
 NKV = 1
-MNV = 8
-RV = 0
+NEAR = 63.5 * 32768.0
+NB = "pE"
 ONV = ()
-N16 = 0
-NY = 4
-SHARE = ((1, 1, 1), (1, 1, 1))
-G3 = 0
-ROUNDS, CLIMB = 20, 1300
+DW = (16, 240, 3600)
+OFS = 192.0 * sum(DW) + 512.0
+ROUNDS, CLIMB = 20, 2500
 LEAD, SEED, NOISE = 4.0, 3, 0.6
 F, B, I, U = "float32", "bfloat16", "int32", "uint16"
 
@@ -28,27 +27,29 @@ def sb(n, d):
 
 
 SCRATCH = {
-    "Y": sb(1280, F), "cA": sb(2048, F), "goals": sb(1024, B), "land": sb(192, F), "snd": sb(192, F),
-    "landb": sb(1024, B), "xb": sb(256, B), "xp": sb(1280, B), "xn": sb(1024, B), "wtI": sb(8, I), "stI": sb(16, I), "actI": sb(512, I),
+    "Y": sb(1280, F), "goals": sb(1024, B), "land": sb(288, F), "snd": sb(288, F),
+    "landb": sb(1024, B), "xb": sb(256, B), "xp": sb(1280, B), "xn": sb(1024, B), "wtI": sb(8, I), "stI": sb(16, I),
+    "actI": sb(256, I), "dg": sb(768, I), "dgb": sb(768, B), "Vc": sb(1536, F), "Pc": sb(1536, B),
     "ci": sb(16, I), "cf": sb(24, F), "io2": sb(128, F), "io3": sb(128, F), "idn": sb(128, F),
-    "blk": sb(128, F), "blkE": sb(128, F), "blk2": sb(128, F), "blk8": sb(8, F), "msk": sb(128, F),
+    "blk": sb(128, F), "blkE": sb(128, F), "blk2": sb(128, B), "blk8": sb(8, F), "msk": sb(128, F),
     "PA": sb(128, F), "PB": sb(128, F), "nI23": sb(128, B), "pI23": sb(128, B), "nI512": sb(128, F),
-    "lp": sb(8, U), "nI24": sb(128, B), "SelY": sb(128, F), "CI": sb(384, B), "Gs": sb(1024, B), "rst": sb(128, F),
-    "Wm": sb(144, B), "Wp": sb(40, B), "We": sb(256, B), "c1": sb(128, B), "c2": sb(128, B),
-    "WN": sb(144, B), "WD": sb(144, B), "WE": sb(144, B), "ones": sb(128, B), "Jm": sb(128, B), "m8": sb(8, B),
-    "OH": sb(32, F), "KP": sb(32, F), "l1": sb(8, U), "cs": sb(40, F),
+    "lp": sb(8, U), "nI": sb(256, B), "SelY": sb(128, B), "rst": sb(128, F), "SB": sb(128, B),
+    "Wy": sb(168, B), "We": sb(256, B), "c12": sb(256, B), "DWf": sb(384, F), "DWb": sb(384, B),
+    "blkB": sb(160, B), "ones": sb(128, B), "Jm": sb(128, B), "m8": sb(24, B),
+    "OH": sb(24, F), "KP": sb(24, F), "l1": sb(8, U), "cs": sb(56, F),
     "EQ": sb(1152, F),
-    "cK": sb(256, F), "mK": sb(256, I), "nK": sb(256, I), "n16": sb(256, U), "TT": sb(768, F), "pen": sb(768, B),
-    "pab": sb(768, B), "Z": sb(256, F), "E": sb(256, F), "eI": sb(256, I), "eM": sb(256, I), "NK": sb(256, B),
-    "kp": sb(256, F), "aK": sb(256, F), "bK": sb(256, F), "NW": sb(512, F), "nb": sb(16, F), "hE": sb(256, F),
-    "ad": ("sbuf", [128, 6, 128], B),
-    "ZW": sb(256, F), "AF": sb(32, F), "go": sb(40, B), "BI": sb(48, I),
+    "cK": sb(256, F), "mK": sb(256, I), "nK": sb(512, I), "n16": sb(256, U),
+    "Z": sb(256, F), "Z2": sb(256, B), "E": sb(256, F), "eI": sb(256, I), "eM": sb(256, I), "NK": sb(256, B),
+    "kq": sb(256, F), "aK": sb(256, F), "bK": sb(256, F), "NW": sb(512, F), "nb": sb(16, F), "hE": sb(256, F),
+    "TT": ("sbuf", [128, 48, 16], B), "pen": ("sbuf", [128, 48, 16], B), "ab": ("sbuf", [128, 48, 16], B),
+    "kp": ("sbuf", [128, 16, 16], F),
+    "ZW": sb(256, F), "AF": sb(96, B), "go": sb(40, B), "BI": sb(48, I),
     "a1": sb(16, I), "a2": sb(16, I), "A0": sb(16, F), "off": sb(48, U),
     "A0p": sb(16, F), "kk1": sb(16, I), "q1": sb(16, F), "q2": sb(16, F),
     "acc": sb(16, F), "q3": sb(16, F), "q4": sb(16, F), "i2": sb(16, I),
-    "Bw2": sb(16, I), "lt0": sb(16, F), "lt2": sb(16, I), "Bw": sb(16, I), "aw": sb(16, I), "le": sb(16, U),
-    "lt": sb(16, I), "P0": sb(48, I), "P1": sb(48, F), "Df": sb(48, F), "Dg": sb(48, F),
-    "Sel": sb(48, F), "ls": sb(48, U), "Pq": sb(256, B), "thr": sb(48, F), "good": sb(48, F),
+    "Bw2": sb(16, I), "lt0": sb(16, F), "lt2": sb(16, I), "Bw": sb(16, I), "aw": sb(16, I), "le": sb(32, U),
+    "lt": sb(16, I), "P0": sb(64, I), "P1": sb(64, F), "Df": sb(64, F), "Dg": sb(64, F),
+    "Sel": sb(64, F), "ls": sb(64, U), "Pq": sb(256, B), "thr": sb(64, F), "good": sb(64, B),
     "mn": sb(16, F), "lfv": sb(16, F), "lf": sb(32, U),
     "cnt": sb(8, F), "An": sb(16, F),
 }
@@ -56,25 +57,23 @@ for s_ in "01":
     for nm, n_, d_ in (("prg", 4096, B), ("W", WS, F), ("ef", 1040, B), ("teamI", 1024, I), ("xr", 2048, B),
                        ("Gm", 2048, B), ("Gp", 2048, B)):
         SCRATCH[nm + s_] = sb(n_, d_)
-    SCRATCH["pK" + s_] = ("psum", [128, 512], F)
-    SCRATCH["pT" + s_] = ("psum", [128, 512], F)
-    SCRATCH["pU" + s_] = ("psum", [128, 4, 128], F)
-    SCRATCH["pE" + s_] = ("psum", [128, 4, 128], F)
+    for nm in ("pK", "pT", "pU", "pE"):
+        SCRATCH[nm + s_] = ("psum", [128, 512], F)
 PSUM = ("pK0", "pK1", "pT0", "pT1", "pU0", "pU1", "pE0", "pE1")
 
 NDMA = 70
 SEMAPHORES = ["cV", "cS", "cP", "cG", "sent", "gin"] + ["d%d" % i for i in range(NDMA)] + ["r%d" % i for i in range(14)]
 
-COSTS = ((0.83e-3, 0.44e-3, 1.56, 3.8, 0.115, 0.8, 2.0, 64, 0.0, -0.015, -0.015, 1.1),
-         (0.85e-3, 0.5e-3, 1.1, 1.8, 0.08, 1.4, 2.8, 64, 0.0, -0.015, -0.015, 1.25),
-         (1.0e-3, 0.52e-3, 1.3, 5.0, 0.17, 1.5, 3.0, 64, 0.0, -0.015, -0.015, 1.1))
+COSTS = ((0.83e-3, 0.5e-3, 1.35, 3.8, 0.14, 0.8, 2.0, 64, 0.1, 0.0, 0.0, 1.1),
+         (0.85e-3, 0.6e-3, 1.15, 1.8, 0.1, 1.4, 2.8, 64, 0.05, -0.015, -0.015, 1.25),
+         (1.0e-3, 0.55e-3, 1.7, 5.0, 0.17, 1.5, 3.0, 64, 0.1, -0.015, -0.015, 1.1))
 LOOK, BETA = 0.15, 15.0
 WAKE = COSTS[0][4]
 GAMMA = 1.0
 NX = 0.0
-OWN = 1.8
-LOADS = ("prg00a", "prg10a", "teamI0", "prg20a", "prg30a", "W40", "W00", "W10", "W20", "prg01a", "prg11a", "prg21a",
-         "prg31a", "teamI1", "W41", "W01", "W11", "W21", "ef10a", "ef10b", "ef11a", "ef11b")
+OWN = 1.4
+LOADS = ("prg00", "prg10", "teamI0", "dq00", "dq10", "dq20", "prg20", "prg30", "dq01", "dq11", "dq21", "prg01", "prg11",
+         "prg21", "prg31", "teamI1", "ef10a", "ef10b", "ef11a", "ef11b")
 F32 = (4, 0.0)
 BUNDLE = 512
 BW = 200000.0
@@ -165,16 +164,13 @@ def build_ops(g, T, topo, core, rank, cost):
     AND, SHR = ALU.bitwise_and, ALU.logical_shift_right
     MUL, ADD, SUB, MAX, MIN, EQ, LT = ALU.mult, ALU.add, ALU.subtract, ALU.max, ALU.min, ALU.is_equal, ALU.is_lt
     CPY, IDN, ABS, RELU = ACT.Copy, ACT.Identity, ACT.Abs, ACT.Relu
-    Y, cA, ci, cf = T.Y, T.cA, T.ci, T.cf
+    Y, ci, cf = T.Y, T.ci, T.cf
 
     def loads(s):
         H = str(s)
         R = slice(64 * s, 64 * s + 64)
         q = "S" if s == 0 else "Y"
-        after = []
         HV = [(h, slice(64 * h, 64 * h + 64), H + "ab"[h]) for h in range(2)]
-        for h, D, t in HV:
-            dma(q, T.actI[D, 256 * s:256 * s + 256], T.act[4 * s:4 * s + 4, :], 65536, [], ["actI" + t])
         for h, D, t in HV:
             dma(q, T.xb[D, 128 * s:128 * s + 128], T.x0[R, 128 * h:128 * h + 128], 16384, [], ["xb" + t])
             dma(q, T.wtI[D, 4 * s:4 * s + 1], T.wt[R, :], 4096, [], ["wtI" + t])
@@ -182,11 +178,18 @@ def build_ops(g, T, topo, core, rank, cost):
         prg = T["prg" + H]
         for c in range(4):
             C = slice(1024 * c, 1024 * c + 1024)
-            dma("Y", prg[0:64, C], T.prog[R, C], 131072, after, ["prg%d%sa" % (c, H)])
-        dma("Y", T["teamI" + H][0:64, :], T.team[R, :], 262144, after, ["teamI" + H])
-        for c in range(4):
-            C = slice(1024 * c, 1024 * c + 1024)
-            move(PV[s][c], prg[64:128, C], prg[0:64, C], ["prg%d%sa" % (c, H)], ["prg%d%sb" % (c, H)], 0.5)
+            dma("Y", prg[0:64, C], T.prog[R, C], 131072, [], ["prg%d%s" % (c, H)])
+        dma("Y", T["teamI" + H][0:64, :], T.team[R, :], 262144, [], ["teamI" + H])
+        for j in range(3):
+            dma("Y", prg[64 + 4 * j:68 + 4 * j, :], T.dgb[R, 256 * j:256 * j + 256], 32768, ["dgb%d_" % j], ["dq%d%s" % (j, H)])
+
+    dma("S", T.actI[:], T.act[:], 131072, [], ["actI"])
+    for j in (1, 2):
+        C = slice(256 * j, 256 * j + 256)
+        ts(T.dg[:, C], T.actI[:], -512.0, 1.0 / 15 ** j, ADD, MUL, ["actI"], ["dg%d_" % j])
+        cp(T.dgb[:, C], T.dg[:, C], ["dg%d_" % j], ["dgb%d_" % j])
+    ts(T.dg[:, 0:256], T.dg[:, 256:512], -15.0, -512.0, MUL, ADD, ["dg1_"], ["dg0_"])
+    tt(T.dgb[:, 0:256], T.dg[:, 0:256], T.actI[:], ADD, ["dg0_", "actI"], ["dgb0_"])
 
     for s in range(2):
         for h in range(2):
@@ -210,7 +213,7 @@ def build_ops(g, T, topo, core, rank, cost):
     iota(T.E[:, 0:128], [[1, 8], [0, 16]], 0, 0, ["E0"])
     iota(T.io2[:], [[0, 8], [1, 16]], 0, 0, ["io2"])
     iota(T.io3[:], [[1, 128]], 0, 0, ["io3"])
-    iota(T.eM[:], [[1, 256]], 0, 256, ["eM0", "eM1"], False)
+    iota(T.eM[:, 0:64], [[1, 64]], 0, 64, ["eM0"], False)
     ts(ci[:, 4:5], ci[:, 0:1], 15, None, AND, None, ["ci0"], ["ci4"])
     ts(ci[:, 8:9], ci[:, 0:1], 4, None, SHR, None, ["ci0"], ["ci8"])
     cp(cf[:, 0:9:4], ci[:, 0:9:4], ["ci0", "ci4", "ci8"], ["cf"])
@@ -221,72 +224,98 @@ def build_ops(g, T, topo, core, rank, cost):
     def pick(out, pat, base, val, w):
         iota(out, [[0, wd(out)]], val, 0, w)
         add("G", 0.17 + 2 * wd(out) * CY, lambda: g.affine_select(out, out, pat, EQ, 0.0, base, 1), w, w)
-    pick(T.SelY[0:8, :], [[-1, 8], [0, 16]], 0, 1, ["SelY"])
+    pick(T.SB[:], [[0, 2], [-1, 64]], 0, 1, ["SB"])
+    add("G", 0.17 + 256 * CY, lambda: g.affine_select(T.SB[:], T.SB[:], [[0, 2], [-1, 4], [-4, 16]], ALU.not_equal,
+                                                      1.0 / 16.0, -64, 1), ["SB"], ["SB"])
+    add("G", 0.17 + 16 * CY, lambda: g.affine_select(T.SB[:, 1:128:16], T.SB[:, 1:128:16], [[0, 2], [-1, 4]], ALU.not_equal,
+                                                     -15.0 / 16.0, -72, 1), ["SB"], ["SB"])
+    for j in range(3):
+        pick(T.DWf[0:64, 128 * j:128 * j + 128], [[0, 2], [-1, 64]], 0, DW[j], ["DWf%d_" % j])
+        pick(T.DWb[0:64, 128 * j:128 * j + 128], [[0, 2], [-1, 64]], 0, -DW[j], ["DWb%d_" % j])
     pick(T.PA[:], [[0, 2], [-1, 64]], 0, 1, ["PA"])
     pick(T.PB[:], [[0, 2], [-1, 64]], -64, 1, ["PB"])
-    act(T.nI24[:], T.idn[:], CPY, ["idn"], ["nI24"], scale=-16777216.0)
+    nI24, nI15, c1, c2 = T.nI[:, 0:128], T.nI[:, 128:256], T.c12[:, 0:128], T.c12[:, 128:256]
+    act(nI24, T.idn[:], CPY, ["idn"], ["nI24"], scale=-16777216.0)
     tt(T.blk2[:, 0:64], T.blk[:, 0:64], T.blk[:, 64:128], ADD, ["blk"], ["blk2a"])
     act(T.blk2[:, 64:128], T.blk2[:, 0:64], CPY, ["blk2a"], ["blk2b"])
     act(T.blkE[:], T.blk[:], CPY, ["blk"], ["blkE"], scale=256.0)
     act(T.Jm[:], T.io3[:], CPY, ["io3", "idn"], ["Jm"], scale=T.idn[:, 0:1])
     act(T.blk8[:], T.blk[:, 0:128:16], CPY, ["blk"], ["blk8"])
-    ms(T.Wm[:], 0.0, ["Wm"], 0.5)
-    act(T.Wm[:, 15:143:16], T.blk[:, 0:128:16], CPY, ["blk"], ["Wm"], scale=-65536.0)
-    act(T.CI[:, 0:128], T.idn[:], CPY, ["idn"], ["CI"], scale=482.0 * 32768.0)
-    ts(cf[:, 7:8], rc, 15.5 - SW, -240.0 * 32768.0, ALU.is_gt, MUL, ["cf"], ["k7"])
-    act(T.CI[:, 128:256], T.idn[:], CPY, ["idn", "k7"], ["CJ"], scale=cf[:, 7:8])
     act(T.nI512[:], T.idn[:], CPY, ["idn"], ["nI512"], scale=-512.0)
+    act(nI15, T.idn[:], CPY, ["idn"], ["nI15"], scale=-32768.0)
     ts(T.rst[:], T.io2[:], 0.5, None, ALU.is_gt, None, ["io2"], ["rst"])
-    act(T.Wp[:, 32:40], T.blk8[:], CPY, ["blk8"], ["Wm8"], scale=-65536.0)
-    ms(T.c1[:], -255.0 / 128.0, ["c1"], 0.5)
-    ms(T.c2[:], 1.5 * 2.0 ** 25, ["c2"], 0.5)
-    ts(cf[:, 5:6], rc, -2048.0, 32768.0, MUL, ADD, ["cf"], ["kb"])
-    act(T.CI[:, 256:384], T.idn[:], CPY, ["idn", "kb"], ["CK"], scale=cf[:, 5:6])
+    ms(c1, -255.0 / 128.0, ["c1"], 0.5)
+    ms(c2, 1.5 * 2.0 ** 25, ["c2"], 0.5)
+    kb, wq, pure, kd, kr, z2 = [cf[:, j:j + 1] for j in (5, 2, 3, 6, 7, 9)]
+    bq = T.m8[:, 16:17]
+    ts(kb, rc, -2048.0, 32767.0 + 241.0 * 32768.0 - OFS, MUL, ADD, ["cf"], ["kb"])
     act(T.nI23[:], T.idn[:], CPY, ["idn"], ["nI23"], scale=-8388608.0)
     act(T.pI23[:], T.idn[:], CPY, ["idn"], ["pI23"], scale=8388608.0)
     m = T.msk
-    tt(cf[:, 1:2], m[:, 0:1], m[:, 1:2], ADD, ["msk"], ["r01"])
-    tt(cf[:, 2:3], m[:, 3:4], m[:, 4:5], ADD, ["msk"], ["r34"])
-    ts(cf[:, 3:4], m[:, 2:3], 32768.0, cf[:, 1:2], MUL, SUB, ["msk", "r01"], ["rp"])
-    act(T.Wp[:, 0:8], T.blk8[:], CPY, ["blk8", "rp"], ["Wp0"], scale=cf[:, 3:4])
-    for j in range(1, 4):
-        act(T.Wp[:, 8 * j:8 * j + 8], T.blk8[:], CPY, ["blk8", "r01"], ["Wp%d" % j], scale=cf[:, 1:2])
-    WP = ["Wp0", "Wp1", "Wp2", "Wp3"]
-    ms(T.WN[:], 0.0, ["WN"], 0.5)
-    ms(T.WD[:], 0.0, ["WD"], 0.5)
-    act(T.WN[:, 15:143:16], T.blk8[:], CPY, ["blk8", "r34"], ["WN"], scale=cf[:, 2:3])
-    act(T.WD[:, 15:143:16], T.blk8[:], CPY, ["blk8"], ["WD"])
-    ms(T.WE[:], 0.0, ["WE"], 0.5)
-    cp(T.WE[:, 15:79:16], T.blk2[:, 0:64:16], ["blk2a"], ["WE"])
-    cp(T.WE[:, 79:143:16], T.blk2[:, 0:64:16], ["blk2a"], ["WE"])
+    ts(bq, rc, 2.5, 192.0, LT, MUL, ["cf"], ["bq"])
+    ts(z2, rc, 2.5, 1.0 / 65536.0, LT, MUL, ["cf"], ["z2"])
+    ts(pure, rc, 2.5, 32768.0, ALU.is_gt, MUL, ["cf"], ["pure"])
+    ts(cf[:, 10:11], m[:, 1:2], 15.0, m[:, 0:1], MUL, ADD, ["msk"], ["k10"])
+    ts(cf[:, 11:12], m[:, 2:3], 225.0, cf[:, 10:11], MUL, ADD, ["msk", "k10"], ["k11"])
+    ts(wq, cf[:, 11:12], 16.0, None, MUL, None, ["k11"], ["wq"])
+    tt(kd, pure, wq, SUB, ["pure", "wq"], ["kd"])
+    ts(kr, pure, -2.0, wq, MUL, ADD, ["pure", "wq"], ["kr"])
+    WG, WX, WR = T.Wy[:, 0:56], T.Wy[:, 56:112], T.Wy[:, 112:168]
+    ms(T.Wy[:, 8:32], 0.0, ["Wy1"], 0.5)
+    act(T.Wy[:, 0:8], T.blk8[:], CPY, ["blk8", "kd"], ["Wy0"], scale=kd)
+    act(T.Wy[:, 112:120], T.blk8[:], CPY, ["blk8", "kr"], ["Wr0"], scale=kr)
+    for j in range(3):
+        act(T.Wy[:, 32 + 8 * j:40 + 8 * j], T.blk8[:], CPY, ["blk8", "wq"], ["Wy%d" % (2 + j)], scale=wq)
+        act(T.Wy[:, 120 + 8 * j:128 + 8 * j], T.blk8[:], CPY, ["blk8", "msk"], ["Wr%d" % (1 + j)], scale=m[:, j:j + 1])
+    WGt = ["Wy%d" % j for j in range(5)]
+    act(WX, WG, CPY, WGt, ["Wx_"], scale=-1.0)
+    act(T.Wy[:, 144:168], T.Wy[:, 32:56], CPY, WGt, ["Wr4"], scale=-1.0)
+    WRt = ["Wr%d" % j for j in range(5)]
+    act(T.blkB[:, 0:128], T.blk[:], CPY, ["blk"], ["blkB"])
+    for j in range(4):
+        cp(T.blkB[:, 128 + 8 * j:136 + 8 * j], T.blk8[:], ["blk8"], ["blkC%d_" % j])
+    BC = ["blkC%d_" % j for j in range(4)]
     ms(T.ones[:], 1.0, ["ones"], 0.5)
-    ms(T.m8[:, 0:8], (PC - 8) / 128.0, ["m8"], 0.5)
+    ms(T.m8[:, 0:8], PC / 128.0, ["m8a"], 0.5)
+    ms(T.m8[:, 8:16], PL / 128.0, ["m8b"], 0.5)
     ts(T.Z[:, 128:144], T.io3[:, 0:16], -1.0, 15.0, MUL, ADD, ["io3"], ["Z1"])
     ts(T.OH[:, 0:16], T.Z[:, 128:144], rc, None, EQ, None, ["Z1", "cf"], ["OHa"])
-    ts(T.OH[:, 16:32], T.io3[:, 0:16], 0.0, cf[:, 1:2], MUL, ADD, ["io3", "r01"], ["OHb"])
+    ts(T.OH[:, 16:17], z2, 4096.0, None, MUL, None, ["z2"], ["OHb"])
+    cp(T.OH[:, 17:18], m[:, 3:4], ["msk"], ["OHc"])
     act(T.KP[:, 0:16], T.OH[:, 0:16], IDN, ["OHa"], ["KPa"], bias=1.0, scale=12.0)
-    act(T.KP[:, 16:32], T.OH[:, 16:32], IDN, ["OHb"], ["KPb"], bias=1.0, scale=-1.0)
+    ts(T.KP[:, 16:18], T.io3[:, 0:2], -1.0, 1.0, MUL, ADD, ["io3"], ["KPb"])
     act(T.Pq[:, 0:128], T.PB[:], CPY, ["PB"], ["Pq0"], scale=-4096.0)
     act(T.Pq[:, 128:256], T.PA[:], CPY, ["PA"], ["Pq1"], scale=-4096.0)
     cp(T.l1[:], T.io3[:, 0:8], ["io3"], ["l1"])
-    cj, cdum, ctop, cnb, cb = [T.cs[:, 8 * j:8 * j + 8] for j in range(5)]
+    cj, cdum, ctop, cnb, cdum2, ctop2 = [T.cs[:, 8 * j:8 * j + 8] for j in range(6)]
     ts(cj, T.io3[:, 0:8], 16.0, rc, MUL, ADD, ["io3", "cf"], ["cj"])
     act(cdum, cj, IDN, ["cj"], ["cdum"], bias=float(DC))
-    act(ctop, cj, IDN, ["cj"], ["ctop"], bias=float(DT))
-    act(cnb, cj, IDN, ["cj"], ["cnb"], bias=-0.25, scale=1.0 / 256.0)
-    ts(cf[:, 6:7], rc, 128.0, 15.0, MUL, ADD, ["cf"], ["k6"])
-    act(cb, T.io3[:, 0:8], IDN, ["io3", "k6"], ["cb"], bias=cf[:, 6:7], scale=16.0)
+    act(ctop, cj, IDN, ["cj"], ["ctop"], bias=DT - NEAR)
+    act(cdum2, cj, IDN, ["cj"], ["cdum2"], bias=float(DC2))
+    act(ctop2, cj, IDN, ["cj"], ["ctop2"], bias=DT2 - NEAR)
+    act(cnb, cj, IDN, ["cj"], ["cnb"], bias=-64.0 * 32768.0, scale=32768.0)
     ts(ci[:, 12:13], ci[:, 0:1], 7, None, AND, None, ["ci0"], ["ci12"])
     ts(ci[:, 13:14], ci[:, 0:1], 3, 1, SHR, AND, ["ci0"], ["ci13"])
     cp(cf[:, 16:17], ci[:, 13:14], ["ci13"], ["k16"])
     ts(cf[:, 17:18], ci[:, 12:13], 16.0, cf[:, 16:17], MUL, ADD, ["ci12", "k16"], ["k17"])
     ts(T.lp[:], T.io3[:, 0:8], 2.0, cf[:, 17:18], MUL, ADD, ["io3", "k17"], ["lp"])
+    cp(cf[:, 18:19], ci[:, 12:13], ["ci12"], ["k18"])
+    ts(T.SelY[0:16, :], T.E[0:16, 0:128], cf[0:16, 18:19], None, EQ, None, ["E0", "k18"], ["SelY"], 0.5)
     ms(T.An[:], -1032.0, ["An0", "An1", "A70", "A71"])
-    ts(T.eI[:], T.eM[:], 4095, None, AND, None, ["eM0", "eM1"], ["eI0", "eI1"])
-    cp(cA[:, 1536:1792], T.eI[:], ["eI0", "eI1"], ["cN"])
-    act(T.pen[:, 0:256], cA[:, 1536:1792], CPY, ["cN"], ["pen0"])
-    tt(cA[:, 1792:2048], cA[:, 1536:1792], T.pen[:, 0:256], SUB, ["cN", "pen0"], ["cN8"])
-    act(cA[:, 1792:2048], cA[:, 1792:2048], IDN, ["cN8"], ["cN8"], bias=8.0)
+    yi, yf = [T.mK[:, 64 * j:64 * j + 64] for j in range(4)], [T.NW[:, 64 * j:64 * j + 64] for j in range(5)]
+    ts(yi[0], T.eM[:, 0:64], 1023, None, AND, None, ["eM0"], ["yi0"])
+    for j in (1, 2):
+        ts(yi[j], yi[0], -512.0, 1.0 / 15 ** j, ADD, MUL, ["yi0"], ["yi%d" % j])
+    ts(yi[3], yi[1], -15.0, -512.0, MUL, ADD, ["yi1"], ["yi3"])
+    tt(yf[0], yi[0], yi[3], ADD, ["yi0", "yi3"], ["yf0"])
+    ts(yf[4], yi[2], -15.0, None, MUL, None, ["yi2"], ["yf4"])
+    tt(yf[1], yi[1], yf[4], ADD, ["yi1", "yf4"], ["yf1"])
+    cp(yf[2], yi[2], ["yi2"], ["yf2"])
+    cp(yf[3], yi[0], ["yi0", "yf0", "yf1", "yf2"], ["NW0", "NW1", "mK0", "mK1"])
+    iota(Y[:, 128:1152], [[0, 1024]], 0, 0, ["Yf"])
+    for j in range(4):
+        dma("Y", Y[j:128:16, 128:1152], yf[j], 32768, ["Yf", "NW0"], ["Y%d" % j])
+    YT = ["Yf", "Y0", "Y1", "Y2", "Y3"]
 
     def k_to_l(out, Wb, src, first, lastf, r, w):
         for rr in range(16):
@@ -317,94 +346,92 @@ def build_ops(g, T, topo, core, rank, cost):
         K = slice(128 * s, 128 * s + 128)
         L = slice(8 * s, 8 * s + 8)
         c4 = slice(4 * s, 4 * s + 1)
-        PAY = k("W0", "W1", "W2", "W4")
-        FILL = k("Wfa", "Wfb", "Wfc", "Wfd")
+        PAY = k(*["W%d_" % c for c in range(8)])
         WALL = PAY + k("Wt", "Wu", "Wz", "Wx")
-        PRG = ab("prg0", "prg1", "prg2", "prg3")
+        FILL = k("Wfa", "Wfb", "Wfc", "Wfd")
         XB = ab("xb")
         NK = k("NK")
         xb = T.xb[:, K]
+        bank = {"pK": pK, "pT": pT, "pU": pU, "pE": pE}
 
-        if s == 0:
-            iota(W[:, PC:PC + 1024], [[1, 1024]], 0, 0, k("Wfa"))
-            act(W[:, PC + 1024:PC + 2048], W[:, PC:PC + 1024], IDN, k("Wfa"), k("Wfb"), bias=1024.0)
-            act(W[:, PC + 2048:PC + 3072], W[:, PC:PC + 1024], IDN, k("Wfa"), k("Wfc"), bias=2048.0)
-            iota(W[:, PC + 3072:DC], [[1, 1024]], 3072, 0, k("Wfd"))
-        else:
-            for j, t in enumerate(FILL):
-                iota(W[:, PC + 1024 * j:PC + 1024 * j + 1024], [[1, 1024]], 1024 * j, 0, [t])
+        def sl(j):
+            return slice(32 * s + 8 * j, 32 * s + 8 * j + 8)
+
         iota(W[:, 0:TC], [[0, TC]], 0, 0, k("Wz"))
-        iota(W[:, DC:WS], [[0, WS - DC]], 0, 0, k("Wx"))
+        iota(W[:, DC:PL], [[0, PL - DC]], 0, 0, k("Wx"))
+        for j, t in enumerate(FILL):
+            iota(W[:, PL + 1088 * j:PL + 1088 * j + 1088], [[0, 1088]], 0, 0, [t])
         iota(ef[:, 0:16], [[0, 16]], 0, 0, k("ef0"))
         cp(W[0:64, TC:PC], T["teamI" + H][0:64, :], k("teamI"), k("Wt"))
-        move(PV[s][4], W[64:128, TC:PC], W[0:64, TC:PC], k("Wt"), k("Wu"))
-        c0 = 768 * s
-        cp(cA[:, c0:c0 + 256], T.actI[:, 256 * s:256 * s + 256], ab("actI"), k("cA0"))
-        hb = T.pab[:, 384 * s:384 * s + 256]
-        act(hb, cA[:, c0:c0 + 256], CPY, k("cA0"), k("pab"))
-        tt(cA[:, c0 + 256:c0 + 512], cA[:, c0:c0 + 256], hb, SUB, k("cA0", "pab"), k("cA1"))
-        act(cA[:, c0 + 256:c0 + 512], cA[:, c0 + 256:c0 + 512], IDN, k("cA1"), k("cA1"), bias=8.0)
-        for q in range(16):
-            mm(pU[:, 0:2, :], T.WE[0:64, 15 - q:143 - q], prg[0:64, 256 * q:256 * q + 256], q == 0, q == 15,
-               ["WE", "prg%d%sa" % (q // 4, H)], k("pU"))
-        act(cA[:, c0 + 512:c0 + 768], pU[:, 0:2, :], CPY, k("pU"), k("cA2"))
-        for row, a, tok in ((4, 1792, "cN8"), (0, c0, "cA0" + H), (1, c0 + 256, "cA1" + H), (2, c0 + 512, "cA2" + H)):
-            dma("Y", W[row:128:16, PC:DC], cA[:, a:a + 256], 131072, [tok] + FILL, k("W%d" % row))
+        move(PV[s][8], W[64:128, TC:PC], W[0:64, TC:PC], k("Wt"), k("Wu"))
         for h in range(2):
             dma("Y", ef[64 * h:64 * h + 64, 16:1040], T.eff[64 * s:64 * s + 64, :], 131072, [], ["ef1" + H + "ab"[h]])
-        if s == 0:
-            iota(Y[:, 128:1152], [[0, 1024]], 0, 0, ["Yf"])
-            dma("Y", Y[0:128:16, 128:1152], W[3:128:16, PC:PC + 1024], 32768, ["Yf", "Wfa0", "W40"], ["Y0"])
-            dma("Y", Y[1:128:16, 128:1152], W[4:128:16, PC:PC + 1024], 32768, ["Yf", "W40"], ["Y1"])
         ts(cf[:, 12 + s:13 + s], T.wtI[:, c4], 2.0, None, MUL, None, ab("wtI"), k("wf"))
         act(T.We[:, K], T.blk[:], CPY, ["blk"] + k("wf"), k("We"), scale=cf[:, 12 + s:13 + s])
-        nd = 3 if G3 else 1
-        D = slice(24, 24 + 8 * nd)
-        TH = slice(24 * s, 24 * s + 8 * nd)
-        ts(T.P0[:, 24 * s + 8:24 * s + 16], cj, 1024.0 * s, None, ADD, None, ["cj"], k("P0b"))
-        ms(T.P1[:, 24 * s + 16:24 * s + 24], 16.0, k("P1c"))
+        D, X = slice(0, 32), slice(32 * s, 32 * s + 32)
+        ts(T.P0[:, sl(1)], cj, 1024.0 * s, None, ADD, None, ["cj"], k("P0b"))
+        ms(T.P0[:, sl(3)], 512, k("P0d"))
+        ms(T.P1[:, sl(2)], 16.0, k("P1c"))
 
         def distance(x, xt, goal, gt):
-            for j in range(nd):
-                mm(pE[:, j, :], T.nI23[:], goal, j == 0, False, ["nI23"] + gt, k("pE"))
-            for j in range(nd):
-                mm(pE[:, j, :], T.pI23[:], x, False, j == nd - 1, ["pI23"] + xt, k("pE"))
-            act(T.ad[:, 3 * s:3 * s + nd, :], pE[:, 0:nd, :], ABS, k("pE"), k("ad"), scale=1.0 / 8388608.0)
-            k_to_l(pU[:, 0, D], T.WD, lambda rr: T.ad[:, 3 * s:3 * s + nd, rr:128:16], True, True, ["WD"] + k("ad"), k("pU"))
+            mm(pE[:, 0:128], T.nI23[:], goal, True, False, ["nI23"] + gt, k("pE"))
+            mm(pE[:, 0:128], T.pI23[:], x, False, True, ["pI23"] + xt, k("pE"))
+            act(T.Z2[:, K], pE[:, 0:128], ABS, k("pE"), k("Zb"), scale=1.0 / 8388608.0)
+            mm(pE[:, 128:256], T.Z2[:, K], T.blkB[:, 0:128], True, True, ["blkB"] + k("Zb"), k("pE"))
+            tt(T.NK[:, K], pE[:, 128:256], T.msk[:], MUL, k("pE") + ["msk"], NK, 1.0)
+            mm(pK[:, D], T.NK[:, K], T.blkB[:, 128:160], True, True, BC + NK, k("pK"))
 
-        def turn(src, n, j, r, bias):
-            mm(pT[0:n, 128:256], src, T.idn[:], True, True, ["idn"] + r, k("pT"), True)
-            act(T.TT[0:n, 384 * s + 128 * j:384 * s + 128 * j + 128], pT[0:n, 128:256], IDN, k("pT"), k("TT%d" % j),
-                bias=bias)
+        def turn(src, j, r):
+            f0 = 48 * s + 16 * j
+            move("V" if j else HI0, T.AF[:, f0:f0 + 8], src, r, k("ah%d" % j))
+            tt(T.AF[:, f0 + 8:f0 + 16], src, T.AF[:, f0:f0 + 8], SUB, r + k("ah%d" % j), k("al%d" % j))
+            mm(pT[0:16, 128:256], T.AF[:, f0:f0 + 16], T.pI23[:], True, True, ["pI23"] + k("ah%d" % j, "al%d" % j), k("pT"))
+            act(T.TT[0:16, 24 * s + 8 * j:24 * s + 8 * j + 8, :], pT[0:16, 128:256], CPY, k("pT"), k("TT%d" % j),
+                scale=1.0 / 8388608.0)
+
+        def tables():
+            for c in range(8):
+                bn = ("pK", "pT", "pU", "pE")[c % 4]
+                mm(bank[bn][:], T.SB[0:76, :], prg[0:76, 512 * c:512 * c + 512], True, True,
+                   ["SB"] + k("prg%d" % (c // 2), "dq0", "dq1", "dq2"), k(bn))
+                move(PV[s][c], W[:, PC + 512 * c:PC + 512 * c + 512], bank[bn][:], k(bn), [PAY[c]])
         ts(T.A0[:, L], T.stI[:, L], -1.0, 1023.0, MUL, ADD, ab("stI"), k("A0"))
 
         for v in range(NV):
             last = v == NV - 1
+            if last:
+                for j in range(3):
+                    C = slice(768 * s + 256 * j, 768 * s + 256 * j + 256)
+                    dma("Y", T.Pc[0:64, C], T.prog[64 * s + j:64 * s + 64:16, :], 32768, k("Wfa"), k("Pc%d_" % j))
+                    dma("Y", T.Vc[0:64, C], W[j:64:16, PC:DC], 65536, PAY, k("Vc%d_" % j))
+                ms(T.P1[:, sl(2)], 17.0, k("P1c"))
             if v > 0:
-                b0 = 32 * (2 * (v - 1) + s)
+                b0 = 48 * (2 * (v - 1) + s)
                 x0 = 256 * (v - 1) + 128 * s
                 xb, XB = T.landb[:, x0:x0 + 128], k("landb%d" % (v - 1))
                 A0, a0t = T.land[:, b0:b0 + 8], k("land%d" % (v - 1))
                 ts(T.off[:, L], A0, -1.0, 1023.0, MUL, ADD, a0t, k("offa"))
-                bar = (T.land[:, b0 + 8:b0 + 8 + 8 * nd], k("land%d" % (v - 1), "A7"))
+                bar = (T.land[:, b0 + 8:b0 + 40], k("land%d" % (v - 1), "A7"))
             else:
                 A0, a0t = T.A0[:, L], k("A0")
                 cp(T.off[:, L], T.stI[:, L], ab("stI"), k("offa"))
-            turn(A0, 8, 0, a0t, -1031.0)
+            act(T.A0p[:, L], A0, IDN, a0t, k("A0p"), bias=1024.0)
+            turn(T.A0p[:, L], 0, k("A0p"))
             uu, ut = T.cK[:, K], k("uK")
+            e1, e2 = pE[:, 128:256], pE[:, 256:384]
             if EV[min(v, 1)]:
-                mm(pE[:, 1, :], T.We[:, K], xb, True, True, k("We") + XB, k("pE"))
-                cp(T.eI[:, K], pE[:, 1, :], k("pE"), k("eI"))
+                mm(e1, T.We[:, K], xb, True, True, k("We") + XB, k("pE"))
+                cp(T.eI[:, K], e1, k("pE"), k("eI"))
                 ts(T.eM[:, K], T.eI[:, K], 511, None, AND, None, k("eI"), k("eM"))
                 ts(uu, T.eM[:, K], 33.0, None, ADD, None, k("eM"), ut)
             else:
-                mm(pE[:, 1, :], T.c1[:], T.ones[:], True, False, ["c1", "ones"], k("pE"))
-                mm(pE[:, 1, :], T.We[:, K], xb, False, True, k("We") + XB, k("pE"))
-                act(T.hE[:, K], pE[:, 1, :], IDN, k("pE"), k("hE"), bias=1.5 * 2.0 ** 23, scale=1.0 / 512.0)
-                mm(pE[:, 2, :], T.nI512[:], T.hE[:, K], True, False, ["nI512"] + k("hE"), k("pE"), True)
-                mm(pE[:, 2, :], T.c2[:], T.ones[:], False, False, ["c2", "ones"], k("pE"))
-                mm(pE[:, 2, :], T.We[:, K], xb, False, True, k("We") + XB, k("pE"))
-                act(uu, pE[:, 2, :], IDN, k("pE"), ut, bias=33.0)
+                mm(e1, c1, T.ones[:], True, False, ["c1", "ones"], k("pE"))
+                mm(e1, T.We[:, K], xb, False, True, k("We") + XB, k("pE"))
+                act(T.hE[:, K], e1, IDN, k("pE"), k("hE"), bias=1.5 * 2.0 ** 23, scale=1.0 / 512.0)
+                mm(e2, T.nI512[:], T.hE[:, K], True, False, ["nI512"] + k("hE"), k("pE"), True)
+                mm(e2, c2, T.ones[:], False, False, ["c2", "ones"], k("pE"))
+                mm(e2, T.We[:, K], xb, False, True, k("We") + XB, k("pE"))
+                act(uu, e2, IDN, k("pE"), ut, bias=33.0)
             first, who, parts = XE[s] if v == 0 else XE[2]
             out, ot = T.xp[:, K], k("xp")
             if first == "V":
@@ -412,100 +439,99 @@ def build_ops(g, T, topo, core, rank, cost):
                     XB + ["lp"], ot)
             else:
                 sga(out, xb, T.lp[:], XB + ["lp"], ot)
-            XJ = k(*["xj%d_" % j for j in range(4)])
-            x4, X4 = T.xp[:, 256 + 512 * s:768 + 512 * s], k(*["xq%d_" % j for j in range(4)])
-            for j, e in enumerate(who + parts):
-                if j < 4:
-                    out, src, rd, wr = T.xp[:, 256 + 512 * s + j:768 + 512 * s:4], T.xp[:, K], k("xp"), [X4[j]]
+            XJ = [k(*["xj%d%s_" % (j, hf) for j in range(4)]) for hf in "ab"]
+            c0, X4 = 256 + 512 * s, k(*["xq%d_" % j for j in range(4)])
+            for j, e in enumerate(who):
+                move(e, T.xp[:, c0 + j:c0 + 512:4], T.xp[:, K], k("xp"), [X4[j]], 0.5)
+            for j, e in enumerate(parts):
+                if len(e) == 1:
+                    move(e, xr[:, j:2048:4], T.xp[:, c0:c0 + 512], X4, [XJ[0][j], XJ[1][j]], 0.5)
                 else:
-                    out, src, rd, wr = xr[:, j - 4:2048:4], x4, X4, [XJ[j - 4]]
-                move(e, out, src, rd, wr, 0.5)
+                    for hf in range(2):
+                        move(e[hf], xr[:, 1024 * hf + j:1024 * hf + 1024:4], T.xp[:, c0 + 256 * hf:c0 + 256 * hf + 256],
+                             X4, [XJ[hf][j]], 0.5)
             act(Y[:, 1152 * s:1152 * s + 128], uu, IDN, ut, k("Ye"), bias=-1599.5, scale=48.5)
-            act(T.A0p[:, L], A0, IDN, a0t, k("A0p"), bias=1024.0)
+            if v == 0:
+                tables()
 
             for st in range(3):
                 nt = st + 1
                 of = T.off[:, 16 * st + 8 * s:16 * st + 8 * s + 8]
                 oft = k("off" + "abc"[st])
-                TKc = 384 * s
                 gtt(T.mK[:, K], W[:, TC:TC + (2048 if st else 1024)], of, T.cK[:, K], MUL,
                     oft + k("Wt", "Wu", "uK") + (PAY if st else []), k("mK"))
-                if N16:
-                    add("V", 0.06 + 128 * GA * CY, lambda: V.tensor_scalar(
-                        T.n16[:, K], T.mK[:, K].indirect(T.lp[:]), 5, 4095, SHR, AND), k("mK") + ["lp"], k("n16"))
-                else:
-                    ts(T.nK[:, K], T.mK[:, K], 5, 4095, SHR, AND, k("mK"), k("nK"))
-                    add("V", NX + 0.06 + 128 * GA * CY, lambda: V.tensor_copy(T.n16[:, K], T.nK[:, K].indirect(T.lp[:])),
-                        k("nK") + ["lp"], k("n16"))
-                share = SHARE[s][st]
+                nK, nkt = (T.nK[:, 256 + 128 * s:384 + 128 * s], k("nKb")) if st else (T.nK[:, K], k("nKa"))
+                ts(nK, T.mK[:, K], 5, 4095, SHR, AND, k("mK"), nkt)
+                add("V", NX + 0.06 + 128 * GA * CY, lambda nK=nK: V.tensor_copy(T.n16[:, K], nK.indirect(T.lp[:])),
+                    nkt + ["lp"], k("n16"))
                 GM, GP = k(*["Gm%d_" % r for r in range(16)]), k(*["Gp%d_" % r for r in range(16)])
-                a = 0
-                for w in VCH[share]:
-                    gtt(Gm[:, 128 * a:128 * (a + w)], prg[:], T.n16[:, 128 * s + 8 * a:128 * s + 8 * (a + w)],
-                        xr[:, 128 * a:128 * (a + w)], MAX, k("n16") + PRG + XJ, GM[a:a + w])
-                    ops[-1]["soft"] = a > 0
-                    a += w
-                if share:
-                    gs = T.Gs[:, 512 * s:512 * s + 128 * SW]
-                    sga(gs, prg[:], T.n16[:, 128 * s + 8 * a:128 * s + 128], k("n16") + PRG, k("Gs"))
-                    mm(pE[:, 0:SW, :], T.nI23[:], xr[:, 128 * a:2048], True, False, ["nI23"] + XJ, k("pE"))
-                    mm(pE[:, 0:SW, :], T.pI23[:], gs, False, True, ["pI23"] + k("Gs"), k("pE"))
-                    act(Gm[:, 128 * a:2048], pE[:, 0:SW, :], RELU, k("pE"), GM[a:16], scale=1.0 / 8388608.0)
-                a = 0
-                for w in SCH:
-                    sga(Gp[:, 128 * a:128 * (a + w)], W[:, PC:DC], T.n16[:, 128 * s + 8 * a:128 * s + 8 * (a + w)],
-                        k("n16") + PAY, GP[a:a + w])
-                    ops[-1]["soft"] = a > 0
-                    a += w
-                mm(pU[:, 0, :], T.CI[:, 256:384], T.ones[:], True, False, ["CK", "ones"], k("pU"))
-                for t in range(nt):
-                    mm(pU[:, 1 + t, :], T.SelY[0:8, :], T.TT[0:8, TKc + 128 * t:TKc + 128 * t + 128], False, False,
-                       ["SelY"] + k("TT%d" % t), k("pU"), True)
-                jobs, a = [], 0
-                for w in SCH:
-                    jobs.append((a + w, 1, a, w))
-                    a += w
-                a = 0
-                for w in VCH[share][:NY]:
-                    jobs.append((a + w, 0, a, w))
-                    a += w
-                ny = a
-                jobs.sort()
-                for job in jobs:
-                    a, w = job[2:]
-                    for r in range(a, a + w):
-                        end = job is jobs[-1] and r == a + w - 1
-                        if job[1]:
-                            mm(pU[:, 0:nt + 1, r:128:16], Gp[:, 128 * r:128 * r + 128], T.Wp[:, 0:8 * (nt + 1)], False, end,
-                               GP[a:a + w] + WP, k("pU"))
+
+                def cols(a, w):
+                    return slice(128 * a, 128 * (a + w))
+
+                def lst(a, w):
+                    return T.n16[:, 128 * s + 8 * a:128 * s + 8 * (a + w)]
+                for hf, (vch, cut, sw) in enumerate(HALF):
+                    a = 8 * hf
+                    for w in vch:
+                        gtt(Gm[:, cols(a, w)], W[:, PC:DC], lst(a, w), xr[:, cols(a, w)], SUB, k("n16") + PAY + XJ[hf], GM[a:a + w])
+                        ops[-1]["soft"] = a > 0
+                        a += w
+                for hf, (vch, cut, sw) in enumerate(HALF):
+                    a = 8 * hf + 8 - sw
+                    if sw:
+                        sga(Gm[:, cols(a, sw)], W[:, PC:DC], lst(a, sw), k("n16") + PAY, GM[a:a + sw])
+                        ops[-1]["soft"] = hf > 0 and HALF[0][2] > 0
+                nb = 8 * (4 + nt)
+                for hf, (vch, cut, sw) in enumerate(HALF):
+                    a0, a, vw = 8 * hf, 8 * hf + 8 - sw, 8 - sw
+                    bn = ("pU", "pK")[hf]
+                    pY, R = bank[bn], slice(8 * hf, 8 * hf + 8)
+                    if vw and cut == "V":
+                        ts(Gp[:, cols(a0, vw)], Gm[:, cols(a0, vw)], bq, 0.0, ADD, MAX, GM[a0:a] + ["bq"], GP[a0:a], 0.5)
+                    elif vw:
+                        act(Gp[:, cols(a0, vw)], Gm[:, cols(a0, vw)], RELU, GM[a0:a] + ["bq"], GP[a0:a], bias=bq)
+                    if sw:
+                        pS = bank[SUB_[hf]][:, 0:128 * sw]
+                        mm(pS, T.nI23[:], xr[:, cols(a, sw)], True, False, ["nI23"] + XJ[hf], k(SUB_[hf]))
+                        mm(pS, T.pI23[:], Gm[:, cols(a, sw)], False, True, ["pI23"] + GM[a:a + sw], k(SUB_[hf]))
+                        act(Gp[:, cols(a, sw)], pS, RELU, k(SUB_[hf]) + ["bq"], GP[a:a + sw], bias=bq, scale=1.0 / 8388608.0)
+                    jobs = [(xr, WX, a, sw, XJ[hf] + ["Wx_"])]
+                    b = a0
+                    for w in vch:
+                        jobs.append((Gm, WG, b, w, GM[b:b + w] + WGt))
+                        b += w
+                    jobs += [(None, None, 0, 1, None), (Gm, WG, a, sw, GM[a:a + sw] + WGt), (Gp, WR, a0, vw, GP[a0:a] + WRt),
+                             (Gp, WR, a, sw, GP[a:a + sw] + WRt)]
+                    jobs = [job for job in jobs if job[3]]
+                    for job in jobs:
+                        src, Wq, b, w, rd = job
+                        if src is None:
+                            mm(pY[:, 256:256 + 64 * nt], T.SelY[0:16, :], T.TT[0:16, 24 * s:24 * s + 8 * nt, R],
+                               False, False, ["SelY"] + k(*["TT%d" % t for t in range(nt)]), k(bn))
+                            continue
+                        for r in range(b, b + w):
+                            mm(pY[:, r - a0:8 * nb:8], src[:, cols(r, 1)], Wq[:, 0:nb], job is jobs[0] and r == b,
+                               job is jobs[-1] and r == b + w - 1, rd, k(bn))
+                    for e in READ[hf]:
+                        if e == "k":
+                            act(T.kp[:, L, R], pY[:, 0:64], IDN, k(bn) + ["kb"], k("kp" + "ab"[hf]), bias=kb)
+                        elif e == "a":
+                            act(T.ab[:, 24 * s:24 * s + 24, R], pY[:, 64:256], ABS, k(bn), k("ab" + "ab"[hf]), bias=-192.0)
                         else:
-                            mm(pU[:, 0, r:128:16], Gm[:, 128 * r:128 * r + 128], T.Wp[:, 32:40], False, end,
-                               GM[a:a + w] + ["Wm8"], k("pU"))
-                act(T.kp[:, K], pU[:, 0, :], IDN, k("pU"), k("kp"), bias=7.0)
-                pen = T.pen[:, TKc:TKc + 128 * nt]
-                if PENV[st]:
-                    ts(pen, pU[:, 1:nt + 1, :], 0.0, None, EQ, None, k("pU"), k("pen"))
-                else:
-                    pab = T.pab[:, TKc:TKc + 128 * nt]
-                    act(pab, pU[:, 1:nt + 1, :], ABS, k("pU"), k("pab"))
-                    act(pen, pab, RELU, k("pab"), k("pen"), bias=1.0, scale=-1.0)
-                KX = pK[:, 0:128]
-                mm(KX, T.CI[:, 0:128], T.ones[:], True, False, ["CI", "ones"], k("pK"))
-                if share:
-                    mm(KX, T.CI[:, 128:256], T.ones[:], False, False, ["CJ", "ones"], k("pK"))
-                a = ny
-                for w in VCH[share][NY:] + ((SW,) if share else ()):
-                    for r in range(a, a + w):
-                        mm(KX, T.Wm[:, 15 - r:143 - r], Gm[:, 128 * r:128 * r + 128], False, False,
-                           GM[a:a + w] + ["Wm"], k("pK"))
-                    a += w
-                mm(KX, T.kp[:, K], T.idn[:], False, False, ["idn"] + k("kp"), k("pK"), True)
+                            ts(T.pen[:, 24 * s:24 * s + 8 * nt, R], pY[:, 256:256 + 64 * nt], 2047.0 - OFS, None, EQ, None,
+                               k(bn), k("pen" + "ab"[hf]))
+                KX = pU[:, 0:128]
+                mm(KX, T.kp[:, L, :], T.idn[:], True, False, ["idn"] + k("kpa", "kpb"), k("pU"), True)
+                for j in range(3):
+                    mm(KX, T.ab[:, 24 * s + 8 * j:24 * s + 8 * j + 8, :], nI15, False, False,
+                       ["nI15"] + k("aba", "abb"), k("pU"))
                 for t in range(nt):
-                    mm(KX, T.pen[:, TKc + 128 * t:TKc + 128 * t + 128], T.nI24[:], False, t == st,
-                       ["nI24"] + k("pen"), k("pK"))
+                    mm(KX, T.pen[:, 24 * s + 8 * t:24 * s + 8 * t + 8, :], nI24, False, t == st,
+                       ["nI24"] + k("pena", "penb"), k("pU"))
                 ps, pst = T.ZW[:, 128 * s + 15:128 * s + 128:16], k("ZW")
-                add("V", cyc(128), lambda: V.tensor_tensor_scan(T.ZW[:, K], T.rst[:], pK[:, 0:128], 0.0, MUL, MAX),
-                    k("pK") + ["rst"], pst)
+                add("V", cyc(128), lambda: V.tensor_tensor_scan(T.ZW[:, K], T.rst[:], pU[:, 0:128], 0.0, MUL, MAX),
+                    k("pU") + ["rst"], pst)
                 bi, bt = T.BI[:, 24 * s + 8 * st:24 * s + 8 * st + 8], k("BI%d" % nt)
                 if st == 0:
                     cp(bi, ps, pst, bt)
@@ -516,29 +542,44 @@ def build_ops(g, T, topo, core, rank, cost):
                     f0 = 16 * s + 8 * st
                     ts(a, bi, 2047, None, AND, None, bt, at)
                     ts(T.off[:, 16 * nt + 8 * s:16 * nt + 8 * s + 8], a, -1.0, 2047.0, MUL, ADD, at, k("off" + "abc"[nt]))
-                    ts(T.AF[:, f0:f0 + 8], a, -2055.0, None, ADD, None, at, k("af%d" % nt))
                     ts(T.go[:, f0:f0 + 8], a, 1024.0, None, ALU.is_ge, None, at, k("go%d" % nt))
-                    turn(T.AF[:, f0:f0 + 8], 8, nt, k("af%d" % nt), 0.0)
+                    turn(a, nt, at)
+                l2 = T.le[:, 16 + 8 * s:24 + 8 * s]
                 if st == 0:
                     act(T.q2[:, L], ps, IDN, pst, k("none", "q2"), bias=4096.0, scale=-1.0)
                     ts(T.kk1[:, L], bi, 11, 15, SHR, AND, bt, k("kk1"))
-                    tt(T.q1[:, L], cb, T.kk1[:, L], SUB, ["cb"] + k("kk1"), k("q1"))
-                    cp(T.le[:, L], T.q1[:, L], k("q1"), k("le"))
-                    sga(T.NK[:, K], Gp[:], T.le[:, L], GP + k("le"), NK)
-                    mm(pT[:, 0:8], T.ones[:], T.m8[:, 0:8], True, False, ["ones", "m8"], k("pT"))
-                    mm(pT[:, 0:8], T.pI23[:], T.ones[:, 0:8], False, False, ["pI23", "ones"], k("pT"))
-                    mm(pT[:, 0:8], T.nI23[:], T.go[:, f0:f0 + 8], False, False, ["nI23"] + k("go1"), k("pT"))
-                    k_to_l(pT[:, 0:8], T.WN, lambda rr: T.NK[:, 128 * s + rr:128 * s + 128:16], False, True,
-                           ["WN"] + NK, k("pT"))
-                    tt(T.P1[:, 24 * s:24 * s + 8], pT[:, 0:8], cdum, MIN, k("pT") + ["cdum"], k("P1a"))
+                    cp(l2, T.kk1[:, L], k("kk1"), k("lk"))
+                    ts(T.P1[:, sl(3)], T.off[:, 16 + 8 * s:24 + 8 * s], 1023.0, None, MIN, None, k("offb"), k("P1d"))
                     tt(T.i2[:, L], bi, T.A0p[:, L], MAX, bt + k("A0p"), k("i2"))
                     ts(T.Bw[:, L], T.i2[:, L], 32767, None, AND, None, k("i2"), k("Bw"))
                     tt(T.lt0[:, L], T.q2[:, L], A0, MAX, k("q2") + a0t, k("lt0"))
                     if v == 0:
                         distance(xb, XB, T.goals[:, K], ab("goal0"))
-                        act(T.thr[:, TH], pU[:, 0, D], CPY, k("pU"), k("thr"))
+                        act(T.thr[:, X], pK[:, D], CPY, k("pK"), k("thr"))
                     else:
-                        act(T.thr[:, TH], bar[0], IDN, bar[1], k("thr"), bias=T.An[:, 8 * s + 4:8 * s + 5])
+                        act(T.thr[:, X], bar[0], IDN, bar[1], k("thr"), bias=T.An[:, 8 * s + 4:8 * s + 5])
+                if st == 0 and last:
+                    for j in range(3):
+                        C = slice(768 * s + 256 * j, 768 * s + 256 * j + 256)
+                        mm(pT[:, 0:256], T.DWb[0:64, 128 * j:128 * j + 128], T.Pc[0:64, C], j == 0, False,
+                           ["DWb%d_" % j] + k("Pc%d_" % j), k("pT"))
+                    for j in range(3):
+                        C = slice(768 * s + 256 * j, 768 * s + 256 * j + 256)
+                        mm(pT[:, 0:256], T.DWf[0:64, 128 * j:128 * j + 128], T.Vc[0:64, C], False, j == 2,
+                           ["DWf%d_" % j] + k("Vc%d_" % j), k("pT"), True)
+                    act(T.NW[:, 256 * s:256 * s + 256], pT[:, 0:256], IDN, k("pT"), k("NW"), bias=512.0)
+                    dma("Y", W[3:128:16, PL:DC2], T.NW[:, 256 * s:256 * s + 256], 131072, k("NW") + FILL, k("Wp"))
+                if st == 2:
+                    pN = bank[NB]
+                    gtt(T.E[:, K], T.OH[:, 0:16], l2, T.nK[:, K], MUL, k("lk", "nKa") + ["OHa"], k("E"))
+                    mm(pN[:, 256:384], T.E[:, K], T.blk[:], True, True, ["blk"] + k("E"), k(NB), True)
+                    tt(T.Z[:, K], pN[:, 256:384], T.msk[:], MUL, k(NB) + ["msk"], k("Z"), 1.0)
+                    m8 = T.m8[:, 8:16] if last else T.m8[:, 0:8]
+                    mm(pN[:, 0:8], T.ones[:], m8, True, False, ["ones", "m8a", "m8b"], k(NB))
+                    mm(pN[:, 0:8], T.pI23[:], T.ones[:, 0:8], False, False, ["pI23", "ones"], k(NB))
+                    mm(pN[:, 0:8], T.nI23[:], T.go[:, 16 * s:16 * s + 8], False, False, ["nI23"] + k("go1"), k(NB))
+                    mm(pN[:, 0:8], T.Z[:, K], T.blk8[:], False, True, ["blk8"] + k("Z"), k(NB), True)
+                    tt(T.P1[:, sl(0)], pN[:, 0:8], cdum2 if last else cdum, MIN, k(NB) + ["cdum", "cdum2"], k("P1a"))
                 if st == 1:
                     tt(T.kk1[:, L], bi, T.Bw[:, L], MAX, bt + k("Bw"), k("kk1"))
                     ts(T.Bw2[:, L], T.kk1[:, L], 32767, None, AND, None, k("kk1"), k("Bw2"))
@@ -556,10 +597,10 @@ def build_ops(g, T, topo, core, rank, cost):
                 act(T.xn[:, X0], T.NK[:, K], ABS, NK, k("xn%d" % v))
             else:
                 sga(T.NK[:, K], ef[:], T.le[:, L], k("le", "ef0") + ab("ef1"), NK)
-                mm(pE[:, 3, :], T.pI23[:], xb, True, False, ["pI23"] + XB, k("pE"))
-                mm(pE[:, 3, :], T.nI23[:], T.NK[:, K], False, True, ["nI23"] + NK, k("pE"))
-                act(T.xn[:, X0], pE[:, 3, :], ABS, k("pE"), k("xn%d" % v), scale=1.0 / 8388608.0)
-            b0 = 32 * (2 * v + s)
+                mm(pE[:, 384:512], T.pI23[:], xb, True, False, ["pI23"] + XB, k("pE"))
+                mm(pE[:, 384:512], T.nI23[:], T.NK[:, K], False, True, ["nI23"] + NK, k("pE"))
+                act(T.xn[:, X0], pE[:, 384:512], ABS, k("pE"), k("xn%d" % v), scale=1.0 / 8388608.0)
+            b0 = 48 * (2 * v + s)
             send(T.landb[:, X0], T.xn[:, X0], k("xn%d" % v), k("landb%d" % v))
             if last:
                 for h in range(2):
@@ -567,7 +608,7 @@ def build_ops(g, T, topo, core, rank, cost):
                         k("landb%d" % v), [])
             distance(T.xn[:, X0], k("xn%d" % v), T.goals[:, 256 * v + 128 * s:256 * v + 128 * s + 128],
                      ab("goal0") if v == 0 else ["goalx"])
-            tt(T.good[:, TH], pU[:, 0, D], T.thr[:, TH], LT, k("pU", "thr"), k("good"))
+            tt(T.good[:, X], pK[:, D], T.thr[:, X], LT, k("pK", "thr"), k("good"), 1.0)
             tt(T.i2[:, L], T.q1[:, L], T.lt2[:, L], MAX, k("q1", "lt2"), k("i2"))
             ts(T.lt[:, L], T.i2[:, L], 5119, None, AND, None, k("i2"), k("lt"))
             ts(T.q2[:, L], T.aw[:, L], 1024.0, 8192.0, LT, MUL, k("aw"), k("q2"))
@@ -575,88 +616,72 @@ def build_ops(g, T, topo, core, rank, cost):
             ts(T.q4[:, L], T.aw[:, L], -1024.0, None, ADD, None, k("aw"), k("q4"))
             cur, ct = (T.lfv[:, L], k("lfv")) if last else (T.snd[:, b0:b0 + 8], k("sa%d" % v))
             tt(cur, T.q3[:, L], T.q4[:, L], MAX, k("q3", "q4"), ct)
-            act(T.P1[:, 24 * s + 8:24 * s + 16], cur, IDN, ct, k("P1b"), bias=1023.0 + 128 * (1 - s), scale=-1.0)
+            act(T.P1[:, sl(1)], cur, IDN, ct, k("P1b"), bias=1023.0 + 128 * (1 - s), scale=-1.0)
             if not last:
-                act(T.snd[:, b0 + 8:b0 + 8 + 8 * nd], pU[:, 0, D], CPY, k("pU"), k("sd%d" % v))
-                send(T.land[:, b0:b0 + 8 + 8 * nd], T.snd[:, b0:b0 + 8 + 8 * nd], k("sa%d" % v, "sd%d" % v), k("land%d" % v))
+                act(T.snd[:, b0 + 8:b0 + 40], pK[:, D], CPY, k("pK"), k("sd%d" % v))
+                send(T.land[:, b0:b0 + 40], T.snd[:, b0:b0 + 40], k("sa%d" % v, "sd%d" % v), k("land%d" % v))
 
-            X = slice(24 * s, 24 * s + 24)
-            ts(T.P0[:, 24 * s + 16:24 * s + 24], T.Bw[:, L], 11, 15, SHR, AND, k("Bw"), k("P0c"))
+            WV, WT = (W[:, 0:WS], WALL + FILL + k("Wp")) if last else (W[:, 0:PL], WALL)
+            ts(T.P0[:, sl(2)], T.Bw[:, L], 11, 15, SHR, AND, k("Bw"), k("P0c"))
             ts(T.q1[:, L], T.lt[:, L], -1.0, float(TC + 1023), MUL, ADD, k("lt"), k("q1"))
-            tt(T.P0[:, 24 * s:24 * s + 8], T.q1[:, L], cj, MAX, k("q1") + ["cj"], k("P0a"))
-            tt(T.Df[:, X], T.P1[:, X], T.P0[:, X], SUB, k("P0a", "P0b", "P0c", "P1a", "P1b", "P1c"), k("Df"))
-            for j in range(3 // nd):
-                c = slice(24 * s + 8 * j, 24 * s + 8 * j + 8 * nd)
-                tt(T.Dg[:, c], T.Df[:, c], T.good[:, TH], MUL, k("Df", "good"),
-                   k("Dg0", "Dg1", "Dg2") if G3 else k("Dg%d" % j))
-            tt(T.Sel[:, X], T.Dg[:, X], T.P0[:, X], ADD, k("Dg0", "Dg1", "Dg2", "P0a", "P0b", "P0c"), k("Sel"))
-            idv = T.Sel[:, 24 * s:24 * s + 8]
+            tt(T.P0[:, sl(0)], T.q1[:, L], cj, MAX, k("q1") + ["cj"], k("P0a"))
+            tt(T.Df[:, X], T.P1[:, X], T.P0[:, X], SUB, k("P0a", "P0b", "P0c", "P0d", "P1a", "P1b", "P1c", "P1d"), k("Df"))
+            tt(T.Dg[:, X], T.Df[:, X], T.good[:, X], MUL, k("Df", "good"), k("Dg"))
+            tt(T.Sel[:, X], T.Dg[:, X], T.P0[:, X], ADD, k("Dg", "P0a", "P0b", "P0c", "P0d"), k("Sel"))
+            idv = T.Sel[:, sl(0)]
             cp(T.ls[:, X], T.Sel[:, X], k("Sel"), k("ls"))
             gtt(T.E[:, K], idv, T.l1[:], T.msk[:], MUL, k("Sel") + ["l1", "msk"], k("E"))
-            mm(pT[:, 16:24], T.nI512[:], cnb, True, False, ["nI512", "cnb"], k("pT"), True)
-            mm(pT[:, 16:24], T.nI512[:], idv, False, True, ["nI512"] + k("Sel"), k("pT"), True)
-            act(T.nb[:, L], pT[:, 16:24], CPY, k("pT"), k("nb"), scale=0.5)
-            mm(pE[:, 0, :], T.ones[:], T.Jm[:], True, False, ["ones", "Jm"], k("pE"))
-            mm(pE[:, 0, :], T.blkE[:], T.E[:, K], False, True, ["blkE"] + k("E"), k("pE"), True)
-            o, AC = 576 * s, []
+            act(T.q3[:, L], idv, CPY, k("Sel"), k("q3"), scale=-256.0 * 32768.0)
+            tt(T.nb[:, L], T.q3[:, L], cnb, SUB, k("q3") + ["cnb"], k("nb"))
+            act(T.acc[:, L], idv, IDN, k("Sel"), k("acc"), bias=-NEAR)
+            mm(pE[:, 0:128], T.ones[:], T.Jm[:], True, False, ["ones", "Jm"], k("pE"))
+            mm(pE[:, 0:128], T.blkE[:], T.E[:, K], False, True, ["blkE"] + k("E"), k("pE"), True)
+            o = 576 * s
             for c in range(7, -1, -1):
                 wdt = 16 * c + 16
                 e, et = T.EQ[:, o:o + wdt], k("EQ%d_" % c)
-                act(e, pE[:, 0, 0:wdt], ABS, k("pE", "nb"), et, bias=T.nb[:, 8 * s + c:8 * s + c + 1])
-                if c >= 8 - MNV:
-                    add("V", cyc(wdt), lambda mo=T.mn[:, 8 * s + c:8 * s + c + 1], e=e:
-                        V.tensor_reduce(mo, e, AxisListType.X, MIN), et, k("mn%d_" % c))
-                else:
-                    act(e, e, RELU, et, et + k("acc%d_" % c), bias=63.5 * 16384.0, scale=-16384.0,
-                        acc=T.acc[:, 8 * s + c:8 * s + c + 1])
-                    AC += k("acc%d_" % c)
+                act(e, pE[:, 0:wdt], ABS, k("pE", "nb"), et, bias=T.nb[:, 8 * s + c:8 * s + c + 1], scale=32768.0)
+                add("V", cyc(wdt), lambda mo=T.mn[:, 8 * s + c:8 * s + c + 1], e=e:
+                    V.tensor_reduce(mo, e, AxisListType.X, MIN, negate=True), et, k("mn%d_" % c))
                 o += wdt
-            if MNV:
-                c = slice(8 * s + 8 - MNV, 8 * s + 8)
-                MN = k(*["mn%d_" % j for j in range(8 - MNV, 8)])
-                if RV:
-                    ts(T.acc[:, c], T.mn[:, c], 63.5, 8192.0, LT, MUL, MN, k("accv"))
-                else:
-                    act(T.acc[:, c], T.mn[:, c], RELU, MN, k("accv"), bias=63.5 * 16384.0, scale=-16384.0)
-                AC += k("accv")
-            tt(T.q2[:, L], T.acc[:, L], ctop, MIN, AC + ["ctop"], k("q2"))
-            tt(T.lfv[:, L], T.q2[:, L], idv, MAX, k("q2", "Sel"), k("lfv"))
+            tt(T.q2[:, L], T.mn[:, L], ctop2 if last else ctop, MIN, k(*["mn%d_" % j for j in range(8)]) + ["ctop", "ctop2"], k("q2"))
+            tt(T.lfv[:, L], T.q2[:, L], T.acc[:, L], MAX, k("q2", "acc"), k("lfv"))
             mm(pT[:, 32:40], T.PB[:], T.lfv[:, L], True, True, ["PB"] + k("lfv"), k("pT"), True)
             mm(pT[:, 40:48], T.PA[:], T.lfv[:, L], True, True, ["PA"] + k("lfv"), k("pT"), True)
-            cp(T.lf[:, 16 * s:16 * s + 16], pT[:, 32:48], k("pT"), k("lf"))
-            lk = T.ls[:, 24 * s + 16:24 * s + 24]
-            sga(T.Z[:, K], Y[:, 128 * s:128 * s + 1152], T.ls[:, 24 * s + 8:24 * s + 16],
-                k("ls", "Ye") + ["Yf", "Y0", "Y1"], k("Z"))
-            sga(T.kp[:, K], T.KP[:], lk, k("ls") + ["KPa", "KPb"], k("kp"))
-            gtt(T.aK[:, K], W[:, 0:WS], T.ls[:, 24 * s:24 * s + 8], T.kp[:, K], MUL, k("ls", "kp") + WALL, k("aK"))
-            gtt(T.bK[:, K], T.OH[:], lk, T.Z[:, K], MUL, k("ls", "Z") + ["OHa", "OHb"], k("bK"))
-            mm(pU[:, 1, :], T.idn[:], T.aK[:, K], True, False, ["idn"] + k("aK"), k("pU"), True)
-            mm(pU[:, 1, :], T.idn[:], T.bK[:, K], False, True, ["idn"] + k("bK"), k("pU"), True)
-            act(T.NK[:, K], pU[:, 1, :], IDN, k("pU"), NK, bias=128.5 + 2.0 ** -13, scale=1.0 / 4096.0)
-            for x, xt in ((T.aK, "aK"), (T.bK, "bK")):
-                for h, Pm, pt in ((0, T.PB, "PB"), (1, T.PA, "PA")):
-                    mm(pK[:, 128 * h:128 * h + 128], Pm[:], x[:, K], (xt, h) == ("aK", 0), False, [pt] + k(xt), k("pK"), True)
-            for h in range(2):
-                mm(pK[:, 128 * h:128 * h + 128], T.Pq[:, 128 * h:128 * h + 128], T.NK[:, K], False, h == 1,
-                   ["Pq0", "Pq1"] + NK, k("pK"))
+            ts(T.lf[:, 16 * s:16 * s + 16], pT[:, 32:48], NEAR, None, ADD, None, k("pT"), k("lf"))
+            lk = T.ls[:, sl(2)]
+            sga(T.Z[:, K], Y[:, 128 * s:128 * s + 1152], T.ls[:, sl(1)], k("ls", "Ye") + YT, k("Z"))
+            sga(T.kq[:, K], T.KP[:, 0:18], lk, k("ls") + ["KPa", "KPb"], k("kq"))
+            gtt(T.aK[:, K], WV, T.ls[:, sl(0)], T.kq[:, K], MUL, k("ls", "kq") + WT, k("aK"))
+            gtt(T.bK[:, K], T.OH[:, 0:18], lk, T.Z[:, K], MUL, k("ls", "Z") + ["OHa", "OHb", "OHc"], k("bK"))
+            if not last:
+                sga(T.Z2[:, K], Y[:, 128:1152], T.ls[:, sl(3)], k("ls") + YT + ["z2"], k("Zb"), scale=z2)
+            tt(T.aK[:, K], T.aK[:, K], T.bK[:, K], ADD, k("aK", "bK"), k("aK"))
+            act(T.NK[:, K], T.aK[:, K], IDN, k("aK"), NK, bias=128.5 + 15 * 2.0 ** -16, scale=1.0 / 4096.0)
+            parts = [(T.Pq, T.Z2, k("Zb"))] * (not last) + [(None, T.aK, k("aK")), (T.Pq, T.NK, NK)]
+            for Pm, x, xt in parts:
+                for h in range(2):
+                    lhs = (T.PB, T.PA)[h][:] if Pm is None else Pm[:, 128 * h:128 * h + 128]
+                    mm(pK[:, 128 * h:128 * h + 128], lhs, x[:, K], xt == parts[0][2] and h == 0, xt == NK and h == 1,
+                       ["Pq0", "Pq1", "PA", "PB"] + xt, k("pK"), Pm is None)
             act(T.NW[:, 256 * s:256 * s + 256], pK[:, 0:256], IDN, k("pK"), k("NW"), bias=129.0 * 4096.0)
             for h in range(2):
                 add("V", 0.06 + 128 * SC * CY,
-                    lambda h=h: V.tensor_copy(W[:, 0:WS].indirect(T.lf[:, 16 * s + 8 * h:16 * s + 8 * h + 8]),
-                                              T.NW[:, 256 * s + 128 * h:256 * s + 128 * h + 128]),
-                    k("lf", "NW"), WALL)
+                    lambda h=h, WV=WV: V.tensor_copy(WV.indirect(T.lf[:, 16 * s + 8 * h:16 * s + 8 * h + 8]),
+                                                     T.NW[:, 256 * s + 128 * h:256 * s + 128 * h + 128]),
+                    k("lf", "NW"), WT)
             if not last:
                 an = T.An[:, 8 * s + v + 1:8 * s + v + 2]
-                act(T.q4[:, L], T.good[:, 24 * s:24 * s + 8], CPY, k("good"), k("cnt", "q4"), acc=T.cnt[:, c4])
-                mm(pT[:, 48:49], T.blk2[:], T.cnt[:, c4], True, True, ["blk2a", "blk2b"] + k("cnt"), k("pT"), True)
-                act(an, pT[:, 48:49], IDN, k("pT", "An"), k("An"), bias=T.An[:, 8 * s + v:8 * s + v + 1], scale=-1.0)
+                mm(pT[:, 48:56], T.blk2[:], T.good[:, sl(0)], True, True, ["blk2a", "blk2b"] + k("good"), k("pT"))
+                act(T.q4[:, L], pT[:, 48:56], CPY, k("pT"), k("cnt", "q4"), acc=T.cnt[:, c4])
+                act(an, T.cnt[:, c4], IDN, k("cnt", "An"), k("An"), bias=T.An[:, 8 * s + v:8 * s + v + 1], scale=-1.0)
                 aq = T.go[:, 32 + 4 * s:33 + 4 * s]
                 act(aq, an, IDN, k("An"), k("Aq"), bias=-0.4375, scale=-0.125)
                 act(T.An[:, 8 * s + 4:8 * s + 5], aq, IDN, k("Aq", "An"), k("A7"), bias=an, scale=8.0)
 
-        dma("Y", T.yteam[64 * s:64 * s + 64, 0:512], W[0:64, TC:TC + 512], 131072, WALL, [])
-        dma("S", T.yteam[64 * s:64 * s + 64, 512:1024], W[64:128, TC + 512:PC], 131072, WALL, [])
-        dma("Y", T.yact[4 * s:4 * s + 4, :], W[64:128:16, PC:DC], 65536, WALL, [])
+        dma("Y", T.yteam[64 * s:64 * s + 64, 0:512], W[0:64, TC:TC + 512], 131072, WT, [])
+        dma("S", T.yteam[64 * s:64 * s + 64, 512:1024], W[64:128, TC + 512:PC], 131072, WT, [])
+        dma("Y", T.yact[4 * s:4 * s + 4, :], W[67:128:16, PL:DC2], 65536, WT, [])
 
     a = len(ops)
     stream(0)

@@ -3,22 +3,30 @@ from concourse.bass import DstId, RemoteDMATransfer
 from concourse.mybir import AluOpType as ALU, AxisListType, ActivationFunctionType as ACT
 
 NV = 4
-TC, PC, DC, DT, PL, DC2, DT2, WS = 128, 1152, 5248, 5376, 5504, 9600, 9728, 9856
-HALF = (((2, 2), "V", 4), ((2, 2), "V", 4))
+TC, PC, DC, DT, PL, DT2, WS = 1, 1032, 5128, 5136, 5264, 9360, 9488
+YT0, YW = 264, 1288
+EXTRA = ((1, 0, 0), (0, 0, 0))
+JS = (2, 2)
 SUB_ = ("pE", "pT")
 READ = ("kap", "kap")
-PV = ("VSVSVSVSS", "VSVSVSVSS")
-XE = (("V", "VVVV", "VVSS"), ("S", "SSSS", "VSSS"), ("S", "VVSS", "GGSV"))
+PV = "SSSSVSVS"
+XE = (("V", "VVVV", "VVSS"), ("S", "SSSS", "VVSS"), ("S", "VVVV", "GGGV"))
 HI0 = "S"
+TB = ("pK1", "pU1", "pK0", "pT1", "pK1", "pU1", "pK0", "pT1")
+ADDP = (1, 1)
+ESP = (((0, 8),), ((0, 6), (6, 8)))
+EARLY = (0, 1)
+SA = "S"
 EV = (1, 0)
 NKV = 1
-NEAR = 63.5 * 32768.0
+NEAR, EPS = 63.5 / 256.0, 2.0 ** -23
 NB = "pE"
-ONV = ()
+ONV = ("acc", "Pb")
 DW = (16, 240, 3600)
 OFS = 192.0 * sum(DW) + 512.0
-ROUNDS, CLIMB = 20, 2500
-LEAD, SEED, NOISE = 4.0, 3, 0.6
+ROUNDS, CLIMB, SWAPS = 20, 2500, 16000
+LEAD, SEED, NOISE = 3.0, 1, 0.6
+APART = 1
 F, B, I, U = "float32", "bfloat16", "int32", "uint16"
 
 
@@ -27,56 +35,60 @@ def sb(n, d):
 
 
 SCRATCH = {
-    "Y": sb(1280, F), "goals": sb(1024, B), "land": sb(288, F), "snd": sb(288, F),
+    "Y": sb(YW, F), "goals": sb(1024, B), "land": sb(288, F), "snd": sb(288, F),
     "landb": sb(1024, B), "xb": sb(256, B), "xp": sb(1280, B), "xn": sb(1024, B), "wtI": sb(8, I), "stI": sb(16, I),
-    "actI": sb(256, I), "dg": sb(768, I), "dgb": sb(768, B), "Vc": sb(1536, F), "Pc": sb(1536, B),
+    "actI": sb(256, I), "dg": sb(768, I), "dgb": sb(768, B), "Vc": sb(768, B), "Pc": sb(768, B),
+    "prg": sb(4096, B), "dq": sb(4096, B), "W": sb(WS, F), "ef": sb(1040, B), "teamI": sb(1024, I),
     "ci": sb(16, I), "cf": sb(24, F), "io2": sb(128, F), "io3": sb(128, F), "idn": sb(128, F),
-    "blk": sb(128, F), "blkE": sb(128, F), "blk2": sb(128, B), "blk8": sb(8, F), "msk": sb(128, F),
-    "PA": sb(128, F), "PB": sb(128, F), "nI23": sb(128, B), "pI23": sb(128, B), "nI512": sb(128, F),
-    "lp": sb(8, U), "nI": sb(256, B), "SelY": sb(128, B), "rst": sb(128, F), "SB": sb(128, B),
-    "Wy": sb(168, B), "We": sb(256, B), "c12": sb(256, B), "DWf": sb(384, F), "DWb": sb(384, B),
-    "blkB": sb(160, B), "ones": sb(128, B), "Jm": sb(128, B), "m8": sb(24, B),
-    "OH": sb(24, F), "KP": sb(24, F), "l1": sb(8, U), "cs": sb(56, F),
-    "EQ": sb(1152, F),
+    "blk": sb(128, F), "blk8": sb(16, F), "msk": sb(128, F),
+    "nI23": sb(128, B), "pI23": sb(128, B), "nI512": sb(128, F),
+    "lp": sb(8, U), "nI": sb(384, B), "SelY": sb(256, B), "rst": sb(128, F), "SB": sb(128, B),
+    "Wy": sb(224, B), "We": sb(128, B), "c12": sb(256, B), "DWf": sb(384, B), "DWb": sb(384, B),
+    "blkB": sb(208, B), "nI12": sb(128, B), "ones": sb(128, B), "Jm": sb(128, B), "Jn": sb(128, B), "mof": sb(128, F), "m8": sb(8, B),
+    "OH": sb(56, F), "KP": sb(24, F), "l1": sb(16, U), "cs": sb(64, F),
+    "EQ": sb(1152, B), "ES": sb(1152, B), "rs2": sb(576, B), "TX": sb(384, B),
     "cK": sb(256, F), "mK": sb(256, I), "nK": sb(512, I), "n16": sb(256, U),
     "Z": sb(256, F), "Z2": sb(256, B), "E": sb(256, F), "eI": sb(256, I), "eM": sb(256, I), "NK": sb(256, B),
     "kq": sb(256, F), "aK": sb(256, F), "bK": sb(256, F), "NW": sb(512, F), "nb": sb(16, F), "hE": sb(256, F),
     "TT": ("sbuf", [128, 48, 16], B), "pen": ("sbuf", [128, 48, 16], B), "ab": ("sbuf", [128, 48, 16], B),
     "kp": ("sbuf", [128, 16, 16], F),
-    "ZW": sb(256, F), "AF": sb(96, B), "go": sb(40, B), "BI": sb(48, I),
-    "a1": sb(16, I), "a2": sb(16, I), "A0": sb(16, F), "off": sb(48, U),
-    "A0p": sb(16, F), "kk1": sb(16, I), "q1": sb(16, F), "q2": sb(16, F),
-    "acc": sb(16, F), "q3": sb(16, F), "q4": sb(16, F), "i2": sb(16, I),
-    "Bw2": sb(16, I), "lt0": sb(16, F), "lt2": sb(16, I), "Bw": sb(16, I), "aw": sb(16, I), "le": sb(32, U),
-    "lt": sb(16, I), "P0": sb(64, I), "P1": sb(64, F), "Df": sb(64, F), "Dg": sb(64, F),
-    "Sel": sb(64, F), "ls": sb(64, U), "Pq": sb(256, B), "thr": sb(64, F), "good": sb(64, B),
-    "mn": sb(16, F), "lfv": sb(16, F), "lf": sb(32, U),
-    "cnt": sb(8, F), "An": sb(16, F),
+    "ZW": sb(256, F), "AF": sb(144, B), "go": sb(40, B), "BI": ("sbuf", [128, 16, 4], I),
+    "I3": ("sbuf", [128, 48, 5], I), "D0": sb(128, F), "D1": sb(128, F), "SC": sb(128, F),
+    "A0": sb(16, F), "off": sb(48, U), "kk1": sb(16, I), "q2": sb(32, F),
+    "acc": sb(16, F), "q4": sb(16, F), "i2": sb(16, I),
+    "le": sb(32, U),
+    "P0": sb(80, I), "P1": sb(80, F), "Dg": sb(80, F),
+    "Sel": sb(80, F), "ls": sb(80, U), "thr": sb(80, F),
+    "lfv": sb(16, F), "lf": sb(16, U),
+    "cnt": sb(8, F), "An": sb(40, B),
 }
 for s_ in "01":
-    for nm, n_, d_ in (("prg", 4096, B), ("W", WS, F), ("ef", 1040, B), ("teamI", 1024, I), ("xr", 2048, B),
-                       ("Gm", 2048, B), ("Gp", 2048, B)):
+    for nm, n_, d_ in (("xr", 1536, B), ("Gm", 2048, B), ("Gp", 2048, B)):
         SCRATCH[nm + s_] = sb(n_, d_)
     for nm in ("pK", "pT", "pU", "pE"):
         SCRATCH[nm + s_] = ("psum", [128, 512], F)
 PSUM = ("pK0", "pK1", "pT0", "pT1", "pU0", "pU1", "pE0", "pE1")
 
 NDMA = 70
-SEMAPHORES = ["cV", "cS", "cP", "cG", "sent", "gin"] + ["d%d" % i for i in range(NDMA)] + ["r%d" % i for i in range(14)]
+SEMAPHORES = ["cV", "cS", "cP", "cG", "sent", "gin"] + ["d%d" % i for i in range(NDMA)] + ["r%d" % i for i in range(20)]
 
-COSTS = ((0.83e-3, 0.5e-3, 1.35, 3.8, 0.14, 0.8, 2.0, 64, 0.1, 0.0, 0.0, 1.1),
-         (0.85e-3, 0.6e-3, 1.15, 1.8, 0.1, 1.4, 2.8, 64, 0.05, -0.015, -0.015, 1.25),
-         (1.0e-3, 0.55e-3, 1.7, 5.0, 0.17, 1.5, 3.0, 64, 0.1, -0.015, -0.015, 1.1))
-LOOK, BETA = 0.15, 15.0
+COSTS = ((0.87e-3, 0.5e-3, 1.45, 3.8, 0.17, 1.0, 2.6, 64, 0.1, 0.0, 0.0, 1.1, 1.2, 3.0, 260e3, 0.002),
+         (0.85e-3, 0.55e-3, 1.15, 1.8, 0.1, 1.4, 2.8, 64, 0.05, -0.015, -0.015, 1.25, 1.4, 5.0, 200e3, 0.001),
+         (1.0e-3, 0.55e-3, 1.7, 5.0, 0.17, 1.5, 3.0, 64, 0.1, -0.015, -0.015, 1.1, 1.4, 5.0, 300e3, 0.003),
+         (1.2e-3, 0.62e-3, 1.9, 4.0, 0.2, 1.0, 2.5, 64, 0.1, 0.0, -0.015, 1.0, 1.0, 4.0, 200e3, 0.001),
+         (1.08e-3, 0.62e-3, 1.2, 3.0, 0.1, 0.8, 2.0, 64, 0.1, 0.02, 0.0, 1.0, 1.8, 2.0, 350e3, 0.002),
+         (0.83e-3, 0.45e-3, 1.3, 3.0, 0.25, 1.2, 3.5, 64, 0.1, 0.0, 0.0, 1.0, 1.0, 4.0, 180e3, 0.003))
+SHARE = (2.0, 1.5, 1.0, 0.5, 1.0, 1.5)
+INORDER = ""
+LOOK, BETA = 0.15, 10.0
 WAKE = COSTS[0][4]
-GAMMA = 1.0
+GAMMA = 1.5
 NX = 0.0
 OWN = 1.4
-LOADS = ("prg00", "prg10", "teamI0", "dq00", "dq10", "dq20", "prg20", "prg30", "dq01", "dq11", "dq21", "prg01", "prg11",
-         "prg21", "prg31", "teamI1", "ef10a", "ef10b", "ef11a", "ef11b")
+PRG, NTM = (4, 2, 1, 1), 2
+LOADS = ("prg0", "prg1", "dq0", "dq1", "dq2", "teamI0", "teamI1", "prg2", "prg3", "goal0", "ef1")
 F32 = (4, 0.0)
 BUNDLE = 512
-BW = 200000.0
 
 
 def build_ops(g, T, topo, core, rank, cost):
@@ -85,8 +97,11 @@ def build_ops(g, T, topo, core, rank, cost):
     N = len(T.cores)
     V, S, P = g.vector, g.scalar, g.tensor
 
+    tag = [(-1, -1)]
+
     def add(eng, dur, fn, r, w, kind="c", lat=0.0, extra=None):
-        ops.append({"e": eng, "d": dur, "f": fn, "r": list(r), "w": list(w), "k": kind, "lat": lat, "x": extra})
+        ops.append({"e": eng, "d": dur, "f": fn, "r": list(r), "w": list(w), "k": kind, "lat": lat, "x": extra,
+                    "tag": tag[0]})
 
     def cyc(n):
         return max(64, n) * CY
@@ -133,9 +148,10 @@ def build_ops(g, T, topo, core, rank, cost):
         add("P", max(min(cost[7], wd(l)), wd(rh)) * (F32[0] if f32 else 1) * PEC + F32[1],
             lambda: P.matmul(out, l, rh, st, sp), r, w, lat=cost[8], extra=n)
 
-    def dma(q, out, a, nbytes, r, w):
+    def dma(q, out, a, nbytes, r, w, rows=128):
         qq = {"Y": g.sync, "S": g.scalar, "G": g}[q]
-        add(q, 0.1, lambda: qq.dma_start(out, a), r, w, kind="dma", lat=nbytes)
+        add(q, cost[5] if q == "G" else 0.1, lambda: qq.dma_start(out, a), r, w, kind="dma",
+            lat=nbytes / cost[14] + rows * cost[15])
 
     def iota(out, pat, base, cm, w, flt=True):
         if flt:
@@ -166,35 +182,34 @@ def build_ops(g, T, topo, core, rank, cost):
     CPY, IDN, ABS, RELU = ACT.Copy, ACT.Identity, ACT.Abs, ACT.Relu
     Y, ci, cf = T.Y, T.ci, T.cf
 
-    def loads(s):
-        H = str(s)
-        R = slice(64 * s, 64 * s + 64)
-        q = "S" if s == 0 else "Y"
-        HV = [(h, slice(64 * h, 64 * h + 64), H + "ab"[h]) for h in range(2)]
-        for h, D, t in HV:
-            dma(q, T.xb[D, 128 * s:128 * s + 128], T.x0[R, 128 * h:128 * h + 128], 16384, [], ["xb" + t])
-            dma(q, T.wtI[D, 4 * s:4 * s + 1], T.wt[R, :], 4096, [], ["wtI" + t])
-            dma(q, T.stI[D, 8 * s:8 * s + 8], T.start[R, 8 * h:8 * h + 8], 4096, [], ["stI" + t])
-        prg = T["prg" + H]
-        for c in range(4):
-            C = slice(1024 * c, 1024 * c + 1024)
-            dma("Y", prg[0:64, C], T.prog[R, C], 131072, [], ["prg%d%s" % (c, H)])
-        dma("Y", T["teamI" + H][0:64, :], T.team[R, :], 262144, [], ["teamI" + H])
-        for j in range(3):
-            dma("Y", prg[64 + 4 * j:68 + 4 * j, :], T.dgb[R, 256 * j:256 * j + 256], 32768, ["dgb%d_" % j], ["dq%d%s" % (j, H)])
-
+    W, ef = T.W, T.ef
+    TE = TC + 1024
     dma("S", T.actI[:], T.act[:], 131072, [], ["actI"])
+    dma("S", T.xb[:], T.x0[:], 65536, [], ["xb"])
+    dma("S", T.wtI[:, 0:1], T.wt[:], 8192, [], ["wtI"])
+    dma("S", T.stI[:], T.start[:], 8192, [], ["stI"])
+    a, PT = 0, []
+    for c, w in enumerate(PRG):
+        C = slice(512 * a, 512 * (a + w))
+        dma("Y", T.prg[:, C], T.prog[:, C], 131072 * w, [], ["prg%d" % c])
+        PT += ["prg%d" % c] * w
+        a += w
+    for h in range(NTM):
+        C = slice(1024 // NTM * h, 1024 // NTM * (h + 1))
+        dma("Y", T.teamI[:, C], T.team[:, C], 524288 // NTM, [], ["teamI%d" % h])
+    for h in range(2):
+        C = slice(512 * h, 512 * h + 512)
+        cp(W[:, TC + 512 * h:TC + 512 * h + 512], T.teamI[:, C], ["teamI%d" % (h * (NTM - 1))], ["Wt%d" % h])
+    dma("Y", ef[:, 16:1040], T.eff[:], 262144, [], ["ef1"])
+    dma("Y", T.goals[:, 0:256], T.goal[:], 65536, [], ["goal0"])
     for j in (1, 2):
         C = slice(256 * j, 256 * j + 256)
         ts(T.dg[:, C], T.actI[:], -512.0, 1.0 / 15 ** j, ADD, MUL, ["actI"], ["dg%d_" % j])
         cp(T.dgb[:, C], T.dg[:, C], ["dg%d_" % j], ["dgb%d_" % j])
     ts(T.dg[:, 0:256], T.dg[:, 256:512], -15.0, -512.0, MUL, ADD, ["dg1_"], ["dg0_"])
     tt(T.dgb[:, 0:256], T.dg[:, 0:256], T.actI[:], ADD, ["dg0_", "actI"], ["dgb0_"])
-
-    for s in range(2):
-        for h in range(2):
-            dma("G", T.goals[64 * h:64 * h + 64, 128 * s:128 * s + 128], T.goal[64 * s:64 * s + 64, 128 * h:128 * h + 128],
-                16384, [], ["goal0%d%s" % (s, "ab"[h])])
+    for j in range(3):
+        dma("Y", T.dq[8 * j:8 * j + 8, :], T.dgb[:, 256 * j:256 * j + 256], 65536, ["dgb%d_" % j], ["dq%d" % j])
 
     def send_goals():
         tr = []
@@ -207,7 +222,7 @@ def build_ops(g, T, topo, core, rank, cost):
         return g.remote_dma_fused(tr, local_sem=T.sem.sent)
     GM3 = (None, (0, 2), (2, 4), (3, 4))
     ngo = sum(split_mask(T.cores[(rank + v) % N], *GM3[v])[1] for v in range(1, NV))
-    add("G", 1.5, send_goals, ["goal00a", "goal00b", "goal01a", "goal01b"], ["goalx"], kind="rem", lat=2.5, extra=("gin", ngo))
+    add("G", cost[13], send_goals, ["goal0"], ["goalx"], kind="rem", lat=2.5, extra=("gin", ngo))
 
     iota(ci[:, 0:1], [[0, 1]], 0, 1, ["ci0"], False)
     iota(T.E[:, 0:128], [[1, 8], [0, 16]], 0, 0, ["E0"])
@@ -224,31 +239,29 @@ def build_ops(g, T, topo, core, rank, cost):
     def pick(out, pat, base, val, w):
         iota(out, [[0, wd(out)]], val, 0, w)
         add("G", 0.17 + 2 * wd(out) * CY, lambda: g.affine_select(out, out, pat, EQ, 0.0, base, 1), w, w)
-    pick(T.SB[:], [[0, 2], [-1, 64]], 0, 1, ["SB"])
-    add("G", 0.17 + 256 * CY, lambda: g.affine_select(T.SB[:], T.SB[:], [[0, 2], [-1, 4], [-4, 16]], ALU.not_equal,
-                                                      1.0 / 16.0, -64, 1), ["SB"], ["SB"])
-    add("G", 0.17 + 16 * CY, lambda: g.affine_select(T.SB[:, 1:128:16], T.SB[:, 1:128:16], [[0, 2], [-1, 4]], ALU.not_equal,
-                                                     -15.0 / 16.0, -72, 1), ["SB"], ["SB"])
+    iota(T.SB[0:32, :], [[0, 128]], 0, 0, ["SB"])
+    add("G", 0.17 + 256 * CY, lambda: g.affine_select(T.SB[0:32, :], T.SB[0:32, :], [[-1, 8], [-8, 16]], ALU.not_equal,
+                                                      2.0 ** 19, 0, 1), ["SB"], ["SB"])
+    add("G", 0.17 + 16 * CY, lambda: g.affine_select(T.SB[0:32, 1:128:16], T.SB[0:32, 1:128:16], [[-1, 8]], ALU.not_equal,
+                                                     -15.0 * 2.0 ** 19, -16, 1), ["SB"], ["SB"])
     for j in range(3):
-        pick(T.DWf[0:64, 128 * j:128 * j + 128], [[0, 2], [-1, 64]], 0, DW[j], ["DWf%d_" % j])
-        pick(T.DWb[0:64, 128 * j:128 * j + 128], [[0, 2], [-1, 64]], 0, -DW[j], ["DWb%d_" % j])
-    pick(T.PA[:], [[0, 2], [-1, 64]], 0, 1, ["PA"])
-    pick(T.PB[:], [[0, 2], [-1, 64]], -64, 1, ["PB"])
+        pick(T.DWf[:, 128 * j:128 * j + 128], [[-1, 128]], 0, DW[j], ["DWf%d_" % j])
+        pick(T.DWb[:, 128 * j:128 * j + 128], [[-1, 128]], 0, -DW[j], ["DWb%d_" % j])
     nI24, nI15, c1, c2 = T.nI[:, 0:128], T.nI[:, 128:256], T.c12[:, 0:128], T.c12[:, 128:256]
     act(nI24, T.idn[:], CPY, ["idn"], ["nI24"], scale=-16777216.0)
-    tt(T.blk2[:, 0:64], T.blk[:, 0:64], T.blk[:, 64:128], ADD, ["blk"], ["blk2a"])
-    act(T.blk2[:, 64:128], T.blk2[:, 0:64], CPY, ["blk2a"], ["blk2b"])
-    act(T.blkE[:], T.blk[:], CPY, ["blk"], ["blkE"], scale=256.0)
-    act(T.Jm[:], T.io3[:], CPY, ["io3", "idn"], ["Jm"], scale=T.idn[:, 0:1])
-    act(T.blk8[:], T.blk[:, 0:128:16], CPY, ["blk"], ["blk8"])
+    ts(T.Jm[:], T.io3[:], T.idn[:, 0:1], 1.0 / 256.0, MUL, MUL, ["io3", "idn"], ["Jm"])
+    act(T.nI12[:], T.idn[:], CPY, ["idn"], ["nI12"], scale=-4096.0)
+    blk8, blk8k = T.blk8[:, 0:8], T.blk8[:, 8:16]
+    act(blk8, T.blk[:, 0:128:16], CPY, ["blk"], ["blk8"])
+    act(blk8k, blk8, CPY, ["blk8"], ["blk8k"], scale=2048.0)
     act(T.nI512[:], T.idn[:], CPY, ["idn"], ["nI512"], scale=-512.0)
     act(nI15, T.idn[:], CPY, ["idn"], ["nI15"], scale=-32768.0)
     ts(T.rst[:], T.io2[:], 0.5, None, ALU.is_gt, None, ["io2"], ["rst"])
     ms(c1, -255.0 / 128.0, ["c1"], 0.5)
     ms(c2, 1.5 * 2.0 ** 25, ["c2"], 0.5)
     kb, wq, pure, kd, kr, z2 = [cf[:, j:j + 1] for j in (5, 2, 3, 6, 7, 9)]
-    bq = T.m8[:, 16:17]
-    ts(kb, rc, -2048.0, 32767.0 + 241.0 * 32768.0 - OFS, MUL, ADD, ["cf"], ["kb"])
+    bq = T.m8[:, 0:1]
+    ts(kb, rc, -2048.0, 2.0 ** 23 + 32767.0 + 241.0 * 32768.0 - OFS, MUL, ADD, ["cf"], ["kb"])
     act(T.nI23[:], T.idn[:], CPY, ["idn"], ["nI23"], scale=-8388608.0)
     act(T.pI23[:], T.idn[:], CPY, ["idn"], ["pI23"], scale=8388608.0)
     m = T.msk
@@ -260,48 +273,68 @@ def build_ops(g, T, topo, core, rank, cost):
     ts(wq, cf[:, 11:12], 16.0, None, MUL, None, ["k11"], ["wq"])
     tt(kd, pure, wq, SUB, ["pure", "wq"], ["kd"])
     ts(kr, pure, -2.0, wq, MUL, ADD, ["pure", "wq"], ["kr"])
-    WG, WX, WR = T.Wy[:, 0:56], T.Wy[:, 56:112], T.Wy[:, 112:168]
+    WG, WR, WGs, WRs = [T.Wy[:, 56 * j:56 * j + 56] for j in range(4)]
     ms(T.Wy[:, 8:32], 0.0, ["Wy1"], 0.5)
-    act(T.Wy[:, 0:8], T.blk8[:], CPY, ["blk8", "kd"], ["Wy0"], scale=kd)
-    act(T.Wy[:, 112:120], T.blk8[:], CPY, ["blk8", "kr"], ["Wr0"], scale=kr)
+    act(T.Wy[:, 0:8], blk8, CPY, ["blk8", "kd"], ["Wy0"], scale=kd)
+    act(T.Wy[:, 56:64], blk8, CPY, ["blk8", "kr"], ["Wr0"], scale=kr)
     for j in range(3):
-        act(T.Wy[:, 32 + 8 * j:40 + 8 * j], T.blk8[:], CPY, ["blk8", "wq"], ["Wy%d" % (2 + j)], scale=wq)
-        act(T.Wy[:, 120 + 8 * j:128 + 8 * j], T.blk8[:], CPY, ["blk8", "msk"], ["Wr%d" % (1 + j)], scale=m[:, j:j + 1])
+        act(T.Wy[:, 32 + 8 * j:40 + 8 * j], blk8, CPY, ["blk8", "wq"], ["Wy%d" % (2 + j)], scale=wq)
+        act(T.Wy[:, 64 + 8 * j:72 + 8 * j], blk8, CPY, ["blk8", "msk"], ["Wr%d" % (1 + j)], scale=m[:, j:j + 1])
     WGt = ["Wy%d" % j for j in range(5)]
-    act(WX, WG, CPY, WGt, ["Wx_"], scale=-1.0)
-    act(T.Wy[:, 144:168], T.Wy[:, 32:56], CPY, WGt, ["Wr4"], scale=-1.0)
+    act(T.Wy[:, 88:112], T.Wy[:, 32:56], CPY, WGt, ["Wr4"], scale=-1.0)
     WRt = ["Wr%d" % j for j in range(5)]
+    cp(T.Wy[:, 120:168], T.Wy[:, 8:56], WGt, ["Wsa"], 0.5)
+    cp(T.Wy[:, 112:120], T.Wy[:, 88:96], WRt, ["Wsb"], 0.5)
+    cp(T.Wy[:, 176:224], T.Wy[:, 64:112], WRt, ["Wsc"], 0.5)
+    ts(T.Wy[:, 168:176], T.Wy[:, 0:8], -1.0, None, MUL, None, WGt, ["Wsd"], 0.5)
+    nIx = T.nI[:, 256:384]
+    ts(cf[:, 19:20], pure, -256.0, None, MUL, None, ["pure"], ["k19"])
+    act(nIx, T.idn[:], CPY, ["idn", "k19"], ["nIx"], scale=cf[:, 19:20])
     act(T.blkB[:, 0:128], T.blk[:], CPY, ["blk"], ["blkB"])
-    for j in range(4):
-        cp(T.blkB[:, 128 + 8 * j:136 + 8 * j], T.blk8[:], ["blk8"], ["blkC%d_" % j])
-    BC = ["blkC%d_" % j for j in range(4)]
+    for j in range(5):
+        ts(T.blkB[:, 128 + 8 * j:136 + 8 * j], blk8, 2.0 ** 20, None, MUL, None, ["blk8"], ["blkC%d_" % j])
+    BC = ["blkC%d_" % j for j in range(5)]
+    ts(T.blkB[:, 168:208], T.blkB[:, 128:168], -1.0, None, MUL, None, BC, ["blkD"], 0.5)
     ms(T.ones[:], 1.0, ["ones"], 0.5)
-    ms(T.m8[:, 0:8], PC / 128.0, ["m8a"], 0.5)
-    ms(T.m8[:, 8:16], PL / 128.0, ["m8b"], 0.5)
     ts(T.Z[:, 128:144], T.io3[:, 0:16], -1.0, 15.0, MUL, ADD, ["io3"], ["Z1"])
-    ts(T.OH[:, 0:16], T.Z[:, 128:144], rc, None, EQ, None, ["Z1", "cf"], ["OHa"])
+    iota(T.OH[:, 24:56:2], [[0, 16]], 0, 0, ["OHo"])
+    ts(T.OH[:, 25:56:2], T.Z[:, 128:144], rc, None, EQ, None, ["Z1", "cf"], ["OHp"])
+    cp(T.OH[:, 0:15], T.OH[:, 27:56:2], ["OHp"], ["OHq"])
+    cp(T.OH[:, 15:16], T.OH[:, 25:26], ["OHp", "OHq"], ["OHa"])
     ts(T.OH[:, 16:17], z2, 4096.0, None, MUL, None, ["z2"], ["OHb"])
     cp(T.OH[:, 17:18], m[:, 3:4], ["msk"], ["OHc"])
     act(T.KP[:, 0:16], T.OH[:, 0:16], IDN, ["OHa"], ["KPa"], bias=1.0, scale=12.0)
     ts(T.KP[:, 16:18], T.io3[:, 0:2], -1.0, 1.0, MUL, ADD, ["io3"], ["KPb"])
-    act(T.Pq[:, 0:128], T.PB[:], CPY, ["PB"], ["Pq0"], scale=-4096.0)
-    act(T.Pq[:, 128:256], T.PA[:], CPY, ["PA"], ["Pq1"], scale=-4096.0)
-    cp(T.l1[:], T.io3[:, 0:8], ["io3"], ["l1"])
-    cj, cdum, ctop, cnb, cdum2, ctop2 = [T.cs[:, 8 * j:8 * j + 8] for j in range(6)]
-    ts(cj, T.io3[:, 0:8], 16.0, rc, MUL, ADD, ["io3", "cf"], ["cj"])
-    act(cdum, cj, IDN, ["cj"], ["cdum"], bias=float(DC))
-    act(ctop, cj, IDN, ["cj"], ["ctop"], bias=DT - NEAR)
-    act(cdum2, cj, IDN, ["cj"], ["cdum2"], bias=float(DC2))
-    act(ctop2, cj, IDN, ["cj"], ["ctop2"], bias=DT2 - NEAR)
-    act(cnb, cj, IDN, ["cj"], ["cnb"], bias=-64.0 * 32768.0, scale=32768.0)
+    l1, ends = T.l1[:, 0:8], T.l1[:, 8:9]
+    cp(l1, T.io3[:, 0:8], ["io3"], ["l1"])
+    cj16, cj, cbot, cnb = T.cs[:, 0:16], T.cs[:, 0:8], T.cs[:, 16:32], T.cs[:, 32:40]
+    ts(cj16, T.io3[:, 0:16], 16.0, rc, MUL, ADD, ["io3", "cf"], ["cj"])
+    cbot2 = T.cs[:, 40:56]
+    act(cbot, cj16, IDN, ["cj"], ["cbot"], bias=NEAR - DT * EPS, scale=-EPS)
+    act(cbot2, cj16, IDN, ["cj"], ["cbot2"], bias=NEAR - DT2 * EPS, scale=-EPS)
+    act(cnb, cj, IDN, ["cj"], ["cnb"], bias=0.25, scale=-1.0 / 256.0)
+    if any(EARLY):
+        ts(T.Jn[:], T.ones[:], T.idn[:, 0:1], -15.0 * 16384.0, MUL, MUL, ["idn", "ones"], ["Jn"])
+        act(T.mof[:], T.msk[:], IDN, ["msk"], ["mof"], bias=16384.0, scale=-16384.0)
+    iota(T.rs2[:], [[0, 576]], 0, 0, ["rs2"])
+    for c in range(8):
+        iota(T.rs2[:, 8 * c * (c + 1):8 * c * (c + 1) + 1], [[0, 1]], 2 ** 23, 0, ["rs2"])
     ts(ci[:, 12:13], ci[:, 0:1], 7, None, AND, None, ["ci0"], ["ci12"])
     ts(ci[:, 13:14], ci[:, 0:1], 3, 1, SHR, AND, ["ci0"], ["ci13"])
-    cp(cf[:, 16:17], ci[:, 13:14], ["ci13"], ["k16"])
+    ts(cf[:, 16:17], ci[:, 13:14], 2.0, None, MUL, None, ["ci13"], ["k16"])
     ts(cf[:, 17:18], ci[:, 12:13], 16.0, cf[:, 16:17], MUL, ADD, ["ci12", "k16"], ["k17"])
-    ts(T.lp[:], T.io3[:, 0:8], 2.0, cf[:, 17:18], MUL, ADD, ["io3", "k17"], ["lp"])
+    iota(T.cs[:, 56:64], [[1, 2], [4, 4]], 0, 0, ["lq"])
+    ts(T.lp[:], T.cs[:, 56:64], cf[:, 17:18], None, ADD, None, ["lq", "k17"], ["lp"])
     cp(cf[:, 18:19], ci[:, 12:13], ["ci12"], ["k18"])
-    ts(T.SelY[0:16, :], T.E[0:16, 0:128], cf[0:16, 18:19], None, EQ, None, ["E0", "k18"], ["SelY"], 0.5)
-    ms(T.An[:], -1032.0, ["An0", "An1", "A70", "A71"])
+    ts(T.SelY[0:16, 0:128], T.E[0:16, 0:128], cf[0:16, 18:19], None, EQ, None, ["E0", "k18"], ["SelY"], 0.5)
+    ts(cf[:, 21:22], pc, -16.0, None, ADD, None, ["cf"], ["k21"])
+    ts(T.SelY[0:24, 128:256], T.E[0:24, 0:128], cf[0:24, 21:22], -2.0 ** 24, EQ, MUL, ["E0", "k21"], ["SelN"])
+    act(cf[:, 20:21], cf[:, 18:19], ACT.Square, ["k18"], ["k20"], bias=1.5)
+    ts(ends, cf[:, 20:21], 8.0, -3.0, MUL, ADD, ["k20"], ["ends"])
+    ms(T.An[:], 0.0, ["An"])
+    iota(T.I3[:], [[0, 240]], 0, 0, ["I30", "I31"], False)
+    for s in range(2):
+        iota(T.I3[:, 24 * s:24 * s + 8, 1], [[0, 8]], 2 ** 22, 0, ["I3%d" % s], False)
     yi, yf = [T.mK[:, 64 * j:64 * j + 64] for j in range(4)], [T.NW[:, 64 * j:64 * j + 64] for j in range(5)]
     ts(yi[0], T.eM[:, 0:64], 1023, None, AND, None, ["eM0"], ["yi0"])
     for j in (1, 2):
@@ -311,15 +344,32 @@ def build_ops(g, T, topo, core, rank, cost):
     ts(yf[4], yi[2], -15.0, None, MUL, None, ["yi2"], ["yf4"])
     tt(yf[1], yi[1], yf[4], ADD, ["yi1", "yf4"], ["yf1"])
     cp(yf[2], yi[2], ["yi2"], ["yf2"])
-    cp(yf[3], yi[0], ["yi0", "yf0", "yf1", "yf2"], ["NW0", "NW1", "mK0", "mK1"])
-    iota(Y[:, 128:1152], [[0, 1024]], 0, 0, ["Yf"])
+    cp(yf[3], yi[0], ["yi0", "yf0", "yf1", "yf2"], ["NW0", "NW1", "NWr", "mK0", "mK1"])
+    iota(Y[:, 256:YW], [[0, YW - 256]], 0, 0, ["Yf"])
     for j in range(4):
-        dma("Y", Y[j:128:16, 128:1152], yf[j], 32768, ["Yf", "NW0"], ["Y%d" % j])
-    YT = ["Yf", "Y0", "Y1", "Y2", "Y3"]
+        dma("Y", Y[j:128:16, YT0:YW], yf[j], 32768, ["Yf", "NW0", "NW1"], ["Y%d_" % j])
+    YT = ["Yf", "Y0_", "Y1_", "Y2_", "Y3_"]
 
-    def k_to_l(out, Wb, src, first, lastf, r, w):
-        for rr in range(16):
-            mm(out, Wb[:, 15 - rr:143 - rr], src(rr), first and rr == 0, lastf and rr == 15, r, w)
+    PAY = ["W%d_" % c for c in range(8)]
+    TEAM = ["Wt0", "Wt1", "Wz", "Wx"]
+    WALL = PAY + TEAM + ["Wv"]
+    FILL = ["Wfa", "Wfb", "Wfc", "Wfd"]
+    iota(W[:, 0:TC], [[0, TC]], 0, 0, ["Wz"])
+    iota(W[:, TE:PC], [[0, PC - TE]], 0, 0, ["Wx"])
+    iota(W[:, DC:PL], [[0, PL - DC]], 0, 0, ["Wv"])
+    for j, t in enumerate(FILL):
+        iota(W[:, PL + 1056 * j:PL + 1056 * j + 1056], [[0, 1056]], 0, 0, [t])
+    iota(ef[:, 0:16], [[0, 16]], 0, 0, ["ef0"])
+    ts(cf[:, 12:13], T.wtI[:, 0:1], 2.0, None, MUL, None, ["wtI"], ["wf"])
+    act(T.We[:], T.blk[:], CPY, ["blk", "wf"], ["We"], scale=cf[:, 12:13])
+    for c in range(8):
+        bn, C = TB[c], slice(512 * c, 512 * c + 512)
+        mm(T[bn][:], T.pI23[:], T.prg[:, C], True, False, ["pI23", PT[c]], [bn])
+        mm(T[bn][:], T.SB[0:24, :], T.dq[0:24, C], False, True, ["SB", "dq0", "dq1", "dq2"], [bn])
+        if PV[c] == "V":
+            ts(W[:, PC + 512 * c:PC + 512 * c + 512], T[bn][:], 2.0 ** -23, None, MUL, None, [bn], [PAY[c]])
+        else:
+            act(W[:, PC + 512 * c:PC + 512 * c + 512], T[bn][:], CPY, [bn], [PAY[c]], scale=2.0 ** -23)
 
     nxt = T.cores[(rank + 1) % N]
     nrid, npid, nse = topo.addr(nxt)
@@ -334,103 +384,97 @@ def build_ops(g, T, topo, core, rank, cost):
 
     def stream(s):
         H = str(s)
-        loads(s)
+        hb = 1 - s
+        tag[0] = (s, -1)
 
         def k(*names):
             return [n + H for n in names]
-
-        def ab(*names):
-            return [n + H + x for n in names for x in "ab"]
-        W, prg, ef, Gm, Gp, xr = T["W" + H], T["prg" + H], T["ef" + H], T["Gm" + H], T["Gp" + H], T["xr" + H]
+        Gm, Gp, xr = T["Gm" + H], T["Gp" + H], T["xr" + H]
         pK, pT, pU, pE = T["pK" + H], T["pT" + H], T["pU" + H], T["pE" + H]
         K = slice(128 * s, 128 * s + 128)
         L = slice(8 * s, 8 * s + 8)
         c4 = slice(4 * s, 4 * s + 1)
-        PAY = k(*["W%d_" % c for c in range(8)])
-        WALL = PAY + k("Wt", "Wu", "Wz", "Wx")
-        FILL = k("Wfa", "Wfb", "Wfc", "Wfd")
-        XB = ab("xb")
+        XB = ["xb"]
         NK = k("NK")
-        xb = T.xb[:, K]
+        xb = T.xb[:, 128 * hb:128 * hb + 128]
         bank = {"pK": pK, "pT": pT, "pU": pU, "pE": pE}
 
         def sl(j):
-            return slice(32 * s + 8 * j, 32 * s + 8 * j + 8)
+            return slice(40 * s + 8 * j, 40 * s + 8 * j + 8)
 
-        iota(W[:, 0:TC], [[0, TC]], 0, 0, k("Wz"))
-        iota(W[:, DC:PL], [[0, PL - DC]], 0, 0, k("Wx"))
-        for j, t in enumerate(FILL):
-            iota(W[:, PL + 1088 * j:PL + 1088 * j + 1088], [[0, 1088]], 0, 0, [t])
-        iota(ef[:, 0:16], [[0, 16]], 0, 0, k("ef0"))
-        cp(W[0:64, TC:PC], T["teamI" + H][0:64, :], k("teamI"), k("Wt"))
-        move(PV[s][8], W[64:128, TC:PC], W[0:64, TC:PC], k("Wt"), k("Wu"))
-        for h in range(2):
-            dma("Y", ef[64 * h:64 * h + 64, 16:1040], T.eff[64 * s:64 * s + 64, :], 131072, [], ["ef1" + H + "ab"[h]])
-        ts(cf[:, 12 + s:13 + s], T.wtI[:, c4], 2.0, None, MUL, None, ab("wtI"), k("wf"))
-        act(T.We[:, K], T.blk[:], CPY, ["blk"] + k("wf"), k("We"), scale=cf[:, 12 + s:13 + s])
-        D, X = slice(0, 32), slice(32 * s, 32 * s + 32)
-        ts(T.P0[:, sl(1)], cj, 1024.0 * s, None, ADD, None, ["cj"], k("P0b"))
-        ms(T.P0[:, sl(3)], 512, k("P0d"))
+        D, X = slice(0, 40), slice(40 * s, 40 * s + 40)
+        cp(T.P0[:, sl(1)], cj, ["cj"], k("P0b"))
+        ms(T.P0[:, 40 * s + 24:40 * s + 40], 0, k("P0d"))
         ms(T.P1[:, sl(2)], 16.0, k("P1c"))
+        ms(T.P1[:, sl(4)], 4096.0, k("P1e"))
+        RAW = pT[:, 64:104]
+        I0 = 24 * s
 
-        def distance(x, xt, goal, gt):
+        def trail(j):
+            return T.I3[:, I0 + 8:I0 + 16, j + 1]
+
+        def distance(x, xt, goal, gt, test, raw):
             mm(pE[:, 0:128], T.nI23[:], goal, True, False, ["nI23"] + gt, k("pE"))
             mm(pE[:, 0:128], T.pI23[:], x, False, True, ["pI23"] + xt, k("pE"))
             act(T.Z2[:, K], pE[:, 0:128], ABS, k("pE"), k("Zb"), scale=1.0 / 8388608.0)
             mm(pE[:, 128:256], T.Z2[:, K], T.blkB[:, 0:128], True, True, ["blkB"] + k("Zb"), k("pE"))
             tt(T.NK[:, K], pE[:, 128:256], T.msk[:], MUL, k("pE") + ["msk"], NK, 1.0)
-            mm(pK[:, D], T.NK[:, K], T.blkB[:, 128:160], True, True, BC + NK, k("pK"))
+            if test:
+                mm(pK[:, D], T.idn[:], test[0], True, False, ["idn"] + test[1], k("pK"), True)
+                mm(pK[:, D], T.pI23[:], T.An[:], False, False, ["pI23", "An"], k("pK"))
+                mm(pK[:, D], T.NK[:, K], T.blkB[:, 168:208], False, True, ["blkD"] + NK, k("pK"))
+            if raw:
+                mm(RAW, T.NK[:, K], T.blkB[:, 128:168], True, True, BC + NK, k("pT"))
 
         def turn(src, j, r):
-            f0 = 48 * s + 16 * j
+            f0, n = 72 * s + 24 * j, 24 if j else 16
             move("V" if j else HI0, T.AF[:, f0:f0 + 8], src, r, k("ah%d" % j))
             tt(T.AF[:, f0 + 8:f0 + 16], src, T.AF[:, f0:f0 + 8], SUB, r + k("ah%d" % j), k("al%d" % j))
-            mm(pT[0:16, 128:256], T.AF[:, f0:f0 + 16], T.pI23[:], True, True, ["pI23"] + k("ah%d" % j, "al%d" % j), k("pT"))
-            act(T.TT[0:16, 24 * s + 8 * j:24 * s + 8 * j + 8, :], pT[0:16, 128:256], CPY, k("pT"), k("TT%d" % j),
+            if j:
+                ts(T.AF[:, f0 + 16:f0 + 24], src, 1024.0, None, LT, None, r, k("ng%d" % j))
+            mm(pT[0:n, 128:256], T.AF[:, f0:f0 + n], T.pI23[:], True, True,
+               ["pI23"] + k("ah%d" % j, "al%d" % j, "ng%d" % j), k("pT"))
+            act(T.TT[0:n, 24 * s + 8 * j:24 * s + 8 * j + 8, :], pT[0:n, 128:256], CPY, k("pT"), k("TT%d" % j),
                 scale=1.0 / 8388608.0)
 
-        def tables():
-            for c in range(8):
-                bn = ("pK", "pT", "pU", "pE")[c % 4]
-                mm(bank[bn][:], T.SB[0:76, :], prg[0:76, 512 * c:512 * c + 512], True, True,
-                   ["SB"] + k("prg%d" % (c // 2), "dq0", "dq1", "dq2"), k(bn))
-                move(PV[s][c], W[:, PC + 512 * c:PC + 512 * c + 512], bank[bn][:], k(bn), [PAY[c]])
-        ts(T.A0[:, L], T.stI[:, L], -1.0, 1023.0, MUL, ADD, ab("stI"), k("A0"))
+        ts(T.A0[:, L], T.stI[:, 8 * hb:8 * hb + 8], -1.0, 2047.0, MUL, ADD, ["stI"], k("A0"))
 
         for v in range(NV):
             last = v == NV - 1
-            if last:
+            tag[0] = (s, v)
+            if last and s == 0:
                 for j in range(3):
-                    C = slice(768 * s + 256 * j, 768 * s + 256 * j + 256)
-                    dma("Y", T.Pc[0:64, C], T.prog[64 * s + j:64 * s + 64:16, :], 32768, k("Wfa"), k("Pc%d_" % j))
-                    dma("Y", T.Vc[0:64, C], W[j:64:16, PC:DC], 65536, PAY, k("Vc%d_" % j))
+                    C = slice(256 * j, 256 * j + 256)
+                    dma("Y", T.Pc[:, C], T.prog[j:128:16, :], 65536, ["Wfa"], ["Pc%d_" % j])
+                    dma("G", T.Vc[:, C], W[j:128:16, PC:DC], 65536, PAY, ["Vc%d_" % j])
+            if last:
                 ms(T.P1[:, sl(2)], 17.0, k("P1c"))
             if v > 0:
                 b0 = 48 * (2 * (v - 1) + s)
-                x0 = 256 * (v - 1) + 128 * s
+                x0 = 256 * (v - 1) + 128 * hb
                 xb, XB = T.landb[:, x0:x0 + 128], k("landb%d" % (v - 1))
                 A0, a0t = T.land[:, b0:b0 + 8], k("land%d" % (v - 1))
-                ts(T.off[:, L], A0, -1.0, 1023.0, MUL, ADD, a0t, k("offa"))
-                bar = (T.land[:, b0 + 8:b0 + 40], k("land%d" % (v - 1), "A7"))
+                bar = (T.land[:, b0 + 8:b0 + 48], k("far%d" % (v - 1)))
             else:
+                bar = (T.thr[:, X], k("thr"))
                 A0, a0t = T.A0[:, L], k("A0")
-                cp(T.off[:, L], T.stI[:, L], ab("stI"), k("offa"))
-            act(T.A0p[:, L], A0, IDN, a0t, k("A0p"), bias=1024.0)
-            turn(T.A0p[:, L], 0, k("A0p"))
+            ts(T.off[:, L], A0, -1.0, 2048.0, MUL, ADD, a0t, k("offa"))
+            cp(trail(0), A0, a0t + k("I3"), k("a0"))
+            turn(A0, 0, a0t)
             uu, ut = T.cK[:, K], k("uK")
             e1, e2 = pE[:, 128:256], pE[:, 256:384]
             if EV[min(v, 1)]:
-                mm(e1, T.We[:, K], xb, True, True, k("We") + XB, k("pE"))
+                mm(e1, T.We[:], xb, True, True, ["We"] + XB, k("pE"))
                 cp(T.eI[:, K], e1, k("pE"), k("eI"))
                 ts(T.eM[:, K], T.eI[:, K], 511, None, AND, None, k("eI"), k("eM"))
                 ts(uu, T.eM[:, K], 33.0, None, ADD, None, k("eM"), ut)
             else:
                 mm(e1, c1, T.ones[:], True, False, ["c1", "ones"], k("pE"))
-                mm(e1, T.We[:, K], xb, False, True, k("We") + XB, k("pE"))
+                mm(e1, T.We[:], xb, False, True, ["We"] + XB, k("pE"))
                 act(T.hE[:, K], e1, IDN, k("pE"), k("hE"), bias=1.5 * 2.0 ** 23, scale=1.0 / 512.0)
                 mm(e2, T.nI512[:], T.hE[:, K], True, False, ["nI512"] + k("hE"), k("pE"), True)
                 mm(e2, c2, T.ones[:], False, False, ["c2", "ones"], k("pE"))
-                mm(e2, T.We[:, K], xb, False, True, k("We") + XB, k("pE"))
+                mm(e2, T.We[:], xb, False, True, ["We"] + XB, k("pE"))
                 act(uu, e2, IDN, k("pE"), ut, bias=33.0)
             first, who, parts = XE[s] if v == 0 else XE[2]
             out, ot = T.xp[:, K], k("xp")
@@ -439,27 +483,26 @@ def build_ops(g, T, topo, core, rank, cost):
                     XB + ["lp"], ot)
             else:
                 sga(out, xb, T.lp[:], XB + ["lp"], ot)
-            XJ = [k(*["xj%d%s_" % (j, hf) for j in range(4)]) for hf in "ab"]
+            XJ = k(*["xj%d_" % j for j in range(4)])
             c0, X4 = 256 + 512 * s, k(*["xq%d_" % j for j in range(4)])
             for j, e in enumerate(who):
                 move(e, T.xp[:, c0 + j:c0 + 512:4], T.xp[:, K], k("xp"), [X4[j]], 0.5)
             for j, e in enumerate(parts):
-                if len(e) == 1:
-                    move(e, xr[:, j:2048:4], T.xp[:, c0:c0 + 512], X4, [XJ[0][j], XJ[1][j]], 0.5)
-                else:
-                    for hf in range(2):
-                        move(e[hf], xr[:, 1024 * hf + j:1024 * hf + 1024:4], T.xp[:, c0 + 256 * hf:c0 + 256 * hf + 256],
-                             X4, [XJ[hf][j]], 0.5)
-            act(Y[:, 1152 * s:1152 * s + 128], uu, IDN, ut, k("Ye"), bias=-1599.5, scale=48.5)
-            if v == 0:
-                tables()
+                w = 8 + max(EXTRA[s])
+                move(e, xr[:, j:128 * w:4], T.xp[:, c0:c0 + 32 * w], X4, [XJ[j]], 0.5)
+            for r in range(8):
+                o = 96 * (r // 4)
+                mm(pU[0:8, o + r % 4:o + 96:4], T.xp[:, 128 * s + 64 + 8 * r:128 * s + 72 + 8 * r], T.Wy[:, 64:88],
+                   r == 0, r == 7, WRt + k("xp"), k("pU"))
+            act(T.TX[0:8, 192 * s:192 * s + 192], pU[0:8, 0:192], CPY, k("pU"), k("TX"), scale=-1.0)
+            act(Y[:, 128 * hb:128 * hb + 128], uu, IDN, ut, k("Ye"), bias=-1599.5, scale=48.5)
 
             for st in range(3):
                 nt = st + 1
                 of = T.off[:, 16 * st + 8 * s:16 * st + 8 * s + 8]
                 oft = k("off" + "abc"[st])
-                gtt(T.mK[:, K], W[:, TC:TC + (2048 if st else 1024)], of, T.cK[:, K], MUL,
-                    oft + k("Wt", "Wu", "uK") + (PAY if st else []), k("mK"))
+                gtt(T.mK[:, K], W[:, 0:2056 if st else PC], of, T.cK[:, K], MUL,
+                    oft + TEAM + k("uK") + (PAY if st else []), k("mK"))
                 nK, nkt = (T.nK[:, 256 + 128 * s:384 + 128 * s], k("nKb")) if st else (T.nK[:, K], k("nKa"))
                 ts(nK, T.mK[:, K], 5, 4095, SHR, AND, k("mK"), nkt)
                 add("V", NX + 0.06 + 128 * GA * CY, lambda nK=nK: V.tensor_copy(T.n16[:, K], nK.indirect(T.lp[:])),
@@ -471,48 +514,47 @@ def build_ops(g, T, topo, core, rank, cost):
 
                 def lst(a, w):
                     return T.n16[:, 128 * s + 8 * a:128 * s + 8 * (a + w)]
-                for hf, (vch, cut, sw) in enumerate(HALF):
-                    a = 8 * hf
-                    for w in vch:
-                        gtt(Gm[:, cols(a, w)], W[:, PC:DC], lst(a, w), xr[:, cols(a, w)], SUB, k("n16") + PAY + XJ[hf], GM[a:a + w])
-                        ops[-1]["soft"] = a > 0
-                        a += w
-                for hf, (vch, cut, sw) in enumerate(HALF):
-                    a = 8 * hf + 8 - sw
-                    if sw:
-                        sga(Gm[:, cols(a, sw)], W[:, PC:DC], lst(a, sw), k("n16") + PAY, GM[a:a + sw])
-                        ops[-1]["soft"] = hf > 0 and HALF[0][2] > 0
+                ex = EXTRA[s][st]
+                vch = ([(0, 2), (2, 2)] + [(8, ex)] * (ex > 0), [(4, 2), (6, 2)])
+                sch = ((8 + ex, 4 - ex), (12, 4))
+                for a, w in vch[0] + vch[1]:
+                    gtt(Gm[:, cols(a, w)], W[:, PC:DC], lst(a, w), xr[:, cols(a, w)], SUB, k("n16") + PAY + XJ, GM[a:a + w])
+                    ops[-1]["soft"] = a > 0
+                for a, w in sch:
+                    sga(Gm[:, cols(a, w)], W[:, PC:DC], lst(a, w), k("n16") + PAY, GM[a:a + w])
+                    ops[-1]["soft"] = a == 12
                 nb = 8 * (4 + nt)
-                for hf, (vch, cut, sw) in enumerate(HALF):
-                    a0, a, vw = 8 * hf, 8 * hf + 8 - sw, 8 - sw
-                    bn = ("pU", "pK")[hf]
-                    pY, R = bank[bn], slice(8 * hf, 8 * hf + 8)
-                    if vw and cut == "V":
-                        ts(Gp[:, cols(a0, vw)], Gm[:, cols(a0, vw)], bq, 0.0, ADD, MAX, GM[a0:a] + ["bq"], GP[a0:a], 0.5)
-                    elif vw:
-                        act(Gp[:, cols(a0, vw)], Gm[:, cols(a0, vw)], RELU, GM[a0:a] + ["bq"], GP[a0:a], bias=bq)
-                    if sw:
-                        pS = bank[SUB_[hf]][:, 0:128 * sw]
-                        mm(pS, T.nI23[:], xr[:, cols(a, sw)], True, False, ["nI23"] + XJ[hf], k(SUB_[hf]))
-                        mm(pS, T.pI23[:], Gm[:, cols(a, sw)], False, True, ["pI23"] + GM[a:a + sw], k(SUB_[hf]))
-                        act(Gp[:, cols(a, sw)], pS, RELU, k(SUB_[hf]) + ["bq"], GP[a:a + sw], bias=bq, scale=1.0 / 8388608.0)
-                    jobs = [(xr, WX, a, sw, XJ[hf] + ["Wx_"])]
-                    b = a0
-                    for w in vch:
-                        jobs.append((Gm, WG, b, w, GM[b:b + w] + WGt))
-                        b += w
-                    jobs += [(None, None, 0, 1, None), (Gm, WG, a, sw, GM[a:a + sw] + WGt), (Gp, WR, a0, vw, GP[a0:a] + WRt),
-                             (Gp, WR, a, sw, GP[a:a + sw] + WRt)]
-                    jobs = [job for job in jobs if job[3]]
+                for hf in range(2):
+                    (a, sw), vcut = sch[hf], [(4 * hf, 4)] + vch[hf][2:]
+                    bn, sn = ("pU", "pK")[hf], SUB_[hf]
+                    pY, pS, R = bank[bn], bank[sn], slice(8 * hf, 8 * hf + 8)
+                    for b, w in vcut:
+                        ts(Gp[:, cols(b, w)], Gm[:, cols(b, w)], bq, 0.0, ADD, MAX, GM[b:b + w] + ["bq"], GP[b:b + w], 0.5)
+                    for j in range(4):
+                        mm(pS[:, j:128 * sw:4], nIx, T.xp[:, c0 + 32 * a:c0 + 32 * (a + sw)], j == 0, False, ["nIx"] + X4, k(sn))
+                    mm(pS[:, 0:128 * sw], T.pI23[:], Gm[:, cols(a, sw)], False, True, ["pI23"] + GM[a:a + sw], k(sn))
+                    act(Gp[:, cols(a, sw)], pS[:, 0:128 * sw], ABS, k(sn) + ["bq"], GP[a:a + sw], bias=bq, scale=2.0 ** -23)
+                    jobs = [(Gm, WG, b, w, GM[b:b + w] + WGt) for b, w in vch[hf]]
+                    jobs.insert(JS[hf], (Gm, WGs, a, sw, GM[a:a + sw] + ["Wsa", "Wsb"]))
+                    jobs += [(None, None, 0, 1, None)] + [(Gp, WR, b, w, GP[b:b + w] + WRt) for b, w in vcut]
+                    jobs += [(Gp, WRs, a, sw, GP[a:a + sw] + ["Wsc", "Wsd"])]
                     for job in jobs:
                         src, Wq, b, w, rd = job
                         if src is None:
-                            mm(pY[:, 256:256 + 64 * nt], T.SelY[0:16, :], T.TT[0:16, 24 * s:24 * s + 8 * nt, R],
+                            o = 192 * s + 96 * hf
+                            if sw == 4:
+                                mm(pY[:, 65:256:2], T.SelY[0:8, 0:128], T.TX[0:8, o:o + 96], False, False,
+                                   ["SelY"] + k("TX"), k(bn))
+                            else:
+                                for r in range(ex, 4):
+                                    mm(pY[:, 65 + 2 * r:256:8], T.SelY[0:8, 0:128], T.TX[0:8, o + r:o + 96:4], False, False,
+                                       ["SelY"] + k("TX"), k(bn))
+                            mm(pY[:, 256:256 + 64 * nt], T.SelY[0:16, 0:128], T.TT[0:16, 24 * s:24 * s + 8 * nt, R],
                                False, False, ["SelY"] + k(*["TT%d" % t for t in range(nt)]), k(bn))
                             continue
                         for r in range(b, b + w):
-                            mm(pY[:, r - a0:8 * nb:8], src[:, cols(r, 1)], Wq[:, 0:nb], job is jobs[0] and r == b,
-                               job is jobs[-1] and r == b + w - 1, rd, k(bn))
+                            mm(pY[:, 2 * (r % 4) + r // 8:8 * nb:8], src[:, cols(r, 1)], Wq[:, 0:nb],
+                               job is jobs[0] and r == b, job is jobs[-1] and r == b + w - 1, rd, k(bn))
                     for e in READ[hf]:
                         if e == "k":
                             act(T.kp[:, L, R], pY[:, 0:64], IDN, k(bn) + ["kb"], k("kp" + "ab"[hf]), bias=kb)
@@ -522,7 +564,10 @@ def build_ops(g, T, topo, core, rank, cost):
                             ts(T.pen[:, 24 * s:24 * s + 8 * nt, R], pY[:, 256:256 + 64 * nt], 2047.0 - OFS, None, EQ, None,
                                k(bn), k("pen" + "ab"[hf]))
                 KX = pU[:, 0:128]
-                mm(KX, T.kp[:, L, :], T.idn[:], True, False, ["idn"] + k("kpa", "kpb"), k("pU"), True)
+                if st:
+                    mm(KX, T.TT[0:24, 24 * s + 8 * st:24 * s + 8 * st + 8, :], T.SelY[0:24, 128:256], True, False,
+                       ["SelN"] + k("TT%d" % st), k("pU"))
+                mm(KX, T.kp[:, L, :], T.idn[:], st == 0, False, ["idn"] + k("kpa", "kpb"), k("pU"), True)
                 for j in range(3):
                     mm(KX, T.ab[:, 24 * s + 8 * j:24 * s + 8 * j + 8, :], nI15, False, False,
                        ["nI15"] + k("aba", "abb"), k("pU"))
@@ -532,177 +577,164 @@ def build_ops(g, T, topo, core, rank, cost):
                 ps, pst = T.ZW[:, 128 * s + 15:128 * s + 128:16], k("ZW")
                 add("V", cyc(128), lambda: V.tensor_tensor_scan(T.ZW[:, K], T.rst[:], pU[:, 0:128], 0.0, MUL, MAX),
                     k("pU") + ["rst"], pst)
-                bi, bt = T.BI[:, 24 * s + 8 * st:24 * s + 8 * st + 8], k("BI%d" % nt)
-                if st == 0:
-                    cp(bi, ps, pst, bt)
-                else:
-                    tt(bi, ps, T.go[:, 16 * s + 8 * st - 8:16 * s + 8 * st], MUL, pst + k("go%d" % st), bt)
+                bi, bt = T.BI[:, L, st], k("BI%d" % nt)
+                tt(bi, ps, trail(st), MAX, pst + k("a%d" % st), bt)
+                a, at = trail(nt), k("a%d" % nt)
+                ts(a, bi, 2047, None, AND, None, bt + k("I3"), at)
                 if st < 2:
-                    a, at = (T.a1, T.a2)[st][:, L], k("a%d" % nt)
-                    f0 = 16 * s + 8 * st
-                    ts(a, bi, 2047, None, AND, None, bt, at)
-                    ts(T.off[:, 16 * nt + 8 * s:16 * nt + 8 * s + 8], a, -1.0, 2047.0, MUL, ADD, at, k("off" + "abc"[nt]))
-                    ts(T.go[:, f0:f0 + 8], a, 1024.0, None, ALU.is_ge, None, at, k("go%d" % nt))
+                    ts(T.off[:, 16 * nt + 8 * s:16 * nt + 8 * s + 8], a, -1.0, 2048.0, MUL, ADD, at, k("off" + "abc"[nt]))
                     turn(a, nt, at)
                 l2 = T.le[:, 16 + 8 * s:24 + 8 * s]
+                if st == 0 and v > 0:
+                    send(bar[0], T.snd[:, b0 + 8:b0 + 48], k("sd%d" % (v - 1)) + bt, bar[1])
                 if st == 0:
-                    act(T.q2[:, L], ps, IDN, pst, k("none", "q2"), bias=4096.0, scale=-1.0)
-                    ts(T.kk1[:, L], bi, 11, 15, SHR, AND, bt, k("kk1"))
+                    ts(T.kk1[:, L], bi, 10, 31, SHR, AND, bt, k("kk1"))
                     cp(l2, T.kk1[:, L], k("kk1"), k("lk"))
-                    ts(T.P1[:, sl(3)], T.off[:, 16 + 8 * s:24 + 8 * s], 1023.0, None, MIN, None, k("offb"), k("P1d"))
-                    tt(T.i2[:, L], bi, T.A0p[:, L], MAX, bt + k("A0p"), k("i2"))
-                    ts(T.Bw[:, L], T.i2[:, L], 32767, None, AND, None, k("i2"), k("Bw"))
-                    tt(T.lt0[:, L], T.q2[:, L], A0, MAX, k("q2") + a0t, k("lt0"))
+                    if not last:
+                        ts(T.P1[:, sl(3)], T.off[:, 16 + 8 * s:24 + 8 * s], 1024.0, 7.0, MIN, ADD, k("offb"), k("P1d"))
                     if v == 0:
-                        distance(xb, XB, T.goals[:, K], ab("goal0"))
-                        act(T.thr[:, X], pK[:, D], CPY, k("pK"), k("thr"))
-                    else:
-                        act(T.thr[:, X], bar[0], IDN, bar[1], k("thr"), bias=T.An[:, 8 * s + 4:8 * s + 5])
-                if st == 0 and last:
+                        distance(xb, XB, T.goals[:, 128 * hb:128 * hb + 128], ["goal0"], False, True)
+                        act(T.thr[:, X], RAW, CPY, k("pT"), k("thr"))
+                if st == 1 and last and s == 0:
                     for j in range(3):
-                        C = slice(768 * s + 256 * j, 768 * s + 256 * j + 256)
-                        mm(pT[:, 0:256], T.DWb[0:64, 128 * j:128 * j + 128], T.Pc[0:64, C], j == 0, False,
-                           ["DWb%d_" % j] + k("Pc%d_" % j), k("pT"))
+                        C = slice(256 * j, 256 * j + 256)
+                        mm(pT[:, 0:256], T.DWb[:, 128 * j:128 * j + 128], T.Pc[:, C], j == 0, False,
+                           ["DWb%d_" % j, "Pc%d_" % j], k("pT"))
                     for j in range(3):
-                        C = slice(768 * s + 256 * j, 768 * s + 256 * j + 256)
-                        mm(pT[:, 0:256], T.DWf[0:64, 128 * j:128 * j + 128], T.Vc[0:64, C], False, j == 2,
-                           ["DWf%d_" % j] + k("Vc%d_" % j), k("pT"), True)
-                    act(T.NW[:, 256 * s:256 * s + 256], pT[:, 0:256], IDN, k("pT"), k("NW"), bias=512.0)
-                    dma("Y", W[3:128:16, PL:DC2], T.NW[:, 256 * s:256 * s + 256], 131072, k("NW") + FILL, k("Wp"))
+                        C = slice(256 * j, 256 * j + 256)
+                        mm(pT[:, 0:256], T.DWf[:, 128 * j:128 * j + 128], T.Vc[:, C], False, j == 2,
+                           ["DWf%d_" % j, "Vc%d_" % j], k("pT"))
+                    act(T.NW[:, 256:512], pT[:, 0:256], IDN, k("pT"), ["NWr"], bias=512.0)
+                    dma("Y", W[3:128:16, PL:DT2], T.NW[:, 256:512], 131072, ["NWr"] + FILL, ["Wp"])
                 if st == 2:
                     pN = bank[NB]
-                    gtt(T.E[:, K], T.OH[:, 0:16], l2, T.nK[:, K], MUL, k("lk", "nKa") + ["OHa"], k("E"))
+                    gtt(T.E[:, K], T.OH[:, 24:56], l2, T.nK[:, K], MUL, k("lk", "nKa") + ["OHo", "OHp"], k("E"))
                     mm(pN[:, 256:384], T.E[:, K], T.blk[:], True, True, ["blk"] + k("E"), k(NB), True)
                     tt(T.Z[:, K], pN[:, 256:384], T.msk[:], MUL, k(NB) + ["msk"], k("Z"), 1.0)
-                    m8 = T.m8[:, 8:16] if last else T.m8[:, 0:8]
-                    mm(pN[:, 0:8], T.ones[:], m8, True, False, ["ones", "m8a", "m8b"], k(NB))
-                    mm(pN[:, 0:8], T.pI23[:], T.ones[:, 0:8], False, False, ["pI23", "ones"], k(NB))
-                    mm(pN[:, 0:8], T.nI23[:], T.go[:, 16 * s:16 * s + 8], False, False, ["nI23"] + k("go1"), k(NB))
-                    mm(pN[:, 0:8], T.Z[:, K], T.blk8[:], False, True, ["blk8"] + k("Z"), k(NB), True)
-                    tt(T.P1[:, sl(0)], pN[:, 0:8], cdum2 if last else cdum, MIN, k(NB) + ["cdum", "cdum2"], k("P1a"))
-                if st == 1:
-                    tt(T.kk1[:, L], bi, T.Bw[:, L], MAX, bt + k("Bw"), k("kk1"))
-                    ts(T.Bw2[:, L], T.kk1[:, L], 32767, None, AND, None, k("kk1"), k("Bw2"))
-                    tt(T.q1[:, L], bi, T.a1[:, L], MIN, bt + k("a1"), k("q1"))
-                    tt(T.i2[:, L], T.q1[:, L], T.lt0[:, L], MAX, k("q1", "lt0"), k("i2"))
-                    ts(T.lt2[:, L], T.i2[:, L], 5119, None, AND, None, k("i2"), k("lt2"))
+                    mm(pN[:, 0:8], (T.nI23 if last else T.pI23)[:], T.AF[:, 72 * s + 40:72 * s + 48], True, False,
+                       ["nI23", "pI23"] + k("ng1"), k(NB))
+                    mm(pN[:, 0:8], T.Z[:, K], blk8k, False, True, ["blk8k"] + k("Z"), k(NB), True)
+                    act(T.P1[:, sl(0)], pN[:, 0:8], IDN, k(NB), k("P1a"), bias=float(PL if last else PC), scale=1.0 / 2048.0)
 
-            tt(T.Bw[:, L], bi, T.Bw2[:, L], MAX, k("BI3", "Bw2"), k("Bw"))
-            tt(T.q1[:, L], bi, T.a2[:, L], MIN, k("BI3", "a2"), k("q1"))
-            ts(T.aw[:, L], T.Bw[:, L], 2047, None, AND, None, k("Bw"), k("aw"))
-            ts(T.le[:, L], T.aw[:, L], -1.0, 1039.0, MUL, ADD, k("aw"), k("le"))
-            X0 = slice(256 * v + 128 * s, 256 * v + 128 * s + 128)
-            if NKV:
-                gtt(T.NK[:, K], ef[:], T.le[:, L], xb, SUB, k("le", "ef0") + XB + ab("ef1"), NK)
-                act(T.xn[:, X0], T.NK[:, K], ABS, NK, k("xn%d" % v))
-            else:
-                sga(T.NK[:, K], ef[:], T.le[:, L], k("le", "ef0") + ab("ef1"), NK)
-                mm(pE[:, 384:512], T.pI23[:], xb, True, False, ["pI23"] + XB, k("pE"))
-                mm(pE[:, 384:512], T.nI23[:], T.NK[:, K], False, True, ["nI23"] + NK, k("pE"))
-                act(T.xn[:, X0], pE[:, 384:512], ABS, k("pE"), k("xn%d" % v), scale=1.0 / 8388608.0)
+            ts(T.le[:, L], trail(3), -1.0, 1039.0, MUL, ADD, k("a3"), k("le"))
+            X0 = slice(256 * v + 128 * hb, 256 * v + 128 * hb + 128)
+            gtt(T.NK[:, K], ef[:], T.le[:, L], xb, SUB, k("le") + ["ef0", "ef1"] + XB, NK)
+            act(T.xn[:, X0], T.NK[:, K], ABS, NK, k("xn%d" % v))
             b0 = 48 * (2 * v + s)
             send(T.landb[:, X0], T.xn[:, X0], k("xn%d" % v), k("landb%d" % v))
             if last:
-                for h in range(2):
-                    dma("Y", T.yx[64 * s:64 * s + 64, 128 * h:128 * h + 128], T.landb[64 * h:64 * h + 64, X0], 16384,
-                        k("landb%d" % v), [])
-            distance(T.xn[:, X0], k("xn%d" % v), T.goals[:, 256 * v + 128 * s:256 * v + 128 * s + 128],
-                     ab("goal0") if v == 0 else ["goalx"])
-            tt(T.good[:, X], pK[:, D], T.thr[:, X], LT, k("pK", "thr"), k("good"), 1.0)
-            tt(T.i2[:, L], T.q1[:, L], T.lt2[:, L], MAX, k("q1", "lt2"), k("i2"))
-            ts(T.lt[:, L], T.i2[:, L], 5119, None, AND, None, k("i2"), k("lt"))
-            ts(T.q2[:, L], T.aw[:, L], 1024.0, 8192.0, LT, MUL, k("aw"), k("q2"))
-            tt(T.q3[:, L], T.q2[:, L], T.lt[:, L], MIN, k("q2", "lt"), k("q3"))
-            ts(T.q4[:, L], T.aw[:, L], -1024.0, None, ADD, None, k("aw"), k("q4"))
-            cur, ct = (T.lfv[:, L], k("lfv")) if last else (T.snd[:, b0:b0 + 8], k("sa%d" % v))
-            tt(cur, T.q3[:, L], T.q4[:, L], MAX, k("q3", "q4"), ct)
-            act(T.P1[:, sl(1)], cur, IDN, ct, k("P1b"), bias=1023.0 + 128 * (1 - s), scale=-1.0)
+                dma("Y", T.yx[:, 128 * hb:128 * hb + 128], T.landb[:, X0], 32768, k("landb%d" % v), [])
+            distance(T.xn[:, X0], k("xn%d" % v), T.goals[:, X0], ["goal0"] if v == 0 else ["goalx"], bar, not last)
+            Q = slice(64 * s, 64 * s + 64)
+            ts(T.I3[:, I0:I0 + 8, 2:5], T.BI[:, L, 0:3], 2 ** 23 + 15 * 2048, None, AND, None,
+               k("BI1", "BI2", "BI3", "I3"), k("KK"))
+            tt(T.D1[:, Q], T.I3[:, I0:I0 + 16, 1:5], T.I3[:, I0 + 8:I0 + 24, 0:4], SUB,
+               k("KK", "a0", "a1", "a2", "a3", "I3"), k("D1"))
+            act(T.D0[:, Q], T.D1[:, Q], IDN, k("D1"), k("D0"), bias=2.0 ** 24, scale=-16384.0)
+            add("V", cyc(64), lambda Q=Q: V.tensor_tensor_scan(T.SC[:, Q], T.D0[:, Q], T.D1[:, Q], 0.0, MIN, MAX),
+                k("D0", "D1"), k("SC"))
+            cur = T.SC[:, 64 * s + 35:64 * s + 64:4]
+            act(T.P1[:, sl(1)], cur, IDN, k("SC"), k("P1b"), bias=YT0 - 128 * hb + 2047.0, scale=-1.0)
             if not last:
-                act(T.snd[:, b0 + 8:b0 + 40], pK[:, D], CPY, k("pK"), k("sd%d" % v))
-                send(T.land[:, b0:b0 + 40], T.snd[:, b0:b0 + 40], k("sa%d" % v, "sd%d" % v), k("land%d" % v))
+                move(SA, T.snd[:, b0:b0 + 8], cur, k("SC"), k("sa%d" % v))
+                send(T.land[:, b0:b0 + 8], T.snd[:, b0:b0 + 8], k("sa%d" % v), k("land%d" % v))
+                act(T.snd[:, b0 + 8:b0 + 48], RAW, CPY, k("pT"), k("sd%d" % v))
 
-            WV, WT = (W[:, 0:WS], WALL + FILL + k("Wp")) if last else (W[:, 0:PL], WALL)
-            ts(T.P0[:, sl(2)], T.Bw[:, L], 11, 15, SHR, AND, k("Bw"), k("P0c"))
-            ts(T.q1[:, L], T.lt[:, L], -1.0, float(TC + 1023), MUL, ADD, k("lt"), k("q1"))
-            tt(T.P0[:, sl(0)], T.q1[:, L], cj, MAX, k("q1") + ["cj"], k("P0a"))
-            tt(T.Df[:, X], T.P1[:, X], T.P0[:, X], SUB, k("P0a", "P0b", "P0c", "P0d", "P1a", "P1b", "P1c", "P1d"), k("Df"))
-            tt(T.Dg[:, X], T.Df[:, X], T.good[:, X], MUL, k("Df", "good"), k("Dg"))
-            tt(T.Sel[:, X], T.Dg[:, X], T.P0[:, X], ADD, k("Dg", "P0a", "P0b", "P0c", "P0d"), k("Sel"))
+            WV, WT = (W[:, 0:WS], WALL + FILL + ["Wp"]) if last else (W[:, 0:PL], WALL)
+            cp(T.i2[:, L], T.SC[:, 64 * s + 3:64 * s + 32:4], k("SC"), k("i2"))
+            ts(T.P0[:, sl(2)], T.i2[:, L], 11, 15, SHR, AND, k("i2"), k("P0c"))
+            ts(T.P0[:, sl(0)], T.i2[:, L], 2047, None, AND, None, k("i2"), k("P0a"))
+            tt(T.Dg[:, X], T.P1[:, X], pK[:, D], MIN, k("pK", "P1a", "P1b", "P1c", "P1d", "P1e"), k("Dg"), 1.0)
+            tt(T.Sel[:, X], T.Dg[:, X], T.P0[:, X], MAX, k("Dg", "P0a", "P0b", "P0c", "P0d"), k("Sel"))
             idv = T.Sel[:, sl(0)]
             cp(T.ls[:, X], T.Sel[:, X], k("Sel"), k("ls"))
-            gtt(T.E[:, K], idv, T.l1[:], T.msk[:], MUL, k("Sel") + ["l1", "msk"], k("E"))
-            act(T.q3[:, L], idv, CPY, k("Sel"), k("q3"), scale=-256.0 * 32768.0)
-            tt(T.nb[:, L], T.q3[:, L], cnb, SUB, k("q3") + ["cnb"], k("nb"))
-            act(T.acc[:, L], idv, IDN, k("Sel"), k("acc"), bias=-NEAR)
-            mm(pE[:, 0:128], T.ones[:], T.Jm[:], True, False, ["ones", "Jm"], k("pE"))
-            mm(pE[:, 0:128], T.blkE[:], T.E[:, K], False, True, ["blkE"] + k("E"), k("pE"), True)
-            o = 576 * s
-            for c in range(7, -1, -1):
-                wdt = 16 * c + 16
-                e, et = T.EQ[:, o:o + wdt], k("EQ%d_" % c)
-                act(e, pE[:, 0:wdt], ABS, k("pE", "nb"), et, bias=T.nb[:, 8 * s + c:8 * s + c + 1], scale=32768.0)
-                add("V", cyc(wdt), lambda mo=T.mn[:, 8 * s + c:8 * s + c + 1], e=e:
-                    V.tensor_reduce(mo, e, AxisListType.X, MIN, negate=True), et, k("mn%d_" % c))
-                o += wdt
-            tt(T.q2[:, L], T.mn[:, L], ctop2 if last else ctop, MIN, k(*["mn%d_" % j for j in range(8)]) + ["ctop", "ctop2"], k("q2"))
-            tt(T.lfv[:, L], T.q2[:, L], T.acc[:, L], MAX, k("q2", "acc"), k("lfv"))
-            mm(pT[:, 32:40], T.PB[:], T.lfv[:, L], True, True, ["PB"] + k("lfv"), k("pT"), True)
-            mm(pT[:, 40:48], T.PA[:], T.lfv[:, L], True, True, ["PA"] + k("lfv"), k("pT"), True)
-            ts(T.lf[:, 16 * s:16 * s + 16], pT[:, 32:48], NEAR, None, ADD, None, k("pT"), k("lf"))
+            if EARLY[s]:
+                gtt(T.hE[:, K], T.P0[:, sl(0)], l1, T.mof[:], MAX, k("P0a") + ["l1", "mof"], k("hE"))
+                gtt(T.E[:, K], T.Dg[:, sl(0)], l1, T.hE[:, K], MAX, k("Dg", "hE") + ["l1"], k("E"))
+            else:
+                gtt(T.E[:, K], idv, l1, T.msk[:], MUL, k("Sel") + ["l1", "msk"], k("E"))
+            tt(T.nb[:, L], cnb, idv, SUB, k("Sel") + ["cnb"], k("nb"))
+            act(T.acc[:, L], idv, IDN, k("Sel"), k("acc"), bias=NEAR, scale=-EPS)
+            mm(pE[:, 0:128], T.ones[:], (T.Jn if EARLY[s] else T.Jm)[:], True, False, ["ones", "Jm", "Jn"], k("pE"))
+            mm(pE[:, 0:128], T.blk[:], T.E[:, K], False, not EARLY[s], ["blk"] + k("E"), k("pE"), True)
+            if EARLY[s]:
+                mm(pE[:, 0:128], T.ones[:], T.Jm[:], False, True, ["ones", "Jm"], k("pE"))
+            for c in range(8):
+                o, wdt = 576 * s + 8 * c * (c + 1), 16 * c + 16
+                act(T.EQ[:, o:o + wdt], pE[:, 0:wdt], ABS, k("pE", "nb"), k("EQ%d_" % c),
+                    bias=T.nb[:, 8 * s + c:8 * s + c + 1])
+            ES = slice(576 * s, 576 * s + 576)
+            for a, b in ESP[s]:
+                lo, hi = 8 * a * (a + 1), 8 * b * (b + 1)
+                C = slice(576 * s + lo, 576 * s + hi)
+                add("V", cyc((hi - lo) // 2),
+                    lambda C=C, lo=lo, hi=hi: V.tensor_tensor_scan(T.ES[:, C], T.rs2[:, lo:hi], T.EQ[:, C], 0.0, MAX, MIN),
+                    k(*["EQ%d_" % j for j in range(a, b)]) + ["rs2"], k("ES%d_" % a))
+            gtt(T.q2[:, 16 * s:16 * s + 16], T.ES[:, ES], ends, cbot2 if last else cbot, MAX,
+                k(*["ES%d_" % a for a, b in ESP[s]]) + ["ends", "cbot", "cbot2"], k("q2"))
+            tt(T.lfv[:, L], T.q2[:, 16 * s:16 * s + 8], T.acc[:, L], MIN, k("q2", "acc"), k("lfv"))
+            ts(T.lf[:, L], T.lfv[:, L], -1.0 / EPS, NEAR / EPS, MUL, ADD, k("lfv"), k("lf"))
             lk = T.ls[:, sl(2)]
-            sga(T.Z[:, K], Y[:, 128 * s:128 * s + 1152], T.ls[:, sl(1)], k("ls", "Ye") + YT, k("Z"))
+            sga(T.Z[:, K], Y[:, 128 * hb:YW], T.ls[:, sl(1)], k("ls", "Ye") + ["Ye0"] + YT, k("Z"))
             sga(T.kq[:, K], T.KP[:, 0:18], lk, k("ls") + ["KPa", "KPb"], k("kq"))
             gtt(T.aK[:, K], WV, T.ls[:, sl(0)], T.kq[:, K], MUL, k("ls", "kq") + WT, k("aK"))
             gtt(T.bK[:, K], T.OH[:, 0:18], lk, T.Z[:, K], MUL, k("ls", "Z") + ["OHa", "OHb", "OHc"], k("bK"))
             if not last:
-                sga(T.Z2[:, K], Y[:, 128:1152], T.ls[:, sl(3)], k("ls") + YT + ["z2"], k("Zb"), scale=z2)
-            tt(T.aK[:, K], T.aK[:, K], T.bK[:, K], ADD, k("aK", "bK"), k("aK"))
-            act(T.NK[:, K], T.aK[:, K], IDN, k("aK"), NK, bias=128.5 + 15 * 2.0 ** -16, scale=1.0 / 4096.0)
-            parts = [(T.Pq, T.Z2, k("Zb"))] * (not last) + [(None, T.aK, k("aK")), (T.Pq, T.NK, NK)]
-            for Pm, x, xt in parts:
-                for h in range(2):
-                    lhs = (T.PB, T.PA)[h][:] if Pm is None else Pm[:, 128 * h:128 * h + 128]
-                    mm(pK[:, 128 * h:128 * h + 128], lhs, x[:, K], xt == parts[0][2] and h == 0, xt == NK and h == 1,
-                       ["Pq0", "Pq1", "PA", "PB"] + xt, k("pK"), Pm is None)
-            act(T.NW[:, 256 * s:256 * s + 256], pK[:, 0:256], IDN, k("pK"), k("NW"), bias=129.0 * 4096.0)
-            for h in range(2):
-                add("V", 0.06 + 128 * SC * CY,
-                    lambda h=h, WV=WV: V.tensor_copy(WV.indirect(T.lf[:, 16 * s + 8 * h:16 * s + 8 * h + 8]),
-                                                     T.NW[:, 256 * s + 128 * h:256 * s + 128 * h + 128]),
-                    k("lf", "NW"), WT)
+                sga(T.Z2[:, K], Y[:, 256:YW], T.ls[:, sl(3)], k("ls") + YT + ["z2"], k("Zb"), scale=z2)
+            if ADDP[s]:
+                mm(pK[:, 0:128], T.idn[:], T.aK[:, K], True, False, ["idn"] + k("aK"), k("pK"), True)
+                mm(pK[:, 0:128], T.idn[:], T.bK[:, K], False, True, ["idn"] + k("bK"), k("pK"), True)
+                act(T.NK[:, K], pK[:, 0:128], IDN, k("pK"), NK, bias=128.5 + 15 * 2.0 ** -16, scale=1.0 / 4096.0)
+                mm(pU[:, 0:128], T.idn[:], T.aK[:, K], True, False, ["idn"] + k("aK"), k("pU"), True)
+                mm(pU[:, 0:128], T.idn[:], T.bK[:, K], False, False, ["idn"] + k("bK"), k("pU"), True)
+                if not last:
+                    mm(pU[:, 0:128], T.nI12[:], T.Z2[:, K], False, False, ["nI12"] + k("Zb"), k("pU"))
+            else:
+                tt(T.aK[:, K], T.aK[:, K], T.bK[:, K], ADD, k("aK", "bK"), k("aK"))
+                act(T.NK[:, K], T.aK[:, K], IDN, k("aK"), NK, bias=128.5 + 15 * 2.0 ** -16, scale=1.0 / 4096.0)
+                if not last:
+                    mm(pU[:, 0:128], T.nI12[:], T.Z2[:, K], True, False, ["nI12"] + k("Zb"), k("pU"))
+                mm(pU[:, 0:128], T.idn[:], T.aK[:, K], last, False, ["idn"] + k("aK"), k("pU"), True)
+            mm(pU[:, 0:128], T.nI12[:], T.NK[:, K], False, True, ["nI12"] + NK, k("pU"))
+            act(T.NW[:, K], pU[:, 0:128], IDN, k("pU"), k("NW"), bias=129.0 * 4096.0)
             if not last:
-                an = T.An[:, 8 * s + v + 1:8 * s + v + 2]
-                mm(pT[:, 48:56], T.blk2[:], T.good[:, sl(0)], True, True, ["blk2a", "blk2b"] + k("good"), k("pT"))
-                act(T.q4[:, L], pT[:, 48:56], CPY, k("pT"), k("cnt", "q4"), acc=T.cnt[:, c4])
-                act(an, T.cnt[:, c4], IDN, k("cnt", "An"), k("An"), bias=T.An[:, 8 * s + v:8 * s + v + 1], scale=-1.0)
-                aq = T.go[:, 32 + 4 * s:33 + 4 * s]
-                act(aq, an, IDN, k("An"), k("Aq"), bias=-0.4375, scale=-0.125)
-                act(T.An[:, 8 * s + 4:8 * s + 5], aq, IDN, k("Aq", "An"), k("A7"), bias=an, scale=8.0)
-
-        dma("Y", T.yteam[64 * s:64 * s + 64, 0:512], W[0:64, TC:TC + 512], 131072, WT, [])
-        dma("S", T.yteam[64 * s:64 * s + 64, 512:1024], W[64:128, TC + 512:PC], 131072, WT, [])
-        dma("Y", T.yact[4 * s:4 * s + 4, :], W[67:128:16, PL:DC2], 65536, WT, [])
+                mm(pT[:, 48:56], T.blk[:], T.Sel[:, sl(4)], True, s == 0, ["blk"] + k("Sel"), k("pT"), True)
+                if s == 0:
+                    act(T.q4[:, L], pT[:, 48:56], IDN, k("pT"), k("cnt", "q4"), bias=-129.0 / 64.0, scale=-2.0 ** -18,
+                        acc=T.cnt[:, c4])
+                else:
+                    mm(pT[:, 48:49], nI15, T.An[:, 0:1], False, True, ["nI15", "An"], k("pT"))
+                    act(T.q4[:, L], pT[:, 48:56], IDN, k("pT") + ["cnt0"], k("cnt", "q4"), bias=T.cnt[:, 0:1],
+                        scale=-2.0 ** -15, acc=T.cnt[:, c4])
+                    aq = T.go[:, 0:1]
+                    act(aq, T.cnt[:, c4], IDN, k("cnt"), ["Aq"], bias=-0.4375, scale=-1.0)
+                    act(T.An[:], T.ones[:, 0:40], IDN, k("cnt") + ["Aq", "ones"], ["An"], bias=aq, scale=T.cnt[:, c4])
+            yield
+            tag[0] = (s, v)
+            add("V", 0.06 + 128 * SC * CY, lambda WV=WV: V.tensor_copy(WV.indirect(T.lf[:, L]), T.NW[:, K]),
+                k("lf", "NW"), WT)
+            yield
 
     a = len(ops)
-    stream(0)
-    b = len(ops)
-    stream(1)
-    return bundle(ops, a, b)
+    both = [stream(0), stream(1)]
+    for step in range(2 * NV):
+        for x in both:
+            next(x)
+    WT = WALL + FILL + ["Wp"]
+    for j, q in enumerate("YS"):
+        dma(q, T.yteam[64 * j:64 * j + 64, :], W[64 * j:64 * j + 64, TC:TE], 262144, WT, [], 64)
+    dma("Y", T.yact[:], W[3:128:16, PL:DT2], 131072, WT, [], 16)
+    return bundle(ops, a), None
 
 
-def bundle(ops, a, b):
-    times = {}
-    for o in ops:
-        for t in o["w"]:
-            times[t] = times.get(t, 0) + 1
-    fixed = set(t for o in ops[:a] for t in o["w"])
+def bundle(ops, a):
+    fixed = set(t for o in ops[:a] if o["k"] == "c" for t in o["w"])
     for o in ops[a:]:
         fixed.difference_update(o["w"])
-    out, cut, room = [], [0, 0], 0.0
+    out, room = [], 0.0
     for i, o in enumerate(ops):
-        cut = [len(out) if i == a else cut[0], len(out) if i == b else cut[1]]
         p = out[-1] if out else None
-        if (o["e"] == "P" and p["e"] == "P" and p["w"] == o["w"] and set(o["r"]) - fixed <= set(p["r"])
+        if (o["e"] == "P" and p is not None and p["e"] == "P" and p["w"] == o["w"] and set(o["r"]) - fixed <= set(p["r"])
                 and (room + o["x"] <= BUNDLE)):
             p["fs"].append(o["f"])
             p["d"] += o["d"]
@@ -715,17 +747,18 @@ def bundle(ops, a, b):
                 o["f"] = lambda fs=fs: [f() for f in fs][-1]
                 room = o["x"]
             out.append(o)
-    return out, cut
+    return out
 
 
 def depend(ops):
     lastw, readers = {}, {}
     deps = []
     for i, o in enumerate(ops):
-        d = set()
+        d, raw = set(), set()
         for t in o["r"]:
             if t in lastw:
                 d.add(lastw[t])
+                raw.add(lastw[t])
             if t in PSUM:
                 for j in readers.get(t, []):
                     if ops[j]["e"] != o["e"]:
@@ -733,9 +766,12 @@ def depend(ops):
         for t in o["w"]:
             if t in lastw:
                 d.add(lastw[t])
+                raw.add(lastw[t])
             d.update(readers.get(t, []))
         d.discard(i)
         deps.append(sorted(d))
+        o["free"] = set(j for j in d if ops[j]["e"] == o["e"] and o["k"] == ops[j]["k"] == "c"
+                        and (o["e"] == "P" or (o["e"] in INORDER and j not in raw)))
         for t in o["r"]:
             readers.setdefault(t, []).append(i)
         for t in o["w"]:
@@ -744,122 +780,223 @@ def depend(ops):
     return deps
 
 
-def place(ops, pred, succ, pr):
-    n = len(ops)
-    left = [len(d) for d in pred]
-    rdy = [0.0] * n
-    free, cand = {}, {}
+def place(ops, pred, succ, pr, first=None):
+    eng, dur, lat, isd = ops
+    n = len(eng)
+    left = list(pred)
+    rdy = list(first) if first else [0.0] * n
+    free, cand, low = [0.0] * 5, [[] for e in range(5)], [1e9] * 5
     for i in range(n):
-        free[ops[i]["e"]] = 0.0
-        cand.setdefault(ops[i]["e"], [])
         if left[i] == 0:
-            cand[ops[i]["e"]].append(i)
+            cand[eng[i]].append(i)
+            low[eng[i]] = min(low[eng[i]], rdy[i])
     order, bus, t0, t1 = [], 0.0, [0.0] * n, [0.0] * n
-    while len(order) < n:
-        best = None
-        for e in cand:
-            if cand[e]:
-                t = max(free[e], min(rdy[i] for i in cand[e]))
-                if best is None or t < best[0]:
-                    best = (t, e)
-        t, e = best
-        i = max((j for j in cand[e] if rdy[j] <= t + LOOK),
-                key=lambda j: (pr[j] - GAMMA * ops[j]["d"] - BETA * max(0.0, rdy[j] - t), -j))
-        t = max(t, rdy[i])
-        cand[e].remove(i)
-        o = ops[i]
-        free[e] = t + o["d"]
-        if o["k"] == "dma":
-            bus = max(bus, t + 1.5) + o["lat"] / BW
+    for step in range(n):
+        t = 1e9
+        for q in range(5):
+            x = free[q] if free[q] > low[q] else low[q]
+            if x < t:
+                t, e = x, q
+        c, top, edge = cand[e], -1e9, t + LOOK
+        for j in c:
+            x = rdy[j]
+            if x <= edge:
+                x = pr[j] - BETA * (x - t) if x > t else pr[j]
+                if x > top:
+                    top, i = x, j
+        if rdy[i] > t:
+            t = rdy[i]
+        c.remove(i)
+        low[e] = min([rdy[j] for j in c]) if c else 1e9
+        f = free[e] = t + dur[i]
+        if isd[i]:
+            bus = (bus if bus > t + 1.5 else t + 1.5) + lat[i]
             fin = bus + 0.5
         else:
-            fin = t + o["d"] + o["lat"]
+            fin = f + lat[i]
         t0[i], t1[i] = t, fin
         order.append(i)
-        for j in succ[i]:
-            if ops[j]["behind"] == i or o["behind"] == j:
-                rdy[j] = max(rdy[j], free[e])
-            else:
-                rdy[j] = max(rdy[j], free[e] if e == "P" and ops[j]["e"] == "P" else fin + (OWN if e == ops[j]["e"] else 1.0) * WAKE)
+        for j, w in succ[i]:
+            x = f if w < 0 else fin + w
+            if x > rdy[j]:
+                rdy[j] = x
             left[j] -= 1
             if left[j] == 0:
-                cand[ops[j]["e"]].append(j)
+                q = eng[j]
+                cand[q].append(j)
+                if rdy[j] < low[q]:
+                    low[q] = rdy[j]
     return order, t0, t1
 
 
-def replay(ops, deps, order, wake):
-    free, fin, bus = {}, [0.0] * len(ops), 0.0
+def model(ops, deps, cost):
+    eng = ["VSPGY".index(o["e"]) for o in ops]
+    waits = [[(j, cost[4] * (cost[12] if eng[j] == eng[i] else 1.0)) for j in deps[i] if j not in o["free"]]
+             for i, o in enumerate(ops)]
+    return (eng, [o["d"] for o in ops], [o["lat"] for o in ops],
+            [o["k"] == "dma" for o in ops]), waits
+
+
+def replay(m, order, trace=False):
+    (eng, dur, lat, isd), waits = m
+    free, fin, bus = [0.0] * 5, [0.0] * len(eng), 0.0
+    if trace:
+        why, last = [None] * len(eng), [None] * 5
+        for i in order:
+            e = eng[i]
+            t = free[e]
+            why[i] = None if last[e] is None else (last[e], True)
+            for j, w in waits[i]:
+                if fin[j] + w > t:
+                    t, why[i] = fin[j] + w, (j, False)
+            last[e] = i
+            f = free[e] = t + dur[i]
+            if isd[i]:
+                bus = max(bus, t + 1.5) + lat[i]
+                fin[i] = bus + 0.5
+            else:
+                fin[i] = f + lat[i]
+        return fin, why
     for i in order:
-        o = ops[i]
-        e = o["e"]
-        t = free.get(e, 0.0)
-        for j in deps[i]:
-            x = fin[j] + wake if e != ops[j]["e"] else 0.0 if e == "P" else fin[j] + OWN * wake
+        e = eng[i]
+        t = free[e]
+        for j, w in waits[i]:
+            x = fin[j] + w
             if x > t:
                 t = x
-        free[e] = t + o["d"]
-        if o["k"] == "dma":
-            bus = max(bus, t + 1.5) + o["lat"] / BW
+        f = free[e] = t + dur[i]
+        if isd[i]:
+            bus = (bus if bus > t + 1.5 else t + 1.5) + lat[i]
             fin[i] = bus + 0.5
         else:
-            fin[i] = t + o["d"] + o["lat"]
+            fin[i] = f + lat[i]
     return max(fin)
 
 
-def schedule(ops, hard, cut, others, lead, seed=0, noise=0.0):
+def schedule(ops, hard, cut, models, lead, seed=0, noise=0.0):
     n = len(ops)
 
     def worth(order, t1):
-        return float(np.log(max(t1)) + sum(np.log(replay(o, hard, order, w)) for o, w in others))
-    for i in range(n):
-        ops[i]["behind"] = i - 1 if ops[i].get("soft") else -1
+        return float(SHARE[0] * np.log(max(t1)) + sum(x * np.log(replay(m, order)) for x, m in zip(SHARE[1:], models[1:])))
+    base, waits = models[0]
+    behind = [[i - 1] if ops[i].get("soft") else [] for i in range(n)]
     where = {o["w"][0]: i for i, o in enumerate(ops) if o["k"] == "dma" and o["w"]}
     for a, b in zip(LOADS, LOADS[1:]):
-        ops[where[b]]["behind"] = where[a]
-    deps = [hard[i] + ([ops[i]["behind"]] if ops[i]["behind"] >= 0 else []) for i in range(n)]
+        behind[where[b]] = [where[a]]
+    deps = [waits[i] + [(j, -1.0) for j in sorted(set(behind[i]) | ops[i]["free"])] for i in range(n)]
     succ = [[] for i in range(n)]
     for i in range(n):
-        for j in deps[i]:
-            succ[j].append(i)
+        for j, w in deps[i]:
+            succ[j].append((i, w))
+    npred, nsucc = [len(d) for d in deps], [len(d) for d in succ]
     pr = [0.0] * n
     rs = np.random.default_rng(seed)
+    eng, dur, lat, isd = base
     for i in range(n - 1, -1, -1):
-        o = ops[i]
-        lat = 2.0 + o["lat"] / BW if o["k"] == "dma" else o["d"] + o["lat"]
-        pr[i] = max([pr[j] + (o["d"] if ops[j]["behind"] == i else
-                              o["d"] if o["e"] == "P" and ops[j]["e"] == "P" else
-                              lat + (OWN if o["e"] == ops[j]["e"] else 1.0) * WAKE) for j in succ[i]]
-                    or [lat + (lead if cut[0] <= i < cut[1] else 0.0)])
-    best = None
+        way = 2.0 + lat[i] if isd[i] else dur[i] + lat[i]
+        pr[i] = max([pr[j] + (dur[i] if w < 0 else way + w) for j, w in succ[i]]
+                    or [way])
+    pr = [x + (lead if o["tag"][0] == 0 else 0.0) for x, o in zip(pr, ops)]
+    best, short = None, GAMMA * np.array(dur)
     for rnd in range(ROUNDS):
-        order, t0, t1 = place(ops, deps, succ, pr)
+        order, t0, t1 = place(base, npred, succ, (np.array(pr) - short).tolist())
         if best is None or worth(order, t1) < best[0]:
             best = (worth(order, t1), order, t0, t1, pr)
-        pr = place(ops, succ, deps, [t + noise * float(x) for t, x in zip(t1, rs.random(n))])[2]
+        pr = place(base, nsucc, deps, (np.array(t1) + noise * rs.random(n) - short).tolist())[2]
     kinds, seen, kind = {}, {}, []
     for i, o in enumerate(ops):
         w = (o["w"] or ["out"])[0]
-        if w.startswith("offa") or i in cut:
-            seen = {}
         key = o["e"] + "".join(c for c in w if c.isalpha())
-        seen[key] = seen.get(key, 0) + 1
-        kind.append(kinds.setdefault((key, seen[key], i >= cut[0]), len(kinds)))
+        seen[key, o["tag"]] = seen.get((key, o["tag"]), 0) + 1
+        kind.append(kinds.setdefault((key, seen[key, o["tag"]], o["tag"][1] >= 0, o["tag"][0] if APART else 0), len(kinds)))
     kind = np.array(kind)
-    pr = np.array(best[4])
+    pr = np.array(best[4]) - short
     for rnd in range(CLIMB):
         d = np.zeros(len(kinds))
         for rep in range(int(rs.integers(1, 4))):
             d[rs.integers(len(kinds))] += rs.normal() * rs.choice([0.3, 1.0, 2.0])
         p = pr + d[kind]
-        order, t0, t1 = place(ops, deps, succ, p.tolist())
+        order, t0, t1 = place(base, npred, succ, p.tolist())
         if max(t1) <= max(best[3]) + 1.0:
             x = worth(order, t1)
             if x <= best[0]:
                 best = (x, order, t0, t1)
                 pr = p
+    order = polish(best[1], [set(j for j, w in d) for d in deps], models, rs)
+    fin = replay(models[0], order, True)[0]
     for i in range(n):
-        ops[i]["t0"], ops[i]["t1"] = best[2][i], best[3][i]
-    return best[1], max(best[3])
+        ops[i]["t0"], ops[i]["t1"] = fin[i] - (2.0 + lat[i] if isd[i] else dur[i] + lat[i]), fin[i]
+    return order, max(fin)
+
+
+def polish(order, need, models, rs):
+    eng = models[0][0][0]
+    n = len(eng)
+
+    def rerun(m, new, start, old):
+        (eng, dur, lat, isd), waits = m
+        fin, gone, busy = old[0][:], old[1][:], old[2][:]
+        free, bus, seen = [0.0] * 5, 0.0, set()
+        for i in new[start - 1::-1] if start else []:
+            if eng[i] not in seen:
+                seen.add(eng[i])
+                free[eng[i]] = gone[i]
+                if len(seen) == 5:
+                    break
+        if start:
+            bus = busy[new[start - 1]]
+        for i in new[start:]:
+            e = eng[i]
+            t = free[e]
+            for j, w in waits[i]:
+                x = fin[j] + w
+                if x > t:
+                    t = x
+            f = gone[i] = free[e] = t + dur[i]
+            if isd[i]:
+                bus = (bus if bus > t + 1.5 else t + 1.5) + lat[i]
+                fin[i] = bus + 0.5
+            else:
+                fin[i] = f + lat[i]
+            busy[i] = bus
+        return fin, gone, busy
+    state = [rerun(m, order, 0, ([0.0] * n, [0.0] * n, [0.0] * n)) for m in models]
+    ends = [np.log(max(x[0])) for x in state]
+    pairs = []
+    for rnd in range(SWAPS):
+        if not pairs:
+            fin, why = replay(models[int(rs.integers(len(models)))], order, True)
+            i = int(np.argmax(fin))
+            while why[i] is not None:
+                j, queue = why[i]
+                if queue and j not in need[i]:
+                    pairs.append((j, i))
+                i = j
+            pairs = [pairs[x] for x in rs.permutation(len(pairs))[:40]]
+            continue
+        a, b = pairs.pop()
+        pa, pb = order.index(a), order.index(b)
+        if pa > pb or any(eng[x] == eng[a] for x in order[pa + 1:pb]):
+            continue
+        move, want, queues = [b], set(need[b]), set()
+        for x in order[pb - 1:pa:-1]:
+            if x in want or eng[x] in queues:
+                move.append(x)
+                want |= need[x]
+                queues.add(eng[x])
+        if a in want:
+            continue
+        taken = set(move)
+        new = order[:pa] + move[::-1] + [x for x in order[pa:pb] if x not in taken] + order[pb + 1:]
+        trial, loss = [], 0.0
+        for m, old, end, x in zip(models, state, ends, SHARE):
+            trial.append(rerun(m, new, pa, old))
+            loss += x * (np.log(max(trial[-1][0])) - end)
+            if loss > 0.002:
+                break
+        if loss <= 0.0:
+            order, state, ends = new, trial, [np.log(max(x[0])) for x in trial]
+    return order
 
 
 def emit(g, T, ops, deps, order):
@@ -871,15 +1008,18 @@ def emit(g, T, ops, deps, order):
             cnt[e] = cnt.get(e, 0) + 1
             pos[i] = cnt[e]
     know = {e: {} for e in Q}
-    clock, waits, need = {}, {}, set()
+    clock, waits, need, prev = {}, {}, set(), []
     for i in order:
         o = ops[i]
         k = know[o["e"]]
-        ws = []
-        for j in sorted(deps[i], key=lambda j: -ops[j]["t1"]):
+        ws, more = [], []
+        if o["e"] == "G" and o["k"] == "c":
+            more = [j for j in prev if o.get("alone") or ops[j].get("alone")]
+            prev = [i]
+        for j in sorted(deps[i] + more, key=lambda j: -ops[j]["t1"]):
             p = ops[j]
             if p["k"] == "c":
-                if p["e"] == "P" and o["e"] == "P":
+                if j in o["free"]:
                     continue
                 key, val = p["e"], pos[j]
             else:
@@ -939,8 +1079,11 @@ def rank_program(g, core, T, topo):
     ops, cut = build_ops(g, T, topo, core, rank, COSTS[0])
     deps = depend(ops)
     if not ORDER:
-        others = [(build_ops(g, T, topo, core, rank, c)[0], c[4]) for c in COSTS[1:]]
-        order, end = schedule(ops, deps, cut, others, LEAD, SEED, NOISE)
+        models = []
+        for c in COSTS:
+            other = build_ops(g, T, topo, core, rank, c)[0]
+            models.append(model(other, depend(other), c))
+        order, end = schedule(ops, deps, cut, models, LEAD, SEED, NOISE)
         ORDER.append((order, [o["t1"] for o in ops]))
     for o, t in zip(ops, ORDER[0][1]):
         o["t1"] = t

import numpy as np
from concourse.bass import DstId, RemoteDMATransfer
from concourse.mybir import AluOpType as ALU, AxisListType, ActivationFunctionType as ACT

NV = 4
TC, PC, DC, DT, PL, DT2, WS = 1, 1032, 5128, 5136, 5264, 9360, 9488
YT0, YW = 264, 1288
EXTRA = ((1, 0, 0), (0, 0, 0))
JS = (2, 2)
SUB_ = ("pE", "pT")
READ = ("kap", "kap")
PV = "SSSSVSVS"
XE = (("V", "VVVV", "VVSS"), ("S", "SSSS", "VVSS"), ("S", "VVVV", "GGGV"))
HI0 = "S"
TB = ("pK1", "pU1", "pK0", "pT1", "pK1", "pU1", "pK0", "pT1")
ADDP = (1, 1)
ESP = (((0, 8),), ((0, 6), (6, 8)))
EARLY = (0, 1)
SA = "S"
EV = (1, 0)
NKV = 1
NEAR, EPS = 63.5 / 256.0, 2.0 ** -23
NB = "pE"
ONV = ("acc", "Pb")
DW = (16, 240, 3600)
OFS = 192.0 * sum(DW) + 512.0
ROUNDS, CLIMB, SWAPS = 20, 2500, 16000
LEAD, SEED, NOISE = 3.0, 1, 0.6
APART = 1
F, B, I, U = "float32", "bfloat16", "int32", "uint16"


def sb(n, d):
    return ("sbuf", [128, n], d)


SCRATCH = {
    "Y": sb(YW, F), "goals": sb(1024, B), "land": sb(288, F), "snd": sb(288, F),
    "landb": sb(1024, B), "xb": sb(256, B), "xp": sb(1280, B), "xn": sb(1024, B), "wtI": sb(8, I), "stI": sb(16, I),
    "actI": sb(256, I), "dg": sb(768, I), "dgb": sb(768, B), "Vc": sb(768, B), "Pc": sb(768, B),
    "prg": sb(4096, B), "dq": sb(4096, B), "W": sb(WS, F), "ef": sb(1040, B), "teamI": sb(1024, I),
    "ci": sb(16, I), "cf": sb(24, F), "io2": sb(128, F), "io3": sb(128, F), "idn": sb(128, F),
    "blk": sb(128, F), "blk8": sb(16, F), "msk": sb(128, F),
    "nI23": sb(128, B), "pI23": sb(128, B), "nI512": sb(128, F),
    "lp": sb(8, U), "nI": sb(384, B), "SelY": sb(256, B), "rst": sb(128, F), "SB": sb(128, B),
    "Wy": sb(224, B), "We": sb(128, B), "c12": sb(256, B), "DWf": sb(384, B), "DWb": sb(384, B),
    "blkB": sb(208, B), "nI12": sb(128, B), "ones": sb(128, B), "Jm": sb(128, B), "Jn": sb(128, B), "mof": sb(128, F), "m8": sb(8, B),
    "OH": sb(56, F), "KP": sb(24, F), "l1": sb(16, U), "cs": sb(64, F),
    "EQ": sb(1152, B), "ES": sb(1152, B), "rs2": sb(576, B), "TX": sb(384, B),
    "cK": sb(256, F), "mK": sb(256, I), "nK": sb(512, I), "n16": sb(256, U),
    "Z": sb(256, F), "Z2": sb(256, B), "E": sb(256, F), "eI": sb(256, I), "eM": sb(256, I), "NK": sb(256, B),
    "kq": sb(256, F), "aK": sb(256, F), "bK": sb(256, F), "NW": sb(512, F), "nb": sb(16, F), "hE": sb(256, F),
    "TT": ("sbuf", [128, 48, 16], B), "pen": ("sbuf", [128, 48, 16], B), "ab": ("sbuf", [128, 48, 16], B),
    "kp": ("sbuf", [128, 16, 16], F),
    "ZW": sb(256, F), "AF": sb(144, B), "go": sb(40, B), "BI": ("sbuf", [128, 16, 4], I),
    "I3": ("sbuf", [128, 48, 5], I), "D0": sb(128, F), "D1": sb(128, F), "SC": sb(128, F),
    "A0": sb(16, F), "off": sb(48, U), "kk1": sb(16, I), "q2": sb(32, F),
    "acc": sb(16, F), "q4": sb(16, F), "i2": sb(16, I),
    "le": sb(32, U),
    "P0": sb(80, I), "P1": sb(80, F), "Dg": sb(80, F),
    "Sel": sb(80, F), "ls": sb(80, U), "thr": sb(80, F),
    "lfv": sb(16, F), "lf": sb(16, U),
    "cnt": sb(8, F), "An": sb(40, B),
}
for s_ in "01":
    for nm, n_, d_ in (("xr", 1536, B), ("Gm", 2048, B), ("Gp", 2048, B)):
        SCRATCH[nm + s_] = sb(n_, d_)
    for nm in ("pK", "pT", "pU", "pE"):
        SCRATCH[nm + s_] = ("psum", [128, 512], F)
PSUM = ("pK0", "pK1", "pT0", "pT1", "pU0", "pU1", "pE0", "pE1")

NDMA = 70
SEMAPHORES = ["cV", "cS", "cP", "cG", "sent", "gin"] + ["d%d" % i for i in range(NDMA)] + ["r%d" % i for i in range(20)]

COSTS = ((0.87e-3, 0.5e-3, 1.45, 3.8, 0.17, 1.0, 2.6, 64, 0.1, 0.0, 0.0, 1.1, 1.2, 3.0, 260e3, 0.002),
         (0.85e-3, 0.55e-3, 1.15, 1.8, 0.1, 1.4, 2.8, 64, 0.05, -0.015, -0.015, 1.25, 1.4, 5.0, 200e3, 0.001),
         (1.0e-3, 0.55e-3, 1.7, 5.0, 0.17, 1.5, 3.0, 64, 0.1, -0.015, -0.015, 1.1, 1.4, 5.0, 300e3, 0.003),
         (1.2e-3, 0.62e-3, 1.9, 4.0, 0.2, 1.0, 2.5, 64, 0.1, 0.0, -0.015, 1.0, 1.0, 4.0, 200e3, 0.001),
         (1.08e-3, 0.62e-3, 1.2, 3.0, 0.1, 0.8, 2.0, 64, 0.1, 0.02, 0.0, 1.0, 1.8, 2.0, 350e3, 0.002),
         (0.83e-3, 0.45e-3, 1.3, 3.0, 0.25, 1.2, 3.5, 64, 0.1, 0.0, 0.0, 1.0, 1.0, 4.0, 180e3, 0.003))
SHARE = (2.0, 1.5, 1.0, 0.5, 1.0, 1.5)
INORDER = ""
LOOK, BETA = 0.15, 10.0
WAKE = COSTS[0][4]
GAMMA = 1.5
NX = 0.0
OWN = 1.4
PRG, NTM = (4, 2, 1, 1), 2
LOADS = ("prg0", "prg1", "dq0", "dq1", "dq2", "teamI0", "teamI1", "prg2", "prg3", "goal0", "ef1")
F32 = (4, 0.0)
BUNDLE = 512


def build_ops(g, T, topo, core, rank, cost):
    CY, PEC, GA, SC = cost[:4]
    ops = []
    N = len(T.cores)
    V, S, P = g.vector, g.scalar, g.tensor

    tag = [(-1, -1)]

    def add(eng, dur, fn, r, w, kind="c", lat=0.0, extra=None):
        ops.append({"e": eng, "d": dur, "f": fn, "r": list(r), "w": list(w), "k": kind, "lat": lat, "x": extra,
                    "tag": tag[0]})

    def cyc(n):
        return max(64, n) * CY

    def wd(ap):
        return int(np.prod(ap.shape[1:]))

    def ts(out, in0, s1, s2, o0, o1, r, w, c=1.0):
        if o1 is None:
            add("V", cyc(wd(out) * c), lambda: V.tensor_scalar(out, in0, s1, None, o0), r, w)
        else:
            add("V", cyc(wd(out) * c), lambda: V.tensor_scalar(out, in0, s1, s2, o0, o1), r, w)

    def tt(out, a, b, op, r, w, c=2.0):
        add("V", cyc(wd(out) * c), lambda: V.tensor_tensor(out, a, b, op), r, w)

    def cp(out, a, r, w, c=1.0):
        add("V", cyc(wd(out) * c), lambda: V.tensor_copy(out, a), r, w)

    def gtt(out, win, off, b, op, r, w):
        add("V", 0.05 + wd(out) * GA * CY, lambda: V.tensor_tensor(out, win.indirect(off), b, op), r, w)

    def ms(ap, val, w, c=1.0):
        add("V", cyc(wd(ap) * c), lambda: V.memset(ap, val), [], w)

    def act(out, a, fn, r, w, bias=0.0, scale=1.0, acc=None):
        if "".join(c for c in w[0] if c.isalpha()) in ONV:
            if acc is not None:
                add("V", cyc(wd(out)), lambda: V.tensor_reduce(acc, a, AxisListType.X, ALU.add), r, w)
            elif fn == ACT.Relu:
                ts(out, a, scale, 0.0, ALU.mult, ALU.max, r, w)
            else:
                ts(out, a, scale, bias, ALU.mult, ALU.add, r, w)
        elif acc is None:
            add("S", cyc(wd(out)) + 0.04 + cost[9], lambda: S.activation(out, a, fn, bias=bias, scale=scale), r, w)
        else:
            add("S", cyc(wd(out)) + 0.06 + cost[9], lambda: S.activation(out, a, fn, bias=bias, scale=scale, accum_out=acc), r, w)

    def sga(out, win, off, r, w, scale=1.0):
        add("S", 0.08 + cost[10] + wd(out) * GA * CY, lambda: S.activation(out, win.indirect(off), ACT.Copy, scale=scale), r, w)

    def mm(out, l, rh, st, sp, r, w, f32=False):
        n = max(min(64, wd(l)), wd(rh)) * (4 if f32 else 1)
        add("P", max(min(cost[7], wd(l)), wd(rh)) * (F32[0] if f32 else 1) * PEC + F32[1],
            lambda: P.matmul(out, l, rh, st, sp), r, w, lat=cost[8], extra=n)

    def dma(q, out, a, nbytes, r, w, rows=128):
        qq = {"Y": g.sync, "S": g.scalar, "G": g}[q]
        add(q, cost[5] if q == "G" else 0.1, lambda: qq.dma_start(out, a), r, w, kind="dma",
            lat=nbytes / cost[14] + rows * cost[15])

    def iota(out, pat, base, cm, w, flt=True):
        if flt:
            add("G", 0.15 + 2 * wd(out) * CY, lambda: g.iota(out, pat, base, cm, allow_small_or_imprecise_dtypes=True),
                ["io2", "io3"] if wd(out) > 128 else [], w)
        else:
            add("G", 0.15 + 2 * wd(out) * CY, lambda: g.iota(out, pat, base, cm), [], w)

    def move(e, out, src, r, w, c=1.0):
        if e == "V":
            cp(out, src, r, w, c)
        elif e == "S":
            act(out, src, ACT.Copy, r, w)
        else:
            add("G", (0.17 + 2 * wd(out) * CY) * cost[11], lambda: g.affine_select(
                out, src, [[0, wd(out)]], ALU.is_ge, 0.0, 0, 0), r, w)

    def split_mask(dst, part, parts):
        en = topo.engines(core, dst)
        n = len(en) // parts
        m = 0
        for e in en[part * n:(part + 1) * n]:
            m |= 1 << e
        return m, n

    AND, SHR = ALU.bitwise_and, ALU.logical_shift_right
    MUL, ADD, SUB, MAX, MIN, EQ, LT = ALU.mult, ALU.add, ALU.subtract, ALU.max, ALU.min, ALU.is_equal, ALU.is_lt
    CPY, IDN, ABS, RELU = ACT.Copy, ACT.Identity, ACT.Abs, ACT.Relu
    Y, ci, cf = T.Y, T.ci, T.cf

    W, ef = T.W, T.ef
    TE = TC + 1024
    dma("S", T.actI[:], T.act[:], 131072, [], ["actI"])
    dma("S", T.xb[:], T.x0[:], 65536, [], ["xb"])
    dma("S", T.wtI[:, 0:1], T.wt[:], 8192, [], ["wtI"])
    dma("S", T.stI[:], T.start[:], 8192, [], ["stI"])
    a, PT = 0, []
    for c, w in enumerate(PRG):
        C = slice(512 * a, 512 * (a + w))
        dma("Y", T.prg[:, C], T.prog[:, C], 131072 * w, [], ["prg%d" % c])
        PT += ["prg%d" % c] * w
        a += w
    for h in range(NTM):
        C = slice(1024 // NTM * h, 1024 // NTM * (h + 1))
        dma("Y", T.teamI[:, C], T.team[:, C], 524288 // NTM, [], ["teamI%d" % h])
    for h in range(2):
        C = slice(512 * h, 512 * h + 512)
        cp(W[:, TC + 512 * h:TC + 512 * h + 512], T.teamI[:, C], ["teamI%d" % (h * (NTM - 1))], ["Wt%d" % h])
    dma("Y", ef[:, 16:1040], T.eff[:], 262144, [], ["ef1"])
    dma("Y", T.goals[:, 0:256], T.goal[:], 65536, [], ["goal0"])
    for j in (1, 2):
        C = slice(256 * j, 256 * j + 256)
        ts(T.dg[:, C], T.actI[:], -512.0, 1.0 / 15 ** j, ADD, MUL, ["actI"], ["dg%d_" % j])
        cp(T.dgb[:, C], T.dg[:, C], ["dg%d_" % j], ["dgb%d_" % j])
    ts(T.dg[:, 0:256], T.dg[:, 256:512], -15.0, -512.0, MUL, ADD, ["dg1_"], ["dg0_"])
    tt(T.dgb[:, 0:256], T.dg[:, 0:256], T.actI[:], ADD, ["dg0_", "actI"], ["dgb0_"])
    for j in range(3):
        dma("Y", T.dq[8 * j:8 * j + 8, :], T.dgb[:, 256 * j:256 * j + 256], 65536, ["dgb%d_" % j], ["dq%d" % j])

    def send_goals():
        tr = []
        for v in range(1, NV):
            dst = T.cores[(rank + v) % N]
            rid, pid, se = topo.addr(dst)
            m, n = split_mask(dst, *GM3[v])
            tr.append(RemoteDMATransfer(dst_ids=[DstId(rid=rid, pnc=pid)], dma_engine_mask=m, remote_sem=T.sem.gin,
                                        src=T.goals[:, 0:256], dst=T.goals[:, 256 * v:256 * v + 256]))
        return g.remote_dma_fused(tr, local_sem=T.sem.sent)
    GM3 = (None, (0, 2), (2, 4), (3, 4))
    ngo = sum(split_mask(T.cores[(rank + v) % N], *GM3[v])[1] for v in range(1, NV))
    add("G", cost[13], send_goals, ["goal0"], ["goalx"], kind="rem", lat=2.5, extra=("gin", ngo))

    iota(ci[:, 0:1], [[0, 1]], 0, 1, ["ci0"], False)
    iota(T.E[:, 0:128], [[1, 8], [0, 16]], 0, 0, ["E0"])
    iota(T.io2[:], [[0, 8], [1, 16]], 0, 0, ["io2"])
    iota(T.io3[:], [[1, 128]], 0, 0, ["io3"])
    iota(T.eM[:, 0:64], [[1, 64]], 0, 64, ["eM0"], False)
    ts(ci[:, 4:5], ci[:, 0:1], 15, None, AND, None, ["ci0"], ["ci4"])
    ts(ci[:, 8:9], ci[:, 0:1], 4, None, SHR, None, ["ci0"], ["ci8"])
    cp(cf[:, 0:9:4], ci[:, 0:9:4], ["ci0", "ci4", "ci8"], ["cf"])
    pc, rc, gc_ = cf[:, 0:1], cf[:, 4:5], cf[:, 8:9]
    ts(T.blk[:], T.E[:, 0:128], gc_, None, EQ, None, ["E0", "cf"], ["blk"])
    ts(T.msk[:], T.io2[:], rc, None, EQ, None, ["io2", "cf"], ["msk"])
    ts(T.idn[:], T.io3[:], pc, None, EQ, None, ["io3", "cf"], ["idn"])
    def pick(out, pat, base, val, w):
        iota(out, [[0, wd(out)]], val, 0, w)
        add("G", 0.17 + 2 * wd(out) * CY, lambda: g.affine_select(out, out, pat, EQ, 0.0, base, 1), w, w)
    iota(T.SB[0:32, :], [[0, 128]], 0, 0, ["SB"])
    add("G", 0.17 + 256 * CY, lambda: g.affine_select(T.SB[0:32, :], T.SB[0:32, :], [[-1, 8], [-8, 16]], ALU.not_equal,
                                                      2.0 ** 19, 0, 1), ["SB"], ["SB"])
    add("G", 0.17 + 16 * CY, lambda: g.affine_select(T.SB[0:32, 1:128:16], T.SB[0:32, 1:128:16], [[-1, 8]], ALU.not_equal,
                                                     -15.0 * 2.0 ** 19, -16, 1), ["SB"], ["SB"])
    for j in range(3):
        pick(T.DWf[:, 128 * j:128 * j + 128], [[-1, 128]], 0, DW[j], ["DWf%d_" % j])
        pick(T.DWb[:, 128 * j:128 * j + 128], [[-1, 128]], 0, -DW[j], ["DWb%d_" % j])
    nI24, nI15, c1, c2 = T.nI[:, 0:128], T.nI[:, 128:256], T.c12[:, 0:128], T.c12[:, 128:256]
    act(nI24, T.idn[:], CPY, ["idn"], ["nI24"], scale=-16777216.0)
    ts(T.Jm[:], T.io3[:], T.idn[:, 0:1], 1.0 / 256.0, MUL, MUL, ["io3", "idn"], ["Jm"])
    act(T.nI12[:], T.idn[:], CPY, ["idn"], ["nI12"], scale=-4096.0)
    blk8, blk8k = T.blk8[:, 0:8], T.blk8[:, 8:16]
    act(blk8, T.blk[:, 0:128:16], CPY, ["blk"], ["blk8"])
    act(blk8k, blk8, CPY, ["blk8"], ["blk8k"], scale=2048.0)
    act(T.nI512[:], T.idn[:], CPY, ["idn"], ["nI512"], scale=-512.0)
    act(nI15, T.idn[:], CPY, ["idn"], ["nI15"], scale=-32768.0)
    ts(T.rst[:], T.io2[:], 0.5, None, ALU.is_gt, None, ["io2"], ["rst"])
    ms(c1, -255.0 / 128.0, ["c1"], 0.5)
    ms(c2, 1.5 * 2.0 ** 25, ["c2"], 0.5)
    kb, wq, pure, kd, kr, z2 = [cf[:, j:j + 1] for j in (5, 2, 3, 6, 7, 9)]
    bq = T.m8[:, 0:1]
    ts(kb, rc, -2048.0, 2.0 ** 23 + 32767.0 + 241.0 * 32768.0 - OFS, MUL, ADD, ["cf"], ["kb"])
    act(T.nI23[:], T.idn[:], CPY, ["idn"], ["nI23"], scale=-8388608.0)
    act(T.pI23[:], T.idn[:], CPY, ["idn"], ["pI23"], scale=8388608.0)
    m = T.msk
    ts(bq, rc, 2.5, 192.0, LT, MUL, ["cf"], ["bq"])
    ts(z2, rc, 2.5, 1.0 / 65536.0, LT, MUL, ["cf"], ["z2"])
    ts(pure, rc, 2.5, 32768.0, ALU.is_gt, MUL, ["cf"], ["pure"])
    ts(cf[:, 10:11], m[:, 1:2], 15.0, m[:, 0:1], MUL, ADD, ["msk"], ["k10"])
    ts(cf[:, 11:12], m[:, 2:3], 225.0, cf[:, 10:11], MUL, ADD, ["msk", "k10"], ["k11"])
    ts(wq, cf[:, 11:12], 16.0, None, MUL, None, ["k11"], ["wq"])
    tt(kd, pure, wq, SUB, ["pure", "wq"], ["kd"])
    ts(kr, pure, -2.0, wq, MUL, ADD, ["pure", "wq"], ["kr"])
    WG, WR, WGs, WRs = [T.Wy[:, 56 * j:56 * j + 56] for j in range(4)]
    ms(T.Wy[:, 8:32], 0.0, ["Wy1"], 0.5)
    act(T.Wy[:, 0:8], blk8, CPY, ["blk8", "kd"], ["Wy0"], scale=kd)
    act(T.Wy[:, 56:64], blk8, CPY, ["blk8", "kr"], ["Wr0"], scale=kr)
    for j in range(3):
        act(T.Wy[:, 32 + 8 * j:40 + 8 * j], blk8, CPY, ["blk8", "wq"], ["Wy%d" % (2 + j)], scale=wq)
        act(T.Wy[:, 64 + 8 * j:72 + 8 * j], blk8, CPY, ["blk8", "msk"], ["Wr%d" % (1 + j)], scale=m[:, j:j + 1])
    WGt = ["Wy%d" % j for j in range(5)]
    act(T.Wy[:, 88:112], T.Wy[:, 32:56], CPY, WGt, ["Wr4"], scale=-1.0)
    WRt = ["Wr%d" % j for j in range(5)]
    cp(T.Wy[:, 120:168], T.Wy[:, 8:56], WGt, ["Wsa"], 0.5)
    cp(T.Wy[:, 112:120], T.Wy[:, 88:96], WRt, ["Wsb"], 0.5)
    cp(T.Wy[:, 176:224], T.Wy[:, 64:112], WRt, ["Wsc"], 0.5)
    ts(T.Wy[:, 168:176], T.Wy[:, 0:8], -1.0, None, MUL, None, WGt, ["Wsd"], 0.5)
    nIx = T.nI[:, 256:384]
    ts(cf[:, 19:20], pure, -256.0, None, MUL, None, ["pure"], ["k19"])
    act(nIx, T.idn[:], CPY, ["idn", "k19"], ["nIx"], scale=cf[:, 19:20])
    act(T.blkB[:, 0:128], T.blk[:], CPY, ["blk"], ["blkB"])
    for j in range(5):
        ts(T.blkB[:, 128 + 8 * j:136 + 8 * j], blk8, 2.0 ** 20, None, MUL, None, ["blk8"], ["blkC%d_" % j])
    BC = ["blkC%d_" % j for j in range(5)]
    ts(T.blkB[:, 168:208], T.blkB[:, 128:168], -1.0, None, MUL, None, BC, ["blkD"], 0.5)
    ms(T.ones[:], 1.0, ["ones"], 0.5)
    ts(T.Z[:, 128:144], T.io3[:, 0:16], -1.0, 15.0, MUL, ADD, ["io3"], ["Z1"])
    iota(T.OH[:, 24:56:2], [[0, 16]], 0, 0, ["OHo"])
    ts(T.OH[:, 25:56:2], T.Z[:, 128:144], rc, None, EQ, None, ["Z1", "cf"], ["OHp"])
    cp(T.OH[:, 0:15], T.OH[:, 27:56:2], ["OHp"], ["OHq"])
    cp(T.OH[:, 15:16], T.OH[:, 25:26], ["OHp", "OHq"], ["OHa"])
    ts(T.OH[:, 16:17], z2, 4096.0, None, MUL, None, ["z2"], ["OHb"])
    cp(T.OH[:, 17:18], m[:, 3:4], ["msk"], ["OHc"])
    act(T.KP[:, 0:16], T.OH[:, 0:16], IDN, ["OHa"], ["KPa"], bias=1.0, scale=12.0)
    ts(T.KP[:, 16:18], T.io3[:, 0:2], -1.0, 1.0, MUL, ADD, ["io3"], ["KPb"])
    l1, ends = T.l1[:, 0:8], T.l1[:, 8:9]
    cp(l1, T.io3[:, 0:8], ["io3"], ["l1"])
    cj16, cj, cbot, cnb = T.cs[:, 0:16], T.cs[:, 0:8], T.cs[:, 16:32], T.cs[:, 32:40]
    ts(cj16, T.io3[:, 0:16], 16.0, rc, MUL, ADD, ["io3", "cf"], ["cj"])
    cbot2 = T.cs[:, 40:56]
    act(cbot, cj16, IDN, ["cj"], ["cbot"], bias=NEAR - DT * EPS, scale=-EPS)
    act(cbot2, cj16, IDN, ["cj"], ["cbot2"], bias=NEAR - DT2 * EPS, scale=-EPS)
    act(cnb, cj, IDN, ["cj"], ["cnb"], bias=0.25, scale=-1.0 / 256.0)
    if any(EARLY):
        ts(T.Jn[:], T.ones[:], T.idn[:, 0:1], -15.0 * 16384.0, MUL, MUL, ["idn", "ones"], ["Jn"])
        act(T.mof[:], T.msk[:], IDN, ["msk"], ["mof"], bias=16384.0, scale=-16384.0)
    iota(T.rs2[:], [[0, 576]], 0, 0, ["rs2"])
    for c in range(8):
        iota(T.rs2[:, 8 * c * (c + 1):8 * c * (c + 1) + 1], [[0, 1]], 2 ** 23, 0, ["rs2"])
    ts(ci[:, 12:13], ci[:, 0:1], 7, None, AND, None, ["ci0"], ["ci12"])
    ts(ci[:, 13:14], ci[:, 0:1], 3, 1, SHR, AND, ["ci0"], ["ci13"])
    ts(cf[:, 16:17], ci[:, 13:14], 2.0, None, MUL, None, ["ci13"], ["k16"])
    ts(cf[:, 17:18], ci[:, 12:13], 16.0, cf[:, 16:17], MUL, ADD, ["ci12", "k16"], ["k17"])
    iota(T.cs[:, 56:64], [[1, 2], [4, 4]], 0, 0, ["lq"])
    ts(T.lp[:], T.cs[:, 56:64], cf[:, 17:18], None, ADD, None, ["lq", "k17"], ["lp"])
    cp(cf[:, 18:19], ci[:, 12:13], ["ci12"], ["k18"])
    ts(T.SelY[0:16, 0:128], T.E[0:16, 0:128], cf[0:16, 18:19], None, EQ, None, ["E0", "k18"], ["SelY"], 0.5)
    ts(cf[:, 21:22], pc, -16.0, None, ADD, None, ["cf"], ["k21"])
    ts(T.SelY[0:24, 128:256], T.E[0:24, 0:128], cf[0:24, 21:22], -2.0 ** 24, EQ, MUL, ["E0", "k21"], ["SelN"])
    act(cf[:, 20:21], cf[:, 18:19], ACT.Square, ["k18"], ["k20"], bias=1.5)
    ts(ends, cf[:, 20:21], 8.0, -3.0, MUL, ADD, ["k20"], ["ends"])
    ms(T.An[:], 0.0, ["An"])
    iota(T.I3[:], [[0, 240]], 0, 0, ["I30", "I31"], False)
    for s in range(2):
        iota(T.I3[:, 24 * s:24 * s + 8, 1], [[0, 8]], 2 ** 22, 0, ["I3%d" % s], False)
    yi, yf = [T.mK[:, 64 * j:64 * j + 64] for j in range(4)], [T.NW[:, 64 * j:64 * j + 64] for j in range(5)]
    ts(yi[0], T.eM[:, 0:64], 1023, None, AND, None, ["eM0"], ["yi0"])
    for j in (1, 2):
        ts(yi[j], yi[0], -512.0, 1.0 / 15 ** j, ADD, MUL, ["yi0"], ["yi%d" % j])
    ts(yi[3], yi[1], -15.0, -512.0, MUL, ADD, ["yi1"], ["yi3"])
    tt(yf[0], yi[0], yi[3], ADD, ["yi0", "yi3"], ["yf0"])
    ts(yf[4], yi[2], -15.0, None, MUL, None, ["yi2"], ["yf4"])
    tt(yf[1], yi[1], yf[4], ADD, ["yi1", "yf4"], ["yf1"])
    cp(yf[2], yi[2], ["yi2"], ["yf2"])
    cp(yf[3], yi[0], ["yi0", "yf0", "yf1", "yf2"], ["NW0", "NW1", "NWr", "mK0", "mK1"])
    iota(Y[:, 256:YW], [[0, YW - 256]], 0, 0, ["Yf"])
    for j in range(4):
        dma("Y", Y[j:128:16, YT0:YW], yf[j], 32768, ["Yf", "NW0", "NW1"], ["Y%d_" % j])
    YT = ["Yf", "Y0_", "Y1_", "Y2_", "Y3_"]

    PAY = ["W%d_" % c for c in range(8)]
    TEAM = ["Wt0", "Wt1", "Wz", "Wx"]
    WALL = PAY + TEAM + ["Wv"]
    FILL = ["Wfa", "Wfb", "Wfc", "Wfd"]
    iota(W[:, 0:TC], [[0, TC]], 0, 0, ["Wz"])
    iota(W[:, TE:PC], [[0, PC - TE]], 0, 0, ["Wx"])
    iota(W[:, DC:PL], [[0, PL - DC]], 0, 0, ["Wv"])
    for j, t in enumerate(FILL):
        iota(W[:, PL + 1056 * j:PL + 1056 * j + 1056], [[0, 1056]], 0, 0, [t])
    iota(ef[:, 0:16], [[0, 16]], 0, 0, ["ef0"])
    ts(cf[:, 12:13], T.wtI[:, 0:1], 2.0, None, MUL, None, ["wtI"], ["wf"])
    act(T.We[:], T.blk[:], CPY, ["blk", "wf"], ["We"], scale=cf[:, 12:13])
    for c in range(8):
        bn, C = TB[c], slice(512 * c, 512 * c + 512)
        mm(T[bn][:], T.pI23[:], T.prg[:, C], True, False, ["pI23", PT[c]], [bn])
        mm(T[bn][:], T.SB[0:24, :], T.dq[0:24, C], False, True, ["SB", "dq0", "dq1", "dq2"], [bn])
        if PV[c] == "V":
            ts(W[:, PC + 512 * c:PC + 512 * c + 512], T[bn][:], 2.0 ** -23, None, MUL, None, [bn], [PAY[c]])
        else:
            act(W[:, PC + 512 * c:PC + 512 * c + 512], T[bn][:], CPY, [bn], [PAY[c]], scale=2.0 ** -23)

    nxt = T.cores[(rank + 1) % N]
    nrid, npid, nse = topo.addr(nxt)
    nmask, neng = split_mask(nxt, 0, 1)
    nsend = [0]

    def send(out, src, r, w):
        sem = "r%d" % nsend[0]
        nsend[0] += 1
        add("G", cost[5], lambda: g.remote_dma(out, src, T.sem[sem], T.sem.sent, npid, nrid, nmask), r, w,
            kind="rem", lat=cost[6], extra=(sem, neng))

    def stream(s):
        H = str(s)
        hb = 1 - s
        tag[0] = (s, -1)

        def k(*names):
            return [n + H for n in names]
        Gm, Gp, xr = T["Gm" + H], T["Gp" + H], T["xr" + H]
        pK, pT, pU, pE = T["pK" + H], T["pT" + H], T["pU" + H], T["pE" + H]
        K = slice(128 * s, 128 * s + 128)
        L = slice(8 * s, 8 * s + 8)
        c4 = slice(4 * s, 4 * s + 1)
        XB = ["xb"]
        NK = k("NK")
        xb = T.xb[:, 128 * hb:128 * hb + 128]
        bank = {"pK": pK, "pT": pT, "pU": pU, "pE": pE}

        def sl(j):
            return slice(40 * s + 8 * j, 40 * s + 8 * j + 8)

        D, X = slice(0, 40), slice(40 * s, 40 * s + 40)
        cp(T.P0[:, sl(1)], cj, ["cj"], k("P0b"))
        ms(T.P0[:, 40 * s + 24:40 * s + 40], 0, k("P0d"))
        ms(T.P1[:, sl(2)], 16.0, k("P1c"))
        ms(T.P1[:, sl(4)], 4096.0, k("P1e"))
        RAW = pT[:, 64:104]
        I0 = 24 * s

        def trail(j):
            return T.I3[:, I0 + 8:I0 + 16, j + 1]

        def distance(x, xt, goal, gt, test, raw):
            mm(pE[:, 0:128], T.nI23[:], goal, True, False, ["nI23"] + gt, k("pE"))
            mm(pE[:, 0:128], T.pI23[:], x, False, True, ["pI23"] + xt, k("pE"))
            act(T.Z2[:, K], pE[:, 0:128], ABS, k("pE"), k("Zb"), scale=1.0 / 8388608.0)
            mm(pE[:, 128:256], T.Z2[:, K], T.blkB[:, 0:128], True, True, ["blkB"] + k("Zb"), k("pE"))
            tt(T.NK[:, K], pE[:, 128:256], T.msk[:], MUL, k("pE") + ["msk"], NK, 1.0)
            if test:
                mm(pK[:, D], T.idn[:], test[0], True, False, ["idn"] + test[1], k("pK"), True)
                mm(pK[:, D], T.pI23[:], T.An[:], False, False, ["pI23", "An"], k("pK"))
                mm(pK[:, D], T.NK[:, K], T.blkB[:, 168:208], False, True, ["blkD"] + NK, k("pK"))
            if raw:
                mm(RAW, T.NK[:, K], T.blkB[:, 128:168], True, True, BC + NK, k("pT"))

        def turn(src, j, r):
            f0, n = 72 * s + 24 * j, 24 if j else 16
            move("V" if j else HI0, T.AF[:, f0:f0 + 8], src, r, k("ah%d" % j))
            tt(T.AF[:, f0 + 8:f0 + 16], src, T.AF[:, f0:f0 + 8], SUB, r + k("ah%d" % j), k("al%d" % j))
            if j:
                ts(T.AF[:, f0 + 16:f0 + 24], src, 1024.0, None, LT, None, r, k("ng%d" % j))
            mm(pT[0:n, 128:256], T.AF[:, f0:f0 + n], T.pI23[:], True, True,
               ["pI23"] + k("ah%d" % j, "al%d" % j, "ng%d" % j), k("pT"))
            act(T.TT[0:n, 24 * s + 8 * j:24 * s + 8 * j + 8, :], pT[0:n, 128:256], CPY, k("pT"), k("TT%d" % j),
                scale=1.0 / 8388608.0)

        ts(T.A0[:, L], T.stI[:, 8 * hb:8 * hb + 8], -1.0, 2047.0, MUL, ADD, ["stI"], k("A0"))

        for v in range(NV):
            last = v == NV - 1
            tag[0] = (s, v)
            if last and s == 0:
                for j in range(3):
                    C = slice(256 * j, 256 * j + 256)
                    dma("Y", T.Pc[:, C], T.prog[j:128:16, :], 65536, ["Wfa"], ["Pc%d_" % j])
                    dma("G", T.Vc[:, C], W[j:128:16, PC:DC], 65536, PAY, ["Vc%d_" % j])
            if last:
                ms(T.P1[:, sl(2)], 17.0, k("P1c"))
            if v > 0:
                b0 = 48 * (2 * (v - 1) + s)
                x0 = 256 * (v - 1) + 128 * hb
                xb, XB = T.landb[:, x0:x0 + 128], k("landb%d" % (v - 1))
                A0, a0t = T.land[:, b0:b0 + 8], k("land%d" % (v - 1))
                bar = (T.land[:, b0 + 8:b0 + 48], k("far%d" % (v - 1)))
            else:
                bar = (T.thr[:, X], k("thr"))
                A0, a0t = T.A0[:, L], k("A0")
            ts(T.off[:, L], A0, -1.0, 2048.0, MUL, ADD, a0t, k("offa"))
            cp(trail(0), A0, a0t + k("I3"), k("a0"))
            turn(A0, 0, a0t)
            uu, ut = T.cK[:, K], k("uK")
            e1, e2 = pE[:, 128:256], pE[:, 256:384]
            if EV[min(v, 1)]:
                mm(e1, T.We[:], xb, True, True, ["We"] + XB, k("pE"))
                cp(T.eI[:, K], e1, k("pE"), k("eI"))
                ts(T.eM[:, K], T.eI[:, K], 511, None, AND, None, k("eI"), k("eM"))
                ts(uu, T.eM[:, K], 33.0, None, ADD, None, k("eM"), ut)
            else:
                mm(e1, c1, T.ones[:], True, False, ["c1", "ones"], k("pE"))
                mm(e1, T.We[:], xb, False, True, ["We"] + XB, k("pE"))
                act(T.hE[:, K], e1, IDN, k("pE"), k("hE"), bias=1.5 * 2.0 ** 23, scale=1.0 / 512.0)
                mm(e2, T.nI512[:], T.hE[:, K], True, False, ["nI512"] + k("hE"), k("pE"), True)
                mm(e2, c2, T.ones[:], False, False, ["c2", "ones"], k("pE"))
                mm(e2, T.We[:], xb, False, True, ["We"] + XB, k("pE"))
                act(uu, e2, IDN, k("pE"), ut, bias=33.0)
            first, who, parts = XE[s] if v == 0 else XE[2]
            out, ot = T.xp[:, K], k("xp")
            if first == "V":
                add("V", 0.06 + 128 * GA * CY, lambda xb=xb, out=out: V.tensor_copy(out, xb.indirect(T.lp[:])),
                    XB + ["lp"], ot)
            else:
                sga(out, xb, T.lp[:], XB + ["lp"], ot)
            XJ = k(*["xj%d_" % j for j in range(4)])
            c0, X4 = 256 + 512 * s, k(*["xq%d_" % j for j in range(4)])
            for j, e in enumerate(who):
                move(e, T.xp[:, c0 + j:c0 + 512:4], T.xp[:, K], k("xp"), [X4[j]], 0.5)
            for j, e in enumerate(parts):
                w = 8 + max(EXTRA[s])
                move(e, xr[:, j:128 * w:4], T.xp[:, c0:c0 + 32 * w], X4, [XJ[j]], 0.5)
            for r in range(8):
                o = 96 * (r // 4)
                mm(pU[0:8, o + r % 4:o + 96:4], T.xp[:, 128 * s + 64 + 8 * r:128 * s + 72 + 8 * r], T.Wy[:, 64:88],
                   r == 0, r == 7, WRt + k("xp"), k("pU"))
            act(T.TX[0:8, 192 * s:192 * s + 192], pU[0:8, 0:192], CPY, k("pU"), k("TX"), scale=-1.0)
            act(Y[:, 128 * hb:128 * hb + 128], uu, IDN, ut, k("Ye"), bias=-1599.5, scale=48.5)

            for st in range(3):
                nt = st + 1
                of = T.off[:, 16 * st + 8 * s:16 * st + 8 * s + 8]
                oft = k("off" + "abc"[st])
                gtt(T.mK[:, K], W[:, 0:2056 if st else PC], of, T.cK[:, K], MUL,
                    oft + TEAM + k("uK") + (PAY if st else []), k("mK"))
                nK, nkt = (T.nK[:, 256 + 128 * s:384 + 128 * s], k("nKb")) if st else (T.nK[:, K], k("nKa"))
                ts(nK, T.mK[:, K], 5, 4095, SHR, AND, k("mK"), nkt)
                add("V", NX + 0.06 + 128 * GA * CY, lambda nK=nK: V.tensor_copy(T.n16[:, K], nK.indirect(T.lp[:])),
                    nkt + ["lp"], k("n16"))
                GM, GP = k(*["Gm%d_" % r for r in range(16)]), k(*["Gp%d_" % r for r in range(16)])

                def cols(a, w):
                    return slice(128 * a, 128 * (a + w))

                def lst(a, w):
                    return T.n16[:, 128 * s + 8 * a:128 * s + 8 * (a + w)]
                ex = EXTRA[s][st]
                vch = ([(0, 2), (2, 2)] + [(8, ex)] * (ex > 0), [(4, 2), (6, 2)])
                sch = ((8 + ex, 4 - ex), (12, 4))
                for a, w in vch[0] + vch[1]:
                    gtt(Gm[:, cols(a, w)], W[:, PC:DC], lst(a, w), xr[:, cols(a, w)], SUB, k("n16") + PAY + XJ, GM[a:a + w])
                    ops[-1]["soft"] = a > 0
                for a, w in sch:
                    sga(Gm[:, cols(a, w)], W[:, PC:DC], lst(a, w), k("n16") + PAY, GM[a:a + w])
                    ops[-1]["soft"] = a == 12
                nb = 8 * (4 + nt)
                for hf in range(2):
                    (a, sw), vcut = sch[hf], [(4 * hf, 4)] + vch[hf][2:]
                    bn, sn = ("pU", "pK")[hf], SUB_[hf]
                    pY, pS, R = bank[bn], bank[sn], slice(8 * hf, 8 * hf + 8)
                    for b, w in vcut:
                        ts(Gp[:, cols(b, w)], Gm[:, cols(b, w)], bq, 0.0, ADD, MAX, GM[b:b + w] + ["bq"], GP[b:b + w], 0.5)
                    for j in range(4):
                        mm(pS[:, j:128 * sw:4], nIx, T.xp[:, c0 + 32 * a:c0 + 32 * (a + sw)], j == 0, False, ["nIx"] + X4, k(sn))
                    mm(pS[:, 0:128 * sw], T.pI23[:], Gm[:, cols(a, sw)], False, True, ["pI23"] + GM[a:a + sw], k(sn))
                    act(Gp[:, cols(a, sw)], pS[:, 0:128 * sw], ABS, k(sn) + ["bq"], GP[a:a + sw], bias=bq, scale=2.0 ** -23)
                    jobs = [(Gm, WG, b, w, GM[b:b + w] + WGt) for b, w in vch[hf]]
                    jobs.insert(JS[hf], (Gm, WGs, a, sw, GM[a:a + sw] + ["Wsa", "Wsb"]))
                    jobs += [(None, None, 0, 1, None)] + [(Gp, WR, b, w, GP[b:b + w] + WRt) for b, w in vcut]
                    jobs += [(Gp, WRs, a, sw, GP[a:a + sw] + ["Wsc", "Wsd"])]
                    for job in jobs:
                        src, Wq, b, w, rd = job
                        if src is None:
                            o = 192 * s + 96 * hf
                            if sw == 4:
                                mm(pY[:, 65:256:2], T.SelY[0:8, 0:128], T.TX[0:8, o:o + 96], False, False,
                                   ["SelY"] + k("TX"), k(bn))
                            else:
                                for r in range(ex, 4):
                                    mm(pY[:, 65 + 2 * r:256:8], T.SelY[0:8, 0:128], T.TX[0:8, o + r:o + 96:4], False, False,
                                       ["SelY"] + k("TX"), k(bn))
                            mm(pY[:, 256:256 + 64 * nt], T.SelY[0:16, 0:128], T.TT[0:16, 24 * s:24 * s + 8 * nt, R],
                               False, False, ["SelY"] + k(*["TT%d" % t for t in range(nt)]), k(bn))
                            continue
                        for r in range(b, b + w):
                            mm(pY[:, 2 * (r % 4) + r // 8:8 * nb:8], src[:, cols(r, 1)], Wq[:, 0:nb],
                               job is jobs[0] and r == b, job is jobs[-1] and r == b + w - 1, rd, k(bn))
                    for e in READ[hf]:
                        if e == "k":
                            act(T.kp[:, L, R], pY[:, 0:64], IDN, k(bn) + ["kb"], k("kp" + "ab"[hf]), bias=kb)
                        elif e == "a":
                            act(T.ab[:, 24 * s:24 * s + 24, R], pY[:, 64:256], ABS, k(bn), k("ab" + "ab"[hf]), bias=-192.0)
                        else:
                            ts(T.pen[:, 24 * s:24 * s + 8 * nt, R], pY[:, 256:256 + 64 * nt], 2047.0 - OFS, None, EQ, None,
                               k(bn), k("pen" + "ab"[hf]))
                KX = pU[:, 0:128]
                if st:
                    mm(KX, T.TT[0:24, 24 * s + 8 * st:24 * s + 8 * st + 8, :], T.SelY[0:24, 128:256], True, False,
                       ["SelN"] + k("TT%d" % st), k("pU"))
                mm(KX, T.kp[:, L, :], T.idn[:], st == 0, False, ["idn"] + k("kpa", "kpb"), k("pU"), True)
                for j in range(3):
                    mm(KX, T.ab[:, 24 * s + 8 * j:24 * s + 8 * j + 8, :], nI15, False, False,
                       ["nI15"] + k("aba", "abb"), k("pU"))
                for t in range(nt):
                    mm(KX, T.pen[:, 24 * s + 8 * t:24 * s + 8 * t + 8, :], nI24, False, t == st,
                       ["nI24"] + k("pena", "penb"), k("pU"))
                ps, pst = T.ZW[:, 128 * s + 15:128 * s + 128:16], k("ZW")
                add("V", cyc(128), lambda: V.tensor_tensor_scan(T.ZW[:, K], T.rst[:], pU[:, 0:128], 0.0, MUL, MAX),
                    k("pU") + ["rst"], pst)
                bi, bt = T.BI[:, L, st], k("BI%d" % nt)
                tt(bi, ps, trail(st), MAX, pst + k("a%d" % st), bt)
                a, at = trail(nt), k("a%d" % nt)
                ts(a, bi, 2047, None, AND, None, bt + k("I3"), at)
                if st < 2:
                    ts(T.off[:, 16 * nt + 8 * s:16 * nt + 8 * s + 8], a, -1.0, 2048.0, MUL, ADD, at, k("off" + "abc"[nt]))
                    turn(a, nt, at)
                l2 = T.le[:, 16 + 8 * s:24 + 8 * s]
                if st == 0 and v > 0:
                    send(bar[0], T.snd[:, b0 + 8:b0 + 48], k("sd%d" % (v - 1)) + bt, bar[1])
                if st == 0:
                    ts(T.kk1[:, L], bi, 10, 31, SHR, AND, bt, k("kk1"))
                    cp(l2, T.kk1[:, L], k("kk1"), k("lk"))
                    if not last:
                        ts(T.P1[:, sl(3)], T.off[:, 16 + 8 * s:24 + 8 * s], 1024.0, 7.0, MIN, ADD, k("offb"), k("P1d"))
                    if v == 0:
                        distance(xb, XB, T.goals[:, 128 * hb:128 * hb + 128], ["goal0"], False, True)
                        act(T.thr[:, X], RAW, CPY, k("pT"), k("thr"))
                if st == 1 and last and s == 0:
                    for j in range(3):
                        C = slice(256 * j, 256 * j + 256)
                        mm(pT[:, 0:256], T.DWb[:, 128 * j:128 * j + 128], T.Pc[:, C], j == 0, False,
                           ["DWb%d_" % j, "Pc%d_" % j], k("pT"))
                    for j in range(3):
                        C = slice(256 * j, 256 * j + 256)
                        mm(pT[:, 0:256], T.DWf[:, 128 * j:128 * j + 128], T.Vc[:, C], False, j == 2,
                           ["DWf%d_" % j, "Vc%d_" % j], k("pT"))
                    act(T.NW[:, 256:512], pT[:, 0:256], IDN, k("pT"), ["NWr"], bias=512.0)
                    dma("Y", W[3:128:16, PL:DT2], T.NW[:, 256:512], 131072, ["NWr"] + FILL, ["Wp"])
                if st == 2:
                    pN = bank[NB]
                    gtt(T.E[:, K], T.OH[:, 24:56], l2, T.nK[:, K], MUL, k("lk", "nKa") + ["OHo", "OHp"], k("E"))
                    mm(pN[:, 256:384], T.E[:, K], T.blk[:], True, True, ["blk"] + k("E"), k(NB), True)
                    tt(T.Z[:, K], pN[:, 256:384], T.msk[:], MUL, k(NB) + ["msk"], k("Z"), 1.0)
                    mm(pN[:, 0:8], (T.nI23 if last else T.pI23)[:], T.AF[:, 72 * s + 40:72 * s + 48], True, False,
                       ["nI23", "pI23"] + k("ng1"), k(NB))
                    mm(pN[:, 0:8], T.Z[:, K], blk8k, False, True, ["blk8k"] + k("Z"), k(NB), True)
                    act(T.P1[:, sl(0)], pN[:, 0:8], IDN, k(NB), k("P1a"), bias=float(PL if last else PC), scale=1.0 / 2048.0)

            ts(T.le[:, L], trail(3), -1.0, 1039.0, MUL, ADD, k("a3"), k("le"))
            X0 = slice(256 * v + 128 * hb, 256 * v + 128 * hb + 128)
            gtt(T.NK[:, K], ef[:], T.le[:, L], xb, SUB, k("le") + ["ef0", "ef1"] + XB, NK)
            act(T.xn[:, X0], T.NK[:, K], ABS, NK, k("xn%d" % v))
            b0 = 48 * (2 * v + s)
            send(T.landb[:, X0], T.xn[:, X0], k("xn%d" % v), k("landb%d" % v))
            if last:
                dma("Y", T.yx[:, 128 * hb:128 * hb + 128], T.landb[:, X0], 32768, k("landb%d" % v), [])
            distance(T.xn[:, X0], k("xn%d" % v), T.goals[:, X0], ["goal0"] if v == 0 else ["goalx"], bar, not last)
            Q = slice(64 * s, 64 * s + 64)
            ts(T.I3[:, I0:I0 + 8, 2:5], T.BI[:, L, 0:3], 2 ** 23 + 15 * 2048, None, AND, None,
               k("BI1", "BI2", "BI3", "I3"), k("KK"))
            tt(T.D1[:, Q], T.I3[:, I0:I0 + 16, 1:5], T.I3[:, I0 + 8:I0 + 24, 0:4], SUB,
               k("KK", "a0", "a1", "a2", "a3", "I3"), k("D1"))
            act(T.D0[:, Q], T.D1[:, Q], IDN, k("D1"), k("D0"), bias=2.0 ** 24, scale=-16384.0)
            add("V", cyc(64), lambda Q=Q: V.tensor_tensor_scan(T.SC[:, Q], T.D0[:, Q], T.D1[:, Q], 0.0, MIN, MAX),
                k("D0", "D1"), k("SC"))
            cur = T.SC[:, 64 * s + 35:64 * s + 64:4]
            act(T.P1[:, sl(1)], cur, IDN, k("SC"), k("P1b"), bias=YT0 - 128 * hb + 2047.0, scale=-1.0)
            if not last:
                move(SA, T.snd[:, b0:b0 + 8], cur, k("SC"), k("sa%d" % v))
                send(T.land[:, b0:b0 + 8], T.snd[:, b0:b0 + 8], k("sa%d" % v), k("land%d" % v))
                act(T.snd[:, b0 + 8:b0 + 48], RAW, CPY, k("pT"), k("sd%d" % v))

            WV, WT = (W[:, 0:WS], WALL + FILL + ["Wp"]) if last else (W[:, 0:PL], WALL)
            cp(T.i2[:, L], T.SC[:, 64 * s + 3:64 * s + 32:4], k("SC"), k("i2"))
            ts(T.P0[:, sl(2)], T.i2[:, L], 11, 15, SHR, AND, k("i2"), k("P0c"))
            ts(T.P0[:, sl(0)], T.i2[:, L], 2047, None, AND, None, k("i2"), k("P0a"))
            tt(T.Dg[:, X], T.P1[:, X], pK[:, D], MIN, k("pK", "P1a", "P1b", "P1c", "P1d", "P1e"), k("Dg"), 1.0)
            tt(T.Sel[:, X], T.Dg[:, X], T.P0[:, X], MAX, k("Dg", "P0a", "P0b", "P0c", "P0d"), k("Sel"))
            idv = T.Sel[:, sl(0)]
            cp(T.ls[:, X], T.Sel[:, X], k("Sel"), k("ls"))
            if EARLY[s]:
                gtt(T.hE[:, K], T.P0[:, sl(0)], l1, T.mof[:], MAX, k("P0a") + ["l1", "mof"], k("hE"))
                gtt(T.E[:, K], T.Dg[:, sl(0)], l1, T.hE[:, K], MAX, k("Dg", "hE") + ["l1"], k("E"))
            else:
                gtt(T.E[:, K], idv, l1, T.msk[:], MUL, k("Sel") + ["l1", "msk"], k("E"))
            tt(T.nb[:, L], cnb, idv, SUB, k("Sel") + ["cnb"], k("nb"))
            act(T.acc[:, L], idv, IDN, k("Sel"), k("acc"), bias=NEAR, scale=-EPS)
            mm(pE[:, 0:128], T.ones[:], (T.Jn if EARLY[s] else T.Jm)[:], True, False, ["ones", "Jm", "Jn"], k("pE"))
            mm(pE[:, 0:128], T.blk[:], T.E[:, K], False, not EARLY[s], ["blk"] + k("E"), k("pE"), True)
            if EARLY[s]:
                mm(pE[:, 0:128], T.ones[:], T.Jm[:], False, True, ["ones", "Jm"], k("pE"))
            for c in range(8):
                o, wdt = 576 * s + 8 * c * (c + 1), 16 * c + 16
                act(T.EQ[:, o:o + wdt], pE[:, 0:wdt], ABS, k("pE", "nb"), k("EQ%d_" % c),
                    bias=T.nb[:, 8 * s + c:8 * s + c + 1])
            ES = slice(576 * s, 576 * s + 576)
            for a, b in ESP[s]:
                lo, hi = 8 * a * (a + 1), 8 * b * (b + 1)
                C = slice(576 * s + lo, 576 * s + hi)
                add("V", cyc((hi - lo) // 2),
                    lambda C=C, lo=lo, hi=hi: V.tensor_tensor_scan(T.ES[:, C], T.rs2[:, lo:hi], T.EQ[:, C], 0.0, MAX, MIN),
                    k(*["EQ%d_" % j for j in range(a, b)]) + ["rs2"], k("ES%d_" % a))
            gtt(T.q2[:, 16 * s:16 * s + 16], T.ES[:, ES], ends, cbot2 if last else cbot, MAX,
                k(*["ES%d_" % a for a, b in ESP[s]]) + ["ends", "cbot", "cbot2"], k("q2"))
            tt(T.lfv[:, L], T.q2[:, 16 * s:16 * s + 8], T.acc[:, L], MIN, k("q2", "acc"), k("lfv"))
            ts(T.lf[:, L], T.lfv[:, L], -1.0 / EPS, NEAR / EPS, MUL, ADD, k("lfv"), k("lf"))
            lk = T.ls[:, sl(2)]
            sga(T.Z[:, K], Y[:, 128 * hb:YW], T.ls[:, sl(1)], k("ls", "Ye") + ["Ye0"] + YT, k("Z"))
            sga(T.kq[:, K], T.KP[:, 0:18], lk, k("ls") + ["KPa", "KPb"], k("kq"))
            gtt(T.aK[:, K], WV, T.ls[:, sl(0)], T.kq[:, K], MUL, k("ls", "kq") + WT, k("aK"))
            gtt(T.bK[:, K], T.OH[:, 0:18], lk, T.Z[:, K], MUL, k("ls", "Z") + ["OHa", "OHb", "OHc"], k("bK"))
            if not last:
                sga(T.Z2[:, K], Y[:, 256:YW], T.ls[:, sl(3)], k("ls") + YT + ["z2"], k("Zb"), scale=z2)
            if ADDP[s]:
                mm(pK[:, 0:128], T.idn[:], T.aK[:, K], True, False, ["idn"] + k("aK"), k("pK"), True)
                mm(pK[:, 0:128], T.idn[:], T.bK[:, K], False, True, ["idn"] + k("bK"), k("pK"), True)
                act(T.NK[:, K], pK[:, 0:128], IDN, k("pK"), NK, bias=128.5 + 15 * 2.0 ** -16, scale=1.0 / 4096.0)
                mm(pU[:, 0:128], T.idn[:], T.aK[:, K], True, False, ["idn"] + k("aK"), k("pU"), True)
                mm(pU[:, 0:128], T.idn[:], T.bK[:, K], False, False, ["idn"] + k("bK"), k("pU"), True)
                if not last:
                    mm(pU[:, 0:128], T.nI12[:], T.Z2[:, K], False, False, ["nI12"] + k("Zb"), k("pU"))
            else:
                tt(T.aK[:, K], T.aK[:, K], T.bK[:, K], ADD, k("aK", "bK"), k("aK"))
                act(T.NK[:, K], T.aK[:, K], IDN, k("aK"), NK, bias=128.5 + 15 * 2.0 ** -16, scale=1.0 / 4096.0)
                if not last:
                    mm(pU[:, 0:128], T.nI12[:], T.Z2[:, K], True, False, ["nI12"] + k("Zb"), k("pU"))
                mm(pU[:, 0:128], T.idn[:], T.aK[:, K], last, False, ["idn"] + k("aK"), k("pU"), True)
            mm(pU[:, 0:128], T.nI12[:], T.NK[:, K], False, True, ["nI12"] + NK, k("pU"))
            act(T.NW[:, K], pU[:, 0:128], IDN, k("pU"), k("NW"), bias=129.0 * 4096.0)
            if not last:
                mm(pT[:, 48:56], T.blk[:], T.Sel[:, sl(4)], True, s == 0, ["blk"] + k("Sel"), k("pT"), True)
                if s == 0:
                    act(T.q4[:, L], pT[:, 48:56], IDN, k("pT"), k("cnt", "q4"), bias=-129.0 / 64.0, scale=-2.0 ** -18,
                        acc=T.cnt[:, c4])
                else:
                    mm(pT[:, 48:49], nI15, T.An[:, 0:1], False, True, ["nI15", "An"], k("pT"))
                    act(T.q4[:, L], pT[:, 48:56], IDN, k("pT") + ["cnt0"], k("cnt", "q4"), bias=T.cnt[:, 0:1],
                        scale=-2.0 ** -15, acc=T.cnt[:, c4])
                    aq = T.go[:, 0:1]
                    act(aq, T.cnt[:, c4], IDN, k("cnt"), ["Aq"], bias=-0.4375, scale=-1.0)
                    act(T.An[:], T.ones[:, 0:40], IDN, k("cnt") + ["Aq", "ones"], ["An"], bias=aq, scale=T.cnt[:, c4])
            yield
            tag[0] = (s, v)
            add("V", 0.06 + 128 * SC * CY, lambda WV=WV: V.tensor_copy(WV.indirect(T.lf[:, L]), T.NW[:, K]),
                k("lf", "NW"), WT)
            yield

    a = len(ops)
    both = [stream(0), stream(1)]
    for step in range(2 * NV):
        for x in both:
            next(x)
    WT = WALL + FILL + ["Wp"]
    for j, q in enumerate("YS"):
        dma(q, T.yteam[64 * j:64 * j + 64, :], W[64 * j:64 * j + 64, TC:TE], 262144, WT, [], 64)
    dma("Y", T.yact[:], W[3:128:16, PL:DT2], 131072, WT, [], 16)
    return bundle(ops, a), None


def bundle(ops, a):
    fixed = set(t for o in ops[:a] if o["k"] == "c" for t in o["w"])
    for o in ops[a:]:
        fixed.difference_update(o["w"])
    out, room = [], 0.0
    for i, o in enumerate(ops):
        p = out[-1] if out else None
        if (o["e"] == "P" and p is not None and p["e"] == "P" and p["w"] == o["w"] and set(o["r"]) - fixed <= set(p["r"])
                and (room + o["x"] <= BUNDLE)):
            p["fs"].append(o["f"])
            p["d"] += o["d"]
            p["r"] = sorted(set(p["r"] + o["r"]))
            room += o["x"]
        else:
            if o["e"] == "P":
                fs = [o["f"]]
                o["fs"] = fs
                o["f"] = lambda fs=fs: [f() for f in fs][-1]
                room = o["x"]
            out.append(o)
    return out


def depend(ops):
    lastw, readers = {}, {}
    deps = []
    for i, o in enumerate(ops):
        d, raw = set(), set()
        for t in o["r"]:
            if t in lastw:
                d.add(lastw[t])
                raw.add(lastw[t])
            if t in PSUM:
                for j in readers.get(t, []):
                    if ops[j]["e"] != o["e"]:
                        d.add(j)
        for t in o["w"]:
            if t in lastw:
                d.add(lastw[t])
                raw.add(lastw[t])
            d.update(readers.get(t, []))
        d.discard(i)
        deps.append(sorted(d))
        o["free"] = set(j for j in d if ops[j]["e"] == o["e"] and o["k"] == ops[j]["k"] == "c"
                        and (o["e"] == "P" or (o["e"] in INORDER and j not in raw)))
        for t in o["r"]:
            readers.setdefault(t, []).append(i)
        for t in o["w"]:
            lastw[t] = i
            readers[t] = []
    return deps


def place(ops, pred, succ, pr, first=None):
    eng, dur, lat, isd = ops
    n = len(eng)
    left = list(pred)
    rdy = list(first) if first else [0.0] * n
    free, cand, low = [0.0] * 5, [[] for e in range(5)], [1e9] * 5
    for i in range(n):
        if left[i] == 0:
            cand[eng[i]].append(i)
            low[eng[i]] = min(low[eng[i]], rdy[i])
    order, bus, t0, t1 = [], 0.0, [0.0] * n, [0.0] * n
    for step in range(n):
        t = 1e9
        for q in range(5):
            x = free[q] if free[q] > low[q] else low[q]
            if x < t:
                t, e = x, q
        c, top, edge = cand[e], -1e9, t + LOOK
        for j in c:
            x = rdy[j]
            if x <= edge:
                x = pr[j] - BETA * (x - t) if x > t else pr[j]
                if x > top:
                    top, i = x, j
        if rdy[i] > t:
            t = rdy[i]
        c.remove(i)
        low[e] = min([rdy[j] for j in c]) if c else 1e9
        f = free[e] = t + dur[i]
        if isd[i]:
            bus = (bus if bus > t + 1.5 else t + 1.5) + lat[i]
            fin = bus + 0.5
        else:
            fin = f + lat[i]
        t0[i], t1[i] = t, fin
        order.append(i)
        for j, w in succ[i]:
            x = f if w < 0 else fin + w
            if x > rdy[j]:
                rdy[j] = x
            left[j] -= 1
            if left[j] == 0:
                q = eng[j]
                cand[q].append(j)
                if rdy[j] < low[q]:
                    low[q] = rdy[j]
    return order, t0, t1


def model(ops, deps, cost):
    eng = ["VSPGY".index(o["e"]) for o in ops]
    waits = [[(j, cost[4] * (cost[12] if eng[j] == eng[i] else 1.0)) for j in deps[i] if j not in o["free"]]
             for i, o in enumerate(ops)]
    return (eng, [o["d"] for o in ops], [o["lat"] for o in ops],
            [o["k"] == "dma" for o in ops]), waits


def replay(m, order, trace=False):
    (eng, dur, lat, isd), waits = m
    free, fin, bus = [0.0] * 5, [0.0] * len(eng), 0.0
    if trace:
        why, last = [None] * len(eng), [None] * 5
        for i in order:
            e = eng[i]
            t = free[e]
            why[i] = None if last[e] is None else (last[e], True)
            for j, w in waits[i]:
                if fin[j] + w > t:
                    t, why[i] = fin[j] + w, (j, False)
            last[e] = i
            f = free[e] = t + dur[i]
            if isd[i]:
                bus = max(bus, t + 1.5) + lat[i]
                fin[i] = bus + 0.5
            else:
                fin[i] = f + lat[i]
        return fin, why
    for i in order:
        e = eng[i]
        t = free[e]
        for j, w in waits[i]:
            x = fin[j] + w
            if x > t:
                t = x
        f = free[e] = t + dur[i]
        if isd[i]:
            bus = (bus if bus > t + 1.5 else t + 1.5) + lat[i]
            fin[i] = bus + 0.5
        else:
            fin[i] = f + lat[i]
    return max(fin)


def schedule(ops, hard, cut, models, lead, seed=0, noise=0.0):
    n = len(ops)

    def worth(order, t1):
        return float(SHARE[0] * np.log(max(t1)) + sum(x * np.log(replay(m, order)) for x, m in zip(SHARE[1:], models[1:])))
    base, waits = models[0]
    behind = [[i - 1] if ops[i].get("soft") else [] for i in range(n)]
    where = {o["w"][0]: i for i, o in enumerate(ops) if o["k"] == "dma" and o["w"]}
    for a, b in zip(LOADS, LOADS[1:]):
        behind[where[b]] = [where[a]]
    deps = [waits[i] + [(j, -1.0) for j in sorted(set(behind[i]) | ops[i]["free"])] for i in range(n)]
    succ = [[] for i in range(n)]
    for i in range(n):
        for j, w in deps[i]:
            succ[j].append((i, w))
    npred, nsucc = [len(d) for d in deps], [len(d) for d in succ]
    pr = [0.0] * n
    rs = np.random.default_rng(seed)
    eng, dur, lat, isd = base
    for i in range(n - 1, -1, -1):
        way = 2.0 + lat[i] if isd[i] else dur[i] + lat[i]
        pr[i] = max([pr[j] + (dur[i] if w < 0 else way + w) for j, w in succ[i]]
                    or [way])
    pr = [x + (lead if o["tag"][0] == 0 else 0.0) for x, o in zip(pr, ops)]
    best, short = None, GAMMA * np.array(dur)
    for rnd in range(ROUNDS):
        order, t0, t1 = place(base, npred, succ, (np.array(pr) - short).tolist())
        if best is None or worth(order, t1) < best[0]:
            best = (worth(order, t1), order, t0, t1, pr)
        pr = place(base, nsucc, deps, (np.array(t1) + noise * rs.random(n) - short).tolist())[2]
    kinds, seen, kind = {}, {}, []
    for i, o in enumerate(ops):
        w = (o["w"] or ["out"])[0]
        key = o["e"] + "".join(c for c in w if c.isalpha())
        seen[key, o["tag"]] = seen.get((key, o["tag"]), 0) + 1
        kind.append(kinds.setdefault((key, seen[key, o["tag"]], o["tag"][1] >= 0, o["tag"][0] if APART else 0), len(kinds)))
    kind = np.array(kind)
    pr = np.array(best[4]) - short
    for rnd in range(CLIMB):
        d = np.zeros(len(kinds))
        for rep in range(int(rs.integers(1, 4))):
            d[rs.integers(len(kinds))] += rs.normal() * rs.choice([0.3, 1.0, 2.0])
        p = pr + d[kind]
        order, t0, t1 = place(base, npred, succ, p.tolist())
        if max(t1) <= max(best[3]) + 1.0:
            x = worth(order, t1)
            if x <= best[0]:
                best = (x, order, t0, t1)
                pr = p
    order = polish(best[1], [set(j for j, w in d) for d in deps], models, rs)
    fin = replay(models[0], order, True)[0]
    for i in range(n):
        ops[i]["t0"], ops[i]["t1"] = fin[i] - (2.0 + lat[i] if isd[i] else dur[i] + lat[i]), fin[i]
    return order, max(fin)


def polish(order, need, models, rs):
    eng = models[0][0][0]
    n = len(eng)

    def rerun(m, new, start, old):
        (eng, dur, lat, isd), waits = m
        fin, gone, busy = old[0][:], old[1][:], old[2][:]
        free, bus, seen = [0.0] * 5, 0.0, set()
        for i in new[start - 1::-1] if start else []:
            if eng[i] not in seen:
                seen.add(eng[i])
                free[eng[i]] = gone[i]
                if len(seen) == 5:
                    break
        if start:
            bus = busy[new[start - 1]]
        for i in new[start:]:
            e = eng[i]
            t = free[e]
            for j, w in waits[i]:
                x = fin[j] + w
                if x > t:
                    t = x
            f = gone[i] = free[e] = t + dur[i]
            if isd[i]:
                bus = (bus if bus > t + 1.5 else t + 1.5) + lat[i]
                fin[i] = bus + 0.5
            else:
                fin[i] = f + lat[i]
            busy[i] = bus
        return fin, gone, busy
    state = [rerun(m, order, 0, ([0.0] * n, [0.0] * n, [0.0] * n)) for m in models]
    ends = [np.log(max(x[0])) for x in state]
    pairs = []
    for rnd in range(SWAPS):
        if not pairs:
            fin, why = replay(models[int(rs.integers(len(models)))], order, True)
            i = int(np.argmax(fin))
            while why[i] is not None:
                j, queue = why[i]
                if queue and j not in need[i]:
                    pairs.append((j, i))
                i = j
            pairs = [pairs[x] for x in rs.permutation(len(pairs))[:40]]
            continue
        a, b = pairs.pop()
        pa, pb = order.index(a), order.index(b)
        if pa > pb or any(eng[x] == eng[a] for x in order[pa + 1:pb]):
            continue
        move, want, queues = [b], set(need[b]), set()
        for x in order[pb - 1:pa:-1]:
            if x in want or eng[x] in queues:
                move.append(x)
                want |= need[x]
                queues.add(eng[x])
        if a in want:
            continue
        taken = set(move)
        new = order[:pa] + move[::-1] + [x for x in order[pa:pb] if x not in taken] + order[pb + 1:]
        trial, loss = [], 0.0
        for m, old, end, x in zip(models, state, ends, SHARE):
            trial.append(rerun(m, new, pa, old))
            loss += x * (np.log(max(trial[-1][0])) - end)
            if loss > 0.002:
                break
        if loss <= 0.0:
            order, state, ends = new, trial, [np.log(max(x[0])) for x in trial]
    return order


def emit(g, T, ops, deps, order):
    Q = {"V": g.vector, "S": g.scalar, "P": g.tensor, "Y": g.sync, "G": g}
    pos, cnt = {}, {}
    for i in order:
        if ops[i]["k"] == "c":
            e = ops[i]["e"]
            cnt[e] = cnt.get(e, 0) + 1
            pos[i] = cnt[e]
    know = {e: {} for e in Q}
    clock, waits, need, prev = {}, {}, set(), []
    for i in order:
        o = ops[i]
        k = know[o["e"]]
        ws, more = [], []
        if o["e"] == "G" and o["k"] == "c":
            more = [j for j in prev if o.get("alone") or ops[j].get("alone")]
            prev = [i]
        for j in sorted(deps[i] + more, key=lambda j: -ops[j]["t1"]):
            p = ops[j]
            if p["k"] == "c":
                if j in o["free"]:
                    continue
                key, val = p["e"], pos[j]
            else:
                key, val = j, 1
            if k.get(key, 0) >= val:
                continue
            ws.append(j)
            need.add(j)
            k[key] = val
            if p["k"] != "rem":
                for a, b in clock[j].items():
                    if k.get(a, 0) < b:
                        k[a] = b
        waits[i] = ws
        clock[i] = dict(k)
    semv, run, nd, fin, sent = {}, {}, 0, [], 0
    for i in order:
        o = ops[i]
        q = Q[o["e"]]
        top = {}
        for j in waits[i]:
            s, val = semv[j]
            top[s] = max(top.get(s, 0), val)
        for s in top:
            q.wait_ge(T.sem[s], top[s])
        ins = o["f"]()
        if o["k"] == "c":
            if i in need:
                s = "c" + o["e"]
                run[s] = run.get(s, 0) + 1
                ins.then_inc(T.sem[s], 1)
                semv[i] = (s, run[s])
        elif o["k"] == "dma":
            s = "d%d" % nd
            nd += 1
            ins.then_inc(T.sem[s], 16)
            semv[i] = (s, 16)
            fin.append(semv[i])
        else:
            semv[i] = o["x"]
            fin.append(semv[i])
            sent += o["x"][1]
    for s in run:
        g.wait_ge(T.sem[s], run[s])
    for s, val in fin:
        g.wait_ge(T.sem[s], val)
    g.wait_ge(T.sem.sent, sent)


ORDER = []


def rank_program(g, core, T, topo):
    rank = T.rank_of(core)
    if rank is None:
        return
    ops, cut = build_ops(g, T, topo, core, rank, COSTS[0])
    deps = depend(ops)
    if not ORDER:
        models = []
        for c in COSTS:
            other = build_ops(g, T, topo, core, rank, c)[0]
            models.append(model(other, depend(other), c))
        order, end = schedule(ops, deps, cut, models, LEAD, SEED, NOISE)
        ORDER.append((order, [o["t1"] for o in ops]))
    for o, t in zip(ops, ORDER[0][1]):
        o["t1"] = t
    emit(g, T, ops, deps, ORDER[0][0])
